import numpy as np, ml_dtypes
CORES = [3,7,11,15,131,135,139,143]
N = 8
BF = ml_dtypes.bfloat16
W, WX, I, B, SH = 2048, 1792, 224, 8, 11
DR, IR, GAP, RO = 6, 12, 4, 4
def parts(rng):
    mid = rng.choice(np.array([0.02, 0.05, 0.15, 0.4]), (N, 8, 1, 1)); e = rng.integers(0, 16, (N, 8, 16, WX)); small = (e * 5) >> 4
    x = np.where(rng.random((N, 8, 1, WX)) < mid, e, np.where(rng.random((N, 8, 1, WX)) < 0.5, small, 11 + small))
    g = np.minimum(np.maximum(rng.integers(1, 10, (N, 8, 1, I)) + rng.integers(-2, 3, (N, 8, 16, I)), 0), 15)
    g = np.where(rng.random((N, 8, 1, I)) < 0.1, rng.integers(0, 16, g.shape), g)
    return x, g, rng.integers(0, W * WX, (N, 8, 16, W)), rng.integers(0, W, (N, 8, 16, I)), rng.integers(0, WX, (N, 8, 16, I))
def pack(x, g, rel, nam, grd):
    return {"xc": np.ascontiguousarray(x.reshape(N, 128, WX)).astype(np.float32).astype(BF), "rel": np.ascontiguousarray(rel.reshape(N, 128, W)).astype(np.int32),
            "nam": np.ascontiguousarray(nam.reshape(N, 128, I)).astype(np.int32), "grd": np.ascontiguousarray(grd.reshape(N, 128, I)).astype(np.int32),
            "lim": np.ascontiguousarray(g.reshape(N, 128, I)).astype(np.float32).astype(BF)}
def setup_inputs(rng):
    return pack(*parts(rng))
def skew(rng, n, shape):
    ex = rng.choice(np.array([1, 3, 6], np.float32), (N, 8, 1, 1))
    return np.minimum((n * rng.random(shape, dtype=np.float32) ** ex).astype(np.int64), n - 1)
def setup_inputs_spread(rng):
    x = np.minimum((16 * rng.random((N, 8, 1, WX), dtype=np.float32) * rng.random((N, 8, 16, WX), dtype=np.float32)).astype(np.int64), 15)
    x = np.where(rng.random((N, 8, 1, WX)) < 0.5, 15 - x, x)
    g = np.minimum((16 * rng.random((N, 8, 1, I)) * rng.random((N, 8, 16, I))).astype(np.int64), 15)
    return pack(x, g, skew(rng, W, (N, 8, 16, W)) + W * skew(rng, WX, (N, 8, 16, W)), skew(rng, W, (N, 8, 16, I)), skew(rng, WX, (N, 8, 16, I)))
def atends(rng, hi, shape, share):
    u = rng.random(shape)
    return np.where(u < 0.5 * share, 0, np.where(u < share, hi, rng.integers(0, hi + 1, shape)))
def kinds(rng, n):
    m = rng.random((N, 8, 1, n)); e = rng.integers(0, 2, (N, 8, 16, n))
    return 15 * np.where(m < 0.25, 0, np.where(m < 0.5, 1, e))
def setup_inputs_ends(rng):
    x = kinds(rng, WX); g = kinds(rng, I); big = W * WX - 1
    u = rng.random((N, 8, 16, W)); two = rng.integers(0, 2, u.shape)
    rel = np.where(u < 0.35, 0, np.where(u < 0.7, big, np.where(u < 0.85, np.where(two == 1, W - 1, W * (WX - 1)), rng.integers(0, W * WX, u.shape))))
    nam = atends(rng, W - 1, (N, 8, 16, I), 0.75); grd = atends(rng, WX - 1, (N, 8, 16, I), 0.75)
    for c in (0, WX - 1):
        x[:, :, :, c] = 15 * rng.integers(0, 2, (N, 8, 16)); x[0, :, :, c] = 0; x[1, :, :, c] = 15; x[N - 1, :, :, c] = 15
    for q in (0, 1, N - 1): grd[q] = (WX - 1) * rng.integers(0, 2, (8, 16, I))
    for q in (1, N - 1):
        turn = (np.arange(16)[None, :, None] + rng.integers(0, 16, (8, 1, I))) & 15
        g[q] = np.where(turn < 8, 0, g[q]); g[q, 7, :, I - 1] = 0; g[q, 0, :, 0] = 0; g[q, 3, :8, I - 1] = 0; g[q, 3, 8:, I - 1] = 15
    for q in range(N):
        if 1 < q < N - 1 or q == 0: g[q, :, :, 0] = 15; g[q, :, :, I - 1] = 15; g[q, :, :, 1] = 0; g[q, :, :, I - 2] = 0
    x[1, 7, :, WX // 2] = 0; grd[1, 7, 15, I - 1] = WX // 2
    for q in range(N):
        rel[q, 7, 15, W - 1] = big; rel[q, 0, 0, 0] = big; rel[q, 7, 15, 0] = 0; nam[q, 0, 0, 0] = 0; nam[q, 7, 15, I - 1] = W - 1; nam[q, 7, 0, I - 1] = W - 1
    return pack(x, g, rel, nam, grd)
def setup_inputs_corners(rng):
    x, g, rel, nam, grd = parts(rng)
    g = rng.integers(0, 15 - GAP, (N, 8, 16, I)); ones = np.arange(16)[:, None]
    ty = np.array([(16, 0), (0, 16), (0, 0), (DR, 16 - DR), (DR - 1, 17 - DR), (0, IR - 1), (0, IR), (DR + 1, 0), (16 - IR, IR), (17 - IR, IR - 1), (DR, 0), (DR - 1, 0)])
    c = np.arange(WX) & (B - 1); which = np.where(c < 8, c, rng.integers(0, 12, (N, 8, WX)))
    over = ty[which, 0][:, :, None, :]; under = ty[which, 1][:, :, None, :]
    role = (ones * (2 * rng.integers(0, 8, (N, 8, 1, WX)) + 1) + rng.integers(0, 16, (N, 8, 1, WX))) & 15
    gg = np.repeat(g, B, axis=3); coin = rng.random(gg.shape) < 0.5
    v = np.where(role < over, np.where(coin, gg + GAP + 1, 15), np.where(role >= 16 - under, np.where(coin, gg, 0), np.where(coin, gg + 1, gg + GAP)))
    ca = (np.arange(I) + rng.integers(0, 10, (N, 8, 1, 1))) % 10; r = rng.integers(0, B, (N, 8, 16, I)); two = rng.integers(0, 2, (N, 8, 16, I))
    cs = np.where(ca == 1, 0, np.where(ca == 2, 1, np.where(ca == 3, 2, r)))
    cs = np.where(ca == 4, np.where(ones == 15, 2, 0), np.where(ca == 5, np.where(ones == 0, 2, two), cs))
    cs = np.where(ca == 6, 3 + (r & 3), np.where(ca == 7, two, np.where(ca == 8, np.where(ones == 15, 0, 1), cs)))
    col = B * np.arange(I) + cs
    for q in range(N):
        for w in range(8):
            o = rng.permutation(WX); x[q, w][:, o] = v[q, w]; grd[q, w] = o[col[q, w]]
    g = np.where(ca == 9, 15, g)
    l = np.arange(W); m = rng.integers(0, 5, rel.shape)
    rel = np.where(m == 0, l + W * np.minimum(l, WX - 1), np.where(m == 1, l + W * (rel >> SH), np.where(m == 2, (W - 1) * rng.integers(0, 2, rel.shape) + W * (WX - 1) * rng.integers(0, 2, rel.shape), rel)))
    nam = np.where(rng.random(nam.shape) < 0.3, (W - 1) * rng.integers(0, 2, nam.shape), nam)
    return pack(x, g, rel, nam, grd)
def setup_inputs_alike(rng):
    x, g, rel, nam, grd = parts(rng)
    grd[:, ::2] = rng.choice(np.array([0, WX - 1, WX // 2, 3]), (N, 4, 16, I)); grd[:, 1] = np.repeat(grd[:, 1, :1], 16, axis=1)
    nam[:, 2] = rng.choice(np.array([0, W - 1]), (N, 16, I)); nam[:, 3] = np.repeat(nam[:, 3, :1], 16, axis=1)
    rel[:, 5] = rng.choice(rng.integers(0, W * WX, 6), (N, 16, W)); rel[:, 7] = np.repeat(rel[:, 7, :1], 16, axis=1)
    x[:, 4] = 4 + GAP + rng.integers(0, 2, (N, 16, WX)); g[:, 4] = rng.choice(np.array([4, 4 + GAP]), (N, 16, I))
    x[N - 1, 4] = rng.integers(5, 5 + GAP, (16, WX)); g[N - 1, 4] = 4
    for q in range(N):
        c = int(rng.choice(np.array([0, WX - 1, WX // 2, 3]))); grd[q, 6] = c; x[q, 6, :, c] = rng.permutation(16)
        grd[q, 7] = rng.permutation(np.arange(16 * I) % WX).reshape(16, I)
    return pack(x, g, rel, nam, grd)
def check_inputs(d):
    bad = []
    for k, hi in (("xc", 15), ("rel", W * WX - 1), ("nam", W - 1), ("grd", WX - 1), ("lim", 15)):
        v = np.asarray(d[k]).astype(np.float64)
        if not (np.min(v) >= 0 and np.max(v) <= hi): bad.append("range of " + k)
        elif np.any(v != np.floor(v)): bad.append("whole numbers of " + k)
    return bad
def reference(xc, rel, nam, grd, lim):
    x = xc.astype(np.float32).astype(np.int32).reshape(N, 8, 16, WX); g = lim.astype(np.float32).astype(np.int32).reshape(N, 8, 16, I)
    tab = rel.reshape(N, 8, 16, W); a = nam.astype(np.int32).reshape(N, 8, 16, I); b = grd.astype(np.int32).reshape(N, 8, 16, I)
    deaths = np.zeros(N, np.int64); wt = (2 * np.arange(16) + 1)[None, :, None]
    for t in range(RO):
        for q in range(N):
            v = np.take_along_axis(x[q], b[q].reshape(8, 1, 16 * I), 2).reshape(8, 16, 16, I)
            gq = g[q][:, :, None, :]
            over = np.sum(v > gq + GAP, axis=1); under = np.sum(v <= gq, axis=1)
            dead = over >= DR + (deaths[q] & 1); imp = ~dead & (under >= IR); und = ~dead & ~imp
            some = np.any(und, axis=1); s = np.argmax(und, axis=1)
            z = np.where(dead, np.take_along_axis(a[q], s[:, None, :], 1), a[q])
            new = np.take_along_axis(tab[q], z, 2)
            vs = np.take_along_axis(v, s[:, None, None, :], 2)[:, :, 0]
            g[q] = np.where(some[:, None, :], np.maximum(g[q], vs), g[q])
            a[q] = np.where(und, a[q], new & (W - 1)); b[q] = np.where(und, b[q], new >> SH)
            deaths[q] = np.sum(dead)
        sent = np.array(g)
        for q in range(N):
            h = sent[(q - 1 - t % (N - 1)) % N]
            if t < RO - 1:
                place = B * np.arange(I) + (np.sum(wt * h, axis=1) & (B - 1))
                place = np.repeat(place[:, None, :], 16, axis=1)
                np.put_along_axis(x[q], place, (np.take_along_axis(x[q], place, 2) + h) >> 1, 2)
            g[q] = np.minimum(sent[q], h + 2)
    return {"yn": a.reshape(N, 128, I).astype(np.float32), "yg": b.reshape(N, 128, I).astype(np.float32), "yl": g.reshape(N, 128, I).astype(np.float32).astype(BF)}

@@ -1,0 +1,359 @@
+import numpy as np
+from concourse.mybir import dt, AluOpType, AxisListType, ActivationFunctionType
+
+I = 224
+WX = 1792
+W = 2048
+RO = 4
+CH = [(0, 80), (80, 160), (160, 224)]
+DG = [(0, 96), (96, 160), (160, 224)]
+
+SB = "sbuf"
+BF, F32, I32, U16 = "bfloat16", "float32", "int32", "uint16"
+SCRATCH = {
+    "x": (SB, [128, WX], BF), "lim0": (SB, [128, I], BF), "grd0": (SB, [128, I], I32), "nam0": (SB, [128, I], I32),
+    "rel0": (SB, [128, W], I32), "mf": (SB, [128, W], F32),
+    "p0": (SB, [128, W], BF), "p1": (SB, [128, W], BF), "p2": (SB, [128, W], BF), "i1": (SB, [128, W], I32), "i2": (SB, [128, W], I32),
+    "wt": (SB, [128, 4 * W], BF),
+    "ku": (SB, [128, I], U16), "lu": (SB, [128, I], U16), "pn": (SB, [128, I], I32), "ki": (SB, [128, I], I32), "li": (SB, [128, I], I32),
+    "d": (SB, [128, 11264], BF), "ov": (SB, [128, 16 * I], BF), "un": (SB, [128, 16 * I], BF), "grep": (SB, [128, 16 * I], BF),
+    "il": (SB, [128, I], F32), "gl": (SB, [128, I], U16), "nf": (SB, [128, 16 * I], F32), "nb": (SB, [128, 16 * I], BF),
+    "gm": (SB, [128, I], BF), "dead": (SB, [128, I], BF), "imp": (SB, [128, I], BF), "hot": (SB, [128, I], "float16"), "hol": (SB, [128, I], BF),
+    "oln": (SB, [128, I], "float16"), "slu": (SB, [128, 14], U16), "llu": (SB, [128, 14], U16),
+    "ya": (SB, [128, I], BF), "w1": (SB, [128, I], F32), "w3": (SB, [128, I], F32),
+    "qi": (SB, [128, 14], I32), "qj": (SB, [128, 14], I32), "qk": (SB, [128, 14], I32), "cu": (SB, [128, 14], U16), "bl": (SB, [128, I], BF),
+    "cnt": (SB, [128, 1], F32), "pi": (SB, [128, 1], I32), "pj": (SB, [128, 1], I32), "thd": (SB, [128, 1], F32),
+    "thb": (SB, [128, 1], F32), "thl": (SB, [128, 1], F32), "kz": (SB, [128, 1], F32), "seg": (SB, [128, 1], F32),
+    "kcol": (SB, [128, 1], F32), "kc16": (SB, [128, 1], F32), "kc8": (SB, [128, 1], F32), "km": (SB, [128, 1], F32), "wcol": (SB, [128, 1], F32),
+    "ones": (SB, [128, I], BF), "half": (SB, [128, I], BF), "onef": (SB, [128, 128], F32),
+    "tri": (SB, [128, 128], BF), "trz": (SB, [128, 128], BF), "idb": (SB, [128, 128], BF), "idf": (SB, [128, 128], "float16"), "nid": (SB, [128, 128], BF),
+    "nbig": (SB, [128, 128], BF),
+    "g8": (SB, [128, 8], BF), "i8": (SB, [128, 8], F32), "k8": (SB, [128, 8], F32), "z32": (SB, [128, 32], F32), "s32": (SB, [128, 32], F32),
+    "q0": (SB, [128, 1], F32), "q1": (SB, [128, 1], F32), "q2": (SB, [128, 1], F32), "q3": (SB, [128, 1], F32),
+    "ib": (SB, [128, 15], F32), "iq": (SB, [128, 14], F32), "bs": (SB, [128, 15], "float16"), "bq": (SB, [128, 14], I32),
+    "cc": (SB, [128, 2048], BF), "cs": (SB, [128, 2048], "float16"), "cw": (SB, [128, 2048], BF), "cf": (SB, [128, 2048], "float16"),
+    "pp": (SB, [128, 2048], BF), "ee": (SB, [128, 2048], F32),
+    "on": (SB, [128, I], F32), "og": (SB, [128, I], F32), "ol": (SB, [128, I], BF),
+}
+for _t in range(RO):
+    SCRATCH["gs%d" % _t] = (SB, [128, I], BF)
+    SCRATCH["h%d" % _t] = (SB, [128, I], BF)
+PSUM = ("po", "pu", "pb", "pl", "pm", "pd", "px", "pg")
+for _b in PSUM:
+    SCRATCH[_b] = ("psum", [128, 512], F32)
+
+SEMAPHORES = ["cv", "ca", "ct", "cg", "sent", "d_x", "d_lim", "d_grd", "d_nam", "d_rel", "d_on", "d_og", "d_ol", "d_wt"]
+SEMAPHORES += ["arr%d" % _t for _t in range(RO)]
+
+
+def rank_program(g, core, T, topo):
+    rank = T.rank_of(core)
+    if rank is None:
+        return
+    A, F, X = AluOpType, ActivationFunctionType, AxisListType.X
+    queue = {"v": g.vector, "a": g.scalar, "t": g.tensor, "g": g, "s": g.sync}
+    count = {q: 0 for q in queue}
+    known = {q: {} for q in queue}
+    wrote, seen = {}, {}
+    dcount = {}
+
+    def need(q, rec):
+        sem, val, snap = rec[1], rec[2], rec[3]
+        if known[q].get(sem, 0) < val:
+            queue[q].wait_ge(T.sem[sem], val)
+            known[q][sem] = val
+            for s in snap:
+                known[q][s] = max(known[q].get(s, 0), snap[s])
+
+    def waits(q, reads, writes):
+        recs = []
+        for k in reads:
+            if k in wrote:
+                recs.append(wrote[k])
+            if k in PSUM:
+                recs += [r for r in seen.get(k, {}).values() if r[0] != q]
+        for k in writes:
+            if k in wrote and (wrote[k][0] != q or (q != "t" and k != "cc")):
+                recs.append(wrote[k])
+            recs += [r for r in seen.get(k, {}).values() if r[0] != q]
+        for r in sorted(recs, key=lambda r: -r[2]):
+            need(q, r)
+
+    def note(rec, reads, writes):
+        for k in reads:
+            seen.setdefault(k, {})[rec[0]] = rec
+        for k in writes:
+            wrote[k] = rec
+            seen[k] = {}
+
+    def op(q, reads, writes, fn):
+        waits(q, reads, writes)
+        ins = fn(queue[q])
+        count[q] += 1
+        ins.then_inc(T.sem["c" + q], 1)
+        snap = dict(known[q])
+        snap["c" + q] = count[q]
+        note((q, "c" + q, count[q], snap), reads, writes)
+
+    def load(q, sem, out, in_, reads, writes):
+        waits(q, reads, writes)
+        queue[q].dma_start(out, in_).then_inc(T.sem[sem], 16)
+        dcount[sem] = dcount.get(sem, 0) + 16
+        snap = dict(known[q])
+        snap[sem] = dcount[sem]
+        note(("dma" + sem, sem, dcount[sem], snap), reads, writes)
+
+    def copy(out, okey, in_, ikeys):
+        op("v", ikeys, [okey], lambda e: e.tensor_copy(out, in_))
+
+    def ts(out, okey, in_, ikeys, s1, s2, op0, op1=None):
+        if op1 is None:
+            op("v", ikeys, [okey], lambda e: e.tensor_scalar(out, in_, s1, None, op0))
+        else:
+            op("v", ikeys, [okey], lambda e: e.tensor_scalar(out, in_, s1, s2, op0, op1))
+
+    def tt(out, okey, a, b, ikeys, o):
+        op("v", ikeys, [okey], lambda e: e.tensor_tensor(out, a, b, o))
+
+    def act(out, okey, in_, ikeys, f=F.Copy, **kw):
+        op("a", ikeys, [okey], lambda e: e.activation(out, in_, f, **kw))
+
+    def mm(bank, a, b, lhs, lkey, rhs, rkey, start, stop):
+        op("t", [lkey, rkey], [bank], lambda e: e.matmul(T[bank][:, a:b], lhs, rhs, start, stop))
+
+    def memset(name, val, key=None):
+        op("v", [], [key or name], lambda e: e.memset(T[name][:], val))
+
+    def select(name, src, pattern, cmp, fill, base, mult):
+        op("g", [src], [name], lambda e: e.affine_select(T[name][:], T[src][:, 0:T[name].shape[1]], pattern, cmp, fill, base, mult))
+
+    def iota(name, pattern, mult):
+        op("g", [], [name], lambda e: e.iota(T[name][:], pattern, 0, mult, allow_small_or_imprecise_dtypes=True))
+
+    def block(name):
+        select(name, name, [[-16, 8], [0, 16]], A.is_ge, 0.0, 0, 1)
+        select(name, name, [[16, 8], [0, 16]], A.is_ge, 0.0, 15, -1)
+
+    def part(name, k):
+        return T[name][:, 128 * k:128 * k + 128]
+
+    def repeat(c, src, bias):
+        a, b = CH[c]
+        act(T.grep[:, 16 * a:16 * b], "grep%d" % c, T[src][:, 0:I].indirect(T.gl[:, a:b]), [src, "gl"], bias=bias)
+
+    def judge(c):
+        a, b = CH[c]
+        tt(T.d[:, 4096 * c:4096 * c + 16 * (b - a)], "d%d" % c, T.x[:, 0:WX].indirect(T.ku[:, a:b]), T.grep[:, 16 * a:16 * b],
+           ["x", "ku", "grep%d" % c], A.subtract)
+
+    def under(c):
+        a, b = CH[c]
+        ts(T.un[:, 16 * a:16 * b], "un%d" % c, T.d[:, 4096 * c:4096 * c + 16 * (b - a)], ["d%d" % c], 0.5, None, A.is_lt)
+
+    def over(c):
+        a, b = CH[c]
+        act(T.ov[:, 16 * a:16 * b], "ov%d" % c, T.d[:, 4096 * c:4096 * c + 16 * (b - a)], ["d%d" % c], F.Sign, bias=-4.5)
+
+    def tally(c, nm):
+        a, b = CH[c]
+        for k in range(16):
+            mm("pu" if nm == "un" else "po", a, b, part("cc", k), "cc", T[nm][:, 16 * a + k:16 * b:16], "%s%d" % (nm, c), k == 0, k == 15)
+
+    def fetch(j):
+        a, b = DG[j]
+        act(T.nb[:, 16 * a:16 * b], "nb%d" % j, T.wt[:, 0:4 * W].indirect(T.lu[:, a:b]), ["wt", "lu"])
+
+    def pick(j):
+        a, b = DG[j]
+        mm("pd", a, b, T.nbig[:], "nbig", T.ones[:, a:b], "ones", True, False)
+        for k in range(16):
+            mm("pd", a, b, part("pp", k), "pp", T.nb[:, 16 * a + k:16 * b:16], "nb%d" % j, False, k == 15)
+
+    def pieces(u):
+        for q in range(4):
+            for v in ((u, 3) if u == 2 else (u,)):
+                load("s", "d_wt", T.wt[v::4, W * q:W * q + W], T["p%d" % u][q::4, :], ["p%d" % u], ["wt%d%d" % (v, q)])
+                wrote["wt"] = wrote["wt%d%d" % (v, q)]
+
+    alld = ["d%d" % c for c in range(len(CH))] + ["dz%d" % c for c in range(len(CH))]
+    late = []
+
+    load("s", "d_grd", T.grd0[:], T.grd[:], [], ["grd0"])
+    load("a", "d_lim", T.lim0[:], T.lim[:], [], ["lim0"])
+    load("s", "d_x", T.x[:], T.xc[:], [], ["x"])
+    load("s", "d_nam", T.nam0[:], T.nam[:], [], ["nam0"])
+    load("s", "d_rel", T.rel0[:], T.rel[:], [], ["rel0"])
+
+    memset("ones", 1.0)
+    memset("tri", 2.0)
+    memset("trz", 1.0)
+    memset("z32", 0.0)
+    memset("s32", 0.0)
+    memset("thd", -5.0)
+    iota("il", [[1, I]], 0)
+    copy(T.gl[:], "gl", T.il[:], ["il"])
+    memset("cc", 0.0, "zero")
+    iota("i8", [[-16, 8]], 1)
+    select("g8", "ones", [[-16, 8]], A.is_ge, 0.0, 0, 1)
+    select("g8", "g8", [[16, 8]], A.is_ge, 0.0, 15, -1)
+    iota("ib", [[4096, 3], [256, 5]], 0)
+    iota("iq", [[128, 14]], 0)
+    select("idb", "ones", [[-1, 128]], A.is_equal, 0.0, 0, 1)
+    select("tri", "tri", [[1, 128]], A.is_gt, 0.0, 0, -1)
+    select("tri", "tri", [[1, 128]], A.not_equal, -1.0, 0, -1)
+    block("tri")
+    select("trz", "trz", [[1, 128]], A.not_equal, -15.0, 0, -1)
+    select("trz", "trz", [[0, 8], [1, 16]], A.is_equal, 0.0, 0, 0)
+    block("trz")
+    for u, w in enumerate((32768.0, 128.0, 1.0)):
+        select("z32", "z32", [[-4, 4], [-16, 8]], A.not_equal, w, -u, 1)
+    for u in (1, 2, 3):
+        select("s32", "s32", [[-4, 4], [-16, 8]], A.not_equal, float(W * u), -u, 1)
+
+    for t in range(RO):
+        last = t == RO - 1
+        h = "h%d" % (t - 1)
+        if t == 0:
+            copy(T.ku[:], "ku", T.grd0[:], ["grd0"])
+            for k in range(16):
+                copy(T.cc[:, 129 * k:128 * k + 128:16], "cc", T.g8[:], ["g8", "zero"])
+            for c in range(len(CH)):
+                repeat(c, "lim0", 0.4375)
+            act(T.pg[:, 0:I], "pg", T.lim0[:], ["lim0"], bias=-192.0)
+        else:
+            tt(T.gm[:], "gm", T[h][:], T.pg[:, 256:256 + I], ["pg", h], A.min)
+            for r in range(16):
+                mm("pl", 32, 46, part("cw", r), "cw", T[h][:, r::16], h, r == 0, r == 15)
+            for c in range(len(CH)):
+                repeat(c, "gm", 2.4375)
+            act(T.pg[:, 0:I], "pg", T.gm[:], ["gm"], bias=-190.0)
+            copy(T.qi[:], "qi", T.pl[:, 32:46], ["pl"])
+            ts(T.qj[:], "qj", T.qi[:], ["qi"], 7, None, A.bitwise_and)
+            tt(T.qk[:], "qk", T.qj[:], T.bq[:], ["qj", "bq"], A.add)
+            copy(T.cu[:], "cu", T.qk[:], ["qk"])
+            tt(T.bl[:], "bl", T.x[:, 0:WX].indirect(T.cu[:]), T[h][:], ["x", "cu", h], A.add)
+            tt(T.x[:, 0:WX].indirect(T.cu[:]), "x", T.bl[:], T.half[:], ["bl", "cu", "half"], A.mult)
+        judge(0)
+        over(0)
+        under(0)
+        if t == 0:
+            tt(T.k8[:], "k8", T.i8[:], T.g8[:], ["i8", "g8"], A.mult)
+            op("v", ["k8"], ["kcol"], lambda e: e.tensor_reduce(T.kcol[:], T.k8[:], X, A.add))
+            op("v", ["s32"], ["seg"], lambda e: e.tensor_reduce(T.seg[:], T.s32[:], X, A.add))
+            ts(T.lu[:], "lu", T.nam0[:], ["nam0", "seg"], T.seg[:], None, A.add)
+            ts(T.kz[:], "kz", T.kcol[:], ["kcol"], 0.5, None, A.is_lt)
+            ts(T.thb[:], "thb", T.kcol[:], ["kcol"], 2.0, -0.5, A.mult, A.add)
+            ts(T.kc16[:], "kc16", T.kcol[:], ["kcol"], 16.0, 2048.0, A.mult, A.add)
+            ts(T.kc8[:], "kc8", T.kcol[:], ["kcol"], 8.0, None, A.mult)
+            ts(T.km[:], "km", T.kcol[:], ["kcol"], -2048.0, None, A.add)
+            ts(T.wcol[:], "wcol", T.kcol[:], ["kcol"], 2.0, 1.0, A.mult, A.add)
+            tt(T.thl[:], "thl", T.thb[:], T.kz[:], ["thb", "kz"], A.subtract)
+            ts(T.bs[:], "bs", T.ib[:], ["ib", "kc16"], T.kc16[:], None, A.add)
+            ts(T.bq[:], "bq", T.iq[:], ["iq", "kc8"], T.kc8[:], None, A.add)
+            for q in range(4):
+                op("v", ["z32"], ["q%d" % q], lambda e, q=q: e.tensor_reduce(T["q%d" % q][:], T.z32[:, 8 * q:8 * q + 8], X, A.add))
+        for fn in late:
+            fn()
+        late = []
+        for c in (1, 2):
+            tally(c - 1, "un")
+            tally(c - 1, "ov")
+            judge(c)
+            over(c)
+            if c == 1:
+                under(1)
+                if t == 0:
+                    for q in range(4):
+                        act(T.pp[:, 512 * q:512 * q + 512], "pp", T.cc[:, 512 * q:512 * q + 512], ["cc", "q%d" % q], scale=T["q%d" % q][:])
+                    act(T.cw[:], "cw", T.cc[:], ["cc", "wcol"], scale=T.wcol[:])
+                    ts(T.p0[:], "p0", T.rel0[:], ["rel0"], 2.0 ** -15, 128.5 + 2.0 ** -16, A.mult, A.add)
+                    pieces(0)
+                    ts(T.i1[:], "i1", T.rel0[:], ["rel0"], 7, 255, A.arith_shift_right, A.bitwise_and)
+                    ts(T.i2[:], "i2", T.rel0[:], ["rel0"], 127, None, A.bitwise_and)
+                    copy(T.p1[:], "p1", T.i1[:], ["i1"])
+                    pieces(1)
+                    copy(T.p2[:], "p2", T.i2[:], ["i2"])
+                    pieces(2)
+        under(2)
+        if t == 0:
+            for c, (a, b) in enumerate(CH):
+                lo = 4096 * c + 2048
+                op("v", [], ["dz%d" % c], lambda e, lo=lo, n=16 * (b - a): e.memset(T.d[:, lo:lo + n], 0.0))
+            copy(T.idf[:], "idf", T.idb[:], ["idb"])
+            tt(T.trz[:], "trz", T.trz[:], T.tri[:], ["trz", "tri"], A.add)
+            ts(T.cs[:], "cs", T.cc[:], ["cc", "km"], T.km[:], None, A.mult)
+            copy(T.cf[:], "cf", T.cc[:], ["cc"])
+        tally(2, "un")
+        tally(2, "ov")
+        for j in range(len(DG)):
+            fetch(j)
+        ts(T.imp[:], "imp", T.pu[:, 0:I], ["pu"], 11.5, None, A.is_gt)
+        ts(T.dead[:], "dead", T.po[:, 0:I], ["po", "thd"], T.thd[:], None, A.is_gt)
+        mm("pb", 0, I, T.trz[:], "trz", T.imp[:], "imp", True, False)
+        mm("pb", 0, I, T.trz[:], "trz", T.dead[:], "dead", False, True)
+        mm("pl", 0, 14, T.idf[:], "idf", T.bs[:, 0:14], "bs", True, False)
+        ts(T.hot[:], "hot", T.pb[:, 0:I], ["pb", "thb"], T.thb[:], None, A.is_gt)
+        for r in range(16):
+            mm("pl", 0, 14, part("cs", r), "cs", T.hot[:, r::16], "hot", False, r == 15)
+        ts(T.hol[:], "hol", T.pb[:, 0:I], ["pb", "thl"], T.thl[:], None, A.is_gt)
+        names = "nam0" if t == 0 else "li"
+        tt(T.oln[:], "oln", T.hol[:], T[names][:], ["hol", names], A.mult)
+        copy(T.slu[:], "slu", T.pl[:, 0:14], ["pl"])
+        ts(T.ya[:], "ya", T.d[:, 0:11264].indirect(T.slu[:]), alld + ["slu"], -0.4375, 192.0, A.max, A.add)
+        gs = "gs%d" % t
+        tt(T[gs][:], gs, T.ya[:], T.pg[:, 0:I], ["ya", "pg"], A.add)
+        dst = T.cores[(rank + 1 + t % 7) % 8]
+        src = T.cores[(rank - 1 - t % 7) % 8]
+        eng = topo.engines(core, dst)[:8]
+        rid, pid = topo.addr(dst, core)
+        waits("g", [gs], [])
+        g.remote_dma(T["h%d" % t][:], T[gs][:], T.sem["arr%d" % t], T.sem.sent, pid, rid, sum(1 << e for e in eng))
+        wrote["h%d" % t] = ("remote", "arr%d" % t, len(topo.engines(src, core)[:8]), {})
+        ts(T.pg[:, 256:256 + I], "pg", T[gs][:], [gs], -2.0, None, A.add)
+        if t == 0:
+            ts(T.nid[:], "nid", T.idb[:], ["idb"], -1.0, None, A.mult)
+            ts(T.ki[:], "ki", T.grd0[:], ["grd0"], 2048.0, None, A.mult)
+            tt(T.pn[:], "pn", T.ki[:], T.nam0[:], ["ki", "nam0"], A.add)
+            memset("onef", 1.0)
+            memset("half", 0.5)
+            ts(T.nbig[:], "nbig", T.idb[:], ["idb"], -129.0 * 32768.0, None, A.mult)
+        for r in range(16):
+            mm("pl", 64, 78, part("cf", r), "cf", T.oln[:, r::16], "oln", r == 0, r == 15)
+        mm("px", 0, I, T.idb[:], "idb", T.ones[:], "ones", True, False)
+        mm("px", 0, I, T.nid[:], "nid", T.dead[:], "dead", False, False)
+        mm("px", 0, I, T.nid[:], "nid", T.imp[:], "imp", False, True)
+        for j in range(len(DG)):
+            pick(j)
+        copy(T.llu[:], "llu", T.pl[:, 64:78], ["pl"])
+        tt(T.px[:, 0:I], "px", T.pn[:], T.px[:, 0:I], ["pn", "px"], A.mult)
+        tt(T.w1[:], "w1", T.rel0[:, 0:W].indirect(T.llu[:]), T.dead[:], ["rel0", "llu", "dead"], A.mult)
+        tt(T.w3[:], "w3", T.w1[:], T.px[:, 0:I], ["w1", "px"], A.add)
+        tt(T.pd[:, 0:I], "pd", T.imp[:], T.pd[:, 0:I], ["imp", "pd"], A.mult)
+        tt(T.pn[:], "pn", T.w3[:], T.pd[:, 0:I], ["w3", "pd"], A.add)
+        ts(T.ki[:], "ki", T.pn[:], ["pn"], 11, None, A.arith_shift_right)
+        if not last:
+            copy(T.ku[:], "ku", T.ki[:], ["ki"])
+            late = [
+                lambda: op("v", ["dead"], ["cnt"], lambda e: e.tensor_reduce(T.cnt[:], T.dead[:], X, A.add)),
+                lambda: ts(T.li[:], "li", T.pn[:], ["pn"], 2047, None, A.bitwise_and),
+                lambda: mm("pm", 0, 1, T.onef[:], "onef", T.cnt[:], "cnt", True, True),
+                lambda: ts(T.lu[:], "lu", T.li[:], ["li", "seg"], T.seg[:], None, A.add),
+                lambda: copy(T.pi[:], "pi", T.pm[:, 0:1], ["pm"]),
+                lambda: ts(T.pj[:], "pj", T.pi[:], ["pi"], 1, None, A.bitwise_and),
+                lambda: ts(T.thd[:], "thd", T.pj[:], ["pj"], 2.0, -5.0, A.mult, A.add)]
+        else:
+            copy(T.og[:], "og", T.ki[:], ["ki"])
+            load("s", "d_og", T.yg[:], T.og[:], ["og"], ["yg"])
+            ts(T.li[:], "li", T.pn[:], ["pn"], 2047, None, A.bitwise_and)
+            copy(T.on[:], "on", T.li[:], ["li"])
+            load("s", "d_on", T.yn[:], T.on[:], ["on"], ["yn"])
+            h = "h%d" % t
+            tt(T.gm[:], "gm", T[h][:], T.pg[:, 256:256 + I], ["pg", h], A.min)
+            ts(T.ol[:], "ol", T.gm[:], ["gm"], 2.0, None, A.add)
+            load("a", "d_ol", T.yl[:], T.ol[:], ["ol"], ["yl"])
+    g.wait_ge(T.sem.sent, sum(len(topo.engines(core, T.cores[(rank + 1 + t % 7) % 8])[:8]) for t in range(RO)))
+    for q in ("v", "a", "t", "g"):
+        if known["g"].get("c" + q, 0) < count[q]:
+            g.wait_ge(T.sem["c" + q], count[q])
+    for s in ("d_on", "d_og", "d_ol"):
+        g.wait_ge(T.sem[s], 16)

@@ -1,48 +1,58 @@
-import numpy as np
+import math
 from concourse.mybir import dt, AluOpType, AxisListType, ActivationFunctionType
 
 I = 224
 WX = 1792
 W = 2048
 RO = 4
-CH = [(0, 80), (80, 160), (160, 224)]
-DG = [(0, 96), (96, 160), (160, 224)]
+JUDGE = [(0, 2), (2, 4), (4, 6), (6, 8), (8, 10), (10, 12), (12, 14), (14, 15), (15, 16)]
+FETCH = [(2 * j, 2 * j + 2) for j in range(8)]
+EARLY = 2
+AMONG = (1, 4)
+AMONG0 = (5,)
+BEFORE_DEAD = 1
+BEFORE_MD = 2
+LH_S = False
+MD_S = False
+ROUND = 1.5 * 2.0 ** 23
+HALF = 1023.5 / 2048
 
 SB = "sbuf"
-BF, F32, I32, U16 = "bfloat16", "float32", "int32", "uint16"
+BF, F32, F16, I32, U16 = "bfloat16", "float32", "float16", "int32", "uint16"
 SCRATCH = {
-    "x": (SB, [128, WX], BF), "lim0": (SB, [128, I], BF), "grd0": (SB, [128, I], I32), "nam0": (SB, [128, I], I32),
-    "rel0": (SB, [128, W], I32), "mf": (SB, [128, W], F32),
-    "p0": (SB, [128, W], BF), "p1": (SB, [128, W], BF), "p2": (SB, [128, W], BF), "i1": (SB, [128, W], I32), "i2": (SB, [128, W], I32),
-    "wt": (SB, [128, 4 * W], BF),
-    "ku": (SB, [128, I], U16), "lu": (SB, [128, I], U16), "pn": (SB, [128, I], I32), "ki": (SB, [128, I], I32), "li": (SB, [128, I], I32),
-    "d": (SB, [128, 11264], BF), "ov": (SB, [128, 16 * I], BF), "un": (SB, [128, 16 * I], BF), "grep": (SB, [128, 16 * I], BF),
-    "il": (SB, [128, I], F32), "gl": (SB, [128, I], U16), "nf": (SB, [128, 16 * I], F32), "nb": (SB, [128, 16 * I], BF),
-    "gm": (SB, [128, I], BF), "dead": (SB, [128, I], BF), "imp": (SB, [128, I], BF), "hot": (SB, [128, I], "float16"), "hol": (SB, [128, I], BF),
-    "oln": (SB, [128, I], "float16"), "slu": (SB, [128, 14], U16), "llu": (SB, [128, 14], U16),
-    "ya": (SB, [128, I], BF), "w1": (SB, [128, I], F32), "w3": (SB, [128, I], F32),
-    "qi": (SB, [128, 14], I32), "qj": (SB, [128, 14], I32), "qk": (SB, [128, 14], I32), "cu": (SB, [128, 14], U16), "bl": (SB, [128, I], BF),
-    "cnt": (SB, [128, 1], F32), "pi": (SB, [128, 1], I32), "pj": (SB, [128, 1], I32), "thd": (SB, [128, 1], F32),
-    "thb": (SB, [128, 1], F32), "thl": (SB, [128, 1], F32), "kz": (SB, [128, 1], F32), "seg": (SB, [128, 1], F32),
-    "kcol": (SB, [128, 1], F32), "kc16": (SB, [128, 1], F32), "kc8": (SB, [128, 1], F32), "km": (SB, [128, 1], F32), "wcol": (SB, [128, 1], F32),
-    "ones": (SB, [128, I], BF), "half": (SB, [128, I], BF), "onef": (SB, [128, 128], F32),
-    "tri": (SB, [128, 128], BF), "trz": (SB, [128, 128], BF), "idb": (SB, [128, 128], BF), "idf": (SB, [128, 128], "float16"), "nid": (SB, [128, 128], BF),
-    "nbig": (SB, [128, 128], BF),
-    "g8": (SB, [128, 8], BF), "i8": (SB, [128, 8], F32), "k8": (SB, [128, 8], F32), "z32": (SB, [128, 32], F32), "s32": (SB, [128, 32], F32),
-    "q0": (SB, [128, 1], F32), "q1": (SB, [128, 1], F32), "q2": (SB, [128, 1], F32), "q3": (SB, [128, 1], F32),
-    "ib": (SB, [128, 15], F32), "iq": (SB, [128, 14], F32), "bs": (SB, [128, 15], "float16"), "bq": (SB, [128, 14], I32),
-    "cc": (SB, [128, 2048], BF), "cs": (SB, [128, 2048], "float16"), "cw": (SB, [128, 2048], BF), "cf": (SB, [128, 2048], "float16"),
-    "pp": (SB, [128, 2048], BF), "ee": (SB, [128, 2048], F32),
+    "x": (SB, [128, 16 + WX], BF), "lim0": (SB, [128, I], BF), "grd0": (SB, [128, I], I32), "nam0": (SB, [128, I], I32),
+    "rel0": (SB, [128, W], I32),
+    "u": (SB, [128, 16 * I], BF), "w": (SB, [128, 16 * I], BF), "nb": (SB, [128, 16 * I], F32),
+    "ku": (SB, [128, I], U16), "lu": (SB, [128, I], U16), "tp": (SB, [128, 480], F32), "tq": (SB, [128, 480], F32),
+    "kt": (SB, [128, I], F32), "lt": (SB, [128, I], F32), "k16": (SB, [128, I], F16), "l16": (SB, [128, I], F16),
+    "gj": (SB, [128, 2 * I], F32), "gr": (SB, [128, I], BF), "rl": (SB, [128, I], BF), "hp": (SB, [128, I], F32),
+    "b": (SB, [128, I], BF), "und": (SB, [128, I], BF), "dead": (SB, [128, I], BF),
+    "kh": (SB, [128, I], F16), "lh": (SB, [128, 2 * I], F16), "sk": (SB, [128, I], F32), "sl": (SB, [128, I], F32),
+    "ks": (SB, [128, 14], U16), "ls": (SB, [128, 14], U16), "cu": (SB, [128, 14], U16),
+    "f8": (SB, [128, 14], BF), "z": (SB, [128, 14], F32), "bm": (SB, [128, 14], F32), "bl": (SB, [128, I], BF), "b2": (SB, [128, I], BF),
+    "md": (SB, [128, I], F32), "mo": (SB, [128, I], F32), "t1": (SB, [128, I], F32), "t2": (SB, [128, I], F32),
+    "cnt": (SB, [128, 1], F32), "pi": (SB, [128, 1], I32), "pj": (SB, [128, 1], I32), "thr": (SB, [128, 1], F32),
+    "ip": (SB, [128, 1], I32), "c1": (SB, [128, 1], I32), "c2": (SB, [128, 1], I32), "c3": (SB, [128, 1], I32),
+    "c4": (SB, [128, 1], I32), "c5": (SB, [128, 1], I32), "c6": (SB, [128, 1], I32),
+    "g16": (SB, [128, 1], F32), "par": (SB, [128, 1], F32), "rc": (SB, [128, 1], F32), "wc": (SB, [128, 1], F32), "kz": (SB, [128, 1], F32),
+    "ff": (SB, [128, 14], F32), "f": (SB, [128, 14], F32), "fk": (SB, [128, 14], I32), "a1": (SB, [128, 14], F32),
+    "a2": (SB, [128, 14], F32), "a3": (SB, [128, 14], F32), "sel": (SB, [128, 14], U16), "base": (SB, [128, 14], BF),
+    "t16": (SB, [128, I], BF), "mk": (SB, [128, I], BF), "rs": (SB, [128, I], BF),
+    "cm": (SB, [128, I], BF), "cn": (SB, [128, 2 * I + 2], BF), "ch": (SB, [128, 2 * I], F16),
+    "ones": (SB, [128, 128], BF), "onef": (SB, [128, 128], F32), "idb": (SB, [128, 128], BF), "idh": (SB, [128, 128], F16),
+    "idl": (SB, [128, 128], F16), "id0": (SB, [128, 128], F16), "idx": (SB, [128, 128], BF), "idn": (SB, [128, 128], BF),
+    "bd": (SB, [128, 128], BF), "bdh": (SB, [128, 128], F16), "nbk": (SB, [128, 128], BF), "low": (SB, [128, 128], BF),
+    "tr": (SB, [128, 128], BF), "zz": (SB, [128, 144], BF), "zw": (SB, [128, 144], BF),
     "on": (SB, [128, I], F32), "og": (SB, [128, I], F32), "ol": (SB, [128, I], BF),
 }
 for _t in range(RO):
     SCRATCH["gs%d" % _t] = (SB, [128, I], BF)
     SCRATCH["h%d" % _t] = (SB, [128, I], BF)
-PSUM = ("po", "pu", "pb", "pl", "pm", "pd", "px", "pg")
+PSUM = ("pa", "pv", "pe", "pk", "pf", "pl", "pm", "pg")
 for _b in PSUM:
     SCRATCH[_b] = ("psum", [128, 512], F32)
 
-SEMAPHORES = ["cv", "ca", "ct", "cg", "sent", "d_x", "d_lim", "d_grd", "d_nam", "d_rel", "d_on", "d_og", "d_ol", "d_wt"]
+SEMAPHORES = ["cv", "ca", "ct", "cg", "sent", "d_x", "d_lim", "d_grd", "d_nam", "d_rel", "d_on", "d_og", "d_ol", "d_mo"]
 SEMAPHORES += ["arr%d" % _t for _t in range(RO)]
 
 
@@ -50,7 +60,7 @@ def rank_program(g, core, T, topo):
     rank = T.rank_of(core)
     if rank is None:
         return
-    A, F, X = AluOpType, ActivationFunctionType, AxisListType.X
+    A, F = AluOpType, ActivationFunctionType
     queue = {"v": g.vector, "a": g.scalar, "t": g.tensor, "g": g, "s": g.sync}
     count = {q: 0 for q in queue}
     known = {q: {} for q in queue}
@@ -73,7 +83,7 @@ def rank_program(g, core, T, topo):
             if k in PSUM:
                 recs += [r for r in seen.get(k, {}).values() if r[0] != q]
         for k in writes:
-            if k in wrote and (wrote[k][0] != q or (q != "t" and k != "cc")):
+            if k in wrote and (wrote[k][0] != q or q != "t"):
                 recs.append(wrote[k])
             recs += [r for r in seen.get(k, {}).values() if r[0] != q]
         for r in sorted(recs, key=lambda r: -r[2]):
@@ -116,192 +126,182 @@ def rank_program(g, core, T, topo):
         op("v", ikeys, [okey], lambda e: e.tensor_tensor(out, a, b, o))
 
     def act(out, okey, in_, ikeys, f=F.Copy, **kw):
-        op("a", ikeys, [okey], lambda e: e.activation(out, in_, f, **kw))
+        op("a", ikeys, okey if isinstance(okey, list) else [okey], lambda e: e.activation(out, in_, f, **kw))
 
-    def mm(bank, a, b, lhs, lkey, rhs, rkey, start, stop):
-        op("t", [lkey, rkey], [bank], lambda e: e.matmul(T[bank][:, a:b], lhs, rhs, start, stop))
+    def mm(bank, a, lkey, rhs, rkey, n, start, stop, lhs=None):
+        op("t", [lkey, rkey], [bank], lambda e: e.matmul(T[bank][:, a:a + n], T[lkey][:] if lhs is None else lhs, rhs, start, stop))
 
-    def memset(name, val, key=None):
-        op("v", [], [key or name], lambda e: e.memset(T[name][:], val))
+    def memset(ap, key, val):
+        op("v", [], [key], lambda e: e.memset(ap, val))
 
     def select(name, src, pattern, cmp, fill, base, mult):
-        op("g", [src], [name], lambda e: e.affine_select(T[name][:], T[src][:, 0:T[name].shape[1]], pattern, cmp, fill, base, mult))
+        op("g", [src], [name], lambda e: e.affine_select(T[name][:], T[src][:], pattern, cmp, fill, base, mult))
 
     def iota(name, pattern, mult):
         op("g", [], [name], lambda e: e.iota(T[name][:], pattern, 0, mult, allow_small_or_imprecise_dtypes=True))
 
-    def block(name):
-        select(name, name, [[-16, 8], [0, 16]], A.is_ge, 0.0, 0, 1)
-        select(name, name, [[16, 8], [0, 16]], A.is_ge, 0.0, 15, -1)
+    pa, pn = T.pv[:, 0:I], T.pv[:, 272:272 + I]
 
-    def part(name, k):
-        return T[name][:, 128 * k:128 * k + 128]
+    def turn(dst):
+        op("v", ["pn"], [dst + "0"], lambda e: e.transpose(T[dst][:, 0:I], pn))
+        op("v", ["pn", "pad"], [dst + "1"], lambda e: e.transpose(T[dst][:, I:480], T.pv[:, 256:512]))
 
-    def repeat(c, src, bias):
-        a, b = CH[c]
-        act(T.grep[:, 16 * a:16 * b], "grep%d" % c, T[src][:, 0:I].indirect(T.gl[:, a:b]), [src, "gl"], bias=bias)
+    def diagonal(bank, out):
+        op("v", [bank, "rs"], [out], lambda e: e.tensor_tensor_scan(T[out][:], T.rs[:], T[bank][:, 0:I], 0.0, A.mult, A.max))
 
-    def judge(c):
-        a, b = CH[c]
-        tt(T.d[:, 4096 * c:4096 * c + 16 * (b - a)], "d%d" % c, T.x[:, 0:WX].indirect(T.ku[:, a:b]), T.grep[:, 16 * a:16 * b],
-           ["x", "ku", "grep%d" % c], A.subtract)
+    def judge(j):
+        a, b = JUDGE[j]
+        tt(T.u[:, I * a:I * b], "u%d" % j, T.x[:, 16:16 + WX].indirect(T.ku[:, 14 * a:14 * b]), T.gj[:, 0:I * (b - a)],
+           ["x", "ku", "gj0", "gj1"], A.subtract)
 
-    def under(c):
-        a, b = CH[c]
-        ts(T.un[:, 16 * a:16 * b], "un%d" % c, T.d[:, 4096 * c:4096 * c + 16 * (b - a)], ["d%d" % c], 0.5, None, A.is_lt)
+    def mark(j):
+        a, b = JUDGE[j]
+        act(T.w[:, I * a:I * b], "w%d" % j, T.u[:, I * a:I * b], ["u%d" % j], F.Sigmoid, scale=4.0, bias=-4.0 * 644 - math.log(32.0))
+        for k in range(a, b):
+            mm("pa", 0, "zz", T.w[:, I * k:I * k + I], "w%d" % j, I, k == 0, k == 15, lhs=T.zz[:, 15 - k:143 - k])
 
-    def over(c):
-        a, b = CH[c]
-        act(T.ov[:, 16 * a:16 * b], "ov%d" % c, T.d[:, 4096 * c:4096 * c + 16 * (b - a)], ["d%d" % c], F.Sign, bias=-4.5)
+    fetched = [0]
 
-    def tally(c, nm):
-        a, b = CH[c]
-        for k in range(16):
-            mm("pu" if nm == "un" else "po", a, b, part("cc", k), "cc", T[nm][:, 16 * a + k:16 * b:16], "%s%d" % (nm, c), k == 0, k == 15)
+    def fetch(n):
+        for j in range(fetched[0], min(fetched[0] + n, len(FETCH))):
+            a, b = FETCH[j]
+            act(T.nb[:, I * a:I * b], "nb%d" % j, T.rel0[:, 0:W].indirect(T.lu[:, 14 * a:14 * b]), ["rel0", "lu"], scale=1.0 / 2048, bias=-HALF)
+            for k in range(a, b):
+                load("s", "d_mo", T.mo[k::16, :], T.nb[k::16, I * k:I * k + I], ["nb%d" % j], ["mo%d" % k])
+            fetched[0] = j + 1
 
-    def fetch(j):
-        a, b = DG[j]
-        act(T.nb[:, 16 * a:16 * b], "nb%d" % j, T.wt[:, 0:4 * W].indirect(T.lu[:, a:b]), ["wt", "lu"])
+    def limits(src, key):
+        for c in range(2):
+            act(T.gj[:, I * c:I * c + I], "gj%d" % c, src, [key], bias=-641.5)
 
-    def pick(j):
-        a, b = DG[j]
-        mm("pd", a, b, T.nbig[:], "nbig", T.ones[:, a:b], "ones", True, False)
-        for k in range(16):
-            mm("pd", a, b, part("pp", k), "pp", T.nb[:, 16 * a + k:16 * b:16], "nb%d" % j, False, k == 15)
+    def lower(h):
+        mm("pg", 0, "idn", T[h][:], h, I, False, True)
+        act(T.rl[:], "rl", T.pg[:, 0:I], ["pg"], F.Relu, bias=-2.0)
 
-    def pieces(u):
-        for q in range(4):
-            for v in ((u, 3) if u == 2 else (u,)):
-                load("s", "d_wt", T.wt[v::4, W * q:W * q + W], T["p%d" % u][q::4, :], ["p%d" % u], ["wt%d%d" % (v, q)])
-                wrote["wt"] = wrote["wt%d%d" % (v, q)]
+    def lowered(gs):
+        mm("pg", 0, "idb", T[gs][:], gs, I, True, False)
+        mm("pg", 0, "idn", T.rl[:], "rl", I, False, True)
 
-    alld = ["d%d" % c for c in range(len(CH))] + ["dz%d" % c for c in range(len(CH))]
-    late = []
+    allmo = ["mo%d" % k for k in range(16)]
 
     load("s", "d_grd", T.grd0[:], T.grd[:], [], ["grd0"])
     load("a", "d_lim", T.lim0[:], T.lim[:], [], ["lim0"])
-    load("s", "d_x", T.x[:], T.xc[:], [], ["x"])
-    load("s", "d_nam", T.nam0[:], T.nam[:], [], ["nam0"])
+    load("s", "d_x", T.x[:, 16:16 + WX], T.xc[:], [], ["x"])
+    load("a", "d_nam", T.nam0[:], T.nam[:], [], ["nam0"])
     load("s", "d_rel", T.rel0[:], T.rel[:], [], ["rel0"])
 
-    memset("ones", 1.0)
-    memset("tri", 2.0)
-    memset("trz", 1.0)
-    memset("z32", 0.0)
-    memset("s32", 0.0)
-    memset("thd", -5.0)
-    iota("il", [[1, I]], 0)
-    copy(T.gl[:], "gl", T.il[:], ["il"])
-    memset("cc", 0.0, "zero")
-    iota("i8", [[-16, 8]], 1)
-    select("g8", "ones", [[-16, 8]], A.is_ge, 0.0, 0, 1)
-    select("g8", "g8", [[16, 8]], A.is_ge, 0.0, 15, -1)
-    iota("ib", [[4096, 3], [256, 5]], 0)
-    iota("iq", [[128, 14]], 0)
+    iota("ip", [[0, 1]], 1)
+    iota("ff", [[16, 14]], 1)
+    memset(T.ones[:], "ones", 1.0)
+    memset(T.pv[:, 256:512], "pad", 0.0)
+    memset(T.zz[:], "zz", 0.0)
+    memset(T.x[:, 0:16], "xz", 0.0)
+    select("bd", "ones", [[-16, 8], [0, 16]], A.is_ge, 0.0, 0, 1)
+    select("bd", "bd", [[16, 8], [0, 16]], A.is_ge, 0.0, 15, -1)
+    iota("t16", [[0, 14], [1, 16]], 0)
     select("idb", "ones", [[-1, 128]], A.is_equal, 0.0, 0, 1)
-    select("tri", "tri", [[1, 128]], A.is_gt, 0.0, 0, -1)
-    select("tri", "tri", [[1, 128]], A.not_equal, -1.0, 0, -1)
-    block("tri")
-    select("trz", "trz", [[1, 128]], A.not_equal, -15.0, 0, -1)
-    select("trz", "trz", [[0, 8], [1, 16]], A.is_equal, 0.0, 0, 0)
-    block("trz")
-    for u, w in enumerate((32768.0, 128.0, 1.0)):
-        select("z32", "z32", [[-4, 4], [-16, 8]], A.not_equal, w, -u, 1)
-    for u in (1, 2, 3):
-        select("s32", "s32", [[-4, 4], [-16, 8]], A.not_equal, float(W * u), -u, 1)
+    select("low", "bd", [[1, 128]], A.is_gt, 0.0, 0, -1)
+    ts(T.c1[:], "c1", T.ip[:], ["ip"], 112, None, A.bitwise_and)
+    ts(T.c2[:], "c2", T.ip[:], ["ip"], 4, None, A.arith_shift_right)
+    copy(T.g16[:], "g16", T.c1[:], ["c1"])
+    tt(T.c3[:], "c3", T.c2[:], T.ip[:], ["c2", "ip"], A.add)
+    ts(T.f[:], "f", T.ff[:], ["ff", "g16"], T.g16[:], None, A.subtract)
+    ts(T.c4[:], "c4", T.c3[:], ["c3"], 1, None, A.bitwise_and)
+    ts(T.fk[:], "fk", T.f[:], ["f"], 1.0 / 14, -13.0 / 28, A.mult, A.add)
+    ts(T.par[:], "par", T.c4[:], ["c4"], 240.0, None, A.mult)
+    ts(T.a2[:], "a2", T.f[:], ["f"], 16.0, None, A.mult)
+    ts(T.a1[:], "a1", T.fk[:], ["fk", "par"], -223.0, T.par[:], A.mult, A.add)
+    tt(T.a3[:], "a3", T.a1[:], T.a2[:], ["a1", "a2"], A.add)
+    copy(T.sel[:], "sel", T.a3[:], ["a3"])
+    wrote["pn"] = wrote["pad"]
+    memset(T.thr[:], "thr", 192 + 4100.5)
+    memset(T.ch[:, 0:I], "ch0", 0.0)
+    memset(T.ch[:, I:2 * I], "ch", 2.0)
+    memset(T.cm[:], "cm", -4096.0)
+    memset(T.cn[:, 0:I], "cn0", -2.0 ** 24)
+    memset(T.cn[:, I:2 * I + 2], "cn", 0.0)
+    memset(T.onef[:], "onef", 1.0)
+    memset(T.zw[:], "zw", 0.0)
+    ts(T.c5[:], "c5", T.ip[:], ["ip"], 15, None, A.bitwise_and)
+    ts(T.c6[:], "c6", T.ip[:], ["ip"], 3, None, A.bitwise_and)
+    ts(T.base[:], "base", T.f[:], ["f"], 8.0, None, A.mult)
+    ts(T.bm[:], "bm", T.f[:], ["f"], 8.0, -1028.5, A.mult, A.add)
+    copy(T.rc[:], "rc", T.c5[:], ["c5"])
+    ts(T.wc[:], "wc", T.c6[:], ["c6"], 2.0, 1.0, A.mult, A.add)
+    ts(T.kz[:], "kz", T.c5[:], ["c5"], 0.5, 2048.0, A.is_lt, A.mult)
 
     for t in range(RO):
         last = t == RO - 1
         h = "h%d" % (t - 1)
+        fetched[0] = 0
         if t == 0:
-            copy(T.ku[:], "ku", T.grd0[:], ["grd0"])
-            for k in range(16):
-                copy(T.cc[:, 129 * k:128 * k + 128:16], "cc", T.g8[:], ["g8", "zero"])
-            for c in range(len(CH)):
-                repeat(c, "lim0", 0.4375)
-            act(T.pg[:, 0:I], "pg", T.lim0[:], ["lim0"], bias=-192.0)
+            copy(pn, "pn", T.grd0[:], ["grd0"])
+            turn("tp")
+            copy(T.ku[:], "ku", T.tp[:, 0:480].indirect(T.sel[:]), ["tp0", "tp1", "sel"])
+            limits(T.lim0[:], "lim0")
+            ts(T.zz[:, 15:143:16], "zz", T.bd[:, 0:128:16], ["bd"], -33.0, None, A.mult)
+            copy(pn, "pn", T.nam0[:], ["nam0"])
+            turn("tq")
+            copy(T.lu[:], "lu", T.tq[:, 0:480].indirect(T.sel[:]), ["tq0", "tq1", "sel"])
+            ts(T.mk[:], "mk", T.t16[:], ["t16", "rc"], T.rc[:], -16384.0, A.not_equal, A.mult)
+            ts(T.id0[:], "id0", T.idb[:], ["idb", "kz"], T.kz[:], None, A.mult)
+            act(T.idx[:], "idx", T.idb[:], ["idb"], scale=4096.0)
+            act(T.idn[:], "idn", T.idb[:], ["idb"], scale=-1.0)
+            act(T.nbk[:], "nbk", T.bd[:], ["bd"], scale=-4096.0)
+            act(T.low[:], "low", T.low[:], ["low"], scale=-4096.0)
+            act(T.zw[:, 15:143:16], "zw", T.bd[:, 0:128:16], ["bd", "wc"], scale=T.wc[:])
         else:
-            tt(T.gm[:], "gm", T[h][:], T.pg[:, 256:256 + I], ["pg", h], A.min)
-            for r in range(16):
-                mm("pl", 32, 46, part("cw", r), "cw", T[h][:, r::16], h, r == 0, r == 15)
-            for c in range(len(CH)):
-                repeat(c, "gm", 2.4375)
-            act(T.pg[:, 0:I], "pg", T.gm[:], ["gm"], bias=-190.0)
-            copy(T.qi[:], "qi", T.pl[:, 32:46], ["pl"])
-            ts(T.qj[:], "qj", T.qi[:], ["qi"], 7, None, A.bitwise_and)
-            tt(T.qk[:], "qk", T.qj[:], T.bq[:], ["qj", "bq"], A.add)
-            copy(T.cu[:], "cu", T.qk[:], ["qk"])
-            tt(T.bl[:], "bl", T.x[:, 0:WX].indirect(T.cu[:]), T[h][:], ["x", "cu", h], A.add)
-            tt(T.x[:, 0:WX].indirect(T.cu[:]), "x", T.bl[:], T.half[:], ["bl", "cu", "half"], A.mult)
-        judge(0)
-        over(0)
-        under(0)
+            fetch(EARLY)
+            tt(T.bl[:], "bl", T.x[:, 16:16 + WX].indirect(T.cu[:]), T.hp[:], ["x", "cu", "hp"], A.add)
+            ts(T.b2[:], "b2", T.bl[:], ["bl"], -288.0, 0.5, A.add, A.mult)
+            copy(T.x[:, 16:16 + WX].indirect(T.cu[:]), "x", T.b2[:], ["b2", "cu"])
+        for j in range(len(JUDGE)):
+            judge(j)
+            mark(j)
+            if j in (AMONG if t > 0 else AMONG0):
+                fetch(1)
+            if j == 1:
+                mm("pk", 0, "idb", T.mk[:], "mk", I, True, False)
+                mm("pl", 0, "idb", T.mk[:], "mk", I, True, False)
+                mm("pf", 0, "id0", T.ch[:], "ch", 2 * I, True, False)
+                mm("pm", 0, "idb", T.cm[:], "cm", I, True, False)
         if t == 0:
-            tt(T.k8[:], "k8", T.i8[:], T.g8[:], ["i8", "g8"], A.mult)
-            op("v", ["k8"], ["kcol"], lambda e: e.tensor_reduce(T.kcol[:], T.k8[:], X, A.add))
-            op("v", ["s32"], ["seg"], lambda e: e.tensor_reduce(T.seg[:], T.s32[:], X, A.add))
-            ts(T.lu[:], "lu", T.nam0[:], ["nam0", "seg"], T.seg[:], None, A.add)
-            ts(T.kz[:], "kz", T.kcol[:], ["kcol"], 0.5, None, A.is_lt)
-            ts(T.thb[:], "thb", T.kcol[:], ["kcol"], 2.0, -0.5, A.mult, A.add)
-            ts(T.kc16[:], "kc16", T.kcol[:], ["kcol"], 16.0, 2048.0, A.mult, A.add)
-            ts(T.kc8[:], "kc8", T.kcol[:], ["kcol"], 8.0, None, A.mult)
-            ts(T.km[:], "km", T.kcol[:], ["kcol"], -2048.0, None, A.add)
-            ts(T.wcol[:], "wcol", T.kcol[:], ["kcol"], 2.0, 1.0, A.mult, A.add)
-            tt(T.thl[:], "thl", T.thb[:], T.kz[:], ["thb", "kz"], A.subtract)
-            ts(T.bs[:], "bs", T.ib[:], ["ib", "kc16"], T.kc16[:], None, A.add)
-            ts(T.bq[:], "bq", T.iq[:], ["iq", "kc8"], T.kc8[:], None, A.add)
-            for q in range(4):
-                op("v", ["z32"], ["q%d" % q], lambda e, q=q: e.tensor_reduce(T["q%d" % q][:], T.z32[:, 8 * q:8 * q + 8], X, A.add))
-        for fn in late:
-            fn()
-        late = []
-        for c in (1, 2):
-            tally(c - 1, "un")
-            tally(c - 1, "ov")
-            judge(c)
-            over(c)
-            if c == 1:
-                under(1)
-                if t == 0:
-                    for q in range(4):
-                        act(T.pp[:, 512 * q:512 * q + 512], "pp", T.cc[:, 512 * q:512 * q + 512], ["cc", "q%d" % q], scale=T["q%d" % q][:])
-                    act(T.cw[:], "cw", T.cc[:], ["cc", "wcol"], scale=T.wcol[:])
-                    ts(T.p0[:], "p0", T.rel0[:], ["rel0"], 2.0 ** -15, 128.5 + 2.0 ** -16, A.mult, A.add)
-                    pieces(0)
-                    ts(T.i1[:], "i1", T.rel0[:], ["rel0"], 7, 255, A.arith_shift_right, A.bitwise_and)
-                    ts(T.i2[:], "i2", T.rel0[:], ["rel0"], 127, None, A.bitwise_and)
-                    copy(T.p1[:], "p1", T.i1[:], ["i1"])
-                    pieces(1)
-                    copy(T.p2[:], "p2", T.i2[:], ["i2"])
-                    pieces(2)
-        under(2)
-        if t == 0:
-            for c, (a, b) in enumerate(CH):
-                lo = 4096 * c + 2048
-                op("v", [], ["dz%d" % c], lambda e, lo=lo, n=16 * (b - a): e.memset(T.d[:, lo:lo + n], 0.0))
-            copy(T.idf[:], "idf", T.idb[:], ["idb"])
-            tt(T.trz[:], "trz", T.trz[:], T.tri[:], ["trz", "tri"], A.add)
-            ts(T.cs[:], "cs", T.cc[:], ["cc", "km"], T.km[:], None, A.mult)
-            copy(T.cf[:], "cf", T.cc[:], ["cc"])
-        tally(2, "un")
-        tally(2, "ov")
-        for j in range(len(DG)):
-            fetch(j)
-        ts(T.imp[:], "imp", T.pu[:, 0:I], ["pu"], 11.5, None, A.is_gt)
-        ts(T.dead[:], "dead", T.po[:, 0:I], ["po", "thd"], T.thd[:], None, A.is_gt)
-        mm("pb", 0, I, T.trz[:], "trz", T.imp[:], "imp", True, False)
-        mm("pb", 0, I, T.trz[:], "trz", T.dead[:], "dead", False, True)
-        mm("pl", 0, 14, T.idf[:], "idf", T.bs[:, 0:14], "bs", True, False)
-        ts(T.hot[:], "hot", T.pb[:, 0:I], ["pb", "thb"], T.thb[:], None, A.is_gt)
-        for r in range(16):
-            mm("pl", 0, 14, part("cs", r), "cs", T.hot[:, r::16], "hot", False, r == 15)
-        ts(T.hol[:], "hol", T.pb[:, 0:I], ["pb", "thl"], T.thl[:], None, A.is_gt)
-        names = "nam0" if t == 0 else "li"
-        tt(T.oln[:], "oln", T.hol[:], T[names][:], ["hol", names], A.mult)
-        copy(T.slu[:], "slu", T.pl[:, 0:14], ["pl"])
-        ts(T.ya[:], "ya", T.d[:, 0:11264].indirect(T.slu[:]), alld + ["slu"], -0.4375, 192.0, A.max, A.add)
-        gs = "gs%d" % t
-        tt(T[gs][:], gs, T.ya[:], T.pg[:, 0:I], ["ya", "pg"], A.add)
+            copy(T.k16[:], "k16", T.grd0[:], ["grd0"])
+            copy(T.idh[:], "idh", T.idb[:], ["idb"])
+            ts(T.l16[:], "l16", T.nam0[:], ["nam0"], 1.0 / 2048, -HALF, A.mult, A.add)
+            ts(T.idl[:], "idl", T.idb[:], ["idb"], 2048.0, None, A.mult)
+            tt(T.tr[:], "tr", T.low[:], T.idx[:], ["low", "idx"], A.add)
+            copy(T.bdh[:], "bdh", T.bd[:], ["bd"])
+            ts(T.rs[:], "rs", T.t16[:], ["t16"], 0.5, None, A.is_gt)
+        else:
+            ts(T.k16[:], "k16", pn, ["pn"], ROUND, -ROUND, A.add, A.add)
+            copy(T.pi[:], "pi", T.pe[:, 448:449], ["pe"])
+            tt(T.l16[:], "l16", pn, T.k16[:], ["pn", "k16"], A.subtract)
+            ts(T.pj[:], "pj", T.pi[:], ["pi"], 1, None, A.bitwise_and)
+            ts(T.thr[:], "thr", T.pj[:], ["pj"], 32.0, 192 + 4100.5, A.mult, A.add)
+        fetch(BEFORE_DEAD)
+        mm("pe", 0, "idh", T.k16[:], "k16", I, True, False)
+        mm("pf", 0, "idl", T.l16[:], "l16", I, False, False)
+        mm("pf", I, "id0", T.l16[:], "l16", I, False, False)
+        ts(pa, "a", T.pa[:, 0:I], ["pa", "thr"], T.thr[:], 4100.5, A.add, A.max)
+        ts(T.b[:], "b", pa, ["a"], 3.5, None, A.add)
+        tt(T.und[:], "und", pa, T.b[:], ["a", "b"], A.is_lt)
+        act(T.dead[:], ["dead", "cnt"], T.b[:], ["b"], F.Relu, scale=-1.0 / 16, bias=257.0, accum_out=T.cnt[:])
+        mm("pe", 0, "tr", T.und[:], "und", I, False, True)
+        mm("pf", 0, "tr", T.und[:], "und", I, False, False)
+        mm("pf", I, "nbk", T.und[:], "und", I, False, True)
+        ts(T.kh[:], "kh", T.pe[:, 0:I], ["pe"], 16.0 - 4096, 0.0, A.add, A.max)
+        mm("pk", 0, "bdh", T.kh[:], "kh", I, False, True)
+        if LH_S:
+            act(T.lh[:], "lh", T.pf[:, 0:2 * I], ["pf"], F.Relu, bias=1024.5 - 4096)
+        else:
+            ts(T.lh[:], "lh", T.pf[:, 0:2 * I], ["pf"], 1024.5 - 4096, 0.0, A.add, A.max)
+        mm("pl", 0, "bdh", T.lh[:, 0:I], "lh", I, False, False)
+        mm("pl", 0, "bdh", T.lh[:, I:2 * I], "lh", I, False, True)
+        diagonal("pk", "sk")
+        copy(T.ks[:], "ks", T.sk[:, 15::16], ["sk"])
+        gs, gr = "gs%d" % t, "lim0" if t == 0 else "gr"
+        tt(T[gs][:], gs, T.x[:, 0:16 + WX].indirect(T.ks[:]), T[gr][:], ["x", "xz", "ks", gr], A.max)
         dst = T.cores[(rank + 1 + t % 7) % 8]
         src = T.cores[(rank - 1 - t % 7) % 8]
         eng = topo.engines(core, dst)[:8]
@@ -309,48 +309,59 @@ def rank_program(g, core, T, topo):
         waits("g", [gs], [])
         g.remote_dma(T["h%d" % t][:], T[gs][:], T.sem["arr%d" % t], T.sem.sent, pid, rid, sum(1 << e for e in eng))
         wrote["h%d" % t] = ("remote", "arr%d" % t, len(topo.engines(src, core)[:8]), {})
-        ts(T.pg[:, 256:256 + I], "pg", T[gs][:], [gs], -2.0, None, A.add)
-        if t == 0:
-            ts(T.nid[:], "nid", T.idb[:], ["idb"], -1.0, None, A.mult)
-            ts(T.ki[:], "ki", T.grd0[:], ["grd0"], 2048.0, None, A.mult)
-            tt(T.pn[:], "pn", T.ki[:], T.nam0[:], ["ki", "nam0"], A.add)
-            memset("onef", 1.0)
-            memset("half", 0.5)
-            ts(T.nbig[:], "nbig", T.idb[:], ["idb"], -129.0 * 32768.0, None, A.mult)
-        for r in range(16):
-            mm("pl", 64, 78, part("cf", r), "cf", T.oln[:, r::16], "oln", r == 0, r == 15)
-        mm("px", 0, I, T.idb[:], "idb", T.ones[:], "ones", True, False)
-        mm("px", 0, I, T.nid[:], "nid", T.dead[:], "dead", False, False)
-        mm("px", 0, I, T.nid[:], "nid", T.imp[:], "imp", False, True)
-        for j in range(len(DG)):
-            pick(j)
-        copy(T.llu[:], "llu", T.pl[:, 64:78], ["pl"])
-        tt(T.px[:, 0:I], "px", T.pn[:], T.px[:, 0:I], ["pn", "px"], A.mult)
-        tt(T.w1[:], "w1", T.rel0[:, 0:W].indirect(T.llu[:]), T.dead[:], ["rel0", "llu", "dead"], A.mult)
-        tt(T.w3[:], "w3", T.w1[:], T.px[:, 0:I], ["w1", "px"], A.add)
-        tt(T.pd[:, 0:I], "pd", T.imp[:], T.pd[:, 0:I], ["imp", "pd"], A.mult)
-        tt(T.pn[:], "pn", T.w3[:], T.pd[:, 0:I], ["w3", "pd"], A.add)
-        ts(T.ki[:], "ki", T.pn[:], ["pn"], 11, None, A.arith_shift_right)
+        h = "h%d" % t
+        mm("pe", 0, "idb", T.cn[:], "cn", 2 * I + 2, True, False)
+        mm("pe", 0, "idx", T.b[:], "b", I, False, False)
+        mm("pe", I, "idx", T.und[:], "und", I, False, False)
+        mm("pe", I, "idx", T.dead[:], "dead", I, False, last)
         if not last:
-            copy(T.ku[:], "ku", T.ki[:], ["ki"])
-            late = [
-                lambda: op("v", ["dead"], ["cnt"], lambda e: e.tensor_reduce(T.cnt[:], T.dead[:], X, A.add)),
-                lambda: ts(T.li[:], "li", T.pn[:], ["pn"], 2047, None, A.bitwise_and),
-                lambda: mm("pm", 0, 1, T.onef[:], "onef", T.cnt[:], "cnt", True, True),
-                lambda: ts(T.lu[:], "lu", T.li[:], ["li", "seg"], T.seg[:], None, A.add),
-                lambda: copy(T.pi[:], "pi", T.pm[:, 0:1], ["pm"]),
-                lambda: ts(T.pj[:], "pj", T.pi[:], ["pi"], 1, None, A.bitwise_and),
-                lambda: ts(T.thd[:], "thd", T.pj[:], ["pj"], 2.0, -5.0, A.mult, A.add)]
+            mm("pe", 448, "onef", T.cnt[:], "cnt", 1, False, True)
+        mm("pm", 0, "idh", T.k16[:], "k16", I, False, False)
+        mm("pm", 0, "idx", T.und[:], "und", I, False, False)
+        mm("pm", 0, "idh", T.l16[:], "l16", I, False, True)
+        mm("pg", 0, "idb", T[gs][:], gs, I, True, False)
+        if not last:
+            mm("pk", 0, "idb", T.base[:], "base", 14, True, False)
+        diagonal("pl", "sl")
+        ts(T.ls[:], "ls", T.sl[:, 15::16], ["sl"], -1.0, None, A.add)
+        if MD_S:
+            fetch(BEFORE_MD)
+            act(T.md[:], "md", T.rel0[:, 0:W].indirect(T.ls[:]), ["rel0", "ls"], scale=1.0 / 2048, bias=-HALF)
         else:
-            copy(T.og[:], "og", T.ki[:], ["ki"])
-            load("s", "d_og", T.yg[:], T.og[:], ["og"], ["yg"])
-            ts(T.li[:], "li", T.pn[:], ["pn"], 2047, None, A.bitwise_and)
-            copy(T.on[:], "on", T.li[:], ["li"])
-            load("s", "d_on", T.yn[:], T.on[:], ["on"], ["yn"])
-            h = "h%d" % t
-            tt(T.gm[:], "gm", T[h][:], T.pg[:, 256:256 + I], ["pg", h], A.min)
-            ts(T.ol[:], "ol", T.gm[:], ["gm"], 2.0, None, A.add)
+            ts(T.md[:], "md", T.rel0[:, 0:W].indirect(T.ls[:]), ["rel0", "ls"], -1023.5, 1.0 / 2048, A.add, A.mult)
+        fetch(len(FETCH))
+        for k in allmo:
+            wrote[k] = wrote["mo15"]
+        tt(T.t1[:], "t1", T.md[:], T.pe[:, 0:I], ["md", "pe"], A.subtract)
+        tt(pn, "pn", T.t1[:], T.pm[:, 0:I], ["t1", "pm"], A.max)
+        tt(T.t2[:], "t2", T.mo[:], T.pe[:, I:2 * I], allmo + ["pe"], A.subtract)
+        tt(pn, "pn", T.t2[:], pn, ["t2", "pn"], A.max)
+        lower(h)
+        if not last:
+            for r in range(16):
+                mm("pk", 0, "zw", T[h][:, r::16], h, 14, False, r == 15, lhs=T.zw[:, 15 - r:143 - r])
+            act(T.hp[:], "hp", T[h][:], [h], bias=287.5)
+            lowered(gs)
+            limits(T.pg[:, 0:I], "pg")
+            act(T.gr[:], "gr", T.pg[:, 0:I], ["pg"])
+            turn("tp")
+            turned = T.tp[:, 0:480].indirect(T.sel[:])
+            ts(T.kt[:], "kt", turned, ["tp0", "tp1", "sel"], ROUND, -ROUND, A.add, A.add)
+            tt(T.lt[:], "lt", turned, T.kt[:], ["tp0", "tp1", "sel", "kt"], A.subtract)
+            ts(T.lu[:], "lu", T.lt[:], ["lt"], 2048.0, 1023.5, A.mult, A.add)
+            copy(T.ku[:], "ku", T.kt[:], ["kt"])
+            tt(T.f8[:], "f8", T.pk[:, 0:14], T.bm[:], ["pk", "bm"], A.subtract)
+            tt(T.z[:], "z", T.pk[:, 0:14], T.f8[:], ["pk", "f8"], A.subtract)
+            ts(T.cu[:], "cu", T.z[:], ["z"], 1032.0, None, A.add)
+        else:
+            lowered(gs)
+            act(T.ol[:], "ol", T.pg[:, 0:I], ["pg"])
             load("a", "d_ol", T.yl[:], T.ol[:], ["ol"], ["yl"])
+            ts(T.og[:], "og", pn, ["pn"], ROUND, -ROUND, A.add, A.add)
+            load("s", "d_og", T.yg[:], T.og[:], ["og"], ["yg"])
+            tt(T.lt[:], "lt", pn, T.og[:], ["pn", "og"], A.subtract)
+            ts(T.on[:], "on", T.lt[:], ["lt"], 2048.0, 1023.5, A.mult, A.add)
+            load("s", "d_on", T.yn[:], T.on[:], ["on"], ["yn"])
     g.wait_ge(T.sem.sent, sum(len(topo.engines(core, T.cores[(rank + 1 + t % 7) % 8])[:8]) for t in range(RO)))
     for q in ("v", "a", "t", "g"):
         if known["g"].get("c" + q, 0) < count[q]:

@@ -6,14 +6,13 @@ WX = 1792
 W = 2048
 RO = 4
 JUDGE = [(0, 2), (2, 4), (4, 6), (6, 8), (8, 10), (10, 12), (12, 14), (14, 15), (15, 16)]
-FETCH = [(2 * j, 2 * j + 2) for j in range(8)]
-EARLY = 2
-AMONG = (1, 4)
-AMONG0 = (5,)
-BEFORE_DEAD = 1
-BEFORE_MD = 2
-LH_S = False
-MD_S = False
+EARLY = 3
+AMONG = (2,)
+AMONG0 = (4,)
+BEFORE_DEAD = 2
+RAISE = "kh lh sk ks gs rest sl ls md"
+NEXT = "t1 t2 m1 land m2 low gr turn kt ku lt f8 lu early z cu bl b2 put"
+END = "t1 t2 m1 m2 og lt h2 on ol"
 ROUND = 1.5 * 2.0 ** 23
 HALF = 1023.5 / 2048
 
@@ -25,11 +24,12 @@ SCRATCH = {
     "u": (SB, [128, 16 * I], BF), "w": (SB, [128, 16 * I], BF), "nb": (SB, [128, 16 * I], F32),
     "ku": (SB, [128, I], U16), "lu": (SB, [128, I], U16), "tp": (SB, [128, 480], F32), "tq": (SB, [128, 480], F32),
     "kt": (SB, [128, I], F32), "lt": (SB, [128, I], F32), "k16": (SB, [128, I], F16), "l16": (SB, [128, I], F16),
-    "gj": (SB, [128, 2 * I], F32), "gr": (SB, [128, I], BF), "rl": (SB, [128, I], BF), "hp": (SB, [128, I], F32),
+    "gj": (SB, [128, 2 * I], F32), "gr": (SB, [128, I], BF), "rl": (SB, [128, I], BF), "gm": (SB, [128, I], BF),
     "b": (SB, [128, I], BF), "und": (SB, [128, I], BF), "dead": (SB, [128, I], BF),
     "kh": (SB, [128, I], F16), "lh": (SB, [128, 2 * I], F16), "sk": (SB, [128, I], F32), "sl": (SB, [128, I], F32),
     "ks": (SB, [128, 14], U16), "ls": (SB, [128, 14], U16), "cu": (SB, [128, 14], U16),
-    "f8": (SB, [128, 14], BF), "z": (SB, [128, 14], F32), "bm": (SB, [128, 14], F32), "bl": (SB, [128, I], BF), "b2": (SB, [128, I], BF),
+    "f8": (SB, [128, 14], BF), "z": (SB, [128, 14], F32), "bm": (SB, [128, 14], F32),
+    "bl": (SB, [128, I], BF), "b2": (SB, [128, I], BF), "c128": (SB, [128, I], BF),
     "md": (SB, [128, I], F32), "mo": (SB, [128, I], F32), "t1": (SB, [128, I], F32), "t2": (SB, [128, I], F32),
     "cnt": (SB, [128, 1], F32), "pi": (SB, [128, 1], I32), "pj": (SB, [128, 1], I32), "thr": (SB, [128, 1], F32),
     "ip": (SB, [128, 1], I32), "c1": (SB, [128, 1], I32), "c2": (SB, [128, 1], I32), "c3": (SB, [128, 1], I32),
@@ -38,7 +38,7 @@ SCRATCH = {
     "ff": (SB, [128, 14], F32), "f": (SB, [128, 14], F32), "fk": (SB, [128, 14], I32), "a1": (SB, [128, 14], F32),
     "a2": (SB, [128, 14], F32), "a3": (SB, [128, 14], F32), "sel": (SB, [128, 14], U16), "base": (SB, [128, 14], BF),
     "t16": (SB, [128, I], BF), "mk": (SB, [128, I], BF), "rs": (SB, [128, I], BF),
-    "cm": (SB, [128, I], BF), "cn": (SB, [128, 2 * I + 2], BF), "ch": (SB, [128, 2 * I], F16),
+    "cm": (SB, [128, I], BF), "cn": (SB, [128, I], BF), "ch": (SB, [128, 2 * I], F16),
     "ones": (SB, [128, 128], BF), "onef": (SB, [128, 128], F32), "idb": (SB, [128, 128], BF), "idh": (SB, [128, 128], F16),
     "idl": (SB, [128, 128], F16), "id0": (SB, [128, 128], F16), "idx": (SB, [128, 128], BF), "idn": (SB, [128, 128], BF),
     "bd": (SB, [128, 128], BF), "bdh": (SB, [128, 128], F16), "nbk": (SB, [128, 128], BF), "low": (SB, [128, 128], BF),
@@ -141,18 +141,21 @@ def rank_program(g, core, T, topo):
         op("g", [], [name], lambda e: e.iota(T[name][:], pattern, 0, mult, allow_small_or_imprecise_dtypes=True))
 
     pa, pn = T.pv[:, 0:I], T.pv[:, 272:272 + I]
+    xw = T.x[:, 16:16 + WX]
 
     def turn(dst):
         op("v", ["pn"], [dst + "0"], lambda e: e.transpose(T[dst][:, 0:I], pn))
         op("v", ["pn", "pad"], [dst + "1"], lambda e: e.transpose(T[dst][:, I:480], T.pv[:, 256:512]))
+
+    def turned(src):
+        return T[src][:, 0:480].indirect(T.sel[:])
 
     def diagonal(bank, out):
         op("v", [bank, "rs"], [out], lambda e: e.tensor_tensor_scan(T[out][:], T.rs[:], T[bank][:, 0:I], 0.0, A.mult, A.max))
 
     def judge(j):
         a, b = JUDGE[j]
-        tt(T.u[:, I * a:I * b], "u%d" % j, T.x[:, 16:16 + WX].indirect(T.ku[:, 14 * a:14 * b]), T.gj[:, 0:I * (b - a)],
-           ["x", "ku", "gj0", "gj1"], A.subtract)
+        tt(T.u[:, I * a:I * b], "u%d" % j, xw.indirect(T.ku[:, 14 * a:14 * b]), T.gj[:, 0:I * (b - a)], ["x", "ku", "gj0", "gj1"], A.subtract)
 
     def mark(j):
         a, b = JUDGE[j]
@@ -163,205 +166,201 @@ def rank_program(g, core, T, topo):
     fetched = [0]
 
     def fetch(n):
-        for j in range(fetched[0], min(fetched[0] + n, len(FETCH))):
-            a, b = FETCH[j]
-            act(T.nb[:, I * a:I * b], "nb%d" % j, T.rel0[:, 0:W].indirect(T.lu[:, 14 * a:14 * b]), ["rel0", "lu"], scale=1.0 / 2048, bias=-HALF)
-            for k in range(a, b):
+        for j in range(fetched[0], min(fetched[0] + n, 8)):
+            act(T.nb[:, 2 * I * j:2 * I * j + 2 * I], "nb%d" % j, T.rel0[:, 0:W].indirect(T.lu[:, 28 * j:28 * j + 28]), ["rel0", "lu"],
+                scale=1.0 / 2048, bias=-HALF)
+            for k in (2 * j, 2 * j + 1):
                 load("s", "d_mo", T.mo[k::16, :], T.nb[k::16, I * k:I * k + I], ["nb%d" % j], ["mo%d" % k])
             fetched[0] = j + 1
+        if fetched[0] == 8:
+            for k in range(16):
+                wrote["mo%d" % k] = wrote["mo15"]
 
     def limits(src, key):
         for c in range(2):
             act(T.gj[:, I * c:I * c + I], "gj%d" % c, src, [key], bias=-641.5)
 
-    def lower(h):
-        mm("pg", 0, "idn", T[h][:], h, I, False, True)
-        act(T.rl[:], "rl", T.pg[:, 0:I], ["pg"], F.Relu, bias=-2.0)
-
-    def lowered(gs):
-        mm("pg", 0, "idb", T[gs][:], gs, I, True, False)
-        mm("pg", 0, "idn", T.rl[:], "rl", I, False, True)
-
-    allmo = ["mo%d" % k for k in range(16)]
-
     load("s", "d_grd", T.grd0[:], T.grd[:], [], ["grd0"])
     load("a", "d_lim", T.lim0[:], T.lim[:], [], ["lim0"])
-    load("s", "d_x", T.x[:, 16:16 + WX], T.xc[:], [], ["x"])
+    load("s", "d_x", xw, T.xc[:], [], ["x"])
     load("a", "d_nam", T.nam0[:], T.nam[:], [], ["nam0"])
     load("s", "d_rel", T.rel0[:], T.rel[:], [], ["rel0"])
 
     iota("ip", [[0, 1]], 1)
     iota("ff", [[16, 14]], 1)
     memset(T.ones[:], "ones", 1.0)
-    memset(T.pv[:, 256:512], "pad", 0.0)
-    memset(T.zz[:], "zz", 0.0)
-    memset(T.x[:, 0:16], "xz", 0.0)
     select("bd", "ones", [[-16, 8], [0, 16]], A.is_ge, 0.0, 0, 1)
     select("bd", "bd", [[16, 8], [0, 16]], A.is_ge, 0.0, 15, -1)
     iota("t16", [[0, 14], [1, 16]], 0)
     select("idb", "ones", [[-1, 128]], A.is_equal, 0.0, 0, 1)
     select("low", "bd", [[1, 128]], A.is_gt, 0.0, 0, -1)
+    memset(T.pv[:, 256:512], "pad", 0.0)
+    wrote["pn"] = wrote["pad"]
     ts(T.c1[:], "c1", T.ip[:], ["ip"], 112, None, A.bitwise_and)
     ts(T.c2[:], "c2", T.ip[:], ["ip"], 4, None, A.arith_shift_right)
+    ts(T.c5[:], "c5", T.ip[:], ["ip"], 15, None, A.bitwise_and)
     copy(T.g16[:], "g16", T.c1[:], ["c1"])
     tt(T.c3[:], "c3", T.c2[:], T.ip[:], ["c2", "ip"], A.add)
+    ts(T.c6[:], "c6", T.ip[:], ["ip"], 3, None, A.bitwise_and)
     ts(T.f[:], "f", T.ff[:], ["ff", "g16"], T.g16[:], None, A.subtract)
     ts(T.c4[:], "c4", T.c3[:], ["c3"], 1, None, A.bitwise_and)
+    memset(T.zz[:], "zz", 0.0)
     ts(T.fk[:], "fk", T.f[:], ["f"], 1.0 / 14, -13.0 / 28, A.mult, A.add)
     ts(T.par[:], "par", T.c4[:], ["c4"], 240.0, None, A.mult)
     ts(T.a2[:], "a2", T.f[:], ["f"], 16.0, None, A.mult)
+    memset(T.x[:, 0:16], "xz", 0.0)
     ts(T.a1[:], "a1", T.fk[:], ["fk", "par"], -223.0, T.par[:], A.mult, A.add)
-    tt(T.a3[:], "a3", T.a1[:], T.a2[:], ["a1", "a2"], A.add)
-    copy(T.sel[:], "sel", T.a3[:], ["a3"])
-    wrote["pn"] = wrote["pad"]
-    memset(T.thr[:], "thr", 192 + 4100.5)
-    memset(T.ch[:, 0:I], "ch0", 0.0)
-    memset(T.ch[:, I:2 * I], "ch", 2.0)
-    memset(T.cm[:], "cm", -4096.0)
-    memset(T.cn[:, 0:I], "cn0", -2.0 ** 24)
-    memset(T.cn[:, I:2 * I + 2], "cn", 0.0)
-    memset(T.onef[:], "onef", 1.0)
     memset(T.zw[:], "zw", 0.0)
-    ts(T.c5[:], "c5", T.ip[:], ["ip"], 15, None, A.bitwise_and)
-    ts(T.c6[:], "c6", T.ip[:], ["ip"], 3, None, A.bitwise_and)
-    ts(T.base[:], "base", T.f[:], ["f"], 8.0, None, A.mult)
-    ts(T.bm[:], "bm", T.f[:], ["f"], 8.0, -1028.5, A.mult, A.add)
     copy(T.rc[:], "rc", T.c5[:], ["c5"])
+    tt(T.a3[:], "a3", T.a1[:], T.a2[:], ["a1", "a2"], A.add)
     ts(T.wc[:], "wc", T.c6[:], ["c6"], 2.0, 1.0, A.mult, A.add)
     ts(T.kz[:], "kz", T.c5[:], ["c5"], 0.5, 2048.0, A.is_lt, A.mult)
+    copy(T.sel[:], "sel", T.a3[:], ["a3"])
 
     for t in range(RO):
         last = t == RO - 1
-        h = "h%d" % (t - 1)
-        fetched[0] = 0
+        h, gs, gr = "h%d" % t, "gs%d" % t, "lim0" if t == 0 else "gr"
         if t == 0:
             copy(pn, "pn", T.grd0[:], ["grd0"])
+            memset(T.ch[:, 0:I], "ch0", 0.0)
             turn("tp")
-            copy(T.ku[:], "ku", T.tp[:, 0:480].indirect(T.sel[:]), ["tp0", "tp1", "sel"])
+            memset(T.ch[:, I:2 * I], "ch", 2.0)
+            copy(T.ku[:], "ku", turned("tp"), ["tp0", "tp1", "sel"])
             limits(T.lim0[:], "lim0")
-            ts(T.zz[:, 15:143:16], "zz", T.bd[:, 0:128:16], ["bd"], -33.0, None, A.mult)
             copy(pn, "pn", T.nam0[:], ["nam0"])
+            ts(T.zz[:, 15:143:16], "zz", T.bd[:, 0:128:16], ["bd"], -33.0, None, A.mult)
             turn("tq")
-            copy(T.lu[:], "lu", T.tq[:, 0:480].indirect(T.sel[:]), ["tq0", "tq1", "sel"])
             ts(T.mk[:], "mk", T.t16[:], ["t16", "rc"], T.rc[:], -16384.0, A.not_equal, A.mult)
+            copy(T.lu[:], "lu", turned("tq"), ["tq0", "tq1", "sel"])
             ts(T.id0[:], "id0", T.idb[:], ["idb", "kz"], T.kz[:], None, A.mult)
-            act(T.idx[:], "idx", T.idb[:], ["idb"], scale=4096.0)
-            act(T.idn[:], "idn", T.idb[:], ["idb"], scale=-1.0)
-            act(T.nbk[:], "nbk", T.bd[:], ["bd"], scale=-4096.0)
-            act(T.low[:], "low", T.low[:], ["low"], scale=-4096.0)
             act(T.zw[:, 15:143:16], "zw", T.bd[:, 0:128:16], ["bd", "wc"], scale=T.wc[:])
-        else:
-            fetch(EARLY)
-            tt(T.bl[:], "bl", T.x[:, 16:16 + WX].indirect(T.cu[:]), T.hp[:], ["x", "cu", "hp"], A.add)
-            ts(T.b2[:], "b2", T.bl[:], ["bl"], -288.0, 0.5, A.add, A.mult)
-            copy(T.x[:, 16:16 + WX].indirect(T.cu[:]), "x", T.b2[:], ["b2", "cu"])
+            act(T.rs[:], "rs", T.t16[:], ["t16"], F.Sigmoid, scale=256.0, bias=-128.0)
+            act(T.cm[:], "cm", T.t16[:], ["t16"], scale=0.0, bias=-4096.0)
+            act(T.idx[:], "idx", T.idb[:], ["idb"], scale=4096.0)
+            act(T.low[:], "low", T.low[:], ["low"], scale=-4096.0)
         for j in range(len(JUDGE)):
+            if j == (1 if t == 0 else 0):
+                mm("pl", 0, "idb", T.mk[:], "mk", I, True, False)
+                mm("pf", 0, "id0", T.ch[:], "ch", 2 * I, True, False)
+                mm("pm", 0, "idb", T.cm[:], "cm", I, True, False)
+                mm("pk", 0, "idb", T.mk[:], "mk", I, True, False)
             judge(j)
             mark(j)
             if j in (AMONG if t > 0 else AMONG0):
                 fetch(1)
-            if j == 1:
-                mm("pk", 0, "idb", T.mk[:], "mk", I, True, False)
-                mm("pl", 0, "idb", T.mk[:], "mk", I, True, False)
-                mm("pf", 0, "id0", T.ch[:], "ch", 2 * I, True, False)
-                mm("pm", 0, "idb", T.cm[:], "cm", I, True, False)
         if t == 0:
             copy(T.k16[:], "k16", T.grd0[:], ["grd0"])
             copy(T.idh[:], "idh", T.idb[:], ["idb"])
             ts(T.l16[:], "l16", T.nam0[:], ["nam0"], 1.0 / 2048, -HALF, A.mult, A.add)
             ts(T.idl[:], "idl", T.idb[:], ["idb"], 2048.0, None, A.mult)
+            memset(T.thr[:], "thr", 192 + 4100.5)
             tt(T.tr[:], "tr", T.low[:], T.idx[:], ["low", "idx"], A.add)
-            copy(T.bdh[:], "bdh", T.bd[:], ["bd"])
-            ts(T.rs[:], "rs", T.t16[:], ["t16"], 0.5, None, A.is_gt)
+            act(T.nbk[:], "nbk", T.bd[:], ["bd"], scale=-4096.0)
+            act(T.cn[:], "cn", T.t16[:], ["t16"], scale=0.0, bias=-2.0 ** 24)
         else:
-            ts(T.k16[:], "k16", pn, ["pn"], ROUND, -ROUND, A.add, A.add)
             copy(T.pi[:], "pi", T.pe[:, 448:449], ["pe"])
-            tt(T.l16[:], "l16", pn, T.k16[:], ["pn", "k16"], A.subtract)
+            ts(T.k16[:], "k16", pn, ["pn"], ROUND, -ROUND, A.add, A.add)
             ts(T.pj[:], "pj", T.pi[:], ["pi"], 1, None, A.bitwise_and)
+            tt(T.l16[:], "l16", pn, T.k16[:], ["pn", "k16"], A.subtract)
             ts(T.thr[:], "thr", T.pj[:], ["pj"], 32.0, 192 + 4100.5, A.mult, A.add)
         fetch(BEFORE_DEAD)
         mm("pe", 0, "idh", T.k16[:], "k16", I, True, False)
         mm("pf", 0, "idl", T.l16[:], "l16", I, False, False)
         mm("pf", I, "id0", T.l16[:], "l16", I, False, False)
         ts(pa, "a", T.pa[:, 0:I], ["pa", "thr"], T.thr[:], 4100.5, A.add, A.max)
+        if t == 0:
+            copy(T.bdh[:], "bdh", T.bd[:], ["bd"])
         ts(T.b[:], "b", pa, ["a"], 3.5, None, A.add)
+        if t == 0:
+            ts(T.base[:], "base", T.f[:], ["f"], 8.0, None, A.mult)
         tt(T.und[:], "und", pa, T.b[:], ["a", "b"], A.is_lt)
         act(T.dead[:], ["dead", "cnt"], T.b[:], ["b"], F.Relu, scale=-1.0 / 16, bias=257.0, accum_out=T.cnt[:])
         mm("pe", 0, "tr", T.und[:], "und", I, False, True)
         mm("pf", 0, "tr", T.und[:], "und", I, False, False)
         mm("pf", I, "nbk", T.und[:], "und", I, False, True)
-        ts(T.kh[:], "kh", T.pe[:, 0:I], ["pe"], 16.0 - 4096, 0.0, A.add, A.max)
-        mm("pk", 0, "bdh", T.kh[:], "kh", I, False, True)
-        if LH_S:
-            act(T.lh[:], "lh", T.pf[:, 0:2 * I], ["pf"], F.Relu, bias=1024.5 - 4096)
-        else:
+        if t == 0:
+            ts(T.bm[:], "bm", T.f[:], ["f"], 8.0, -1028.5, A.mult, A.add)
+            act(T.onef[:], "onef", T.ones[:], ["ones"])
+            act(T.idn[:], "idn", T.idb[:], ["idb"], scale=-1.0)
+
+        def kh():
+            ts(T.kh[:], "kh", T.pe[:, 0:I], ["pe"], 16.0 - 4096, 0.0, A.add, A.max)
+            mm("pk", 0, "bdh", T.kh[:], "kh", I, False, True)
+
+        def lh():
             ts(T.lh[:], "lh", T.pf[:, 0:2 * I], ["pf"], 1024.5 - 4096, 0.0, A.add, A.max)
-        mm("pl", 0, "bdh", T.lh[:, 0:I], "lh", I, False, False)
-        mm("pl", 0, "bdh", T.lh[:, I:2 * I], "lh", I, False, True)
-        diagonal("pk", "sk")
-        copy(T.ks[:], "ks", T.sk[:, 15::16], ["sk"])
-        gs, gr = "gs%d" % t, "lim0" if t == 0 else "gr"
-        tt(T[gs][:], gs, T.x[:, 0:16 + WX].indirect(T.ks[:]), T[gr][:], ["x", "xz", "ks", gr], A.max)
-        dst = T.cores[(rank + 1 + t % 7) % 8]
-        src = T.cores[(rank - 1 - t % 7) % 8]
-        eng = topo.engines(core, dst)[:8]
-        rid, pid = topo.addr(dst, core)
-        waits("g", [gs], [])
-        g.remote_dma(T["h%d" % t][:], T[gs][:], T.sem["arr%d" % t], T.sem.sent, pid, rid, sum(1 << e for e in eng))
-        wrote["h%d" % t] = ("remote", "arr%d" % t, len(topo.engines(src, core)[:8]), {})
-        h = "h%d" % t
-        mm("pe", 0, "idb", T.cn[:], "cn", 2 * I + 2, True, False)
-        mm("pe", 0, "idx", T.b[:], "b", I, False, False)
-        mm("pe", I, "idx", T.und[:], "und", I, False, False)
-        mm("pe", I, "idx", T.dead[:], "dead", I, False, last)
-        if not last:
-            mm("pe", 448, "onef", T.cnt[:], "cnt", 1, False, True)
-        mm("pm", 0, "idh", T.k16[:], "k16", I, False, False)
-        mm("pm", 0, "idx", T.und[:], "und", I, False, False)
-        mm("pm", 0, "idh", T.l16[:], "l16", I, False, True)
-        mm("pg", 0, "idb", T[gs][:], gs, I, True, False)
-        if not last:
-            mm("pk", 0, "idb", T.base[:], "base", 14, True, False)
-        diagonal("pl", "sl")
-        ts(T.ls[:], "ls", T.sl[:, 15::16], ["sl"], -1.0, None, A.add)
-        if MD_S:
-            fetch(BEFORE_MD)
-            act(T.md[:], "md", T.rel0[:, 0:W].indirect(T.ls[:]), ["rel0", "ls"], scale=1.0 / 2048, bias=-HALF)
-        else:
-            ts(T.md[:], "md", T.rel0[:, 0:W].indirect(T.ls[:]), ["rel0", "ls"], -1023.5, 1.0 / 2048, A.add, A.mult)
-        fetch(len(FETCH))
-        for k in allmo:
-            wrote[k] = wrote["mo15"]
-        tt(T.t1[:], "t1", T.md[:], T.pe[:, 0:I], ["md", "pe"], A.subtract)
-        tt(pn, "pn", T.t1[:], T.pm[:, 0:I], ["t1", "pm"], A.max)
-        tt(T.t2[:], "t2", T.mo[:], T.pe[:, I:2 * I], allmo + ["pe"], A.subtract)
-        tt(pn, "pn", T.t2[:], pn, ["t2", "pn"], A.max)
-        lower(h)
-        if not last:
+            mm("pa", 0, "idb", T.cn[:], "cn", I, True, False)
+            mm("pl", 0, "bdh", T.lh[:, 0:I], "lh", I, False, False)
+            mm("pl", 0, "bdh", T.lh[:, I:2 * I], "lh", I, False, True)
+            mm("pa", 0, "idx", T.b[:], "b", I, False, True)
+            mm("pm", 0, "idh", T.k16[:], "k16", I, False, False)
+            mm("pm", 0, "idx", T.und[:], "und", I, False, False)
+            mm("pm", 0, "idh", T.l16[:], "l16", I, False, True)
+            mm("pe", 0, "idx", T.und[:], "und", I, True, False)
+            mm("pe", 0, "idx", T.dead[:], "dead", I, False, True)
+            if not last:
+                mm("pe", 448, "onef", T.cnt[:], "cnt", 1, True, True)
+
+        def send():
+            tt(T[gs][:], gs, T.x[:, 0:16 + WX].indirect(T.ks[:]), T[gr][:], ["x", "xz", "ks", gr], A.max)
+            dst = T.cores[(rank + 1 + t % 7) % 8]
+            src = T.cores[(rank - 1 - t % 7) % 8]
+            eng = topo.engines(core, dst)[:8]
+            rid, pid = topo.addr(dst, core)
+            waits("g", [gs], [])
+            g.remote_dma(T[h][:], T[gs][:], T.sem["arr%d" % t], T.sem.sent, pid, rid, sum(1 << e for e in eng))
+            wrote[h] = ("remote", "arr%d" % t, len(topo.engines(src, core)[:8]), {})
+            mm("pg", 0, "idb", T[gs][:], gs, I, True, last)
+            if not last:
+                mm("pk", 0, "idb", T.base[:], "base", 14, True, False)
+
+        def rest():
+            fetch(8)
+            fetched[0] = 0
+            if t == 0:
+                act(T.c128[:], "c128", T.t16[:], ["t16"], scale=0.0, bias=-128.0)
+
+        def land():
+            mm("pg", 0, "idn", T[h][:], h, I, False, True)
+            act(T.rl[:], "rl", T.pg[:, 0:I], ["pg"], F.Relu, bias=-2.0)
             for r in range(16):
                 mm("pk", 0, "zw", T[h][:, r::16], h, 14, False, r == 15, lhs=T.zw[:, 15 - r:143 - r])
-            act(T.hp[:], "hp", T[h][:], [h], bias=287.5)
-            lowered(gs)
+
+        def low():
+            mm("pg", 0, "idb", T[gs][:], gs, I, True, False)
+            mm("pg", 0, "idn", T.rl[:], "rl", I, False, True)
             limits(T.pg[:, 0:I], "pg")
-            act(T.gr[:], "gr", T.pg[:, 0:I], ["pg"])
-            turn("tp")
-            turned = T.tp[:, 0:480].indirect(T.sel[:])
-            ts(T.kt[:], "kt", turned, ["tp0", "tp1", "sel"], ROUND, -ROUND, A.add, A.add)
-            tt(T.lt[:], "lt", turned, T.kt[:], ["tp0", "tp1", "sel", "kt"], A.subtract)
-            ts(T.lu[:], "lu", T.lt[:], ["lt"], 2048.0, 1023.5, A.mult, A.add)
-            copy(T.ku[:], "ku", T.kt[:], ["kt"])
-            tt(T.f8[:], "f8", T.pk[:, 0:14], T.bm[:], ["pk", "bm"], A.subtract)
-            tt(T.z[:], "z", T.pk[:, 0:14], T.f8[:], ["pk", "f8"], A.subtract)
-            ts(T.cu[:], "cu", T.z[:], ["z"], 1032.0, None, A.add)
-        else:
-            lowered(gs)
-            act(T.ol[:], "ol", T.pg[:, 0:I], ["pg"])
-            load("a", "d_ol", T.yl[:], T.ol[:], ["ol"], ["yl"])
-            ts(T.og[:], "og", pn, ["pn"], ROUND, -ROUND, A.add, A.add)
-            load("s", "d_og", T.yg[:], T.og[:], ["og"], ["yg"])
-            tt(T.lt[:], "lt", pn, T.og[:], ["pn", "og"], A.subtract)
-            ts(T.on[:], "on", T.lt[:], ["lt"], 2048.0, 1023.5, A.mult, A.add)
-            load("s", "d_on", T.yn[:], T.on[:], ["on"], ["yn"])
+
+        step = {
+            "kh": kh, "lh": lh, "gs": send, "rest": rest, "land": land, "low": low, "early": lambda: fetch(EARLY),
+            "sk": lambda: diagonal("pk", "sk"), "sl": lambda: diagonal("pl", "sl"),
+            "ks": lambda: copy(T.ks[:], "ks", T.sk[:, 15::16], ["sk"]),
+            "ls": lambda: ts(T.ls[:], "ls", T.sl[:, 15::16], ["sl"], -1.0, None, A.add),
+            "md": lambda: ts(T.md[:], "md", T.rel0[:, 0:W].indirect(T.ls[:]), ["rel0", "ls"], -1023.5, 1.0 / 2048, A.add, A.mult),
+            "t1": lambda: tt(T.t1[:], "t1", T.md[:], T.pa[:, 0:I], ["md", "pa"], A.subtract),
+            "t2": lambda: tt(T.t2[:], "t2", T.mo[:], T.pe[:, 0:I], ["mo%d" % k for k in range(16)] + ["pe"], A.subtract),
+            "m1": lambda: tt(pn, "pn", T.t1[:], T.pm[:, 0:I], ["t1", "pm"], A.max),
+            "m2": lambda: tt(pn, "pn", T.t2[:], pn, ["t2", "pn"], A.max),
+            "turn": lambda: turn("tp"),
+            "kt": lambda: ts(T.kt[:], "kt", turned("tp"), ["tp0", "tp1", "sel"], ROUND, -ROUND, A.add, A.add),
+            "lt": lambda: tt(T.lt[:], "lt", pn if last else turned("tp"), T.og[:] if last else T.kt[:],
+                             ["pn", "og"] if last else ["tp0", "tp1", "sel", "kt"], A.subtract),
+            "lu": lambda: ts(T.lu[:], "lu", T.lt[:], ["lt"], 2048.0, 1023.5, A.mult, A.add),
+            "ku": lambda: copy(T.ku[:], "ku", T.kt[:], ["kt"]),
+            "gr": lambda: act(T.gr[:], "gr", T.pg[:, 0:I], ["pg"]),
+            "f8": lambda: tt(T.f8[:], "f8", T.pk[:, 0:14], T.bm[:], ["pk", "bm"], A.subtract),
+            "z": lambda: tt(T.z[:], "z", T.pk[:, 0:14], T.f8[:], ["pk", "f8"], A.subtract),
+            "cu": lambda: ts(T.cu[:], "cu", T.z[:], ["z"], 1032.0, None, A.add),
+            "bl": lambda: tt(T.bl[:], "bl", xw.indirect(T.cu[:]), T[h][:], ["x", "cu", h], A.add),
+            "b2": lambda: ts(T.b2[:], "b2", T.bl[:], ["bl"], 0.5, 127.75, A.mult, A.add),
+            "put": lambda: tt(xw.indirect(T.cu[:]), "x", T.b2[:], T.c128[:], ["b2", "cu", "c128"], A.add),
+            "og": lambda: (ts(T.og[:], "og", pn, ["pn"], ROUND, -ROUND, A.add, A.add), load("s", "d_og", T.yg[:], T.og[:], ["og"], ["yg"])),
+            "on": lambda: (ts(T.on[:], "on", T.lt[:], ["lt"], 2048.0, 1023.5, A.mult, A.add), load("s", "d_on", T.yn[:], T.on[:], ["on"], ["yn"])),
+            "h2": lambda: ts(T.gm[:], "gm", T[h][:], [h], 2.0, None, A.add),
+            "ol": lambda: (tt(T.ol[:], "ol", T.gm[:], T.pg[:, 0:I], ["gm", "pg"], A.min), load("a", "d_ol", T.yl[:], T.ol[:], ["ol"], ["yl"])),
+        }
+        for s in (RAISE + " " + (END if last else NEXT)).split():
+            step[s]()
     g.wait_ge(T.sem.sent, sum(len(topo.engines(core, T.cores[(rank + 1 + t % 7) % 8])[:8]) for t in range(RO)))
     for q in ("v", "a", "t", "g"):
         if known["g"].get("c" + q, 0) < count[q]:

@@ -5,44 +5,47 @@ I = 224
 WX = 1792
 W = 2048
 RO = 4
-JUDGE = [(0, 2), (2, 4), (4, 6), (6, 8), (8, 10), (10, 12), (12, 14), (14, 15), (15, 16)]
+JUDGE = [28, 56, 84, 112, 140, 168, 196, 210, 218, 224]
 EARLY = 3
-AMONG = (2,)
-AMONG0 = (4,)
+AMONG = (1,)
 BEFORE_DEAD = 2
-RAISE = "kh lh sk ks gs rest sl ls md"
-NEXT = "t1 t2 m1 land m2 low gr turn kt ku lt f8 lu early z cu bl b2 put"
-END = "t1 t2 m1 m2 og lt h2 on ol"
+HELP0 = (3, 5)
+RAISE = "kh lh sk ks gs rest sl"
+NEXT = "land ls md t2 t1 m1 pi m2 turn sq kt low f8 z ku cu gr lt bl lu early put"
+END = "ls md t2 t1 m1 m2 og lt h2 on ol"
+SUMS = "eu l0 l1 ed mk mu ml cn b cnt"
 ROUND = 1.5 * 2.0 ** 23
 HALF = 1023.5 / 2048
+UP = 144.0
 
 SB = "sbuf"
 BF, F32, F16, I32, U16 = "bfloat16", "float32", "float16", "int32", "uint16"
 SCRATCH = {
-    "x": (SB, [128, 16 + WX], BF), "lim0": (SB, [128, I], BF), "grd0": (SB, [128, I], I32), "nam0": (SB, [128, I], I32),
-    "rel0": (SB, [128, W], I32),
+    "x": (SB, [128, 16 + WX], BF), "x0": (SB, [128, 16 + WX], BF), "lim0": (SB, [128, I], BF),
+    "grd0": (SB, [128, I], I32), "nam0": (SB, [128, I], I32), "rel0": (SB, [128, W], I32),
     "u": (SB, [128, 16 * I], BF), "w": (SB, [128, 16 * I], BF), "nb": (SB, [128, 16 * I], F32),
     "ku": (SB, [128, I], U16), "lu": (SB, [128, I], U16), "tp": (SB, [128, 480], F32), "tq": (SB, [128, 480], F32),
     "kt": (SB, [128, I], F32), "lt": (SB, [128, I], F32), "k16": (SB, [128, I], F16), "l16": (SB, [128, I], F16),
-    "gj": (SB, [128, 2 * I], F32), "gr": (SB, [128, I], BF), "rl": (SB, [128, I], BF), "gm": (SB, [128, I], BF),
+    "gj": (SB, [128, 2 * I], F32), "gr": (SB, [128, I], BF), "rl": (SB, [128, I], BF), "gm": (SB, [128, I], BF), "hp": (SB, [128, I], F32),
     "b": (SB, [128, I], BF), "und": (SB, [128, I], BF), "dead": (SB, [128, I], BF),
-    "kh": (SB, [128, I], F16), "lh": (SB, [128, 2 * I], F16), "sk": (SB, [128, I], F32), "sl": (SB, [128, I], F32),
+    "kh": (SB, [128, I], F16), "lh": (SB, [128, 2 * I], F16),
+    "sk": (SB, [128, I], F32), "sl": (SB, [128, I], F32), "sq": (SB, [128, I], F32),
     "ks": (SB, [128, 14], U16), "ls": (SB, [128, 14], U16), "cu": (SB, [128, 14], U16),
-    "f8": (SB, [128, 14], BF), "z": (SB, [128, 14], F32), "bm": (SB, [128, 14], F32),
-    "bl": (SB, [128, I], BF), "b2": (SB, [128, I], BF), "c128": (SB, [128, I], BF),
+    "f8": (SB, [128, 14], BF), "z": (SB, [128, 14], F32), "bm0": (SB, [128, 14], F32), "bm": (SB, [128, 14], F32),
+    "bl": (SB, [128, I], BF), "half": (SB, [128, I], BF),
     "md": (SB, [128, I], F32), "mo": (SB, [128, I], F32), "t1": (SB, [128, I], F32), "t2": (SB, [128, I], F32),
     "cnt": (SB, [128, 1], F32), "pi": (SB, [128, 1], I32), "pj": (SB, [128, 1], I32), "thr": (SB, [128, 1], F32),
     "ip": (SB, [128, 1], I32), "c1": (SB, [128, 1], I32), "c2": (SB, [128, 1], I32), "c3": (SB, [128, 1], I32),
     "c4": (SB, [128, 1], I32), "c5": (SB, [128, 1], I32), "c6": (SB, [128, 1], I32),
     "g16": (SB, [128, 1], F32), "par": (SB, [128, 1], F32), "rc": (SB, [128, 1], F32), "wc": (SB, [128, 1], F32), "kz": (SB, [128, 1], F32),
     "ff": (SB, [128, 14], F32), "f": (SB, [128, 14], F32), "fk": (SB, [128, 14], I32), "a1": (SB, [128, 14], F32),
-    "a2": (SB, [128, 14], F32), "a3": (SB, [128, 14], F32), "sel": (SB, [128, 14], U16), "base": (SB, [128, 14], BF),
-    "t16": (SB, [128, I], BF), "mk": (SB, [128, I], BF), "rs": (SB, [128, I], BF),
+    "a2": (SB, [128, 14], F32), "a3": (SB, [128, 14], F32), "sel": (SB, [128, 14], U16),
+    "t16": (SB, [128, I], BF), "t8": (SB, [128, I], BF), "mk": (SB, [128, I], BF), "rs": (SB, [128, I], BF),
     "cm": (SB, [128, I], BF), "cn": (SB, [128, I], BF), "ch": (SB, [128, 2 * I], F16),
     "ones": (SB, [128, 128], BF), "onef": (SB, [128, 128], F32), "idb": (SB, [128, 128], BF), "idh": (SB, [128, 128], F16),
     "idl": (SB, [128, 128], F16), "id0": (SB, [128, 128], F16), "idx": (SB, [128, 128], BF), "idn": (SB, [128, 128], BF),
     "bd": (SB, [128, 128], BF), "bdh": (SB, [128, 128], F16), "nbk": (SB, [128, 128], BF), "low": (SB, [128, 128], BF),
-    "tr": (SB, [128, 128], BF), "zz": (SB, [128, 144], BF), "zw": (SB, [128, 144], BF),
+    "tr": (SB, [128, 128], BF), "bw": (SB, [128, 128], BF), "zz": (SB, [128, 144], BF),
     "on": (SB, [128, I], F32), "og": (SB, [128, I], F32), "ol": (SB, [128, I], BF),
 }
 for _t in range(RO):
@@ -153,22 +156,28 @@ def rank_program(g, core, T, topo):
     def diagonal(bank, out):
         op("v", [bank, "rs"], [out], lambda e: e.tensor_tensor_scan(T[out][:], T.rs[:], T[bank][:, 0:I], 0.0, A.mult, A.max))
 
-    def judge(j):
-        a, b = JUDGE[j]
-        tt(T.u[:, I * a:I * b], "u%d" % j, xw.indirect(T.ku[:, 14 * a:14 * b]), T.gj[:, 0:I * (b - a)], ["x", "ku", "gj0", "gj1"], A.subtract)
+    def judge(j, x):
+        a, b = ([0] + JUDGE)[j], JUDGE[j]
+        c = 16 * (a % 14)
+        tt(T.u[:, 16 * a:16 * b], "u%d" % j, T[x][:, 16:16 + WX].indirect(T.ku[:, a:b]), T.gj[:, c:c + 16 * (b - a)],
+           [x, "ku", "gj0", "gj1"], A.subtract)
 
     def mark(j):
-        a, b = JUDGE[j]
-        act(T.w[:, I * a:I * b], "w%d" % j, T.u[:, I * a:I * b], ["u%d" % j], F.Sigmoid, scale=4.0, bias=-4.0 * 644 - math.log(32.0))
-        for k in range(a, b):
-            mm("pa", 0, "zz", T.w[:, I * k:I * k + I], "w%d" % j, I, k == 0, k == 15, lhs=T.zz[:, 15 - k:143 - k])
+        a, b = 16 * ([0] + JUDGE)[j], 16 * JUDGE[j]
+        act(T.w[:, a:b], "w%d" % j, T.u[:, a:b], ["u%d" % j], F.Sigmoid, scale=4.0, bias=-4.0 * 644 - math.log(32.0))
+        for c in range(a, b, I):
+            k, n = c // I, min(I, b - c)
+            mm("pa", c % I, "zz", T.w[:, c:c + n], "w%d" % j, n, c == 0, c + n == 16 * I, lhs=T.zz[:, 15 - k:143 - k])
 
     fetched = [0]
 
-    def fetch(n):
+    def fetch(n, helped=()):
         for j in range(fetched[0], min(fetched[0] + n, 8)):
-            act(T.nb[:, 2 * I * j:2 * I * j + 2 * I], "nb%d" % j, T.rel0[:, 0:W].indirect(T.lu[:, 28 * j:28 * j + 28]), ["rel0", "lu"],
-                scale=1.0 / 2048, bias=-HALF)
+            out, got = T.nb[:, 2 * I * j:2 * I * j + 2 * I], T.rel0[:, 0:W].indirect(T.lu[:, 28 * j:28 * j + 28])
+            if j in helped:
+                ts(out, "nb%d" % j, got, ["rel0", "lu"], -1023.5, 1.0 / 2048, A.add, A.mult)
+            else:
+                act(out, "nb%d" % j, got, ["rel0", "lu"], scale=1.0 / 2048, bias=-HALF)
             for k in (2 * j, 2 * j + 1):
                 load("s", "d_mo", T.mo[k::16, :], T.nb[k::16, I * k:I * k + I], ["nb%d" % j], ["mo%d" % k])
             fetched[0] = j + 1
@@ -176,24 +185,25 @@ def rank_program(g, core, T, topo):
             for k in range(16):
                 wrote["mo%d" % k] = wrote["mo15"]
 
-    def limits(src, key):
+    def limits(src, key, up):
         for c in range(2):
-            act(T.gj[:, I * c:I * c + I], "gj%d" % c, src, [key], bias=-641.5)
+            act(T.gj[:, I * c:I * c + I], "gj%d" % c, src, [key], bias=up - 641.5)
 
     load("s", "d_grd", T.grd0[:], T.grd[:], [], ["grd0"])
     load("a", "d_lim", T.lim0[:], T.lim[:], [], ["lim0"])
-    load("s", "d_x", xw, T.xc[:], [], ["x"])
-    load("a", "d_nam", T.nam0[:], T.nam[:], [], ["nam0"])
+    load("s", "d_x", T.x0[:, 16:16 + WX], T.xc[:], [], ["x0"])
+    load("s", "d_nam", T.nam0[:], T.nam[:], [], ["nam0"])
     load("s", "d_rel", T.rel0[:], T.rel[:], [], ["rel0"])
 
     iota("ip", [[0, 1]], 1)
     iota("ff", [[16, 14]], 1)
+    iota("t16", [[0, 14], [1, 16]], 0)
     memset(T.ones[:], "ones", 1.0)
     select("bd", "ones", [[-16, 8], [0, 16]], A.is_ge, 0.0, 0, 1)
     select("bd", "bd", [[16, 8], [0, 16]], A.is_ge, 0.0, 15, -1)
-    iota("t16", [[0, 14], [1, 16]], 0)
     select("idb", "ones", [[-1, 128]], A.is_equal, 0.0, 0, 1)
     select("low", "bd", [[1, 128]], A.is_gt, 0.0, 0, -1)
+    iota("t8", [[8, I]], 0)
     memset(T.pv[:, 256:512], "pad", 0.0)
     wrote["pn"] = wrote["pad"]
     ts(T.c1[:], "c1", T.ip[:], ["ip"], 112, None, A.bitwise_and)
@@ -208,80 +218,78 @@ def rank_program(g, core, T, topo):
     ts(T.fk[:], "fk", T.f[:], ["f"], 1.0 / 14, -13.0 / 28, A.mult, A.add)
     ts(T.par[:], "par", T.c4[:], ["c4"], 240.0, None, A.mult)
     ts(T.a2[:], "a2", T.f[:], ["f"], 16.0, None, A.mult)
-    memset(T.x[:, 0:16], "xz", 0.0)
+    memset(T.ch[:, 0:I], "ch0", 0.0)
     ts(T.a1[:], "a1", T.fk[:], ["fk", "par"], -223.0, T.par[:], A.mult, A.add)
-    memset(T.zw[:], "zw", 0.0)
+    memset(T.ch[:, I:2 * I], "ch", 2.0)
     copy(T.rc[:], "rc", T.c5[:], ["c5"])
     tt(T.a3[:], "a3", T.a1[:], T.a2[:], ["a1", "a2"], A.add)
-    ts(T.wc[:], "wc", T.c6[:], ["c6"], 2.0, 1.0, A.mult, A.add)
+    copy(pn, "pn", T.grd0[:], ["grd0"])
     ts(T.kz[:], "kz", T.c5[:], ["c5"], 0.5, 2048.0, A.is_lt, A.mult)
     copy(T.sel[:], "sel", T.a3[:], ["a3"])
 
     for t in range(RO):
         last = t == RO - 1
-        h, gs, gr = "h%d" % t, "gs%d" % t, "lim0" if t == 0 else "gr"
+        h, gs = "h%d" % t, "gs%d" % t
+        x, gr, up, bm = ("x0", "lim0", UP, "bm0") if t == 0 else ("x", "gr", 0.0, "bm")
         if t == 0:
-            copy(pn, "pn", T.grd0[:], ["grd0"])
-            memset(T.ch[:, 0:I], "ch0", 0.0)
             turn("tp")
-            memset(T.ch[:, I:2 * I], "ch", 2.0)
-            copy(T.ku[:], "ku", turned("tp"), ["tp0", "tp1", "sel"])
-            limits(T.lim0[:], "lim0")
-            copy(pn, "pn", T.nam0[:], ["nam0"])
-            ts(T.zz[:, 15:143:16], "zz", T.bd[:, 0:128:16], ["bd"], -33.0, None, A.mult)
-            turn("tq")
             ts(T.mk[:], "mk", T.t16[:], ["t16", "rc"], T.rc[:], -16384.0, A.not_equal, A.mult)
-            copy(T.lu[:], "lu", turned("tq"), ["tq0", "tq1", "sel"])
+            ts(T.zz[:, 15:143:16], "zz", T.bd[:, 0:128:16], ["bd"], -33.0, None, A.mult)
+            copy(T.ku[:], "ku", turned("tp"), ["tp0", "tp1", "sel"])
             ts(T.id0[:], "id0", T.idb[:], ["idb", "kz"], T.kz[:], None, A.mult)
-            act(T.zw[:, 15:143:16], "zw", T.bd[:, 0:128:16], ["bd", "wc"], scale=T.wc[:])
+            limits(T.lim0[:], "lim0", 0.0)
             act(T.rs[:], "rs", T.t16[:], ["t16"], F.Sigmoid, scale=256.0, bias=-128.0)
             act(T.cm[:], "cm", T.t16[:], ["t16"], scale=0.0, bias=-4096.0)
             act(T.idx[:], "idx", T.idb[:], ["idb"], scale=4096.0)
             act(T.low[:], "low", T.low[:], ["low"], scale=-4096.0)
+        mm("pl", 0, "idb", T.mk[:], "mk", I, True, False)
+        mm("pf", 0, "id0", T.ch[:], "ch", 2 * I, True, False)
+        mm("pm", 0, "idb", T.cm[:], "cm", I, True, False)
+        mm("pk", 0, "idb", T.mk[:], "mk", I, True, False)
         for j in range(len(JUDGE)):
-            if j == (1 if t == 0 else 0):
-                mm("pl", 0, "idb", T.mk[:], "mk", I, True, False)
-                mm("pf", 0, "id0", T.ch[:], "ch", 2 * I, True, False)
-                mm("pm", 0, "idb", T.cm[:], "cm", I, True, False)
-                mm("pk", 0, "idb", T.mk[:], "mk", I, True, False)
-            judge(j)
+            judge(j, x)
             mark(j)
-            if j in (AMONG if t > 0 else AMONG0):
+            if t > 0 and j in AMONG:
                 fetch(1)
+            if t == 0 and j == len(JUDGE) - 2:
+                copy(pn, "pn", T.nam0[:], ["nam0"])
         if t == 0:
+            turn("tq")
             copy(T.k16[:], "k16", T.grd0[:], ["grd0"])
+            copy(T.lu[:], "lu", turned("tq"), ["tq0", "tq1", "sel"])
             copy(T.idh[:], "idh", T.idb[:], ["idb"])
-            ts(T.l16[:], "l16", T.nam0[:], ["nam0"], 1.0 / 2048, -HALF, A.mult, A.add)
-            ts(T.idl[:], "idl", T.idb[:], ["idb"], 2048.0, None, A.mult)
             memset(T.thr[:], "thr", 192 + 4100.5)
-            tt(T.tr[:], "tr", T.low[:], T.idx[:], ["low", "idx"], A.add)
             act(T.nbk[:], "nbk", T.bd[:], ["bd"], scale=-4096.0)
             act(T.cn[:], "cn", T.t16[:], ["t16"], scale=0.0, bias=-2.0 ** 24)
         else:
-            copy(T.pi[:], "pi", T.pe[:, 448:449], ["pe"])
             ts(T.k16[:], "k16", pn, ["pn"], ROUND, -ROUND, A.add, A.add)
             ts(T.pj[:], "pj", T.pi[:], ["pi"], 1, None, A.bitwise_and)
             tt(T.l16[:], "l16", pn, T.k16[:], ["pn", "k16"], A.subtract)
             ts(T.thr[:], "thr", T.pj[:], ["pj"], 32.0, 192 + 4100.5, A.mult, A.add)
         fetch(BEFORE_DEAD)
         mm("pe", 0, "idh", T.k16[:], "k16", I, True, False)
-        mm("pf", 0, "idl", T.l16[:], "l16", I, False, False)
-        mm("pf", I, "id0", T.l16[:], "l16", I, False, False)
         ts(pa, "a", T.pa[:, 0:I], ["pa", "thr"], T.thr[:], 4100.5, A.add, A.max)
         if t == 0:
-            copy(T.bdh[:], "bdh", T.bd[:], ["bd"])
+            ts(T.l16[:], "l16", T.nam0[:], ["nam0"], 1.0 / 2048, -HALF, A.mult, A.add)
+            ts(T.idl[:], "idl", T.idb[:], ["idb"], 2048.0, None, A.mult)
+        mm("pf", 0, "idl", T.l16[:], "l16", I, False, False)
+        mm("pf", I, "id0", T.l16[:], "l16", I, False, False)
         ts(T.b[:], "b", pa, ["a"], 3.5, None, A.add)
         if t == 0:
-            ts(T.base[:], "base", T.f[:], ["f"], 8.0, None, A.mult)
+            tt(T.tr[:], "tr", T.low[:], T.idx[:], ["low", "idx"], A.add)
         tt(T.und[:], "und", pa, T.b[:], ["a", "b"], A.is_lt)
         act(T.dead[:], ["dead", "cnt"], T.b[:], ["b"], F.Relu, scale=-1.0 / 16, bias=257.0, accum_out=T.cnt[:])
         mm("pe", 0, "tr", T.und[:], "und", I, False, True)
         mm("pf", 0, "tr", T.und[:], "und", I, False, False)
         mm("pf", I, "nbk", T.und[:], "und", I, False, True)
         if t == 0:
-            ts(T.bm[:], "bm", T.f[:], ["f"], 8.0, -1028.5, A.mult, A.add)
+            copy(T.bdh[:], "bdh", T.bd[:], ["bd"])
+            memset(T.x0[:, 0:16], "x0z", 0.0)
+            memset(T.x[:, 0:16], "xz", UP)
+            ts(T.wc[:], "wc", T.c6[:], ["c6"], 2.0, 1.0, A.mult, A.add)
+            ts(T.bm0[:], "bm0", T.f[:], ["f"], 8.0, -1028.5, A.mult, A.add)
+            ts(T.bm[:], "bm", T.f[:], ["f"], 8.0, 64 * UP - 1028.5, A.mult, A.add)
             act(T.onef[:], "onef", T.ones[:], ["ones"])
-            act(T.idn[:], "idn", T.idb[:], ["idb"], scale=-1.0)
 
         def kh():
             ts(T.kh[:], "kh", T.pe[:, 0:I], ["pe"], 16.0 - 4096, 0.0, A.add, A.max)
@@ -289,20 +297,18 @@ def rank_program(g, core, T, topo):
 
         def lh():
             ts(T.lh[:], "lh", T.pf[:, 0:2 * I], ["pf"], 1024.5 - 4096, 0.0, A.add, A.max)
-            mm("pa", 0, "idb", T.cn[:], "cn", I, True, False)
-            mm("pl", 0, "bdh", T.lh[:, 0:I], "lh", I, False, False)
-            mm("pl", 0, "bdh", T.lh[:, I:2 * I], "lh", I, False, True)
-            mm("pa", 0, "idx", T.b[:], "b", I, False, True)
-            mm("pm", 0, "idh", T.k16[:], "k16", I, False, False)
-            mm("pm", 0, "idx", T.und[:], "und", I, False, False)
-            mm("pm", 0, "idh", T.l16[:], "l16", I, False, True)
-            mm("pe", 0, "idx", T.und[:], "und", I, True, False)
-            mm("pe", 0, "idx", T.dead[:], "dead", I, False, True)
-            if not last:
-                mm("pe", 448, "onef", T.cnt[:], "cnt", 1, True, True)
+            sums = {"cn": ("pa", 0, "idb", T.cn[:], "cn", I, True, False), "b": ("pa", 0, "idx", T.b[:], "b", I, False, True),
+                    "l0": ("pl", 0, "bdh", T.lh[:, 0:I], "lh", I, False, False), "l1": ("pl", 0, "bdh", T.lh[:, I:2 * I], "lh", I, False, True),
+                    "mk": ("pm", 0, "idh", T.k16[:], "k16", I, False, False), "mu": ("pm", 0, "idx", T.und[:], "und", I, False, False),
+                    "ml": ("pm", 0, "idh", T.l16[:], "l16", I, False, True),
+                    "eu": ("pe", 0, "idx", T.und[:], "und", I, True, False), "ed": ("pe", 0, "idx", T.dead[:], "dead", I, False, True),
+                    "cnt": ("pf", 0, "onef", T.cnt[:], "cnt", 1, True, True)}
+            for s in SUMS.split():
+                if s != "cnt" or not last:
+                    mm(*sums[s])
 
         def send():
-            tt(T[gs][:], gs, T.x[:, 0:16 + WX].indirect(T.ks[:]), T[gr][:], ["x", "xz", "ks", gr], A.max)
+            tt(T[gs][:], gs, T[x][:, 0:16 + WX].indirect(T.ks[:]), T[gr][:], [x, x + "z", "ks", gr], A.max)
             dst = T.cores[(rank + 1 + t % 7) % 8]
             src = T.cores[(rank - 1 - t % 7) % 8]
             eng = topo.engines(core, dst)[:8]
@@ -310,53 +316,59 @@ def rank_program(g, core, T, topo):
             waits("g", [gs], [])
             g.remote_dma(T[h][:], T[gs][:], T.sem["arr%d" % t], T.sem.sent, pid, rid, sum(1 << e for e in eng))
             wrote[h] = ("remote", "arr%d" % t, len(topo.engines(src, core)[:8]), {})
-            mm("pg", 0, "idb", T[gs][:], gs, I, True, last)
             if not last:
-                mm("pk", 0, "idb", T.base[:], "base", 14, True, False)
+                mm("pg", 0, "idb", T[gs][:], gs, I, True, False)
+                mm("pk", 0, "idb", T.mk[:], "mk", I, True, False)
+                mm("pk", 0, "idb", T.t8[:], "t8", I, False, False)
 
         def rest():
-            fetch(8)
+            fetch(8, HELP0 if t == 0 else ())
             fetched[0] = 0
             if t == 0:
-                act(T.c128[:], "c128", T.t16[:], ["t16"], scale=0.0, bias=-128.0)
+                act(T.bw[:], "bw", T.bd[:], ["bd", "wc"], scale=T.wc[:])
+                act(T.idn[:], "idn", T.idb[:], ["idb"], scale=-1.0)
+                act(xw, "x", T.x0[:, 16:16 + WX], ["x0"], bias=UP)
+                act(T.half[:], "half", T.t16[:], ["t16"], scale=0.0, bias=0.5)
+            if last:
+                act(T.pg[:, 0:I], "pg", T[gs][:], [gs], bias=-UP)
 
         def land():
+            act(T.hp[:], "hp", T[h][:], [h], bias=up - 0.5)
+            mm("pk", 0, "bw", T[h][:], h, I, False, True)
             mm("pg", 0, "idn", T[h][:], h, I, False, True)
             act(T.rl[:], "rl", T.pg[:, 0:I], ["pg"], F.Relu, bias=-2.0)
-            for r in range(16):
-                mm("pk", 0, "zw", T[h][:, r::16], h, 14, False, r == 15, lhs=T.zw[:, 15 - r:143 - r])
 
         def low():
             mm("pg", 0, "idb", T[gs][:], gs, I, True, False)
             mm("pg", 0, "idn", T.rl[:], "rl", I, False, True)
-            limits(T.pg[:, 0:I], "pg")
+            limits(T.pg[:, 0:I], "pg", up)
 
+        q = T.sq[:, 15::16]
         step = {
             "kh": kh, "lh": lh, "gs": send, "rest": rest, "land": land, "low": low, "early": lambda: fetch(EARLY),
-            "sk": lambda: diagonal("pk", "sk"), "sl": lambda: diagonal("pl", "sl"),
+            "sk": lambda: diagonal("pk", "sk"), "sl": lambda: diagonal("pl", "sl"), "sq": lambda: diagonal("pk", "sq"),
             "ks": lambda: copy(T.ks[:], "ks", T.sk[:, 15::16], ["sk"]),
             "ls": lambda: ts(T.ls[:], "ls", T.sl[:, 15::16], ["sl"], -1.0, None, A.add),
             "md": lambda: ts(T.md[:], "md", T.rel0[:, 0:W].indirect(T.ls[:]), ["rel0", "ls"], -1023.5, 1.0 / 2048, A.add, A.mult),
             "t1": lambda: tt(T.t1[:], "t1", T.md[:], T.pa[:, 0:I], ["md", "pa"], A.subtract),
             "t2": lambda: tt(T.t2[:], "t2", T.mo[:], T.pe[:, 0:I], ["mo%d" % k for k in range(16)] + ["pe"], A.subtract),
-            "m1": lambda: tt(pn, "pn", T.t1[:], T.pm[:, 0:I], ["t1", "pm"], A.max),
-            "m2": lambda: tt(pn, "pn", T.t2[:], pn, ["t2", "pn"], A.max),
-            "turn": lambda: turn("tp"),
+            "m1": lambda: tt(pn, "pn", T.t2[:], T.pm[:, 0:I], ["t2", "pm"], A.max),
+            "m2": lambda: tt(pn, "pn", T.t1[:], pn, ["t1", "pn"], A.max),
+            "turn": lambda: turn("tp"), "pi": lambda: copy(T.pi[:], "pi", T.pf[:, 0:1], ["pf"]),
             "kt": lambda: ts(T.kt[:], "kt", turned("tp"), ["tp0", "tp1", "sel"], ROUND, -ROUND, A.add, A.add),
             "lt": lambda: tt(T.lt[:], "lt", pn if last else turned("tp"), T.og[:] if last else T.kt[:],
                              ["pn", "og"] if last else ["tp0", "tp1", "sel", "kt"], A.subtract),
             "lu": lambda: ts(T.lu[:], "lu", T.lt[:], ["lt"], 2048.0, 1023.5, A.mult, A.add),
             "ku": lambda: copy(T.ku[:], "ku", T.kt[:], ["kt"]),
-            "gr": lambda: act(T.gr[:], "gr", T.pg[:, 0:I], ["pg"]),
-            "f8": lambda: tt(T.f8[:], "f8", T.pk[:, 0:14], T.bm[:], ["pk", "bm"], A.subtract),
-            "z": lambda: tt(T.z[:], "z", T.pk[:, 0:14], T.f8[:], ["pk", "f8"], A.subtract),
-            "cu": lambda: ts(T.cu[:], "cu", T.z[:], ["z"], 1032.0, None, A.add),
-            "bl": lambda: tt(T.bl[:], "bl", xw.indirect(T.cu[:]), T[h][:], ["x", "cu", h], A.add),
-            "b2": lambda: ts(T.b2[:], "b2", T.bl[:], ["bl"], 0.5, 127.75, A.mult, A.add),
-            "put": lambda: tt(xw.indirect(T.cu[:]), "x", T.b2[:], T.c128[:], ["b2", "cu", "c128"], A.add),
+            "gr": lambda: act(T.gr[:], "gr", T.pg[:, 0:I], ["pg"], bias=up),
+            "f8": lambda: tt(T.f8[:], "f8", q, T[bm][:], ["sq", bm], A.subtract),
+            "z": lambda: tt(T.z[:], "z", q, T.f8[:], ["sq", "f8"], A.subtract),
+            "cu": lambda: ts(T.cu[:], "cu", T.z[:], ["z"], 1032.0 - 64 * (UP - up), None, A.add),
+            "bl": lambda: tt(T.bl[:], "bl", xw.indirect(T.cu[:]), T.hp[:], ["x", "cu", "hp"], A.add),
+            "put": lambda: tt(xw.indirect(T.cu[:]), "x", T.bl[:], T.half[:], ["bl", "cu", "half"], A.mult),
             "og": lambda: (ts(T.og[:], "og", pn, ["pn"], ROUND, -ROUND, A.add, A.add), load("s", "d_og", T.yg[:], T.og[:], ["og"], ["yg"])),
             "on": lambda: (ts(T.on[:], "on", T.lt[:], ["lt"], 2048.0, 1023.5, A.mult, A.add), load("s", "d_on", T.yn[:], T.on[:], ["on"], ["yn"])),
-            "h2": lambda: ts(T.gm[:], "gm", T[h][:], [h], 2.0, None, A.add),
+            "h2": lambda: ts(T.gm[:], "gm", T[h][:], [h], 2.0 - UP, None, A.add),
             "ol": lambda: (tt(T.ol[:], "ol", T.gm[:], T.pg[:, 0:I], ["gm", "pg"], A.min), load("a", "d_ol", T.yl[:], T.ol[:], ["ol"], ["yl"])),
         }
         for s in (RAISE + " " + (END if last else NEXT)).split():

@@ -2,18 +2,19 @@ import math
 from concourse.mybir import dt, AluOpType, AxisListType, ActivationFunctionType
 
 I = 224
+H = 112
 WX = 1792
 W = 2048
 RO = 4
-JUDGE = [28, 56, 84, 112, 140, 168, 196, 210, 218, 224]
-EARLY = 3
-AMONG = (1,)
-BEFORE_DEAD = 2
+JUDGE = [[4, 8, 12, 16], [4, 8, 10, 12, 14, 16]]
 HELP0 = (3, 5)
-RAISE = "kh lh sk ks gs rest sl"
-NEXT = "land ls md t2 t1 m1 pi m2 turn sq kt low f8 z ku cu gr lt bl lu early put"
-END = "ls md t2 t1 m1 m2 og lt h2 on ol"
-SUMS = "eu l0 l1 ed mk mu ml cn b cnt"
+ORDER = ("j0 j0 j0 w0 G0 j0 w0 w0 k1 j1 P0 j1 w0 E j1 N0 L0 a0 j1 w1 b0 w1 w1 j1 u0 d0 w1 j1 l1 w1 kh0 w1 lt1 lh0 lu1 sk0 f a1 N1 so0 ks0 G1 "
+         "sl0 s0 b1 gs0 u1 ls0 si0 d1 P1 md0 kh1 L1 lh1 t0 o0 F sk1 m0 so1 ks1 n0 sl1 gs1 R0 land0 turn0 ls1 si1 kt0 s1 sq0 md1 r0 rl0 lt0 z0 "
+         "t1 C ku0 hp0 lu0 f cu0 R1 m1 low0 f land1 pi hp1 o1 bl0 n1 k0 sq1 rl1 low1 turn1 r1 gj0 put0 f z1 f kt1 gj1 cu1 bl1 pj l0 gr0 put1 "
+         "ku1 thr gr1")
+LATE = ("lt1", "lu1", "k1", "l1")
+NEXT = ("R", "land", "rl", "low", "gj", "gr", "hp", "z", "cu", "bl", "put", "k", "l", "lt", "lu")
+LAST = {"sq": "h", "r": "y", "turn": "og", "kt": "ot", "ku": "on"}
 ROUND = 1.5 * 2.0 ** 23
 HALF = 1023.5 / 2048
 UP = 144.0
@@ -26,37 +27,37 @@ SCRATCH = {
     "u": (SB, [128, 16 * I], BF), "w": (SB, [128, 16 * I], BF), "nb": (SB, [128, 16 * I], F32),
     "ku": (SB, [128, I], U16), "lu": (SB, [128, I], U16), "tp": (SB, [128, 480], F32), "tq": (SB, [128, 480], F32),
     "kt": (SB, [128, I], F32), "lt": (SB, [128, I], F32), "k16": (SB, [128, I], F16), "l16": (SB, [128, I], F16),
-    "gj": (SB, [128, 2 * I], F32), "gr": (SB, [128, I], BF), "rl": (SB, [128, I], BF), "gm": (SB, [128, I], BF), "hp": (SB, [128, I], F32),
+    "gj": (SB, [128, 8 * H], F32), "gr": (SB, [128, I], BF), "rl": (SB, [128, I], BF), "gm": (SB, [128, I], BF), "hp": (SB, [128, I], F32),
     "b": (SB, [128, I], BF), "und": (SB, [128, I], BF), "dead": (SB, [128, I], BF),
     "kh": (SB, [128, I], F16), "lh": (SB, [128, 2 * I], F16),
     "sk": (SB, [128, I], F32), "sl": (SB, [128, I], F32), "sq": (SB, [128, I], F32),
-    "ks": (SB, [128, 14], U16), "ls": (SB, [128, 14], U16), "cu": (SB, [128, 14], U16),
+    "ks": (SB, [128, 16], U16), "ls": (SB, [128, 16], U16), "cu": (SB, [128, 16], U16), "sel": (SB, [128, 16], U16),
     "f8": (SB, [128, 14], BF), "z": (SB, [128, 14], F32), "bm0": (SB, [128, 14], F32), "bm": (SB, [128, 14], F32),
-    "bl": (SB, [128, I], BF), "half": (SB, [128, I], BF),
+    "bl": (SB, [128, I], BF), "half": (SB, [128, H], BF),
     "md": (SB, [128, I], F32), "mo": (SB, [128, I], F32), "t1": (SB, [128, I], F32), "t2": (SB, [128, I], F32),
-    "cnt": (SB, [128, 1], F32), "pi": (SB, [128, 1], I32), "pj": (SB, [128, 1], I32), "thr": (SB, [128, 1], F32),
-    "ip": (SB, [128, 1], I32), "c1": (SB, [128, 1], I32), "c2": (SB, [128, 1], I32), "c3": (SB, [128, 1], I32),
-    "c4": (SB, [128, 1], I32), "c5": (SB, [128, 1], I32), "c6": (SB, [128, 1], I32),
-    "g16": (SB, [128, 1], F32), "par": (SB, [128, 1], F32), "rc": (SB, [128, 1], F32), "wc": (SB, [128, 1], F32), "kz": (SB, [128, 1], F32),
-    "ff": (SB, [128, 14], F32), "f": (SB, [128, 14], F32), "fk": (SB, [128, 14], I32), "a1": (SB, [128, 14], F32),
-    "a2": (SB, [128, 14], F32), "a3": (SB, [128, 14], F32), "sel": (SB, [128, 14], U16),
-    "t16": (SB, [128, I], BF), "t8": (SB, [128, I], BF), "mk": (SB, [128, I], BF), "rs": (SB, [128, I], BF),
-    "cm": (SB, [128, I], BF), "cn": (SB, [128, I], BF), "ch": (SB, [128, 2 * I], F16),
-    "ones": (SB, [128, 128], BF), "onef": (SB, [128, 128], F32), "idb": (SB, [128, 128], BF), "idh": (SB, [128, 128], F16),
-    "idl": (SB, [128, 128], F16), "id0": (SB, [128, 128], F16), "idx": (SB, [128, 128], BF), "idn": (SB, [128, 128], BF),
-    "bd": (SB, [128, 128], BF), "bdh": (SB, [128, 128], F16), "nbk": (SB, [128, 128], BF), "low": (SB, [128, 128], BF),
-    "tr": (SB, [128, 128], BF), "bw": (SB, [128, 128], BF), "zz": (SB, [128, 144], BF),
+    "cnt": (SB, [128, 2], F32), "pi": (SB, [128, 1], I32), "pj": (SB, [128, 1], I32), "thr": (SB, [128, 1], F32),
+    "ip": (SB, [128, 1], I32), "c1": (SB, [128, 1], I32), "c2": (SB, [128, 1], I32), "c5": (SB, [128, 1], I32), "c6": (SB, [128, 1], I32),
+    "g16": (SB, [128, 1], F32), "gf": (SB, [128, 1], F32), "rc": (SB, [128, 1], F32), "wc": (SB, [128, 1], F32), "kz": (SB, [128, 1], F32),
+    "ff": (SB, [128, 14], F32), "f": (SB, [128, 14], F32), "e1": (SB, [128, 7], I32), "e2": (SB, [128, 7], I32), "e3": (SB, [128, 7], I32),
+    "d1": (SB, [128, 7], F32), "d2": (SB, [128, 7], F32), "d3": (SB, [128, 7], F32), "d4": (SB, [128, 14], F32), "d5": (SB, [128, 14], F32),
+    "a2": (SB, [128, 7], F32),
+    "t16": (SB, [128, H], BF), "t8": (SB, [128, I], BF), "mk": (SB, [128, H], BF), "rs": (SB, [128, H], BF),
+    "cc": (SB, [128, I], BF), "ch": (SB, [128, I], F16),
+    "ones": (SB, [128, 128], BF), "onef": (SB, [128, 128], F32), "idb": (SB, [128, 128], BF), "idl": (SB, [128, 128], BF),
+    "id0": (SB, [128, 128], BF), "idx": (SB, [128, 128], BF), "idn": (SB, [128, 128], BF), "bd": (SB, [128, 128], BF),
+    "nbk": (SB, [128, 128], BF), "low": (SB, [128, 128], BF), "tr": (SB, [128, 128], BF), "bw": (SB, [128, 128], BF), "zz": (SB, [128, 144], BF),
     "on": (SB, [128, I], F32), "og": (SB, [128, I], F32), "ol": (SB, [128, I], BF),
 }
 for _t in range(RO):
-    SCRATCH["gs%d" % _t] = (SB, [128, I], BF)
-    SCRATCH["h%d" % _t] = (SB, [128, I], BF)
-PSUM = ("pa", "pv", "pe", "pk", "pf", "pl", "pm", "pg")
+    for _u in range(2):
+        SCRATCH["gs%d%d" % (_t, _u)] = (SB, [128, H], BF)
+        SCRATCH["h%d%d" % (_t, _u)] = (SB, [128, H], BF)
+PSUM = ("pa0", "pa1", "pv", "pe", "pk", "pf", "pl", "pg")
 for _b in PSUM:
     SCRATCH[_b] = ("psum", [128, 512], F32)
 
-SEMAPHORES = ["cv", "ca", "ct", "cg", "sent", "d_x", "d_lim", "d_grd", "d_nam", "d_rel", "d_on", "d_og", "d_ol", "d_mo"]
-SEMAPHORES += ["arr%d" % _t for _t in range(RO)]
+SEMAPHORES = ["cv", "ca", "ct", "cg", "sent", "d_x", "d_lim", "d_grd", "d_nam", "d_rel", "d_on", "d_og", "d_ol", "d_m0", "d_m1"]
+SEMAPHORES += ["arr%d%d" % (_t, _u) for _t in range(RO) for _u in range(2)]
 
 
 def rank_program(g, core, T, topo):
@@ -143,51 +144,109 @@ def rank_program(g, core, T, topo):
     def iota(name, pattern, mult):
         op("g", [], [name], lambda e: e.iota(T[name][:], pattern, 0, mult, allow_small_or_imprecise_dtypes=True))
 
-    pa, pn = T.pv[:, 0:I], T.pv[:, 272:272 + I]
+    pn = T.pv[:, 272:272 + I]
     xw = T.x[:, 16:16 + WX]
+    pns, tb, pg = ["pn0", "pn1"], ["tp", "tq"], ["pg", "pe"]
 
-    def turn(dst):
-        op("v", ["pn"], [dst + "0"], lambda e: e.transpose(T[dst][:, 0:I], pn))
-        op("v", ["pn", "pad"], [dst + "1"], lambda e: e.transpose(T[dst][:, I:480], T.pv[:, 256:512]))
+    def half(name, u):
+        return T[name][:, H * u:H * u + H]
 
-    def turned(src):
-        return T[src][:, 0:480].indirect(T.sel[:])
+    def own(u):
+        return T.pv[:, 272 + H * u:272 + H * u + H]
 
-    def diagonal(bank, out):
-        op("v", [bank, "rs"], [out], lambda e: e.tensor_tensor_scan(T[out][:], T.rs[:], T[bank][:, 0:I], 0.0, A.mult, A.max))
+    def count_of(u):
+        return T.pv[:, 128 * u:128 * u + H]
 
-    def judge(j, x):
-        a, b = ([0] + JUDGE)[j], JUDGE[j]
-        c = 16 * (a % 14)
-        tt(T.u[:, 16 * a:16 * b], "u%d" % j, T[x][:, 16:16 + WX].indirect(T.ku[:, a:b]), T.gj[:, c:c + 16 * (b - a)],
-           [x, "ku", "gj0", "gj1"], A.subtract)
+    def picked(name, u):
+        return T[name][:, H * u + 15:H * u + H:16]
 
-    def mark(j):
-        a, b = 16 * ([0] + JUDGE)[j], 16 * JUDGE[j]
-        act(T.w[:, a:b], "w%d" % j, T.u[:, a:b], ["u%d" % j], F.Sigmoid, scale=4.0, bias=-4.0 * 644 - math.log(32.0))
-        for c in range(a, b, I):
-            k, n = c // I, min(I, b - c)
-            mm("pa", c % I, "zz", T.w[:, c:c + n], "w%d" % j, n, c == 0, c + n == 16 * I, lhs=T.zz[:, 15 - k:143 - k])
+    def listed(name, u):
+        return T[name][:, 8 * u:8 * u + 7]
+
+    def seven(name, u):
+        return T[name][:, 7 * u:7 * u + 7]
+
+    def turned(src, u):
+        return T[src][:, 0:480].indirect(listed("sel", u))
+
+    def turn(dst, a=0, b=I, c=0, e=256):
+        op("v", pns, [dst + "0"], lambda q: q.transpose(T[dst][:, a:b], T.pv[:, 272 + a:272 + b]))
+        op("v", pns, [dst + "1"], lambda q: q.transpose(T[dst][:, I + c:I + e], T.pv[:, 256 + c:256 + e]))
+
+    def diagonal(bank, out, u):
+        op("v", [bank, "rs"], [out + str(u)], lambda e: e.tensor_tensor_scan(half(out, u), T.rs[:], T[bank][:, 0:H], 0.0, A.mult, A.max))
 
     fetched = [0]
 
     def fetch(n, helped=()):
         for j in range(fetched[0], min(fetched[0] + n, 8)):
-            out, got = T.nb[:, 2 * I * j:2 * I * j + 2 * I], T.rel0[:, 0:W].indirect(T.lu[:, 28 * j:28 * j + 28])
+            a, u = 4 * (j % 4), j // 4
+            c = 16 * u + a
+            out, got = T.nb[:, H * c:H * c + 4 * H], T.rel0[:, 0:W].indirect(T.lu[:, 7 * c:7 * c + 28])
             if j in helped:
-                ts(out, "nb%d" % j, got, ["rel0", "lu"], -1023.5, 1.0 / 2048, A.add, A.mult)
+                ts(out, "nb%d" % j, got, ["rel0", "lu%d" % u], -1023.5, 1.0 / 2048, A.add, A.mult)
             else:
-                act(out, "nb%d" % j, got, ["rel0", "lu"], scale=1.0 / 2048, bias=-HALF)
-            for k in (2 * j, 2 * j + 1):
-                load("s", "d_mo", T.mo[k::16, :], T.nb[k::16, I * k:I * k + I], ["nb%d" % j], ["mo%d" % k])
+                act(out, "nb%d" % j, got, ["rel0", "lu%d" % u], scale=1.0 / 2048, bias=-HALF)
+            for k in range(a, a + 4):
+                load("s", "d_m%d" % u, T.mo[k::16, H * u:H * u + H], T.nb[k::16, H * (16 * u + k):H * (16 * u + k) + H], ["nb%d" % j],
+                     ["mo%d_%d" % (u, k)])
+            if a == 12:
+                for k in range(16):
+                    wrote["mo%d_%d" % (u, k)] = wrote["mo%d_15" % u]
             fetched[0] = j + 1
-        if fetched[0] == 8:
-            for k in range(16):
-                wrote["mo%d" % k] = wrote["mo15"]
 
-    def limits(src, key, up):
-        for c in range(2):
-            act(T.gj[:, I * c:I * c + I], "gj%d" % c, src, [key], bias=up - 641.5)
+    def limits(src, key, up, u):
+        for c in range(4 * u, 4 * u + 4):
+            act(half("gj", c), "gj%d" % c, src, [key], bias=up - 641.5)
+
+    def masks(bank):
+        mm(bank, 0, "idb", T.mk[:], "mk", H, True, False)
+
+    def guards(u):
+        mm("pe", 0, "idb", half("k16", u), "k16%d" % u, H, True, False)
+
+    def names(u):
+        mm("pf", 0, "id0", T.ch[:], "ch", I, True, False)
+        mm("pf", 0, "idl", half("l16", u), "l16%d" % u, H, False, False)
+        mm("pf", H, "id0", half("l16", u), "l16%d" % u, H, False, False)
+
+    def und(u):
+        tt(half("und", u), "und%d" % u, count_of(u), half("b", u), ["a%d" % u, "b%d" % u], A.is_lt)
+        mm("pe", 0, "tr", half("und", u), "und%d" % u, H, False, True)
+        mm("pf", 0, "tr", half("und", u), "und%d" % u, H, False, False)
+        mm("pf", H, "nbk", half("und", u), "und%d" % u, H, False, True)
+
+    def kh(u):
+        ts(half("kh", u), "kh%d" % u, T.pe[:, 0:H], ["pe"], 16.0 - 4096, 0.0, A.add, A.max)
+        mm("pk", 0, "bd", half("kh", u), "kh%d" % u, H, False, True)
+
+    def lh(u):
+        ts(T.lh[:, I * u:I * u + I], "lh%d" % u, T.pf[:, 0:I], ["pf"], 1024.5 - 4096, 0.0, A.add, A.max)
+        mm("pl", 0, "bd", half("lh", 2 * u), "lh%d" % u, H, False, False)
+        mm("pl", 0, "bd", half("lh", 2 * u + 1), "lh%d" % u, H, False, True)
+
+    def alive(u):
+        mm("pa%d" % u, 0, "idb", half("cc", 0), "cc", H, True, False)
+        mm("pa%d" % u, 0, "idx", half("b", u), "b%d" % u, H, False, True)
+
+    def implied(u):
+        mm("pa%d" % u, H, "idx", half("und", u), "und%d" % u, H, True, False)
+        mm("pa%d" % u, H, "idx", half("dead", u), "dead%d" % u, H, False, True)
+
+    def old(u):
+        mm("pa%d" % u, I, "idb", half("cc", 1), "cc", H, True, False)
+        mm("pa%d" % u, I, "idb", half("k16", u), "k16%d" % u, H, False, False)
+        mm("pa%d" % u, I, "idx", half("und", u), "und%d" % u, H, False, False)
+        mm("pa%d" % u, I, "idb", half("l16", u), "l16%d" % u, H, False, True)
+
+    def deaths():
+        mm("pf", 0, "onef", T.cnt[:, 0:1], "cnt0", 1, True, False)
+        mm("pf", 0, "onef", T.cnt[:, 1:2], "cnt1", 1, False, True)
+
+    def limits_out(u):
+        tt(half("ol", u), "ol%d" % u, half("gm", u), half("pg", u), ["gm%d" % u, "pg"], A.min)
+        if u == 1:
+            load("a", "d_ol", T.yl[:], T.ol[:], ["ol0", "ol1"], ["yl"])
 
     load("s", "d_grd", T.grd0[:], T.grd[:], [], ["grd0"])
     load("a", "d_lim", T.lim0[:], T.lim[:], [], ["lim0"])
@@ -197,185 +256,208 @@ def rank_program(g, core, T, topo):
 
     iota("ip", [[0, 1]], 1)
     iota("ff", [[16, 14]], 1)
-    iota("t16", [[0, 14], [1, 16]], 0)
+    iota("t16", [[0, 7], [1, 16]], 0)
     memset(T.ones[:], "ones", 1.0)
     select("bd", "ones", [[-16, 8], [0, 16]], A.is_ge, 0.0, 0, 1)
     select("bd", "bd", [[16, 8], [0, 16]], A.is_ge, 0.0, 15, -1)
     select("idb", "ones", [[-1, 128]], A.is_equal, 0.0, 0, 1)
-    select("low", "bd", [[1, 128]], A.is_gt, 0.0, 0, -1)
-    iota("t8", [[8, I]], 0)
-    memset(T.pv[:, 256:512], "pad", 0.0)
-    wrote["pn"] = wrote["pad"]
+    memset(T.pv[:, 256:512], "pn0", 0.0)
+    f7 = T.f[:, 0:7]
     ts(T.c1[:], "c1", T.ip[:], ["ip"], 112, None, A.bitwise_and)
     ts(T.c2[:], "c2", T.ip[:], ["ip"], 4, None, A.arith_shift_right)
     ts(T.c5[:], "c5", T.ip[:], ["ip"], 15, None, A.bitwise_and)
     copy(T.g16[:], "g16", T.c1[:], ["c1"])
-    tt(T.c3[:], "c3", T.c2[:], T.ip[:], ["c2", "ip"], A.add)
+    copy(T.gf[:], "gf", T.c2[:], ["c2"])
     ts(T.c6[:], "c6", T.ip[:], ["ip"], 3, None, A.bitwise_and)
     ts(T.f[:], "f", T.ff[:], ["ff", "g16"], T.g16[:], None, A.subtract)
-    ts(T.c4[:], "c4", T.c3[:], ["c3"], 1, None, A.bitwise_and)
     memset(T.zz[:], "zz", 0.0)
-    ts(T.fk[:], "fk", T.f[:], ["f"], 1.0 / 14, -13.0 / 28, A.mult, A.add)
-    ts(T.par[:], "par", T.c4[:], ["c4"], 240.0, None, A.mult)
-    ts(T.a2[:], "a2", T.f[:], ["f"], 16.0, None, A.mult)
-    memset(T.ch[:, 0:I], "ch0", 0.0)
-    ts(T.a1[:], "a1", T.fk[:], ["fk", "par"], -223.0, T.par[:], A.mult, A.add)
-    memset(T.ch[:, I:2 * I], "ch", 2.0)
     copy(T.rc[:], "rc", T.c5[:], ["c5"])
-    tt(T.a3[:], "a3", T.a1[:], T.a2[:], ["a1", "a2"], A.add)
-    copy(pn, "pn", T.grd0[:], ["grd0"])
+    ts(T.e1[:], "e1", f7, ["f"], 1.0 / 7, -3.0 / 7, A.mult, A.add)
+    ts(T.a2[:], "a2", f7, ["f"], 16.0, None, A.mult)
+    ts(T.d2[:], "d2", f7, ["f", "gf"], T.gf[:], None, A.add)
+    ts(T.d1[:], "d1", T.e1[:], ["e1"], -111.0, None, A.mult)
+    tt(T.e2[:], "e2", T.d2[:], T.e1[:], ["d2", "e1"], A.add)
+    memset(T.ch[:, 0:H], "ch0", 0.0)
+    memset(T.x0[:, 0:16], "x0z", 0.0)
+    tt(T.d3[:], "d3", T.d1[:], T.a2[:], ["d1", "a2"], A.add)
+    ts(T.e3[:], "e3", T.e2[:], ["e2"], 1, None, A.bitwise_and)
+    copy(pn, "pn0", T.grd0[:], ["grd0"])
+    ts(seven("d4", 0), "d40", T.e3[:], ["e3"], 240.0, None, A.mult)
+    ts(seven("d4", 1), "d41", T.e3[:], ["e3"], -240.0, 352.0, A.mult, A.add)
+    turn("tp")
+    for u in range(2):
+        tt(seven("d5", u), "d5%d" % u, T.d3[:], seven("d4", u), ["d3", "d4%d" % u], A.add)
+    memset(T.ch[:, H:I], "ch", 2.0)
+    memset(T.thr[:], "thr", 192 + 4100.5)
     ts(T.kz[:], "kz", T.c5[:], ["c5"], 0.5, 2048.0, A.is_lt, A.mult)
-    copy(T.sel[:], "sel", T.a3[:], ["a3"])
+    for u in range(2):
+        copy(listed("sel", u), "sel%d" % u, seven("d5", u), ["d5%d" % u])
+    ts(T.mk[:], "mk", T.t16[:], ["t16", "rc"], T.rc[:], -16384.0, A.not_equal, A.mult)
+    ts(T.zz[:, 15:143:16], "zz", T.bd[:, 0:128:16], ["bd"], -33.0, None, A.mult)
+    copy(half("ku", 0), "ku0", turned("tp", 0), ["tp0", "tp1", "sel0"])
+    limits(half("lim0", 0), "lim0", 0.0, 0)
+    act(T.rs[:], "rs", T.t16[:], ["t16"], F.Sigmoid, scale=256.0, bias=-128.0)
+    limits(half("lim0", 1), "lim0", 0.0, 1)
+    act(T.nbk[:], "nbk", T.bd[:], ["bd"], scale=-4096.0)
+    act(T.id0[:], "id0", T.idb[:], ["idb", "kz"], scale=T.kz[:])
+    act(T.idl[:], "idl", T.idb[:], ["idb"], scale=2048.0)
+    act(T.idx[:], "idx", T.idb[:], ["idb"], scale=4096.0)
+    iota("t8", [[8, I]], 0)
+    select("low", "nbk", [[1, 128]], A.is_gt, 0.0, 0, -1)
+    select("tr", "low", [[-1, 128]], A.not_equal, 4096.0, 0, 1)
 
-    for t in range(RO):
-        last = t == RO - 1
-        h, gs = "h%d" % t, "gs%d" % t
-        x, gr, up, bm = ("x0", "lim0", UP, "bm0") if t == 0 else ("x", "gr", 0.0, "bm")
-        if t == 0:
-            turn("tp")
-            ts(T.mk[:], "mk", T.t16[:], ["t16", "rc"], T.rc[:], -16384.0, A.not_equal, A.mult)
-            ts(T.zz[:, 15:143:16], "zz", T.bd[:, 0:128:16], ["bd"], -33.0, None, A.mult)
-            copy(T.ku[:], "ku", turned("tp"), ["tp0", "tp1", "sel"])
-            ts(T.id0[:], "id0", T.idb[:], ["idb", "kz"], T.kz[:], None, A.mult)
-            limits(T.lim0[:], "lim0", 0.0)
-            act(T.rs[:], "rs", T.t16[:], ["t16"], F.Sigmoid, scale=256.0, bias=-128.0)
-            act(T.cm[:], "cm", T.t16[:], ["t16"], scale=0.0, bias=-4096.0)
-            act(T.idx[:], "idx", T.idb[:], ["idb"], scale=4096.0)
-            act(T.low[:], "low", T.low[:], ["low"], scale=-4096.0)
-        mm("pl", 0, "idb", T.mk[:], "mk", I, True, False)
-        mm("pf", 0, "id0", T.ch[:], "ch", 2 * I, True, False)
-        mm("pm", 0, "idb", T.cm[:], "cm", I, True, False)
-        mm("pk", 0, "idb", T.mk[:], "mk", I, True, False)
-        for j in range(len(JUDGE)):
-            judge(j, x)
-            mark(j)
-            if t > 0 and j in AMONG:
-                fetch(1)
-            if t == 0 and j == len(JUDGE) - 2:
-                copy(pn, "pn", T.nam0[:], ["nam0"])
-        if t == 0:
+    def first(s):
+        if s == "j00":
+            copy(half("ku", 1), "ku1", turned("tp", 1), ["tp0", "tp1", "sel1"])
+        if s == "j01":
+            copy(T.k16[:], "k160", T.grd0[:], ["grd0"])
+            ts(T.l16[:], "l160", T.nam0[:], ["nam0"], 1.0 / 2048, -HALF, A.mult, A.add)
+            wrote["k161"], wrote["l161"] = wrote["k160"], wrote["l160"]
+            copy(pn, "pn0", T.nam0[:], ["nam0"])
+        if s == "j02":
             turn("tq")
-            copy(T.k16[:], "k16", T.grd0[:], ["grd0"])
-            copy(T.lu[:], "lu", turned("tq"), ["tq0", "tq1", "sel"])
-            copy(T.idh[:], "idh", T.idb[:], ["idb"])
-            memset(T.thr[:], "thr", 192 + 4100.5)
-            act(T.nbk[:], "nbk", T.bd[:], ["bd"], scale=-4096.0)
-            act(T.cn[:], "cn", T.t16[:], ["t16"], scale=0.0, bias=-2.0 ** 24)
-        else:
-            ts(T.k16[:], "k16", pn, ["pn"], ROUND, -ROUND, A.add, A.add)
-            ts(T.pj[:], "pj", T.pi[:], ["pi"], 1, None, A.bitwise_and)
-            tt(T.l16[:], "l16", pn, T.k16[:], ["pn", "k16"], A.subtract)
-            ts(T.thr[:], "thr", T.pj[:], ["pj"], 32.0, 192 + 4100.5, A.mult, A.add)
-        fetch(BEFORE_DEAD)
-        mm("pe", 0, "idh", T.k16[:], "k16", I, True, False)
-        ts(pa, "a", T.pa[:, 0:I], ["pa", "thr"], T.thr[:], 4100.5, A.add, A.max)
-        if t == 0:
-            ts(T.l16[:], "l16", T.nam0[:], ["nam0"], 1.0 / 2048, -HALF, A.mult, A.add)
-            ts(T.idl[:], "idl", T.idb[:], ["idb"], 2048.0, None, A.mult)
-        mm("pf", 0, "idl", T.l16[:], "l16", I, False, False)
-        mm("pf", I, "id0", T.l16[:], "l16", I, False, False)
-        ts(T.b[:], "b", pa, ["a"], 3.5, None, A.add)
-        if t == 0:
-            tt(T.tr[:], "tr", T.low[:], T.idx[:], ["low", "idx"], A.add)
-        tt(T.und[:], "und", pa, T.b[:], ["a", "b"], A.is_lt)
-        act(T.dead[:], ["dead", "cnt"], T.b[:], ["b"], F.Relu, scale=-1.0 / 16, bias=257.0, accum_out=T.cnt[:])
-        mm("pe", 0, "tr", T.und[:], "und", I, False, True)
-        mm("pf", 0, "tr", T.und[:], "und", I, False, False)
-        mm("pf", I, "nbk", T.und[:], "und", I, False, True)
-        if t == 0:
-            copy(T.bdh[:], "bdh", T.bd[:], ["bd"])
-            memset(T.x0[:, 0:16], "x0z", 0.0)
+        if s == "j03":
+            for u in range(2):
+                copy(half("lu", u), "lu%d" % u, turned("tq", u), ["tq0", "tq1", "sel%d" % u])
+            for c, v in enumerate((-2.0 ** 24, -4096.0)):
+                act(half("cc", c), "cc%d" % c, T.t16[:], ["t16"], scale=0.0, bias=v)
+            wrote["cc"] = wrote["cc1"]
+        if s in ("w00", "w01", "w02"):
+            a = 16 + 600 * int(s[2])
+            b = min(a + 600, 16 + WX)
+            act(T.x[:, a:b], "x", T.x0[:, a:b], ["x0"], bias=UP)
+        if s == "u1":
             memset(T.x[:, 0:16], "xz", UP)
             ts(T.wc[:], "wc", T.c6[:], ["c6"], 2.0, 1.0, A.mult, A.add)
             ts(T.bm0[:], "bm0", T.f[:], ["f"], 8.0, -1028.5, A.mult, A.add)
             ts(T.bm[:], "bm", T.f[:], ["f"], 8.0, 64 * UP - 1028.5, A.mult, A.add)
+        if s == "d1":
             act(T.onef[:], "onef", T.ones[:], ["ones"])
+        if s == "F":
+            act(T.bw[:], "bw", T.bd[:], ["bd", "wc"], scale=T.wc[:])
+            act(T.idn[:], "idn", T.idb[:], ["idb"], scale=-1.0)
+            act(T.half[:], "half", T.t16[:], ["t16"], scale=0.0, bias=0.5)
 
-        def kh():
-            ts(T.kh[:], "kh", T.pe[:, 0:I], ["pe"], 16.0 - 4096, 0.0, A.add, A.max)
-            mm("pk", 0, "bdh", T.kh[:], "kh", I, False, True)
+    for t in range(RO):
+        last = t == RO - 1
+        x, gr, up, bm = ("x0", "lim0", UP, "bm0") if t == 0 else ("x", "gr", 0.0, "bm")
+        h, gs = ["h%d%d" % (t, u) for u in range(2)], ["gs%d%d" % (t, u) for u in range(2)]
+        helped = HELP0 if t == 0 else ()
+        done = {"j0": 0, "j1": 0, "w0": 0, "w1": 0}
 
-        def lh():
-            ts(T.lh[:], "lh", T.pf[:, 0:2 * I], ["pf"], 1024.5 - 4096, 0.0, A.add, A.max)
-            sums = {"cn": ("pa", 0, "idb", T.cn[:], "cn", I, True, False), "b": ("pa", 0, "idx", T.b[:], "b", I, False, True),
-                    "l0": ("pl", 0, "bdh", T.lh[:, 0:I], "lh", I, False, False), "l1": ("pl", 0, "bdh", T.lh[:, I:2 * I], "lh", I, False, True),
-                    "mk": ("pm", 0, "idh", T.k16[:], "k16", I, False, False), "mu": ("pm", 0, "idx", T.und[:], "und", I, False, False),
-                    "ml": ("pm", 0, "idh", T.l16[:], "l16", I, False, True),
-                    "eu": ("pe", 0, "idx", T.und[:], "und", I, True, False), "ed": ("pe", 0, "idx", T.dead[:], "dead", I, False, True),
-                    "cnt": ("pf", 0, "onef", T.cnt[:], "cnt", 1, True, True)}
-            for s in SUMS.split():
-                if s != "cnt" or not last:
-                    mm(*sums[s])
+        def piece(s, u):
+            j = done[s + str(u)]
+            done[s + str(u)] = j + 1
+            a, b = ([0] + JUDGE[u])[j], JUDGE[u][j]
+            return a, b, H * (16 * u + a), H * (16 * u + b), "%d%d" % (u, j)
 
-        def send():
-            tt(T[gs][:], gs, T[x][:, 0:16 + WX].indirect(T.ks[:]), T[gr][:], [x, x + "z", "ks", gr], A.max)
+        def judge(u):
+            a, b, c, e, key = piece("j", u)
+            tt(T.u[:, c:e], "u" + key, T[x][:, 16:16 + WX].indirect(T.ku[:, c // 16:e // 16]), T.gj[:, 4 * H * u:4 * H * u + e - c],
+               [x, "ku%d" % u] + ["gj%d" % n for n in range(4 * u, 4 * u + b - a)], A.subtract)
+            if t == 0:
+                first("j" + key)
+
+        def mark(u):
+            a, b, c, e, key = piece("w", u)
+            act(T.w[:, c:e], "w" + key, T.u[:, c:e], ["u" + key], F.Sigmoid, scale=4.0, bias=-4.0 * 644 - math.log(32.0))
+            for k in range(a, b):
+                mm("pa%d" % u, 0, "zz", half("w", 16 * u + k), "w" + key, H, k == 0, k == 15, lhs=T.zz[:, 15 - k:143 - k])
+            if t == 0:
+                first("w" + key)
+
+        def send(u):
+            tt(T[gs[u]][:], gs[u], T[x][:, 0:16 + WX].indirect(listed("ks", u)), half(gr, u),
+               [x, x + "z", "ks%d" % u, gr if t == 0 else "gr%d" % u], A.max)
             dst = T.cores[(rank + 1 + t % 7) % 8]
             src = T.cores[(rank - 1 - t % 7) % 8]
             eng = topo.engines(core, dst)[:8]
             rid, pid = topo.addr(dst, core)
-            waits("g", [gs], [])
-            g.remote_dma(T[h][:], T[gs][:], T.sem["arr%d" % t], T.sem.sent, pid, rid, sum(1 << e for e in eng))
-            wrote[h] = ("remote", "arr%d" % t, len(topo.engines(src, core)[:8]), {})
-            if not last:
-                mm("pg", 0, "idb", T[gs][:], gs, I, True, False)
-                mm("pk", 0, "idb", T.mk[:], "mk", I, True, False)
-                mm("pk", 0, "idb", T.t8[:], "t8", I, False, False)
+            waits("g", [gs[u]], [])
+            g.remote_dma(T[h[u]][:], T[gs[u]][:], T.sem["arr%d%d" % (t, u)], T.sem.sent, pid, rid, sum(1 << e for e in eng))
+            wrote[h[u]] = ("remote", "arr%d%d" % (t, u), len(topo.engines(src, core)[:8]), {})
+            if last:
+                act(half("pg", u), "pg", T[gs[u]][:], [gs[u]], bias=-UP)
+
+        def ready(u):
+            masks("pk")
+            mm("pk", 0, "idb", half("t8", u), "t8", H, False, False)
+            mm(pg[u], 0, "idb", T[gs[u]][:], gs[u], H, True, False)
+
+        def land(u):
+            mm("pk", 0, "bw", T[h[u]][:], h[u], H, False, True)
+            mm(pg[u], 0, "idn", T[h[u]][:], h[u], H, False, True)
+
+        def low(u):
+            mm(pg[u], 0, "idb", T[gs[u]][:], gs[u], H, True, False)
+            mm(pg[u], 0, "idn", half("rl", u), "rl%d" % u, H, False, True)
 
         def rest():
-            fetch(8, HELP0 if t == 0 else ())
+            fetch(8, helped)
             fetched[0] = 0
-            if t == 0:
-                act(T.bw[:], "bw", T.bd[:], ["bd", "wc"], scale=T.wc[:])
-                act(T.idn[:], "idn", T.idb[:], ["idb"], scale=-1.0)
-                act(xw, "x", T.x0[:, 16:16 + WX], ["x0"], bias=UP)
-                act(T.half[:], "half", T.t16[:], ["t16"], scale=0.0, bias=0.5)
-            if last:
-                act(T.pg[:, 0:I], "pg", T[gs][:], [gs], bias=-UP)
 
-        def land():
-            act(T.hp[:], "hp", T[h][:], [h], bias=up - 0.5)
-            mm("pk", 0, "bw", T[h][:], h, I, False, True)
-            mm("pg", 0, "idn", T[h][:], h, I, False, True)
-            act(T.rl[:], "rl", T.pg[:, 0:I], ["pg"], F.Relu, bias=-2.0)
-
-        def low():
-            mm("pg", 0, "idb", T[gs][:], gs, I, True, False)
-            mm("pg", 0, "idn", T.rl[:], "rl", I, False, True)
-            limits(T.pg[:, 0:I], "pg", up)
-
-        q = T.sq[:, 15::16]
-        step = {
-            "kh": kh, "lh": lh, "gs": send, "rest": rest, "land": land, "low": low, "early": lambda: fetch(EARLY),
-            "sk": lambda: diagonal("pk", "sk"), "sl": lambda: diagonal("pl", "sl"), "sq": lambda: diagonal("pk", "sq"),
-            "ks": lambda: copy(T.ks[:], "ks", T.sk[:, 15::16], ["sk"]),
-            "ls": lambda: ts(T.ls[:], "ls", T.sl[:, 15::16], ["sl"], -1.0, None, A.add),
-            "md": lambda: ts(T.md[:], "md", T.rel0[:, 0:W].indirect(T.ls[:]), ["rel0", "ls"], -1023.5, 1.0 / 2048, A.add, A.mult),
-            "t1": lambda: tt(T.t1[:], "t1", T.md[:], T.pa[:, 0:I], ["md", "pa"], A.subtract),
-            "t2": lambda: tt(T.t2[:], "t2", T.mo[:], T.pe[:, 0:I], ["mo%d" % k for k in range(16)] + ["pe"], A.subtract),
-            "m1": lambda: tt(pn, "pn", T.t2[:], T.pm[:, 0:I], ["t2", "pm"], A.max),
-            "m2": lambda: tt(pn, "pn", T.t1[:], pn, ["t1", "pn"], A.max),
-            "turn": lambda: turn("tp"), "pi": lambda: copy(T.pi[:], "pi", T.pf[:, 0:1], ["pf"]),
-            "kt": lambda: ts(T.kt[:], "kt", turned("tp"), ["tp0", "tp1", "sel"], ROUND, -ROUND, A.add, A.add),
-            "lt": lambda: tt(T.lt[:], "lt", pn if last else turned("tp"), T.og[:] if last else T.kt[:],
-                             ["pn", "og"] if last else ["tp0", "tp1", "sel", "kt"], A.subtract),
-            "lu": lambda: ts(T.lu[:], "lu", T.lt[:], ["lt"], 2048.0, 1023.5, A.mult, A.add),
-            "ku": lambda: copy(T.ku[:], "ku", T.kt[:], ["kt"]),
-            "gr": lambda: act(T.gr[:], "gr", T.pg[:, 0:I], ["pg"], bias=up),
-            "f8": lambda: tt(T.f8[:], "f8", q, T[bm][:], ["sq", bm], A.subtract),
-            "z": lambda: tt(T.z[:], "z", q, T.f8[:], ["sq", "f8"], A.subtract),
-            "cu": lambda: ts(T.cu[:], "cu", T.z[:], ["z"], 1032.0 - 64 * (UP - up), None, A.add),
-            "bl": lambda: tt(T.bl[:], "bl", xw.indirect(T.cu[:]), T.hp[:], ["x", "cu", "hp"], A.add),
-            "put": lambda: tt(xw.indirect(T.cu[:]), "x", T.bl[:], T.half[:], ["bl", "cu", "half"], A.mult),
-            "og": lambda: (ts(T.og[:], "og", pn, ["pn"], ROUND, -ROUND, A.add, A.add), load("s", "d_og", T.yg[:], T.og[:], ["og"], ["yg"])),
-            "on": lambda: (ts(T.on[:], "on", T.lt[:], ["lt"], 2048.0, 1023.5, A.mult, A.add), load("s", "d_on", T.yn[:], T.on[:], ["on"], ["yn"])),
-            "h2": lambda: ts(T.gm[:], "gm", T[h][:], [h], 2.0 - UP, None, A.add),
-            "ol": lambda: (tt(T.ol[:], "ol", T.gm[:], T.pg[:, 0:I], ["gm", "pg"], A.min), load("a", "d_ol", T.yl[:], T.ol[:], ["ol"], ["yl"])),
+        halves = {
+            "j": judge, "w": mark, "G": guards, "N": names, "P": lambda u: masks("pk"), "L": lambda u: masks("pl"),
+            "u": und, "kh": kh, "lh": lh, "s": alive, "si": implied, "so": old, "gs": send, "R": ready, "land": land, "low": low,
+            "a": lambda u: ts(count_of(u), "a%d" % u, T["pa%d" % u][:, 0:H], ["pa%d" % u, "thr"], T.thr[:], 4100.5, A.add, A.max),
+            "b": lambda u: ts(half("b", u), "b%d" % u, count_of(u), ["a%d" % u], 3.5, None, A.add),
+            "d": lambda u: act(half("dead", u), ["dead%d" % u, "cnt%d" % u], half("b", u), ["b%d" % u], F.Relu, scale=-1.0 / 16, bias=257.0,
+                               accum_out=T.cnt[:, u:u + 1]),
+            "sk": lambda u: diagonal("pk", "sk", u), "sl": lambda u: diagonal("pl", "sl", u), "sq": lambda u: diagonal("pk", "sq", u),
+            "ks": lambda u: copy(listed("ks", u), "ks%d" % u, picked("sk", u), ["sk%d" % u]),
+            "ls": lambda u: ts(listed("ls", u), "ls%d" % u, picked("sl", u), ["sl%d" % u], -1.0, None, A.add),
+            "md": lambda u: ts(half("md", u), "md%d" % u, T.rel0[:, 0:W].indirect(listed("ls", u)), ["rel0", "ls%d" % u], -1023.5, 1.0 / 2048,
+                               A.add, A.mult),
+            "t": lambda u: tt(half("t1", u), "t1%d" % u, half("md", u), half("pa%d" % u, 0), ["md%d" % u, "pa%d" % u], A.subtract),
+            "o": lambda u: tt(half("t2", u), "t2%d" % u, half("mo", u), half("pa%d" % u, 1),
+                              ["mo%d_%d" % (u, k) for k in range(16)] + ["pa%d" % u], A.subtract),
+            "m": lambda u: tt(own(u), pns[u], half("t1", u), half("pa%d" % u, 2), ["t1%d" % u, "pa%d" % u], A.max),
+            "n": lambda u: tt(own(u), pns[u], half("t2", u), own(u), ["t2%d" % u, pns[u]], A.max),
+            "k": lambda u: ts(half("k16", u), "k16%d" % u, own(u), [pns[u]], ROUND, -ROUND, A.add, A.add),
+            "l": lambda u: tt(half("l16", u), "l16%d" % u, own(u), half("k16", u), [pns[u], "k16%d" % u], A.subtract),
+            "turn": lambda u: turn("tq", 96, I, 128, 256) if u else turn("tp", 0, 128, 0, 128),
+            "kt": lambda u: ts(half("kt", u), "kt%d" % u, turned(tb[u], u), [tb[u] + "0", tb[u] + "1"], ROUND, -ROUND, A.add, A.add),
+            "lt": lambda u: tt(half("lt", u), "lt%d" % u, turned(tb[u], u), half("kt", u), [tb[u] + "0", tb[u] + "1", "kt%d" % u], A.subtract),
+            "lu": lambda u: ts(half("lu", u), "lu%d" % u, half("lt", u), ["lt%d" % u], 2048.0, 1023.5, A.mult, A.add),
+            "ku": lambda u: copy(half("ku", u), "ku%d" % u, half("kt", u), ["kt%d" % u]),
+            "hp": lambda u: act(half("hp", u), "hp%d" % u, T[h[u]][:], [h[u]], bias=up - 0.5),
+            "rl": lambda u: act(half("rl", u), "rl%d" % u, half(pg[u], 0), [pg[u]], F.Relu, bias=-2.0),
+            "gj": lambda u: limits(half(pg[u], 0), pg[u], up, u),
+            "gr": lambda u: act(half("gr", u), "gr%d" % u, half(pg[u], 0), [pg[u]], bias=up),
+            "r": lambda u: tt(seven("f8", u), "f8%d" % u, picked("sq", u), seven(bm, u), ["sq%d" % u, bm], A.subtract),
+            "z": lambda u: tt(seven("z", u), "z%d" % u, picked("sq", u), seven("f8", u), ["sq%d" % u, "f8%d" % u], A.subtract),
+            "cu": lambda u: ts(listed("cu", u), "cu%d" % u, seven("z", u), ["z%d" % u], 1032.0 - 64 * (UP - up), None, A.add),
+            "bl": lambda u: tt(half("bl", u), "bl%d" % u, xw.indirect(listed("cu", u)), half("hp", u), ["x", "cu%d" % u, "hp%d" % u], A.add),
+            "put": lambda u: tt(xw.indirect(listed("cu", u)), "x", half("bl", u), T.half[:], ["bl%d" % u, "cu%d" % u, "half"], A.mult),
+            "h": lambda u: ts(half("gm", u), "gm%d" % u, T[h[u]][:], [h[u]], 2.0 - UP, None, A.add),
+            "y": limits_out,
+            "og": lambda u: (ts(half("og", u), "og%d" % u, own(u), [pns[u]], ROUND, -ROUND, A.add, A.add),
+                             load("s", "d_og", half("yg", u), half("og", u), ["og%d" % u], ["yg%d" % u])),
+            "ot": lambda u: tt(half("lt", u), "lt%d" % u, own(u), half("og", u), [pns[u], "og%d" % u], A.subtract),
+            "on": lambda u: (ts(half("on", u), "on%d" % u, half("lt", u), ["lt%d" % u], 2048.0, 1023.5, A.mult, A.add),
+                             load("s", "d_on", half("yn", u), half("on", u), ["on%d" % u], ["yn%d" % u])),
         }
-        for s in (RAISE + " " + (END if last else NEXT)).split():
-            step[s]()
-    g.wait_ge(T.sem.sent, sum(len(topo.engines(core, T.cores[(rank + 1 + t % 7) % 8])[:8]) for t in range(RO)))
+        whole = {
+            "E": lambda: fetch(4 - fetched[0], helped), "F": rest, "f": lambda: fetch(1), "C": deaths,
+            "pi": lambda: copy(T.pi[:], "pi", T.pf[:, 0:1], ["pf"]),
+            "pj": lambda: ts(T.pj[:], "pj", T.pi[:], ["pi"], 1, None, A.bitwise_and),
+            "thr": lambda: ts(T.thr[:], "thr", T.pj[:], ["pj"], 32.0, 192 + 4100.5, A.mult, A.add),
+        }
+        order = ORDER.split()
+        for n, s in enumerate(order):
+            if s in whole:
+                if not (last and n > order.index("F")):
+                    whole[s]()
+            elif s in LATE:
+                if t > 0:
+                    halves[s[:-1]](int(s[-1]))
+            elif not (last and s[:-1] in NEXT):
+                halves[LAST.get(s[:-1], s[:-1]) if last else s[:-1]](int(s[-1]))
+            if t == 0:
+                first(s)
+    g.wait_ge(T.sem.sent, 2 * sum(len(topo.engines(core, T.cores[(rank + 1 + t % 7) % 8])[:8]) for t in range(RO)))
     for q in ("v", "a", "t", "g"):
         if known["g"].get("c" + q, 0) < count[q]:
             g.wait_ge(T.sem["c" + q], count[q])
     for s in ("d_on", "d_og", "d_ol"):
-        g.wait_ge(T.sem[s], 16)
+        g.wait_ge(T.sem[s], dcount[s])

@@ -2,47 +2,49 @@ import math
 from concourse.mybir import dt, AluOpType, AxisListType, ActivationFunctionType
 
 I = 224
-H = 112
 WX = 1792
 W = 2048
 RO = 4
-JUDGE = [[4, 8, 12, 16], [4, 8, 10, 12, 14, 16]]
-HELP0 = (3, 5)
-ORDER = ("j0 j0 j0 w0 G0 j0 w0 w0 k1 j1 P0 j1 w0 E j1 N0 L0 a0 j1 w1 b0 w1 w1 j1 u0 d0 w1 j1 l1 w1 kh0 w1 lt1 lh0 lu1 sk0 f a1 N1 so0 ks0 G1 "
-         "sl0 s0 b1 gs0 u1 ls0 si0 d1 P1 md0 kh1 L1 lh1 t0 o0 F sk1 m0 so1 ks1 n0 sl1 gs1 R0 land0 turn0 ls1 si1 kt0 s1 sq0 md1 r0 rl0 lt0 z0 "
-         "t1 C ku0 hp0 lu0 f cu0 R1 m1 low0 f land1 pi hp1 o1 bl0 n1 k0 sq1 rl1 low1 turn1 r1 gj0 put0 f z1 f kt1 gj1 cu1 bl1 pj l0 gr0 put1 "
-         "ku1 thr gr1")
+NC = (8, 6)
+JUDGE = [[4, 8, 12, 16], [5, 10, 13, 15, 16]]
+FETCH = [(0, 0, 4), (0, 4, 8), (0, 8, 12), (0, 12, 16), (1, 0, 6), (1, 6, 11), (1, 11, 16)]
+AMONG0 = ("w02", "w03")
+OWN = (2, 3)
+ORDER = ("j0 j0 j0 k1 N0 G0 w0 P0 j0 j1 j1 w0 l1 w0 j1 w0 N1 a0 w1 w1 b0 j1 u0 lt1 w1 j1 d0 lu1 w1 w1 kh0 E L0 lh0 b1 si0 a1 G1 sk0 P1 u1 ks0 "
+         "sl0 so1 gs0 kh1 s0 L1 ls0 lh1 sk1 f d1 F md0 so0 si1 s1 ks1 sl1 gs1 hp0 t0 R1 ls1 o0 m0 md1 n0 t1 R0 land0 rl0 C hp1 turn0 sq0 land1 "
+         "kt0 m1 low0 k0 o1 lt0 sq1 rl1 n1 low1 pi gj0 lu0 r gr0 f turn1 gr1 z l0 ku0 f f cu kt1 bl pj put f gj1 ku1 thr")
+END = "md1 t0 t1 m0 m1 o1 n0 n1 og0 og1 h0 ot0 ot1 y0 on0 on1 h1 y1"
 LATE = ("lt1", "lu1", "k1", "l1")
-NEXT = ("R", "land", "rl", "low", "gj", "gr", "hp", "z", "cu", "bl", "put", "k", "l", "lt", "lu")
-LAST = {"sq": "h", "r": "y", "turn": "og", "kt": "ot", "ku": "on"}
+NEXT = ("R", "land", "rl", "low", "gj", "gr", "sq", "turn", "kt", "ku", "k", "l", "lt", "lu")
 ROUND = 1.5 * 2.0 ** 23
 HALF = 1023.5 / 2048
 UP = 144.0
+M = 160
 
 SB = "sbuf"
 BF, F32, F16, I32, U16 = "bfloat16", "float32", "float16", "int32", "uint16"
 SCRATCH = {
     "x": (SB, [128, 16 + WX], BF), "x0": (SB, [128, 16 + WX], BF), "lim0": (SB, [128, I], BF),
-    "grd0": (SB, [128, I], I32), "nam0": (SB, [128, I], I32), "rel0": (SB, [128, W], I32),
+    "grd0": (SB, [128, 256], I32), "nam0": (SB, [128, 256], I32), "rel0": (SB, [128, W], I32),
     "u": (SB, [128, 16 * I], BF), "w": (SB, [128, 16 * I], BF), "nb": (SB, [128, 16 * I], F32),
-    "ku": (SB, [128, I], U16), "lu": (SB, [128, I], U16), "tp": (SB, [128, 480], F32), "tq": (SB, [128, 480], F32),
+    "ku": (SB, [128, I], U16), "lu": (SB, [128, I], U16), "tp": (SB, [128, 512], F32), "tg": (SB, [128, 512], I32), "tn": (SB, [128, 512], I32),
     "kt": (SB, [128, I], F32), "lt": (SB, [128, I], F32), "k16": (SB, [128, I], F16), "l16": (SB, [128, I], F16),
-    "gj": (SB, [128, 8 * H], F32), "gr": (SB, [128, I], BF), "rl": (SB, [128, I], BF), "gm": (SB, [128, I], BF), "hp": (SB, [128, I], F32),
+    "gj": (SB, [128, 1536], F32), "gr": (SB, [128, I], BF), "rl": (SB, [128, I], BF), "gm": (SB, [128, I], BF), "hp": (SB, [128, I], F32),
     "b": (SB, [128, I], BF), "und": (SB, [128, I], BF), "dead": (SB, [128, I], BF),
     "kh": (SB, [128, I], F16), "lh": (SB, [128, 2 * I], F16),
     "sk": (SB, [128, I], F32), "sl": (SB, [128, I], F32), "sq": (SB, [128, I], F32),
-    "ks": (SB, [128, 16], U16), "ls": (SB, [128, 16], U16), "cu": (SB, [128, 16], U16), "sel": (SB, [128, 16], U16),
+    "ks": (SB, [128, 14], U16), "ls": (SB, [128, 14], U16), "cu": (SB, [128, 14], U16), "sel": (SB, [128, 14], U16),
     "f8": (SB, [128, 14], BF), "z": (SB, [128, 14], F32), "bm0": (SB, [128, 14], F32), "bm": (SB, [128, 14], F32),
-    "bl": (SB, [128, I], BF), "half": (SB, [128, H], BF),
+    "bl": (SB, [128, I], BF), "half": (SB, [128, I], BF),
     "md": (SB, [128, I], F32), "mo": (SB, [128, I], F32), "t1": (SB, [128, I], F32), "t2": (SB, [128, I], F32),
     "cnt": (SB, [128, 2], F32), "pi": (SB, [128, 1], I32), "pj": (SB, [128, 1], I32), "thr": (SB, [128, 1], F32),
-    "ip": (SB, [128, 1], I32), "c1": (SB, [128, 1], I32), "c2": (SB, [128, 1], I32), "c5": (SB, [128, 1], I32), "c6": (SB, [128, 1], I32),
-    "g16": (SB, [128, 1], F32), "gf": (SB, [128, 1], F32), "rc": (SB, [128, 1], F32), "wc": (SB, [128, 1], F32), "kz": (SB, [128, 1], F32),
-    "ff": (SB, [128, 14], F32), "f": (SB, [128, 14], F32), "e1": (SB, [128, 7], I32), "e2": (SB, [128, 7], I32), "e3": (SB, [128, 7], I32),
-    "d1": (SB, [128, 7], F32), "d2": (SB, [128, 7], F32), "d3": (SB, [128, 7], F32), "d4": (SB, [128, 14], F32), "d5": (SB, [128, 14], F32),
-    "a2": (SB, [128, 7], F32),
-    "t16": (SB, [128, H], BF), "t8": (SB, [128, I], BF), "mk": (SB, [128, H], BF), "rs": (SB, [128, H], BF),
-    "cc": (SB, [128, I], BF), "ch": (SB, [128, I], F16),
+    "ip": (SB, [128, 1], I32), "c1": (SB, [128, 1], I32), "c2": (SB, [128, 1], I32), "c3": (SB, [128, 1], I32), "c4": (SB, [128, 1], I32),
+    "c5": (SB, [128, 1], I32), "c6": (SB, [128, 1], I32), "par": (SB, [128, 2], F32),
+    "g16": (SB, [128, 1], F32), "rc": (SB, [128, 1], F32), "wc": (SB, [128, 1], F32), "kz": (SB, [128, 1], F32),
+    "ff": (SB, [128, 14], F32), "f": (SB, [128, 14], F32), "fk": (SB, [128, 14], I32), "a1": (SB, [128, 14], F32), "a2": (SB, [128, 14], F32),
+    "a3": (SB, [128, 14], F32),
+    "t16": (SB, [128, M], BF), "t8": (SB, [128, I], BF), "mk": (SB, [128, M], BF), "rs": (SB, [128, M], BF),
+    "cc": (SB, [128, 2 * M], BF), "ch": (SB, [128, 2 * M], F16),
     "ones": (SB, [128, 128], BF), "onef": (SB, [128, 128], F32), "idb": (SB, [128, 128], BF), "idl": (SB, [128, 128], BF),
     "id0": (SB, [128, 128], BF), "idx": (SB, [128, 128], BF), "idn": (SB, [128, 128], BF), "bd": (SB, [128, 128], BF),
     "nbk": (SB, [128, 128], BF), "low": (SB, [128, 128], BF), "tr": (SB, [128, 128], BF), "bw": (SB, [128, 128], BF), "zz": (SB, [128, 144], BF),
@@ -50,13 +52,13 @@ SCRATCH = {
 }
 for _t in range(RO):
     for _u in range(2):
-        SCRATCH["gs%d%d" % (_t, _u)] = (SB, [128, H], BF)
-        SCRATCH["h%d%d" % (_t, _u)] = (SB, [128, H], BF)
-PSUM = ("pa0", "pa1", "pv", "pe", "pk", "pf", "pl", "pg")
+        SCRATCH["gs%d%d" % (_t, _u)] = (SB, [128, M], BF)
+        SCRATCH["h%d%d" % (_t, _u)] = (SB, [128, M], BF)
+PSUM = ("pa0", "pa1", "pv", "pe0", "pe1", "pf0", "pf1", "pk")
 for _b in PSUM:
     SCRATCH[_b] = ("psum", [128, 512], F32)
 
-SEMAPHORES = ["cv", "ca", "ct", "cg", "sent", "d_x", "d_lim", "d_grd", "d_nam", "d_rel", "d_on", "d_og", "d_ol", "d_m0", "d_m1"]
+SEMAPHORES = ["cv", "ca", "ct", "cg", "sent", "d_x", "d_lim", "d_grd", "d_nam", "d_rel", "d_up", "d_on", "d_og", "d_ol", "d_m0", "d_m1"]
 SEMAPHORES += ["arr%d%d" % (_t, _u) for _t in range(RO) for _u in range(2)]
 
 
@@ -89,7 +91,7 @@ def rank_program(g, core, T, topo):
         for k in writes:
             if k in wrote and (wrote[k][0] != q or q != "t"):
                 recs.append(wrote[k])
-            recs += [r for r in seen.get(k, {}).values() if r[0] != q]
+            recs += [r for r in seen.get(k, {}).values() if r[0] != q or q != "t"]
         for r in sorted(recs, key=lambda r: -r[2]):
             need(q, r)
 
@@ -109,9 +111,9 @@ def rank_program(g, core, T, topo):
         snap["c" + q] = count[q]
         note((q, "c" + q, count[q], snap), reads, writes)
 
-    def load(q, sem, out, in_, reads, writes):
+    def load(q, sem, out, in_, reads, writes, **kw):
         waits(q, reads, writes)
-        queue[q].dma_start(out, in_).then_inc(T.sem[sem], 16)
+        queue[q].dma_start(out, in_, **kw).then_inc(T.sem[sem], 16)
         dcount[sem] = dcount.get(sem, 0) + 16
         snap = dict(known[q])
         snap[sem] = dcount[sem]
@@ -141,323 +143,337 @@ def rank_program(g, core, T, topo):
     def select(name, src, pattern, cmp, fill, base, mult):
         op("g", [src], [name], lambda e: e.affine_select(T[name][:], T[src][:], pattern, cmp, fill, base, mult))
 
-    def iota(name, pattern, mult):
-        op("g", [], [name], lambda e: e.iota(T[name][:], pattern, 0, mult, allow_small_or_imprecise_dtypes=True))
+    def iota(name, pattern, mult, base=0):
+        op("g", [], [name], lambda e: e.iota(T[name][:], pattern, base, mult, allow_small_or_imprecise_dtypes=True))
 
-    pn = T.pv[:, 272:272 + I]
+    H = [16 * n for n in NC]
+    O = [0, H[0]]
+    wide = [max(b - a for a, b in zip([0] + JUDGE[u], JUDGE[u])) for u in range(2)]
     xw = T.x[:, 16:16 + WX]
-    pns, tb, pg = ["pn0", "pn1"], ["tp", "tq"], ["pg", "pe"]
+    pns, pa, pe, pf = ["pn0", "pn1"], ["pa0", "pa1"], ["pe0", "pe1"], ["pf0", "pf1"]
 
-    def half(name, u):
-        return T[name][:, H * u:H * u + H]
+    def part(name, u, at=0):
+        return T[name][:, at + O[u]:at + O[u] + H[u]]
+
+    def cols(name, u, at=0):
+        return T[name][:, at:at + H[u]]
 
     def own(u):
-        return T.pv[:, 272 + H * u:272 + H * u + H]
+        return part("pv", u, 272)
 
-    def count_of(u):
-        return T.pv[:, 128 * u:128 * u + H]
+    def lanes(name, u, a, b):
+        return T[name][:, 16 * O[u] + H[u] * a:16 * O[u] + H[u] * b]
+
+    def entries(name, u, a, b):
+        return T[name][:, O[u] + NC[u] * a:O[u] + NC[u] * b]
 
     def picked(name, u):
-        return T[name][:, H * u + 15:H * u + H:16]
+        return T[name][:, O[u] + 15:O[u] + H[u]:16]
 
     def listed(name, u):
-        return T[name][:, 8 * u:8 * u + 7]
-
-    def seven(name, u):
-        return T[name][:, 7 * u:7 * u + 7]
+        return T[name][:, O[u] // 16:O[u] // 16 + NC[u]]
 
     def turned(src, u):
-        return T[src][:, 0:480].indirect(listed("sel", u))
+        a = (2 * H[0] + 32) * u
+        return T[src][:, a:a + 2 * H[u] + 32].indirect(listed("sel", u))
 
-    def turn(dst, a=0, b=I, c=0, e=256):
-        op("v", pns, [dst + "0"], lambda q: q.transpose(T[dst][:, a:b], T.pv[:, 272 + a:272 + b]))
-        op("v", pns, [dst + "1"], lambda q: q.transpose(T[dst][:, I + c:I + e], T.pv[:, 256 + c:256 + e]))
+    def turn(dst, src, keys, at, u):
+        a, n = (2 * H[0] + 32) * u, H[u]
+        op("v", keys, [dst + "%d0" % u], lambda q: q.transpose(T[dst][:, a:a + n], part(src, u, at + 16)))
+        op("v", keys, [dst + "%d1" % u], lambda q: q.transpose(T[dst][:, a + n:a + 2 * n + 32], T[src][:, at + O[u]:at + O[u] + n + 32]))
+
+    def listing(out, dst, u):
+        copy(part(out, u), out + str(u), turned(dst, u), [dst + "%d0" % u, dst + "%d1" % u, "sel%d" % u])
 
     def diagonal(bank, out, u):
-        op("v", [bank, "rs"], [out + str(u)], lambda e: e.tensor_tensor_scan(half(out, u), T.rs[:], T[bank][:, 0:H], 0.0, A.mult, A.max))
+        op("v", [bank, "rs"], [out + str(u)], lambda e: e.tensor_tensor_scan(part(out, u), cols("rs", u), cols(bank, u), 0.0, A.mult, A.max))
 
     fetched = [0]
+    firsts = len([c for c in FETCH if c[0] == 0])
 
-    def fetch(n, helped=()):
-        for j in range(fetched[0], min(fetched[0] + n, 8)):
-            a, u = 4 * (j % 4), j // 4
-            c = 16 * u + a
-            out, got = T.nb[:, H * c:H * c + 4 * H], T.rel0[:, 0:W].indirect(T.lu[:, 7 * c:7 * c + 28])
-            if j in helped:
-                ts(out, "nb%d" % j, got, ["rel0", "lu%d" % u], -1023.5, 1.0 / 2048, A.add, A.mult)
-            else:
-                act(out, "nb%d" % j, got, ["rel0", "lu%d" % u], scale=1.0 / 2048, bias=-HALF)
-            for k in range(a, a + 4):
-                load("s", "d_m%d" % u, T.mo[k::16, H * u:H * u + H], T.nb[k::16, H * (16 * u + k):H * (16 * u + k) + H], ["nb%d" % j],
-                     ["mo%d_%d" % (u, k)])
-            if a == 12:
+    def fetch(n):
+        for j in range(fetched[0], min(fetched[0] + n, len(FETCH))):
+            u, a, b = FETCH[j]
+            act(lanes("nb", u, a, b), "nb%d" % j, T.rel0[:, 0:W].indirect(entries("lu", u, a, b)), ["rel0", "lu%d" % u],
+                scale=1.0 / 2048, bias=-HALF)
+            for k in range(a, b):
+                c = 16 * O[u] + H[u] * k
+                load("s", "d_m%d" % u, T.mo[k::16, O[u]:O[u] + H[u]], T.nb[k::16, c:c + H[u]], ["nb%d" % j], ["mo%d_%d" % (u, k)])
+            if b == 16:
                 for k in range(16):
                     wrote["mo%d_%d" % (u, k)] = wrote["mo%d_15" % u]
             fetched[0] = j + 1
 
     def limits(src, key, up, u):
-        for c in range(4 * u, 4 * u + 4):
-            act(half("gj", c), "gj%d" % c, src, [key], bias=up - 641.5)
+        a, own_, keys = 768 * u, wide[u] if key == "lim0" else OWN[u], ["gj%d%d" % (u, c) for c in range(wide[u])]
+        for c in range(own_):
+            act(cols("gj", u, a + H[u] * c), keys[c], src, [key], bias=up - 641.5)
+        n = wide[u] - own_
+        if n:
+            op("g", keys[:n], keys[own_:], lambda e: e.affine_select(T.gj[:, a + H[u] * own_:a + H[u] * wide[u]], T.gj[:, a:a + H[u] * n],
+                                                                     [[0, H[u] * n]], A.is_ge, 0.0, 0, 0))
 
-    def masks(bank):
-        mm(bank, 0, "idb", T.mk[:], "mk", H, True, False)
+    def masks(bank, u):
+        mm(bank, 0, "idb", cols("mk", u), "mk", H[u], True, False)
 
     def guards(u):
-        mm("pe", 0, "idb", half("k16", u), "k16%d" % u, H, True, False)
+        mm(pe[u], 0, "idb", part("k16", u), "k16%d" % u, H[u], True, False)
 
     def names(u):
-        mm("pf", 0, "id0", T.ch[:], "ch", I, True, False)
-        mm("pf", 0, "idl", half("l16", u), "l16%d" % u, H, False, False)
-        mm("pf", H, "id0", half("l16", u), "l16%d" % u, H, False, False)
+        mm(pf[u], 0, "id0", T.ch[:, M - H[u]:M + H[u]], "ch", 2 * H[u], True, False)
+        mm(pf[u], 0, "idl", part("l16", u), "l16%d" % u, H[u], False, False)
+        mm(pf[u], H[u], "id0", part("l16", u), "l16%d" % u, H[u], False, False)
+
+    def counted(out, key, u):
+        ts(out, key + str(u), cols(pa[u], u), [pa[u], "thr"], T.thr[:], 4100.5, A.add, A.max)
 
     def und(u):
-        tt(half("und", u), "und%d" % u, count_of(u), half("b", u), ["a%d" % u, "b%d" % u], A.is_lt)
-        mm("pe", 0, "tr", half("und", u), "und%d" % u, H, False, True)
-        mm("pf", 0, "tr", half("und", u), "und%d" % u, H, False, False)
-        mm("pf", H, "nbk", half("und", u), "und%d" % u, H, False, True)
+        tt(part("und", u), "und%d" % u, part("pv", u), part("b", u), ["a%d" % u, "b%d" % u], A.is_lt)
+        mm(pe[u], 0, "tr", part("und", u), "und%d" % u, H[u], False, True)
+        mm(pf[u], 0, "tr", part("und", u), "und%d" % u, H[u], False, False)
+        mm(pf[u], H[u], "nbk", part("und", u), "und%d" % u, H[u], False, True)
 
     def kh(u):
-        ts(half("kh", u), "kh%d" % u, T.pe[:, 0:H], ["pe"], 16.0 - 4096, 0.0, A.add, A.max)
-        mm("pk", 0, "bd", half("kh", u), "kh%d" % u, H, False, True)
+        ts(part("kh", u), "kh%d" % u, cols(pe[u], u), [pe[u]], 16.0 - 4096, 0.0, A.add, A.max)
+        mm("pk", 0, "bd", part("kh", u), "kh%d" % u, H[u], False, True)
 
     def lh(u):
-        ts(T.lh[:, I * u:I * u + I], "lh%d" % u, T.pf[:, 0:I], ["pf"], 1024.5 - 4096, 0.0, A.add, A.max)
-        mm("pl", 0, "bd", half("lh", 2 * u), "lh%d" % u, H, False, False)
-        mm("pl", 0, "bd", half("lh", 2 * u + 1), "lh%d" % u, H, False, True)
+        c = 2 * O[u]
+        ts(T.lh[:, c:c + 2 * H[u]], "lh%d" % u, T[pf[u]][:, 0:2 * H[u]], [pf[u]], 1024.5 - 4096, 0.0, A.add, A.max)
+        mm(pe[u], 0, "bd", cols("lh", u, c), "lh%d" % u, H[u], False, False)
+        mm(pe[u], 0, "bd", cols("lh", u, c + H[u]), "lh%d" % u, H[u], False, True)
 
     def alive(u):
-        mm("pa%d" % u, 0, "idb", half("cc", 0), "cc", H, True, False)
-        mm("pa%d" % u, 0, "idx", half("b", u), "b%d" % u, H, False, True)
+        mm(pa[u], 0, "idb", cols("cc", u), "cc", H[u], True, False)
+        mm(pa[u], 0, "idx", part("b", u), "b%d" % u, H[u], False, True)
 
     def implied(u):
-        mm("pa%d" % u, H, "idx", half("und", u), "und%d" % u, H, True, False)
-        mm("pa%d" % u, H, "idx", half("dead", u), "dead%d" % u, H, False, True)
+        mm(pa[u], M, "idx", part("und", u), "und%d" % u, H[u], True, False)
+        mm(pa[u], M, "idx", part("dead", u), "dead%d" % u, H[u], False, True)
 
     def old(u):
-        mm("pa%d" % u, I, "idb", half("cc", 1), "cc", H, True, False)
-        mm("pa%d" % u, I, "idb", half("k16", u), "k16%d" % u, H, False, False)
-        mm("pa%d" % u, I, "idx", half("und", u), "und%d" % u, H, False, False)
-        mm("pa%d" % u, I, "idb", half("l16", u), "l16%d" % u, H, False, True)
+        mm(pa[u], 2 * M, "idb", cols("cc", u, M), "cc", H[u], True, False)
+        mm(pa[u], 2 * M, "idb", part("k16", u), "k16%d" % u, H[u], False, False)
+        mm(pa[u], 2 * M, "idx", part("und", u), "und%d" % u, H[u], False, False)
+        mm(pa[u], 2 * M, "idb", part("l16", u), "l16%d" % u, H[u], False, True)
 
     def deaths():
-        mm("pf", 0, "onef", T.cnt[:, 0:1], "cnt0", 1, True, False)
-        mm("pf", 0, "onef", T.cnt[:, 1:2], "cnt1", 1, False, True)
+        mm("pk", 0, "onef", T.cnt[:, 0:1], "cnt0", 1, True, False)
+        mm("pk", 0, "onef", T.cnt[:, 1:2], "cnt1", 1, False, True)
 
     def limits_out(u):
-        tt(half("ol", u), "ol%d" % u, half("gm", u), half("pg", u), ["gm%d" % u, "pg"], A.min)
-        if u == 1:
-            load("a", "d_ol", T.yl[:], T.ol[:], ["ol0", "ol1"], ["yl"])
+        tt(part("ol", u), "ol%d" % u, part("gm", u), cols(pf[u], u), ["gm%d" % u, pf[u]], A.min)
+        load("a", "d_ol", part("yl", u), part("ol", u), ["ol%d" % u], ["yl%d" % u])
 
-    load("s", "d_grd", T.grd0[:], T.grd[:], [], ["grd0"])
+    load("s", "d_grd", T.grd0[:, 16:16 + I], T.grd[:], [], ["grd0"])
     load("a", "d_lim", T.lim0[:], T.lim[:], [], ["lim0"])
     load("s", "d_x", T.x0[:, 16:16 + WX], T.xc[:], [], ["x0"])
-    load("s", "d_nam", T.nam0[:], T.nam[:], [], ["nam0"])
+    load("s", "d_nam", T.nam0[:, 16:16 + I], T.nam[:], [], ["nam0"])
     load("s", "d_rel", T.rel0[:], T.rel[:], [], ["rel0"])
 
     iota("ip", [[0, 1]], 1)
     iota("ff", [[16, 14]], 1)
-    iota("t16", [[0, 7], [1, 16]], 0)
+    iota("t16", [[0, M // 16], [1, 16]], 0)
     memset(T.ones[:], "ones", 1.0)
     select("bd", "ones", [[-16, 8], [0, 16]], A.is_ge, 0.0, 0, 1)
     select("bd", "bd", [[16, 8], [0, 16]], A.is_ge, 0.0, 15, -1)
     select("idb", "ones", [[-1, 128]], A.is_equal, 0.0, 0, 1)
-    memset(T.pv[:, 256:512], "pn0", 0.0)
-    f7 = T.f[:, 0:7]
+    for name in ("grd0", "nam0"):
+        memset(T[name][:, 0:16], name + "a", 0)
+        memset(T[name][:, 16 + I:256], name + "b", 0)
     ts(T.c1[:], "c1", T.ip[:], ["ip"], 112, None, A.bitwise_and)
     ts(T.c2[:], "c2", T.ip[:], ["ip"], 4, None, A.arith_shift_right)
     ts(T.c5[:], "c5", T.ip[:], ["ip"], 15, None, A.bitwise_and)
     copy(T.g16[:], "g16", T.c1[:], ["c1"])
-    copy(T.gf[:], "gf", T.c2[:], ["c2"])
+    tt(T.c3[:], "c3", T.c2[:], T.ip[:], ["c2", "ip"], A.add)
     ts(T.c6[:], "c6", T.ip[:], ["ip"], 3, None, A.bitwise_and)
     ts(T.f[:], "f", T.ff[:], ["ff", "g16"], T.g16[:], None, A.subtract)
+    ts(T.c4[:], "c4", T.c3[:], ["c3"], 1, None, A.bitwise_and)
     memset(T.zz[:], "zz", 0.0)
-    copy(T.rc[:], "rc", T.c5[:], ["c5"])
-    ts(T.e1[:], "e1", f7, ["f"], 1.0 / 7, -3.0 / 7, A.mult, A.add)
-    ts(T.a2[:], "a2", f7, ["f"], 16.0, None, A.mult)
-    ts(T.d2[:], "d2", f7, ["f", "gf"], T.gf[:], None, A.add)
-    ts(T.d1[:], "d1", T.e1[:], ["e1"], -111.0, None, A.mult)
-    tt(T.e2[:], "e2", T.d2[:], T.e1[:], ["d2", "e1"], A.add)
-    memset(T.ch[:, 0:H], "ch0", 0.0)
-    memset(T.x0[:, 0:16], "x0z", 0.0)
-    tt(T.d3[:], "d3", T.d1[:], T.a2[:], ["d1", "a2"], A.add)
-    ts(T.e3[:], "e3", T.e2[:], ["e2"], 1, None, A.bitwise_and)
-    copy(pn, "pn0", T.grd0[:], ["grd0"])
-    ts(seven("d4", 0), "d40", T.e3[:], ["e3"], 240.0, None, A.mult)
-    ts(seven("d4", 1), "d41", T.e3[:], ["e3"], -240.0, 352.0, A.mult, A.add)
-    turn("tp")
     for u in range(2):
-        tt(seven("d5", u), "d5%d" % u, T.d3[:], seven("d4", u), ["d3", "d4%d" % u], A.add)
-    memset(T.ch[:, H:I], "ch", 2.0)
-    memset(T.thr[:], "thr", 192 + 4100.5)
+        ts(listed("fk", u), "fk%d" % u, T.f[:, 0:NC[u]], ["f"], 1.0 / NC[u], (1.0 / NC[u] - 1) / 2, A.mult, A.add)
+        ts(T.par[:, u:u + 1], "par%d" % u, T.c4[:], ["c4"], H[u] + 16.0, None, A.mult)
+    ts(T.a2[:], "a2", T.f[:], ["f"], 16.0, None, A.mult)
+    for u in range(2):
+        ts(listed("a1", u), "a1%d" % u, listed("fk", u), ["fk%d" % u, "par%d" % u], 1.0 - H[u], T.par[:, u:u + 1], A.mult, A.add)
+    turn("tg", "grd0", ["grd0", "grd0a", "grd0b"], 0, 0)
+    for u in range(2):
+        tt(listed("a3", u), "a3%d" % u, listed("a1", u), T.a2[:, 0:NC[u]], ["a1%d" % u, "a2"], A.add)
+    copy(T.rc[:], "rc", T.c5[:], ["c5"])
     ts(T.kz[:], "kz", T.c5[:], ["c5"], 0.5, 2048.0, A.is_lt, A.mult)
     for u in range(2):
-        copy(listed("sel", u), "sel%d" % u, seven("d5", u), ["d5%d" % u])
-    ts(T.mk[:], "mk", T.t16[:], ["t16", "rc"], T.rc[:], -16384.0, A.not_equal, A.mult)
+        copy(listed("sel", u), "sel%d" % u, listed("a3", u), ["a3%d" % u])
+    memset(T.ch[:, 0:M], "ch0", 0.0)
+    memset(T.ch[:, M:2 * M], "ch", 2.0)
+    listing("ku", "tg", 0)
     ts(T.zz[:, 15:143:16], "zz", T.bd[:, 0:128:16], ["bd"], -33.0, None, A.mult)
-    copy(half("ku", 0), "ku0", turned("tp", 0), ["tp0", "tp1", "sel0"])
-    limits(half("lim0", 0), "lim0", 0.0, 0)
+    ts(T.mk[:], "mk", T.t16[:], ["t16", "rc"], T.rc[:], -16384.0, A.not_equal, A.mult)
+    copy(T.k16[:], "k160", T.grd0[:, 16:16 + I], ["grd0"])
+    memset(T.thr[:], "thr", 192 + 4100.5)
+    memset(T.x0[:, 0:16], "x0z", 0.0)
+    for a, key in ((256, "pn0"), (272 + H[0], "pn1"), (496, "pad")):
+        memset(T.pv[:, a:a + 16], key, 0.0)
+    limits(part("lim0", 0), "lim0", 0.0, 0)
     act(T.rs[:], "rs", T.t16[:], ["t16"], F.Sigmoid, scale=256.0, bias=-128.0)
-    limits(half("lim0", 1), "lim0", 0.0, 1)
     act(T.nbk[:], "nbk", T.bd[:], ["bd"], scale=-4096.0)
     act(T.id0[:], "id0", T.idb[:], ["idb", "kz"], scale=T.kz[:])
     act(T.idl[:], "idl", T.idb[:], ["idb"], scale=2048.0)
-    act(T.idx[:], "idx", T.idb[:], ["idb"], scale=4096.0)
     iota("t8", [[8, I]], 0)
     select("low", "nbk", [[1, 128]], A.is_gt, 0.0, 0, -1)
     select("tr", "low", [[-1, 128]], A.not_equal, 4096.0, 0, 1)
+    iota("x", [[0, 16 + WX]], 0, int(UP))
+    wrote["xz"] = wrote["x"]
+    load("g", "d_up", xw, T.xc[:], [], ["x"], accum_op=A.add)
 
     def first(s):
         if s == "j00":
-            copy(half("ku", 1), "ku1", turned("tp", 1), ["tp0", "tp1", "sel1"])
-        if s == "j01":
-            copy(T.k16[:], "k160", T.grd0[:], ["grd0"])
-            ts(T.l16[:], "l160", T.nam0[:], ["nam0"], 1.0 / 2048, -HALF, A.mult, A.add)
+            turn("tn", "nam0", ["nam0", "nam0a", "nam0b"], 0, 0)
+            ts(T.l16[:], "l160", T.nam0[:, 16:16 + I], ["nam0"], 1.0 / 2048, -HALF, A.mult, A.add)
             wrote["k161"], wrote["l161"] = wrote["k160"], wrote["l160"]
-            copy(pn, "pn0", T.nam0[:], ["nam0"])
+            listing("lu", "tn", 0)
+        if s == "j01":
+            turn("tg", "grd0", ["grd0", "grd0a", "grd0b"], 0, 1)
+            turn("tn", "nam0", ["nam0", "nam0a", "nam0b"], 0, 1)
         if s == "j02":
-            turn("tq")
-        if s == "j03":
-            for u in range(2):
-                copy(half("lu", u), "lu%d" % u, turned("tq", u), ["tq0", "tq1", "sel%d" % u])
+            listing("ku", "tg", 1)
+            listing("lu", "tn", 1)
+        if s == "w00":
+            limits(part("lim0", 1), "lim0", 0.0, 1)
+        if s == "w01":
+            act(T.idx[:], "idx", T.idb[:], ["idb"], scale=4096.0)
             for c, v in enumerate((-2.0 ** 24, -4096.0)):
-                act(half("cc", c), "cc%d" % c, T.t16[:], ["t16"], scale=0.0, bias=v)
+                act(T.cc[:, M * c:M * c + M], "cc%d" % c, T.t16[:], ["t16"], scale=0.0, bias=v)
             wrote["cc"] = wrote["cc1"]
-        if s in ("w00", "w01", "w02"):
-            a = 16 + 600 * int(s[2])
-            b = min(a + 600, 16 + WX)
-            act(T.x[:, a:b], "x", T.x0[:, a:b], ["x0"], bias=UP)
-        if s == "u1":
-            memset(T.x[:, 0:16], "xz", UP)
+        if s in AMONG0:
+            fetch(1)
+        if s == "u0":
             ts(T.wc[:], "wc", T.c6[:], ["c6"], 2.0, 1.0, A.mult, A.add)
             ts(T.bm0[:], "bm0", T.f[:], ["f"], 8.0, -1028.5, A.mult, A.add)
             ts(T.bm[:], "bm", T.f[:], ["f"], 8.0, 64 * UP - 1028.5, A.mult, A.add)
-        if s == "d1":
-            act(T.onef[:], "onef", T.ones[:], ["ones"])
         if s == "F":
+            act(T.onef[:], "onef", T.ones[:], ["ones"])
             act(T.bw[:], "bw", T.bd[:], ["bd", "wc"], scale=T.wc[:])
             act(T.idn[:], "idn", T.idb[:], ["idb"], scale=-1.0)
-            act(T.half[:], "half", T.t16[:], ["t16"], scale=0.0, bias=0.5)
+            act(T.half[:], "half", T.t8[:], ["t8"], scale=0.0, bias=0.5)
 
     for t in range(RO):
         last = t == RO - 1
         x, gr, up, bm = ("x0", "lim0", UP, "bm0") if t == 0 else ("x", "gr", 0.0, "bm")
         h, gs = ["h%d%d" % (t, u) for u in range(2)], ["gs%d%d" % (t, u) for u in range(2)]
-        helped = HELP0 if t == 0 else ()
         done = {"j0": 0, "j1": 0, "w0": 0, "w1": 0}
 
         def piece(s, u):
             j = done[s + str(u)]
             done[s + str(u)] = j + 1
-            a, b = ([0] + JUDGE[u])[j], JUDGE[u][j]
-            return a, b, H * (16 * u + a), H * (16 * u + b), "%d%d" % (u, j)
+            return ([0] + JUDGE[u])[j], JUDGE[u][j], "%d%d" % (u, j)
 
         def judge(u):
-            a, b, c, e, key = piece("j", u)
-            tt(T.u[:, c:e], "u" + key, T[x][:, 16:16 + WX].indirect(T.ku[:, c // 16:e // 16]), T.gj[:, 4 * H * u:4 * H * u + e - c],
-               [x, "ku%d" % u] + ["gj%d" % n for n in range(4 * u, 4 * u + b - a)], A.subtract)
+            a, b, key = piece("j", u)
+            tt(lanes("u", u, a, b), "u" + key, T[x][:, 16:16 + WX].indirect(entries("ku", u, a, b)), T.gj[:, 768 * u:768 * u + H[u] * (b - a)],
+               [x, "ku%d" % u] + ["gj%d%d" % (u, c) for c in range(b - a)], A.subtract)
             if t == 0:
                 first("j" + key)
 
         def mark(u):
-            a, b, c, e, key = piece("w", u)
-            act(T.w[:, c:e], "w" + key, T.u[:, c:e], ["u" + key], F.Sigmoid, scale=4.0, bias=-4.0 * 644 - math.log(32.0))
+            a, b, key = piece("w", u)
+            act(lanes("w", u, a, b), "w" + key, lanes("u", u, a, b), ["u" + key], F.Sigmoid, scale=4.0, bias=-4.0 * 644 - math.log(32.0))
             for k in range(a, b):
-                mm("pa%d" % u, 0, "zz", half("w", 16 * u + k), "w" + key, H, k == 0, k == 15, lhs=T.zz[:, 15 - k:143 - k])
+                mm(pa[u], 0, "zz", lanes("w", u, k, k + 1), "w" + key, H[u], k == 0, k == 15, lhs=T.zz[:, 15 - k:143 - k])
             if t == 0:
                 first("w" + key)
 
         def send(u):
-            tt(T[gs[u]][:], gs[u], T[x][:, 0:16 + WX].indirect(listed("ks", u)), half(gr, u),
+            tt(cols(gs[u], u), gs[u], T[x][:, 0:16 + WX].indirect(listed("ks", u)), part(gr, u),
                [x, x + "z", "ks%d" % u, gr if t == 0 else "gr%d" % u], A.max)
             dst = T.cores[(rank + 1 + t % 7) % 8]
             src = T.cores[(rank - 1 - t % 7) % 8]
             eng = topo.engines(core, dst)[:8]
             rid, pid = topo.addr(dst, core)
             waits("g", [gs[u]], [])
-            g.remote_dma(T[h[u]][:], T[gs[u]][:], T.sem["arr%d%d" % (t, u)], T.sem.sent, pid, rid, sum(1 << e for e in eng))
+            g.remote_dma(cols(h[u], u), cols(gs[u], u), T.sem["arr%d%d" % (t, u)], T.sem.sent, pid, rid, sum(1 << e for e in eng))
             wrote[h[u]] = ("remote", "arr%d%d" % (t, u), len(topo.engines(src, core)[:8]), {})
-            if last:
-                act(half("pg", u), "pg", T[gs[u]][:], [gs[u]], bias=-UP)
 
         def ready(u):
-            masks("pk")
-            mm("pk", 0, "idb", half("t8", u), "t8", H, False, False)
-            mm(pg[u], 0, "idb", T[gs[u]][:], gs[u], H, True, False)
+            masks(pf[u], u)
+            mm(pf[u], 0, "idb", part("t8", u), "t8", H[u], False, False)
+            mm(pe[u], 0, "idb", cols(gs[u], u), gs[u], H[u], True, False)
 
         def land(u):
-            mm("pk", 0, "bw", T[h[u]][:], h[u], H, False, True)
-            mm(pg[u], 0, "idn", T[h[u]][:], h[u], H, False, True)
+            mm(pf[u], 0, "bw", cols(h[u], u), h[u], H[u], False, True)
+            mm(pe[u], 0, "idn", cols(h[u], u), h[u], H[u], False, True)
 
         def low(u):
-            mm(pg[u], 0, "idb", T[gs[u]][:], gs[u], H, True, False)
-            mm(pg[u], 0, "idn", half("rl", u), "rl%d" % u, H, False, True)
+            mm(pe[u], 0, "idb", cols(gs[u], u), gs[u], H[u], True, False)
+            mm(pe[u], 0, "idn", part("rl", u), "rl%d" % u, H[u], False, True)
 
         def rest():
-            fetch(8, helped)
+            fetch(len(FETCH))
             fetched[0] = 0
 
-        halves = {
-            "j": judge, "w": mark, "G": guards, "N": names, "P": lambda u: masks("pk"), "L": lambda u: masks("pl"),
+        tp = [["tp%d0" % u, "tp%d1" % u] for u in range(2)]
+        parts = {
+            "j": judge, "w": mark, "G": guards, "N": names, "P": lambda u: masks("pk", u), "L": lambda u: masks(pe[u], u),
             "u": und, "kh": kh, "lh": lh, "s": alive, "si": implied, "so": old, "gs": send, "R": ready, "land": land, "low": low,
-            "a": lambda u: ts(count_of(u), "a%d" % u, T["pa%d" % u][:, 0:H], ["pa%d" % u, "thr"], T.thr[:], 4100.5, A.add, A.max),
-            "b": lambda u: ts(half("b", u), "b%d" % u, count_of(u), ["a%d" % u], 3.5, None, A.add),
-            "d": lambda u: act(half("dead", u), ["dead%d" % u, "cnt%d" % u], half("b", u), ["b%d" % u], F.Relu, scale=-1.0 / 16, bias=257.0,
+            "a": lambda u: counted(part("pv", u), "a", u), "b": lambda u: counted(part("b", u), "b", u),
+            "d": lambda u: act(part("dead", u), ["dead%d" % u, "cnt%d" % u], part("b", u), ["b%d" % u], F.Relu, scale=-1.0 / 16, bias=257.0,
                                accum_out=T.cnt[:, u:u + 1]),
-            "sk": lambda u: diagonal("pk", "sk", u), "sl": lambda u: diagonal("pl", "sl", u), "sq": lambda u: diagonal("pk", "sq", u),
+            "sk": lambda u: diagonal("pk", "sk", u), "sl": lambda u: diagonal(pe[u], "sl", u), "sq": lambda u: diagonal(pf[u], "sq", u),
             "ks": lambda u: copy(listed("ks", u), "ks%d" % u, picked("sk", u), ["sk%d" % u]),
             "ls": lambda u: ts(listed("ls", u), "ls%d" % u, picked("sl", u), ["sl%d" % u], -1.0, None, A.add),
-            "md": lambda u: ts(half("md", u), "md%d" % u, T.rel0[:, 0:W].indirect(listed("ls", u)), ["rel0", "ls%d" % u], -1023.5, 1.0 / 2048,
+            "md": lambda u: ts(part("md", u), "md%d" % u, T.rel0[:, 0:W].indirect(listed("ls", u)), ["rel0", "ls%d" % u], -1023.5, 1.0 / 2048,
                                A.add, A.mult),
-            "t": lambda u: tt(half("t1", u), "t1%d" % u, half("md", u), half("pa%d" % u, 0), ["md%d" % u, "pa%d" % u], A.subtract),
-            "o": lambda u: tt(half("t2", u), "t2%d" % u, half("mo", u), half("pa%d" % u, 1),
-                              ["mo%d_%d" % (u, k) for k in range(16)] + ["pa%d" % u], A.subtract),
-            "m": lambda u: tt(own(u), pns[u], half("t1", u), half("pa%d" % u, 2), ["t1%d" % u, "pa%d" % u], A.max),
-            "n": lambda u: tt(own(u), pns[u], half("t2", u), own(u), ["t2%d" % u, pns[u]], A.max),
-            "k": lambda u: ts(half("k16", u), "k16%d" % u, own(u), [pns[u]], ROUND, -ROUND, A.add, A.add),
-            "l": lambda u: tt(half("l16", u), "l16%d" % u, own(u), half("k16", u), [pns[u], "k16%d" % u], A.subtract),
-            "turn": lambda u: turn("tq", 96, I, 128, 256) if u else turn("tp", 0, 128, 0, 128),
-            "kt": lambda u: ts(half("kt", u), "kt%d" % u, turned(tb[u], u), [tb[u] + "0", tb[u] + "1"], ROUND, -ROUND, A.add, A.add),
-            "lt": lambda u: tt(half("lt", u), "lt%d" % u, turned(tb[u], u), half("kt", u), [tb[u] + "0", tb[u] + "1", "kt%d" % u], A.subtract),
-            "lu": lambda u: ts(half("lu", u), "lu%d" % u, half("lt", u), ["lt%d" % u], 2048.0, 1023.5, A.mult, A.add),
-            "ku": lambda u: copy(half("ku", u), "ku%d" % u, half("kt", u), ["kt%d" % u]),
-            "hp": lambda u: act(half("hp", u), "hp%d" % u, T[h[u]][:], [h[u]], bias=up - 0.5),
-            "rl": lambda u: act(half("rl", u), "rl%d" % u, half(pg[u], 0), [pg[u]], F.Relu, bias=-2.0),
-            "gj": lambda u: limits(half(pg[u], 0), pg[u], up, u),
-            "gr": lambda u: act(half("gr", u), "gr%d" % u, half(pg[u], 0), [pg[u]], bias=up),
-            "r": lambda u: tt(seven("f8", u), "f8%d" % u, picked("sq", u), seven(bm, u), ["sq%d" % u, bm], A.subtract),
-            "z": lambda u: tt(seven("z", u), "z%d" % u, picked("sq", u), seven("f8", u), ["sq%d" % u, "f8%d" % u], A.subtract),
-            "cu": lambda u: ts(listed("cu", u), "cu%d" % u, seven("z", u), ["z%d" % u], 1032.0 - 64 * (UP - up), None, A.add),
-            "bl": lambda u: tt(half("bl", u), "bl%d" % u, xw.indirect(listed("cu", u)), half("hp", u), ["x", "cu%d" % u, "hp%d" % u], A.add),
-            "put": lambda u: tt(xw.indirect(listed("cu", u)), "x", half("bl", u), T.half[:], ["bl%d" % u, "cu%d" % u, "half"], A.mult),
-            "h": lambda u: ts(half("gm", u), "gm%d" % u, T[h[u]][:], [h[u]], 2.0 - UP, None, A.add),
-            "y": limits_out,
-            "og": lambda u: (ts(half("og", u), "og%d" % u, own(u), [pns[u]], ROUND, -ROUND, A.add, A.add),
-                             load("s", "d_og", half("yg", u), half("og", u), ["og%d" % u], ["yg%d" % u])),
-            "ot": lambda u: tt(half("lt", u), "lt%d" % u, own(u), half("og", u), [pns[u], "og%d" % u], A.subtract),
-            "on": lambda u: (ts(half("on", u), "on%d" % u, half("lt", u), ["lt%d" % u], 2048.0, 1023.5, A.mult, A.add),
-                             load("s", "d_on", half("yn", u), half("on", u), ["on%d" % u], ["yn%d" % u])),
+            "t": lambda u: tt(part("t1", u), "t1%d" % u, part("md", u), cols(pa[u], u), ["md%d" % u, pa[u]], A.subtract),
+            "o": lambda u: tt(part("t2", u), "t2%d" % u, part("mo", u), cols(pa[u], u, M), ["mo%d_%d" % (u, k) for k in range(16)] + [pa[u]],
+                              A.subtract),
+            "m": lambda u: tt(own(u), pns[u], part("t1", u), cols(pa[u], u, 2 * M), ["t1%d" % u, pa[u]], A.max),
+            "n": lambda u: tt(own(u), pns[u], part("t2", u), own(u), ["t2%d" % u, pns[u]], A.max),
+            "k": lambda u: ts(part("k16", u), "k16%d" % u, own(u), [pns[u]], ROUND, -ROUND, A.add, A.add),
+            "l": lambda u: tt(part("l16", u), "l16%d" % u, own(u), part("k16", u), [pns[u], "k16%d" % u], A.subtract),
+            "turn": lambda u: turn("tp", "pv", pns + ["pad"], 256, u),
+            "kt": lambda u: ts(part("kt", u), "kt%d" % u, turned("tp", u), tp[u], ROUND, -ROUND, A.add, A.add),
+            "lt": lambda u: tt(part("lt", u), "lt%d" % u, turned("tp", u), part("kt", u), tp[u] + ["kt%d" % u], A.subtract),
+            "lu": lambda u: ts(part("lu", u), "lu%d" % u, part("lt", u), ["lt%d" % u], 2048.0, 1023.5, A.mult, A.add),
+            "ku": lambda u: copy(part("ku", u), "ku%d" % u, part("kt", u), ["kt%d" % u]),
+            "hp": lambda u: (act(cols(pf[u], u), pf[u], cols(gs[u], u), [gs[u]], bias=-UP) if last else
+                             act(part("hp", u), "hp%d" % u, cols(h[u], u), [h[u]], bias=up - 0.5)),
+            "rl": lambda u: act(part("rl", u), "rl%d" % u, cols(pe[u], u), [pe[u]], F.Relu, bias=-2.0),
+            "gj": lambda u: limits(cols(pe[u], u), pe[u], up, u),
+            "gr": lambda u: act(part("gr", u), "gr%d" % u, cols(pe[u], u), [pe[u]], bias=up),
+            "h": lambda u: ts(part("gm", u), "gm%d" % u, cols(h[u], u), [h[u]], 2.0 - UP, None, A.add), "y": limits_out,
+            "og": lambda u: (ts(part("og", u), "og%d" % u, own(u), [pns[u]], ROUND, -ROUND, A.add, A.add),
+                             load("s", "d_og", part("yg", u), part("og", u), ["og%d" % u], ["yg%d" % u])),
+            "ot": lambda u: tt(part("lt", u), "lt%d" % u, own(u), part("og", u), [pns[u], "og%d" % u], A.subtract),
+            "on": lambda u: (ts(part("on", u), "on%d" % u, part("lt", u), ["lt%d" % u], 2048.0, 1023.5, A.mult, A.add),
+                             load("s", "d_on", part("yn", u), part("on", u), ["on%d" % u], ["yn%d" % u])),
         }
         whole = {
-            "E": lambda: fetch(4 - fetched[0], helped), "F": rest, "f": lambda: fetch(1), "C": deaths,
-            "pi": lambda: copy(T.pi[:], "pi", T.pf[:, 0:1], ["pf"]),
+            "E": lambda: fetch(firsts - fetched[0]), "F": rest, "f": lambda: fetch(1), "C": deaths,
+            "r": lambda: tt(T.f8[:], "f8", T.sq[:, 15::16], T[bm][:], ["sq0", "sq1", bm], A.subtract),
+            "z": lambda: tt(T.z[:], "z", T.sq[:, 15::16], T.f8[:], ["sq0", "sq1", "f8"], A.subtract),
+            "cu": lambda: ts(T.cu[:], "cu", T.z[:], ["z"], 1032.0 - 64 * (UP - up), None, A.add),
+            "bl": lambda: tt(T.bl[:], "bl", xw.indirect(T.cu[:]), T.hp[:], ["x", "cu", "hp0", "hp1"], A.add),
+            "put": lambda: tt(xw.indirect(T.cu[:]), "x", T.bl[:], T.half[:], ["bl", "cu", "half"], A.mult),
+            "pi": lambda: copy(T.pi[:], "pi", T.pk[:, 0:1], ["pk"]),
             "pj": lambda: ts(T.pj[:], "pj", T.pi[:], ["pi"], 1, None, A.bitwise_and),
             "thr": lambda: ts(T.thr[:], "thr", T.pj[:], ["pj"], 32.0, 192 + 4100.5, A.mult, A.add),
         }
         order = ORDER.split()
-        for n, s in enumerate(order):
+        if last:
+            order = [s for n, s in enumerate(order) if s not in END.split() and (s not in whole or n <= order.index("F"))] + END.split()
+        for s in order:
             if s in whole:
-                if not (last and n > order.index("F")):
+                if not (last and s not in "EFf"):
                     whole[s]()
             elif s in LATE:
                 if t > 0:
-                    halves[s[:-1]](int(s[-1]))
+                    parts[s[:-1]](int(s[-1]))
             elif not (last and s[:-1] in NEXT):
-                halves[LAST.get(s[:-1], s[:-1]) if last else s[:-1]](int(s[-1]))
+                parts[s[:-1]](int(s[-1]))
             if t == 0:
                 first(s)
     g.wait_ge(T.sem.sent, 2 * sum(len(topo.engines(core, T.cores[(rank + 1 + t % 7) % 8])[:8]) for t in range(RO)))
     for q in ("v", "a", "t", "g"):
         if known["g"].get("c" + q, 0) < count[q]:
             g.wait_ge(T.sem["c" + q], count[q])
-    for s in ("d_on", "d_og", "d_ol"):
+    for s in ("d_up", "d_on", "d_og", "d_ol"):
         g.wait_ge(T.sem[s], dcount[s])

@@ -6,60 +6,150 @@ WX = 1792
 W = 2048
 RO = 4
 NC = (8, 6)
-JUDGE = [[4, 8, 12, 16], [5, 10, 13, 15, 16]]
-FETCH = [(0, 0, 4), (0, 4, 8), (0, 8, 12), (0, 12, 16), (1, 0, 6), (1, 6, 11), (1, 11, 16)]
-AMONG0 = ("w02", "w03")
-OWN = (2, 3)
-ORDER = ("j0 j0 j0 k1 N0 G0 w0 P0 j0 j1 j1 w0 l1 w0 j1 w0 N1 a0 w1 w1 b0 j1 u0 lt1 w1 j1 d0 lu1 w1 w1 kh0 E L0 lh0 b1 si0 a1 G1 sk0 P1 u1 ks0 "
-         "sl0 so1 gs0 kh1 s0 L1 ls0 lh1 sk1 f d1 F md0 so0 si1 s1 ks1 sl1 gs1 hp0 t0 R1 ls1 o0 m0 md1 n0 t1 R0 land0 rl0 C hp1 turn0 sq0 land1 "
-         "kt0 m1 low0 k0 o1 lt0 sq1 rl1 n1 low1 pi gj0 lu0 r gr0 f turn1 gr1 z l0 ku0 f f cu kt1 bl pj put f gj1 ku1 thr")
-END = "md1 t0 t1 m0 m1 o1 n0 n1 og0 og1 h0 ot0 ot1 y0 on0 on1 h1 y1"
-LATE = ("lt1", "lu1", "k1", "l1")
-NEXT = ("R", "land", "rl", "low", "gj", "gr", "sq", "turn", "kt", "ku", "k", "l", "lt", "lu")
-ROUND = 1.5 * 2.0 ** 23
+JUDGE = [[4, 8, 12, 16], [5, 10, 13, 16]]
+VL = (16, 13)
+FETCH = [(0, 0, 5), (0, 5, 10), (0, 10, 16), (1, 0, 6), (1, 6, 11), (1, 11, 16)]
+OWN = (2, 2)
+KV = "vv"
+START = "pads rs ka lima zz cst kb limb nbk tr idf mk na nb va vb bdf xg gr2 ids cc bw mq c8"
+LATE = ""
+ROUND = "F0 F1 S0 S1 G0 G1 M0 M1 J0 J1 b0 a0 u0 d0 U0 kv0 P0 sk0 ks0 gs0 b1 a1 u1 d1 U1 kv1 P1 sk1 ks1 gs1 si0 sa0 ls0 md0 D0 E0 r0 c0 n0 si1 sa1 ls1 md1 D1 E1 r1 c1 n1"
+BLEND = "turn0 ti0 ku0 la0 lu0 turn1 ti1 ku1 la1 lu1 R0 land0 sq0 cu0 hp0 bl0 put0 T0 H0 gr0 gj0 gk0 R1 land1 sq1 cu1 hp1 bl1 put1 T1 H1 gr1 gj1 gk1 C tb thr"
+ROUND0 = ROUND
+FILL = "v"
+FILLX = "g"
+LOADS = "glxnr"
+END = "g0 h0 y0 g1 h1 y1 k0 l0 og0 on0 k1 l1 og1 on1"
+FIRST = ".ip cst' zz'' cst .ones pads'' .c1 pads' .c2 .c5 .c6 .ff .g16 pads''' .c3 cst'''' .rc .f cst'' .c4 pads zz .fk1 .par0 .par1 .a2 mk'' .fk0 .t16 .idb .bd cst'''''' cst'''''''' .a11 ids .a10 .bdx cc'''' lima''' lima' limb''' limb'' lima'' limb'''' lima cc''' gr2 rs limb ka' .a31 kb .a30 cst''''' ka .sel0 kb' zz' .sel1 ka'' nbk mk' mk xg j00 j02 na j01 j03 na' kb'' tr xg' mq tr' bdf limb' w00 idf w02 w01 w03 M1 na'' cst''' cc' nb' S0 w00' w01' w02' w03' j10 va cst''''''' j11 vb b0 a0 S1 j12 u0 j13 cc'' nb zz''' w13 f0 w10 f2 w11 w12 f1 d0 w10' M0 G0 G1 U0 w11' w12' w13' kv0 nb'' .pada cc c8 .wd a1 b1 na''' P0 sk0 nb''' u1 .wc si0 ks0 ids' ids'' .padb f3 f5 f4 d1 U1 sa0 gs0 kv1 ls0 mq' D0 c0 P1 T0 E0 gs0' md0 sk1 c8' c8'' bw' ks1 si1 r0 gs1 n0 bw sa1 turn0' ls1 gs1' bw'' turn0 md1 ti0 la0 R0 R1 D1 c1 E1 r1 ku0 lu0 n1 H0 land0 land1 T1 H1 gr0 sq0 turn1 sq1 turn1' cu0 cu1 gr1 ti1 hp1 hp0 gj0 gj0' bl1 bl0 la1 put1 put0 >S1 >M1 C >S0 gk0 >f2 >G1"
+ORDER = "<ku1 <lu1 j00 R1 j01 <tb <gj1' <gj1 f1 f0 w00 w01 j02 j03 <thr w02 w03 <gk1 <gk1' j10 w10 w00' M0 w01' w02' w03' G0 R0 w10' j11 w11 w11' j12 a0 b0 j13 u0 w13 w12 w12' U0 w13' kv0 P0 b1 a1 u1 sk0 U1 c0 si0 ks0 kv1 sa0 gs0 ls0 gs0' P1 f3 f4 d0 f5 D0 E0 d1 sk1 md0 ks1 r0 gs1 si1 n0 gs1' sa1 turn0 turn0' ls1 ti0 md1 T0 c1 D1 E1 >S0 H0 T1 land0 la0 r1 ku0 lu0 n1 gr0 sq0 turn1 turn1' cu0 land1 H1 sq1 gr1 ti1 cu1 hp0 hp1 gj0 gj0' bl0 la1 bl1 put0 put1 >M1 >S1 gk0 C >f2 >G1"
+LAST = "<ku1 <lu1 j01 <gj1' <tb <thr <gj1 f1 f0 w01 j00 w00 G0 <gk1' <gk1 j02 j03 j10 w02 w03 w00' w01' M0 w02' w03' w10 w10' j11 j12 w11 a0 b0 w11' j13 u0 w12 U0 w12' w13 w13' d0 f3 f5 f4 kv0 P0 a1 b1 sk0 u1 U1 D0 E0 si0 ks0 sa0 kv1 P1 c0 ls0 gs0 gs0' md0 sk1 ks1 r0 si1 gs1 gs1' g0 d1 c1 D1 E1 sa1 n0 ls1 l0 md1 k0 on0 r1 h0 og0 n1 y0 k1 l1 g1 y0' og1 h1 on1 y1 y1'"
+FIXED = {"v": 0.02, "a": 0.04, "t": 0.015, "g": 0.17}
+LEAST = {"v": 48, "a": 0, "t": 0, "g": 0}
+CYCLE = {"v": 0.00092, "a": 0.00092, "t": 0.00047, "g": 0.00092}
+ISSUE = {"s": 0.05, "a": 0.05, "g": 2.0}
+WAKE = 0.21
+FAR = 1.5
+GATHER, SCATTER, LAND, RATE, SEND, OPEN = 1.3, 2.6, 1.1, 420e3, 0.2, 1.0
+PASSES = 150
+SHAKE = 0.6
+SPAN = 6.0
+SEED = 1
 HALF = 1023.5 / 2048
+BIG = 2.0 ** 22
+EIGHT = 1.5 * 2.0 ** 26
+KILO = 1.5 * 2.0 ** 33
 UP = 144.0
 M = 160
+TOP = 4096.0
 
 SB = "sbuf"
 BF, F32, F16, I32, U16 = "bfloat16", "float32", "float16", "int32", "uint16"
 SCRATCH = {
-    "x": (SB, [128, 16 + WX], BF), "x0": (SB, [128, 16 + WX], BF), "lim0": (SB, [128, I], BF),
-    "grd0": (SB, [128, 256], I32), "nam0": (SB, [128, 256], I32), "rel0": (SB, [128, W], I32),
-    "u": (SB, [128, 16 * I], BF), "w": (SB, [128, 16 * I], BF), "nb": (SB, [128, 16 * I], F32),
-    "ku": (SB, [128, I], U16), "lu": (SB, [128, I], U16), "tp": (SB, [128, 512], F32), "tg": (SB, [128, 512], I32), "tn": (SB, [128, 512], I32),
-    "kt": (SB, [128, I], F32), "lt": (SB, [128, I], F32), "k16": (SB, [128, I], F16), "l16": (SB, [128, I], F16),
-    "gj": (SB, [128, 1536], F32), "gr": (SB, [128, I], BF), "rl": (SB, [128, I], BF), "gm": (SB, [128, I], BF), "hp": (SB, [128, I], F32),
+    "x": (SB, [128, 16 + WX], BF), "x0": (SB, [128, WX], BF), "lim0": (SB, [128, I], BF),
+    "grd0": (SB, [128, 256], I32), "nam0": (SB, [128, 256], I32), "grd0t": (SB, [128, 512], I32), "nam0t": (SB, [128, 512], I32), "rel0": (SB, [128, W], I32),
+    "u": (SB, [128, 16 * I], BF), "w": (SB, [128, 16 * I], BF), "wv": (SB, [128, 16 * I], F16), "nb": (SB, [128, 16 * I], F32),
+    "ku": (SB, [128, I], U16), "lu": (SB, [128, I], U16), "tp": (SB, [128, 512], F32),
+    "v": (SB, [128, 256], F32), "ti": (SB, [128, I], I32), "la": (SB, [128, I], I32), "vi": (SB, [128, I], I32),
+    "gj": (SB, [128, 1536], F32), "gr": (SB, [128, I], BF), "gm": (SB, [128, I], BF), "hp": (SB, [128, I], F32),
     "b": (SB, [128, I], BF), "und": (SB, [128, I], BF), "dead": (SB, [128, I], BF),
-    "kh": (SB, [128, I], F16), "lh": (SB, [128, 2 * I], F16),
-    "sk": (SB, [128, I], F32), "sl": (SB, [128, I], F32), "sq": (SB, [128, I], F32),
+    "kv": (SB, [128, I], F32), "r2": (SB, [128, I], F32), "sk": (SB, [128, I], F32), "sq": (SB, [128, I], F32),
     "ks": (SB, [128, 14], U16), "ls": (SB, [128, 14], U16), "cu": (SB, [128, 14], U16), "sel": (SB, [128, 14], U16),
-    "f8": (SB, [128, 14], BF), "z": (SB, [128, 14], F32), "bm0": (SB, [128, 14], F32), "bm": (SB, [128, 14], F32),
-    "bl": (SB, [128, I], BF), "half": (SB, [128, I], BF),
-    "md": (SB, [128, I], F32), "mo": (SB, [128, I], F32), "t1": (SB, [128, I], F32), "t2": (SB, [128, I], F32),
-    "cnt": (SB, [128, 2], F32), "pi": (SB, [128, 1], I32), "pj": (SB, [128, 1], I32), "thr": (SB, [128, 1], F32),
+    "si": (SB, [128, 14], I32), "sa": (SB, [128, 14], I32), "bl": (SB, [128, I], BF), "half": (SB, [128, I], BF),
+    "md": (SB, [128, I], F32), "mo": (SB, [128, I], F32), "cnt": (SB, [128, 2], F32), "tb": (SB, [128, 1], F32), "thr": (SB, [128, 1], F32), "kc": (SB, [128, 2], BF),
     "ip": (SB, [128, 1], I32), "c1": (SB, [128, 1], I32), "c2": (SB, [128, 1], I32), "c3": (SB, [128, 1], I32), "c4": (SB, [128, 1], I32),
     "c5": (SB, [128, 1], I32), "c6": (SB, [128, 1], I32), "par": (SB, [128, 2], F32),
-    "g16": (SB, [128, 1], F32), "rc": (SB, [128, 1], F32), "wc": (SB, [128, 1], F32), "kz": (SB, [128, 1], F32),
+    "g16": (SB, [128, 1], F32), "wc": (SB, [128, 1], F32), "wd": (SB, [128, 1], F32), "wn": (SB, [128, 1], F32), "rc": (SB, [128, 1], F32),
     "ff": (SB, [128, 14], F32), "f": (SB, [128, 14], F32), "fk": (SB, [128, 14], I32), "a1": (SB, [128, 14], F32), "a2": (SB, [128, 14], F32),
     "a3": (SB, [128, 14], F32),
-    "t16": (SB, [128, M], BF), "t8": (SB, [128, I], BF), "mk": (SB, [128, M], BF), "rs": (SB, [128, M], BF),
-    "cc": (SB, [128, 2 * M], BF), "ch": (SB, [128, 2 * M], F16),
-    "ones": (SB, [128, 128], BF), "onef": (SB, [128, 128], F32), "idb": (SB, [128, 128], BF), "idl": (SB, [128, 128], BF),
-    "id0": (SB, [128, 128], BF), "idx": (SB, [128, 128], BF), "idn": (SB, [128, 128], BF), "bd": (SB, [128, 128], BF),
-    "nbk": (SB, [128, 128], BF), "low": (SB, [128, 128], BF), "tr": (SB, [128, 128], BF), "bw": (SB, [128, 128], BF), "zz": (SB, [128, 144], BF),
+    "t16": (SB, [128, I], BF), "t8": (SB, [128, I], BF), "mk": (SB, [128, I], BF), "mq": (SB, [128, I], BF), "rs": (SB, [128, I], BF),
+    "cc": (SB, [128, M], BF), "two": (SB, [128, M], BF), "c8": (SB, [128, M], BF),
+    "one": (SB, [128, M], BF), "ones": (SB, [128, 128], BF), "onp": (SB, [128, 128], F32), "onn": (SB, [128, 128], F32), "idb": (SB, [128, 128], BF),
+    "idn": (SB, [128, 128], BF), "idf": (SB, [128, 128], F32), "idg": (SB, [128, 128], F32), "bdf": (SB, [128, 128], F32),
+    "idp": (SB, [128, 128], BF), "idm": (SB, [128, 128], BF), "id4": (SB, [128, 128], BF), "bd": (SB, [128, 128], BF),
+    "nbk": (SB, [128, 128], BF), "low": (SB, [128, 128], BF), "tr": (SB, [128, 128], BF), "trn": (SB, [128, 128], BF),
+    "bw": (SB, [128, 128], BF), "bn": (SB, [128, 128], BF), "cst0": (SB, [128, 128], BF), "cst1": (SB, [128, 128], BF),
+    "zz": (SB, [128, 144], BF), "zv": (SB, [128, 144], BF),
     "on": (SB, [128, I], F32), "og": (SB, [128, I], F32), "ol": (SB, [128, I], BF),
 }
 for _t in range(RO):
-    for _u in range(2):
-        SCRATCH["gs%d%d" % (_t, _u)] = (SB, [128, M], BF)
-        SCRATCH["h%d%d" % (_t, _u)] = (SB, [128, M], BF)
-PSUM = ("pa0", "pa1", "pv", "pe0", "pe1", "pf0", "pf1", "pk")
+    SCRATCH["gs%d" % _t] = (SB, [128, I], BF)
+    SCRATCH["h%d" % _t] = (SB, [128, I], BF)
+PSUM = ("pa0", "pa1", "pe0", "pe1", "pf0", "pf1", "pq0", "pq1")
 for _b in PSUM:
     SCRATCH[_b] = ("psum", [128, 512], F32)
 
 SEMAPHORES = ["cv", "ca", "ct", "cg", "sent", "d_x", "d_lim", "d_grd", "d_nam", "d_rel", "d_up", "d_on", "d_og", "d_ol", "d_m0", "d_m1"]
 SEMAPHORES += ["arr%d%d" % (_t, _u) for _t in range(RO) for _u in range(2)]
+
+
+def arrange(calls, ahead):
+    n = len(calls)
+    before, after, wrote, seen = [{} for _ in calls], [{} for _ in calls], {}, {}
+    for i, (q, reads, writes, busy, late, size) in enumerate(calls):
+        for j in [wrote[k] for k in reads + writes if k in wrote] + [j for k in writes for j in seen.get(k, [])]:
+            before[i][j] = after[j][i] = 0.0 if q == calls[j][0] == "t" else WAKE
+        for k in reads:
+            seen.setdefault(k, []).append(i)
+        for k in writes:
+            wrote[k], seen[k] = i, []
+    banks = [sorted(set(k for k in c[1] + c[2] if k in PSUM)) for c in calls]
+
+    def room(taken, at, length, gap, q):
+        for a, b, o in taken:
+            if a - gap >= at + length:
+                break
+            if o != q and at < b + gap:
+                at = b + gap
+        return at
+
+    def lay(rank, back):
+        need, give = (after, before) if back else (before, after)
+        taken, start, end = {}, [0.0] * n, [0.0] * n
+        left = [len(b) for b in need]
+        ready = [i for i in range(n) if not left[i]]
+        while ready:
+            i = min(ready, key=lambda j: rank[j])
+            ready.remove(i)
+            q, busy, late, size = calls[i][0], calls[i][3], calls[i][4], calls[i][5]
+            at, was = max([0.0] + [end[j] + w for j, w in need[i].items()]) + (late + size / RATE if back else 0.0), -1.0
+            while at != was:
+                was = at
+                at = room(taken.get(q, []), at, busy, 0.0, None)
+                for k in banks[i]:
+                    at = room(taken.get(k, []), at, busy, WAKE, q)
+            start[i], end[i] = at, at + busy
+            if not back:
+                end[i] += late
+            if size and not back:
+                end[i] = room(taken.get("dma", []), end[i], size / RATE, 0.0, None) + size / RATE
+                taken["dma"] = sorted(taken.get("dma", []) + [(end[i] - size / RATE, end[i], q)])
+            for k in [q] + banks[i]:
+                taken[k] = sorted(taken.get(k, []) + [(at, at + busy, q)])
+            for j in give[i]:
+                left[j] -= 1
+                if not left[j]:
+                    ready.append(j)
+        return start, end
+
+    def better(rank):
+        start, end = lay(rank, False)
+        plain = max(end), start
+        start, end = lay([-e for e in end], True)
+        start, end = lay([i - 1e9 if i < ahead else -end[i] for i in range(n)], False)
+        return min(plain, (max(end), start))
+
+    best, seed = better(list(range(n))), SEED
+    for k in range(PASSES):
+        rank = []
+        for i in range(n):
+            seed = (seed * 1103515245 + 12345) % 2 ** 31
+            near = abs(best[1][i] - best[0] * (k * 0.618 % 1)) < SPAN
+            rank.append(i - 1e9 if i < ahead else best[1][i] + near * SHAKE * seed / 2 ** 31)
+        best = min(best, better(rank))
+    return sorted(range(n), key=lambda i: (best[1][i], i))
+
+
+PLAN = []
 
 
 def rank_program(g, core, T, topo):
@@ -102,55 +192,80 @@ def rank_program(g, core, T, topo):
             wrote[k] = rec
             seen[k] = {}
 
-    def op(q, reads, writes, fn):
-        waits(q, reads, writes)
-        ins = fn(queue[q])
-        count[q] += 1
-        ins.then_inc(T.sem["c" + q], 1)
-        snap = dict(known[q])
-        snap["c" + q] = count[q]
-        note((q, "c" + q, count[q], snap), reads, writes)
+    calls = []
 
-    def load(q, sem, out, in_, reads, writes, **kw):
-        waits(q, reads, writes)
-        queue[q].dma_start(out, in_, **kw).then_inc(T.sem[sem], 16)
-        dcount[sem] = dcount.get(sem, 0) + 16
-        snap = dict(known[q])
-        snap[sem] = dcount[sem]
-        note(("dma" + sem, sem, dcount[sem], snap), reads, writes)
+    def op(q, reads, writes, fn, cycles, also=()):
+        writes = writes if isinstance(writes, list) else [writes]
 
-    def copy(out, okey, in_, ikeys):
-        op("v", ikeys, [okey], lambda e: e.tensor_copy(out, in_))
+        def issue():
+            waits(q, reads + list(also), writes)
+            ins = fn(queue[q])
+            count[q] += 1
+            ins.then_inc(T.sem["c" + q], 1)
+            snap = dict(known[q])
+            snap["c" + q] = count[q]
+            note((q, "c" + q, count[q], snap), reads + list(also), writes)
+        calls.append((q, reads, writes, FIXED[q] + max(LEAST[q], cycles) * CYCLE[q], 0.0, 0, issue))
 
-    def ts(out, okey, in_, ikeys, s1, s2, op0, op1=None):
+    def load(q, sem, out, in_, reads, writes, size, whole=(), **kw):
+        def issue():
+            waits(q, reads, writes)
+            queue[q].dma_start(out, in_, **kw).then_inc(T.sem[sem], 16)
+            dcount[sem] = dcount.get(sem, 0) + 16
+            snap = dict(known[q])
+            snap[sem] = dcount[sem]
+            note(("dma" + sem, sem, dcount[sem], snap), reads, writes)
+            if whole and dcount[sem] % (16 * len(whole)) == 0:
+                for k in whole:
+                    wrote[k] = wrote[writes[0]]
+        calls.append((q, reads, writes, ISSUE[q], LAND, size, issue))
+
+    def copy(out, okey, in_, ikeys, per=1.0):
+        op("v", ikeys, okey, lambda e: e.tensor_copy(out, in_), per * out.shape[1])
+
+    def ts(out, okey, in_, ikeys, s1, s2, op0, op1=None, per=1.0):
         if op1 is None:
-            op("v", ikeys, [okey], lambda e: e.tensor_scalar(out, in_, s1, None, op0))
+            op("v", ikeys, okey, lambda e: e.tensor_scalar(out, in_, s1, None, op0), per * out.shape[1])
         else:
-            op("v", ikeys, [okey], lambda e: e.tensor_scalar(out, in_, s1, s2, op0, op1))
+            op("v", ikeys, okey, lambda e: e.tensor_scalar(out, in_, s1, s2, op0, op1), per * out.shape[1])
 
-    def tt(out, okey, a, b, ikeys, o):
-        op("v", ikeys, [okey], lambda e: e.tensor_tensor(out, a, b, o))
+    def tt(out, okey, a, b, ikeys, o, per=1.0):
+        op("v", ikeys, okey, lambda e: e.tensor_tensor(out, a, b, o), per * b.shape[1])
 
-    def act(out, okey, in_, ikeys, f=F.Copy, **kw):
-        op("a", ikeys, okey if isinstance(okey, list) else [okey], lambda e: e.activation(out, in_, f, **kw))
+    def act(out, okey, in_, ikeys, f=F.Copy, per=1.0, more=0, **kw):
+        op("a", ikeys, okey, lambda e: e.activation(out, in_, f, **kw), per * out.shape[1] + more)
 
-    def mm(bank, a, lkey, rhs, rkey, n, start, stop, lhs=None):
-        op("t", [lkey, rkey], [bank], lambda e: e.matmul(T[bank][:, a:a + n], T[lkey][:] if lhs is None else lhs, rhs, start, stop))
+    def mm(bank, a, lkey, rhs, rkeys, n, start, stop, lhs=None):
+        op("t", [lkey] + rkeys, bank, lambda e: e.matmul(T[bank][:, a:a + n], T[lkey][:] if lhs is None else lhs, rhs, start, stop),
+           max(64, n) * (4 if SCRATCH[lkey][2] == F32 else 1))
 
     def memset(ap, key, val):
-        op("v", [], [key], lambda e: e.memset(ap, val))
+        op("v", [], key, lambda e: e.memset(ap, val), ap.shape[1])
 
-    def select(name, src, pattern, cmp, fill, base, mult):
-        op("g", [src], [name], lambda e: e.affine_select(T[name][:], T[src][:], pattern, cmp, fill, base, mult))
+    def fill(name, val):
+        op("v", [], name, lambda e: e.memset(T[name][:], val), T[name].shape[1] / 2)
 
-    def iota(name, pattern, mult, base=0):
-        op("g", [], [name], lambda e: e.iota(T[name][:], pattern, base, mult, allow_small_or_imprecise_dtypes=True))
+    def times(name, src, by):
+        keys_, by = ([src, by], T[by][:]) if isinstance(by, str) else ([src], by)
+        if FILL == "a" or SCRATCH[name][2] == F32:
+            act(T[name][:], name, T[src][:], keys_, scale=by)
+        else:
+            ts(T[name][:], name, T[src][:], keys_, by, None, A.mult, per=0.5)
 
-    H = [16 * n for n in NC]
-    O = [0, H[0]]
+    def select(name, src, pattern, cmp, fill_, base, mult):
+        op("g", [src], name, lambda e: e.affine_select(T[name][:], T[src][:], pattern, cmp, fill_, base, mult), 2 * T[name].shape[1])
+
+    def iota(name, pattern, mult, base=0, okeys=None):
+        op("g", [], okeys or name, lambda e: e.iota(T[name][:], pattern, base, mult, allow_small_or_imprecise_dtypes=True), 2 * T[name].shape[1])
+
+    H = [16 * n for n in NC] + [I]
+    O = [0, H[0], 0]
     wide = [max(b - a for a, b in zip([0] + JUDGE[u], JUDGE[u])) for u in range(2)]
     xw = T.x[:, 16:16 + WX]
-    pns, pa, pe, pf = ["pn0", "pn1"], ["pa0", "pa1"], ["pe0", "pe1"], ["pf0", "pf1"]
+    vs, xs, pa, pe, pf, pq = ["v0", "v1"], ["x0", "x1"], ["pa0", "pa1"], ["pe0", "pe1"], ["pf0", "pf1"], ["pq0", "pq1"]
+
+    def keys(name, u):
+        return [name + "0", name + "1"] if u == 2 else [name + str(u)]
 
     def part(name, u, at=0):
         return T[name][:, at + O[u]:at + O[u] + H[u]]
@@ -158,8 +273,11 @@ def rank_program(g, core, T, topo):
     def cols(name, u, at=0):
         return T[name][:, at:at + H[u]]
 
+    def xp(u):
+        return T.x[:, 16 + 8 * O[u]:16 + 8 * (O[u] + H[u])]
+
     def own(u):
-        return part("pv", u, 272)
+        return part("v", u, 16)
 
     def lanes(name, u, a, b):
         return T[name][:, 16 * O[u] + H[u] * a:16 * O[u] + H[u] * b]
@@ -171,116 +289,94 @@ def rank_program(g, core, T, topo):
         return T[name][:, O[u] + 15:O[u] + H[u]:16]
 
     def listed(name, u):
-        return T[name][:, O[u] // 16:O[u] // 16 + NC[u]]
+        return T[name][:, O[u] // 16:(O[u] + H[u]) // 16]
 
-    def turned(src, u):
-        a = (2 * H[0] + 32) * u
-        return T[src][:, a:a + 2 * H[u] + 32].indirect(listed("sel", u))
+    def pm(bank, lkey, name, u, start, stop):
+        mm(bank[u], 0, lkey, own(u) if name == "v" else part(name, u), [name + str(u)], H[u], start, stop)
 
-    def turn(dst, src, keys, at, u):
+    def cm(bank, lkey, name, u, start, stop):
+        mm(bank[u], 0, lkey, cols(name, u), [name], H[u], start, stop)
+
+    def turn(u):
         a, n = (2 * H[0] + 32) * u, H[u]
-        op("v", keys, [dst + "%d0" % u], lambda q: q.transpose(T[dst][:, a:a + n], part(src, u, at + 16)))
-        op("v", keys, [dst + "%d1" % u], lambda q: q.transpose(T[dst][:, a + n:a + 2 * n + 32], T[src][:, at + O[u]:at + O[u] + n + 32]))
+        op("v", [vs[u], "pada", "padb"], "tp%d0" % u, lambda q: q.transpose(T.tp[:, a:a + n], own(u)), n)
+        op("v", [vs[u], "pada", "padb"], "tp%d1" % u, lambda q: q.transpose(T.tp[:, a + n:a + 2 * n + 32], T.v[:, O[u]:O[u] + n + 32]), n + 32,
+           [vs[1 - u]])
 
-    def listing(out, dst, u):
-        copy(part(out, u), out + str(u), turned(dst, u), [dst + "%d0" % u, dst + "%d1" % u, "sel%d" % u])
+    def listing(u):
+        a = (2 * H[0] + 32) * u
+        copy(part("ti", u), "ti%d" % u, T.tp[:, a:a + 2 * H[u] + 32].indirect(listed("sel", u)), ["tp%d0" % u, "tp%d1" % u, "sel%d" % u], GATHER)
 
     def diagonal(bank, out, u):
-        op("v", [bank, "rs"], [out + str(u)], lambda e: e.tensor_tensor_scan(part(out, u), cols("rs", u), cols(bank, u), 0.0, A.mult, A.max))
+        op("v", [bank, "rs"], out + str(u), lambda e: e.tensor_tensor_scan(part(out, u), cols("rs", u), cols(bank, u), 0.0, A.mult, A.max), H[u])
 
-    fetched = [0]
-    firsts = len([c for c in FETCH if c[0] == 0])
+    def fetch(j):
+        u, a, b = FETCH[j]
+        act(lanes("nb", u, a, b), "nb%d" % j, T.rel0[:, 0:W].indirect(entries("lu", u, a, b)), ["rel0", "lu%d" % u], per=GATHER)
+        for k in range(a, b):
+            c = 16 * O[u] + H[u] * k
+            load("s", "d_m%d" % u, T.mo[k::16, O[u]:O[u] + H[u]], T.nb[k::16, c:c + H[u]], ["nb%d" % j], ["mo%d_%d" % (u, k)], 32 * H[u],
+                 ["mo%d_%d" % (u, c) for c in range(16)])
 
-    def fetch(n):
-        for j in range(fetched[0], min(fetched[0] + n, len(FETCH))):
-            u, a, b = FETCH[j]
-            act(lanes("nb", u, a, b), "nb%d" % j, T.rel0[:, 0:W].indirect(entries("lu", u, a, b)), ["rel0", "lu%d" % u],
-                scale=1.0 / 2048, bias=-HALF)
-            for k in range(a, b):
-                c = 16 * O[u] + H[u] * k
-                load("s", "d_m%d" % u, T.mo[k::16, O[u]:O[u] + H[u]], T.nb[k::16, c:c + H[u]], ["nb%d" % j], ["mo%d_%d" % (u, k)])
-            if b == 16:
-                for k in range(16):
-                    wrote["mo%d_%d" % (u, k)] = wrote["mo%d_15" % u]
-            fetched[0] = j + 1
+    def double(u, n, m):
+        a, ks = 768 * u, ["gj%d%d" % (u, c) for c in range(wide[u])]
+        op("g", ks[:m], ks[n:n + m], lambda e: e.affine_select(T.gj[:, a + H[u] * n:a + H[u] * (n + m)], T.gj[:, a:a + H[u] * m],
+                                                               [[0, H[u] * m]], A.is_ge, 0.0, 0, 0), 2 * H[u] * m)
 
-    def limits(src, key, up, u):
-        a, own_, keys = 768 * u, wide[u] if key == "lim0" else OWN[u], ["gj%d%d" % (u, c) for c in range(wide[u])]
-        for c in range(own_):
-            act(cols("gj", u, a + H[u] * c), keys[c], src, [key], bias=up - 641.5)
-        n = wide[u] - own_
-        if n:
-            op("g", keys[:n], keys[own_:], lambda e: e.affine_select(T.gj[:, a + H[u] * own_:a + H[u] * wide[u]], T.gj[:, a:a + H[u] * n],
-                                                                     [[0, H[u] * n]], A.is_ge, 0.0, 0, 0))
+    def limits(name, key, n, u, late=0):
+        for c in range(0 if late else n):
+            act(cols("gj", u, 768 * u + H[u] * c), "gj%d%d" % (u, c), part(name, u), [key], bias=-510.0)
+        while late and n < wide[u]:
+            double(u, n, min(n, wide[u] - n))
+            n += min(n, wide[u] - n)
 
-    def masks(bank, u):
-        mm(bank, 0, "idb", cols("mk", u), "mk", H[u], True, False)
+    def clip(u):
+        if KV[u] == "v":
+            ts(part("kv", u), "kv%d" % u, cols(pe[u], u), [pe[u]], -BIG, 0.0, A.add, A.max)
+        else:
+            act(part("kv", u), "kv%d" % u, cols(pe[u], u), [pe[u]], F.Relu, bias=-BIG)
 
-    def guards(u):
-        mm(pe[u], 0, "idb", part("k16", u), "k16%d" % u, H[u], True, False)
+    def decided(u):
+        pm(pq, "id4", "und", u, True, False)
+        pm(pq, "id4", "dead", u, False, False)
 
-    def names(u):
-        mm(pf[u], 0, "id0", T.ch[:, M - H[u]:M + H[u]], "ch", 2 * H[u], True, False)
-        mm(pf[u], 0, "idl", part("l16", u), "l16%d" % u, H[u], False, False)
-        mm(pf[u], H[u], "id0", part("l16", u), "l16%d" % u, H[u], False, False)
-
-    def counted(out, key, u):
-        ts(out, key + str(u), cols(pa[u], u), [pa[u], "thr"], T.thr[:], 4100.5, A.add, A.max)
-
-    def und(u):
-        tt(part("und", u), "und%d" % u, part("pv", u), part("b", u), ["a%d" % u, "b%d" % u], A.is_lt)
-        mm(pe[u], 0, "tr", part("und", u), "und%d" % u, H[u], False, True)
-        mm(pf[u], 0, "tr", part("und", u), "und%d" % u, H[u], False, False)
-        mm(pf[u], H[u], "nbk", part("und", u), "und%d" % u, H[u], False, True)
-
-    def kh(u):
-        ts(part("kh", u), "kh%d" % u, cols(pe[u], u), [pe[u]], 16.0 - 4096, 0.0, A.add, A.max)
-        mm("pk", 0, "bd", part("kh", u), "kh%d" % u, H[u], False, True)
-
-    def lh(u):
-        c = 2 * O[u]
-        ts(T.lh[:, c:c + 2 * H[u]], "lh%d" % u, T[pf[u]][:, 0:2 * H[u]], [pf[u]], 1024.5 - 4096, 0.0, A.add, A.max)
-        mm(pe[u], 0, "bd", cols("lh", u, c), "lh%d" % u, H[u], False, False)
-        mm(pe[u], 0, "bd", cols("lh", u, c + H[u]), "lh%d" % u, H[u], False, True)
-
-    def alive(u):
-        mm(pa[u], 0, "idb", cols("cc", u), "cc", H[u], True, False)
-        mm(pa[u], 0, "idx", part("b", u), "b%d" % u, H[u], False, True)
-
-    def implied(u):
-        mm(pa[u], M, "idx", part("und", u), "und%d" % u, H[u], True, False)
-        mm(pa[u], M, "idx", part("dead", u), "dead%d" % u, H[u], False, True)
+    def fetched(u):
+        mm(pq[u], 0, "idf", part("mo", u), ["mo%d_%d" % (u, k) for k in range(16)], H[u], False, True)
 
     def old(u):
-        mm(pa[u], 2 * M, "idb", cols("cc", u, M), "cc", H[u], True, False)
-        mm(pa[u], 2 * M, "idb", part("k16", u), "k16%d" % u, H[u], False, False)
-        mm(pa[u], 2 * M, "idx", part("und", u), "und%d" % u, H[u], False, False)
-        mm(pa[u], 2 * M, "idb", part("l16", u), "l16%d" % u, H[u], False, True)
+        cm(pa, "idb", "cc", u, True, False)
+        pm(pa, "idp", "und", u, False, False)
+        pm(pa, "idf", "v", u, False, True)
 
     def deaths():
-        mm("pk", 0, "onef", T.cnt[:, 0:1], "cnt0", 1, True, False)
-        mm("pk", 0, "onef", T.cnt[:, 1:2], "cnt1", 1, False, True)
+        for n, (lkey, rhs, key) in enumerate((("onp", T.cnt[:, 0:1], "cnt0"), ("onp", T.cnt[:, 1:2], "cnt1"), ("idb", T.kc[:, 0:1], "kc0"),
+                                              ("idb", T.kc[:, 1:2], "kc1"), ("idn", T.kc[:, 1:2], "kc1"),
+                                              ("onn", T.cnt[:, 0:1], "cnt0"), ("onn", T.cnt[:, 1:2], "cnt1"))):
+            mm(pe[0], 2 * M, lkey, rhs, [key], 1, n == 0, n == 6)
+
+    def ready(u):
+        cm(pf, "idb", "c8", u, True, False)
+        mm(pf[u], 0, "idb", part("mq", u), ["mq"], H[u], False, False)
 
     def limits_out(u):
         tt(part("ol", u), "ol%d" % u, part("gm", u), cols(pf[u], u), ["gm%d" % u, pf[u]], A.min)
-        load("a", "d_ol", part("yl", u), part("ol", u), ["ol%d" % u], ["yl%d" % u])
+        load("a", "d_ol", part("yl", u), part("ol", u), ["ol%d" % u], ["yl%d" % u], 256 * H[u])
 
-    load("s", "d_grd", T.grd0[:, 16:16 + I], T.grd[:], [], ["grd0"])
-    load("a", "d_lim", T.lim0[:], T.lim[:], [], ["lim0"])
-    load("s", "d_x", T.x0[:, 16:16 + WX], T.xc[:], [], ["x0"])
-    load("s", "d_nam", T.nam0[:, 16:16 + I], T.nam[:], [], ["nam0"])
-    load("s", "d_rel", T.rel0[:], T.rel[:], [], ["rel0"])
+    inputs = {"g": ("s", "d_grd", part("grd0", 2, 16), T.grd[:], [], ["grd0"], 512 * I), "n": ("s", "d_nam", part("nam0", 2, 16), T.nam[:], [], ["nam0"], 512 * I),
+              "l": ("a", "d_lim", T.lim0[:], T.lim[:], [], ["lim0"], 256 * I), "x": ("s", "d_x", T.x0[:], T.xc[:], [], ["xc"], 256 * WX),
+              "r": ("s", "d_rel", T.rel0[:], T.rel[:], [], ["rel0"], 512 * W)}
+    for s in LOADS:
+        load(*inputs[s])
+    ahead = len(calls)
 
     iota("ip", [[0, 1]], 1)
     iota("ff", [[16, 14]], 1)
-    iota("t16", [[0, M // 16], [1, 16]], 0)
     memset(T.ones[:], "ones", 1.0)
+    iota("t16", [[0, I // 16], [1, 16]], 0)
     select("bd", "ones", [[-16, 8], [0, 16]], A.is_ge, 0.0, 0, 1)
     select("bd", "bd", [[16, 8], [0, 16]], A.is_ge, 0.0, 15, -1)
     select("idb", "ones", [[-1, 128]], A.is_equal, 0.0, 0, 1)
-    for name in ("grd0", "nam0"):
-        memset(T[name][:, 0:16], name + "a", 0)
-        memset(T[name][:, 16 + I:256], name + "b", 0)
+    memset(T.v[:, 0:16], "pada", 0.0)
     ts(T.c1[:], "c1", T.ip[:], ["ip"], 112, None, A.bitwise_and)
     ts(T.c2[:], "c2", T.ip[:], ["ip"], 4, None, A.arith_shift_right)
     ts(T.c5[:], "c5", T.ip[:], ["ip"], 15, None, A.bitwise_and)
@@ -289,77 +385,85 @@ def rank_program(g, core, T, topo):
     ts(T.c6[:], "c6", T.ip[:], ["ip"], 3, None, A.bitwise_and)
     ts(T.f[:], "f", T.ff[:], ["ff", "g16"], T.g16[:], None, A.subtract)
     ts(T.c4[:], "c4", T.c3[:], ["c3"], 1, None, A.bitwise_and)
-    memset(T.zz[:], "zz", 0.0)
+    memset(T.v[:, 16 + I:256], "padb", 0.0)
     for u in range(2):
         ts(listed("fk", u), "fk%d" % u, T.f[:, 0:NC[u]], ["f"], 1.0 / NC[u], (1.0 / NC[u] - 1) / 2, A.mult, A.add)
         ts(T.par[:, u:u + 1], "par%d" % u, T.c4[:], ["c4"], H[u] + 16.0, None, A.mult)
     ts(T.a2[:], "a2", T.f[:], ["f"], 16.0, None, A.mult)
     for u in range(2):
         ts(listed("a1", u), "a1%d" % u, listed("fk", u), ["fk%d" % u, "par%d" % u], 1.0 - H[u], T.par[:, u:u + 1], A.mult, A.add)
-    turn("tg", "grd0", ["grd0", "grd0a", "grd0b"], 0, 0)
+    copy(T.rc[:], "rc", T.c5[:], ["c5"])
     for u in range(2):
         tt(listed("a3", u), "a3%d" % u, listed("a1", u), T.a2[:, 0:NC[u]], ["a1%d" % u, "a2"], A.add)
-    copy(T.rc[:], "rc", T.c5[:], ["c5"])
-    ts(T.kz[:], "kz", T.c5[:], ["c5"], 0.5, 2048.0, A.is_lt, A.mult)
+    ts(T.wc[:], "wc", T.c6[:], ["c6"], 2.0, 1.0, A.mult, A.add)
+    ts(T.wd[:], "wd", T.c5[:], ["c5"], 0.5, 3.0 / 128, A.is_lt, A.mult)
     for u in range(2):
         copy(listed("sel", u), "sel%d" % u, listed("a3", u), ["a3%d" % u])
-    memset(T.ch[:, 0:M], "ch0", 0.0)
-    memset(T.ch[:, M:2 * M], "ch", 2.0)
-    listing("ku", "tg", 0)
-    ts(T.zz[:, 15:143:16], "zz", T.bd[:, 0:128:16], ["bd"], -33.0, None, A.mult)
-    ts(T.mk[:], "mk", T.t16[:], ["t16", "rc"], T.rc[:], -16384.0, A.not_equal, A.mult)
-    copy(T.k16[:], "k160", T.grd0[:, 16:16 + I], ["grd0"])
-    memset(T.thr[:], "thr", 192 + 4100.5)
-    memset(T.x0[:, 0:16], "x0z", 0.0)
-    for a, key in ((256, "pn0"), (272 + H[0], "pn1"), (496, "pad")):
-        memset(T.pv[:, a:a + 16], key, 0.0)
-    limits(part("lim0", 0), "lim0", 0.0, 0)
-    act(T.rs[:], "rs", T.t16[:], ["t16"], F.Sigmoid, scale=256.0, bias=-128.0)
-    act(T.nbk[:], "nbk", T.bd[:], ["bd"], scale=-4096.0)
-    act(T.id0[:], "id0", T.idb[:], ["idb", "kz"], scale=T.kz[:])
-    act(T.idl[:], "idl", T.idb[:], ["idb"], scale=2048.0)
-    iota("t8", [[8, I]], 0)
-    select("low", "nbk", [[1, 128]], A.is_gt, 0.0, 0, -1)
-    select("tr", "low", [[-1, 128]], A.not_equal, 4096.0, 0, 1)
-    iota("x", [[0, 16 + WX]], 0, int(UP))
-    wrote["xz"] = wrote["x"]
-    load("g", "d_up", xw, T.xc[:], [], ["x"], accum_op=A.add)
 
-    def first(s):
-        if s == "j00":
-            turn("tn", "nam0", ["nam0", "nam0a", "nam0b"], 0, 0)
-            ts(T.l16[:], "l160", T.nam0[:, 16:16 + I], ["nam0"], 1.0 / 2048, -HALF, A.mult, A.add)
-            wrote["k161"], wrote["l161"] = wrote["k160"], wrote["l160"]
-            listing("lu", "tn", 0)
-        if s == "j01":
-            turn("tg", "grd0", ["grd0", "grd0a", "grd0b"], 0, 1)
-            turn("tn", "nam0", ["nam0", "nam0a", "nam0b"], 0, 1)
-        if s == "j02":
-            listing("ku", "tg", 1)
-            listing("lu", "tn", 1)
-        if s == "w00":
-            limits(part("lim0", 1), "lim0", 0.0, 1)
-        if s == "w01":
-            act(T.idx[:], "idx", T.idb[:], ["idb"], scale=4096.0)
-            for c, v in enumerate((-2.0 ** 24, -4096.0)):
-                act(T.cc[:, M * c:M * c + M], "cc%d" % c, T.t16[:], ["t16"], scale=0.0, bias=v)
-            wrote["cc"] = wrote["cc1"]
-        if s in AMONG0:
-            fetch(1)
-        if s == "u0":
-            ts(T.wc[:], "wc", T.c6[:], ["c6"], 2.0, 1.0, A.mult, A.add)
-            ts(T.bm0[:], "bm0", T.f[:], ["f"], 8.0, -1028.5, A.mult, A.add)
-            ts(T.bm[:], "bm", T.f[:], ["f"], 8.0, 64 * UP - 1028.5, A.mult, A.add)
-        if s == "F":
-            act(T.onef[:], "onef", T.ones[:], ["ones"])
-            act(T.bw[:], "bw", T.bd[:], ["bd", "wc"], scale=T.wc[:])
-            act(T.idn[:], "idn", T.idb[:], ["idb"], scale=-1.0)
-            act(T.half[:], "half", T.t8[:], ["t8"], scale=0.0, bias=0.5)
+    def sums():
+        for name, by in (("zz", -17.0), ("zv", -4.0))[:1 + (min(VL) < 16)]:
+            fill(name, 0.0)
+            ts(T[name][:, 15:143:16], name, T.bd[:, 0:128:16], ["bd"], by, None, A.mult)
 
-    for t in range(RO):
+    def offsets():
+        fill("one", 1.0)
+        for u in range(1 + (VL[0] != VL[1])):
+            name = "cst%d" % u
+            fill(name, 0.0)
+            for p, val in ((0, TOP), (32, 4.5)):
+                ts(T[name][p:p + 1, :], name + str(p), T[name][p:p + 1, :], [name], val, None, A.add, per=0.5)
+            for p, val in ((64, 32768.0), (96, -16.0))[:2 * (VL[u] < 16)]:
+                ts(T[name][p:p + 1, :], name + str(p), T.t16[p:p + 1, 0:128], ["t16", name], VL[u] - 0.5, val, A.is_ge, A.mult, 0.5)
+
+    cst = ["cst0", "cst1" if VL[0] != VL[1] else "cst0"]
+
+    def plain(name, src, u):
+        a, n = (2 * H[0] + 32) * u, H[u]
+        op("v", [src, src + "a", src + "b"], name + "t0%d" % u, lambda q: q.transpose(T[src + "t"][:, a:a + n], part(src, u, 16)), n)
+        op("v", [src, src + "a", src + "b"], name + "t1%d" % u,
+           lambda q: q.transpose(T[src + "t"][:, a + n:a + 2 * n + 32], T[src][:, O[u]:O[u] + n + 32]), n + 32)
+        copy(part(name, u), name + str(u), T[src + "t"][:, a:a + 2 * n + 32].indirect(listed("sel", u)),
+             [name + "t0%d" % u, name + "t1%d" % u, "sel%d" % u], GATHER)
+
+    def raised():
+        if FILLX == "g":
+            iota("x", [[0, 16 + WX]], 0, int(UP), xs + ["xz"])
+        else:
+            op("v", [], xs + ["xz"], lambda e: e.memset(T.x[:], UP), (16 + WX) / 2)
+        load("g", "d_up", xw, T.xc[:], [], xs, 512 * WX, accum_op=A.add)
+
+    constants = {
+        "zz": sums, "cst": offsets, "xg": raised,
+        "rs": lambda: act(T.rs[:], "rs", T.t16[:], ["t16"], F.Sigmoid, more=1600, scale=256.0, bias=-128.0),
+        "idf": lambda: times("idf", "idb", 1.0), "idg": lambda: times("idg", "idb", -1.0), "bdf": lambda: times("bdf", "bd", 1.0),
+        "nbk": lambda: times("nbk", "bd", -2 * BIG), "trn": lambda: times("trn", "tr", -1.0),
+        "tr": lambda: (select("low", "nbk", [[1, 128]], A.is_gt, 0.0, 0, -1), select("tr", "low", [[-1, 128]], A.not_equal, 2 * BIG, 0, 1)),
+        "mk": lambda: (ts(T.mk[:], "mk", T.t16[:], ["t16", "rc"], T.rc[:], -8 * BIG, A.not_equal, A.mult), memset(T.tb[:], "tb", 32 * (TOP - 88)),
+                       memset(T.thr[:], "thr", TOP - 96)),
+        "ids": lambda: [times(name, "idb", by) for name, by in (("id4", -2 * BIG), ("idp", BIG), ("idn", -1.0))],
+        "cc": lambda: (fill("cc", -BIG), fill("two", 2.0), fill("half", 0.5), times("onp", "ones", 512.0), times("onn", "ones", -512.0)),
+        "bw": lambda: (tt(T.wn[:], "wn", T.wd[:], T.wc[:], ["wd", "wc"], A.subtract), times("bw", "bd", "wc"), times("bn", "bd", "wn")),
+        "mq": lambda: (iota("t8", [[8, I]], 0), tt(T.mq[:], "mq", T.mk[:], T.t8[:], ["mk", "t8"], A.add, 2.0)),
+        "c8": lambda: (fill("c8", EIGHT), memset(T.kc[:, 0:1], "kc0", -256.0), memset(T.kc[:, 1:2], "kc1", KILO)),
+        "va": lambda: ts(T.md[:], keys("md", 2), part("grd0", 2, 16), ["grd0"], 2048.0, None, A.mult),
+        "vb": lambda: tt(own(2), vs, T.md[:], part("nam0", 2, 16), ["md0", "nam0"], A.add, 2.0),
+        "pads": lambda: [memset(T[name][:, a:a + 16], name + key, 0) for name in ("grd0", "nam0") for a, key in ((0, "a"), (16 + I, "b"))],
+        "ka": lambda: plain("ku", "grd0", 0), "kb": lambda: plain("ku", "grd0", 1),
+        "na": lambda: (plain("lu", "nam0", 0), copy(entries("ti", 0, 0, 1), "ti0", entries("lu", 0, 0, 1), ["lu0"])),
+        "nb": lambda: (plain("lu", "nam0", 1), copy(entries("ti", 1, 0, 1), "ti1", entries("lu", 1, 0, 1), ["lu1"])),
+        "lima": lambda: limits("lim0", "lim0", wide[0], 0), "limb": lambda: limits("lim0", "lim0", wide[1], 1),
+        "gr2": lambda: act(T.gr[:], keys("gr", 2), T.lim0[:], ["lim0"], bias=UP),
+        "xz": lambda: memset(T.x[:, 0:16], "xz", UP),
+        "xa": lambda: act(xp(0), xs[0], T.x0[:, 0:8 * H[0]], ["xc"], bias=UP),
+        "xb": lambda: act(xp(1), xs[1], T.x0[:, 8 * H[0]:WX], ["xc"], bias=UP),
+        "C": deaths, "tb": lambda: act(T.tb[:], "tb", T[pe[0]][:, 2 * M:2 * M + 1], [pe[0]], bias=32 * (TOP - 88)),
+        "thr": lambda: act(T.thr[:], "thr", T[pe[0]][:, 2 * M:2 * M + 1], [pe[0]], scale=1.0 / 32, bias=TOP - 96),
+    }
+
+    def steps(t):
         last = t == RO - 1
-        x, gr, up, bm = ("x0", "lim0", UP, "bm0") if t == 0 else ("x", "gr", 0.0, "bm")
-        h, gs = ["h%d%d" % (t, u) for u in range(2)], ["gs%d%d" % (t, u) for u in range(2)]
+        xj, xk = (T.x0[:], ["xc"]) if t == 0 else (xw, xs)
+        h, gs = "h%d" % t, "gs%d" % t
         done = {"j0": 0, "j1": 0, "w0": 0, "w1": 0}
 
         def piece(s, u):
@@ -369,111 +473,120 @@ def rank_program(g, core, T, topo):
 
         def judge(u):
             a, b, key = piece("j", u)
-            tt(lanes("u", u, a, b), "u" + key, T[x][:, 16:16 + WX].indirect(entries("ku", u, a, b)), T.gj[:, 768 * u:768 * u + H[u] * (b - a)],
-               [x, "ku%d" % u] + ["gj%d%d" % (u, c) for c in range(b - a)], A.subtract)
-            if t == 0:
-                first("j" + key)
+            tt(lanes("u", u, a, b), "u" + key, xj.indirect(entries("ku", u, a, b)), T.gj[:, 768 * u:768 * u + H[u] * (b - a)],
+               xk + ["ku%d" % u] + ["gj%d%d" % (u, c) for c in range(b - a)], A.subtract, GATHER)
 
         def mark(u):
             a, b, key = piece("w", u)
-            act(lanes("w", u, a, b), "w" + key, lanes("u", u, a, b), ["u" + key], F.Sigmoid, scale=4.0, bias=-4.0 * 644 - math.log(32.0))
+            if a < VL[u]:
+                w, z = "w", "zz"
+                act(lanes(w, u, a, b), "w" + key, lanes("u", u, a, b), ["u" + key, "rs"], F.Sigmoid, scale=8.0, bias=-8.0 * 512 - math.log(16.0))
+            else:
+                w, z = "wv", "zv"
+                ts(lanes(w, u, a, b), "w" + key, lanes("u", u, a, b), ["u" + key], 511.75, 516.0, A.max, A.min, 0.5)
             for k in range(a, b):
-                mm(pa[u], 0, "zz", lanes("w", u, k, k + 1), "w" + key, H[u], k == 0, k == 15, lhs=T.zz[:, 15 - k:143 - k])
-            if t == 0:
-                first("w" + key)
+                mm(pa[u], 0, z, lanes(w, u, k, k + 1), ["w" + key], H[u], False, k == 15, lhs=T[z][:, 15 - k:143 - k])
 
         def send(u):
-            tt(cols(gs[u], u), gs[u], T[x][:, 0:16 + WX].indirect(listed("ks", u)), part(gr, u),
-               [x, x + "z", "ks%d" % u, gr if t == 0 else "gr%d" % u], A.max)
+            tt(part(gs, u), gs + str(u), T.x[:, 0:16 + WX].indirect(listed("ks", u)), part("gr", u), xs + ["xz", "ks%d" % u, "gr%d" % u], A.max, GATHER)
             dst = T.cores[(rank + 1 + t % 7) % 8]
             src = T.cores[(rank - 1 - t % 7) % 8]
             eng = topo.engines(core, dst)[:8]
             rid, pid = topo.addr(dst, core)
-            waits("g", [gs[u]], [])
-            g.remote_dma(cols(h[u], u), cols(gs[u], u), T.sem["arr%d%d" % (t, u)], T.sem.sent, pid, rid, sum(1 << e for e in eng))
-            wrote[h[u]] = ("remote", "arr%d%d" % (t, u), len(topo.engines(src, core)[:8]), {})
 
-        def ready(u):
-            masks(pf[u], u)
-            mm(pf[u], 0, "idb", part("t8", u), "t8", H[u], False, False)
-            mm(pe[u], 0, "idb", cols(gs[u], u), gs[u], H[u], True, False)
+            def issue():
+                waits("g", [gs + str(u)], [])
+                g.remote_dma(part(h, u), part(gs, u), T.sem["arr%d%d" % (t, u)], T.sem.sent, pid, rid, sum(1 << e for e in eng))
+                wrote[h + str(u)] = ("remote", "arr%d%d" % (t, u), len(topo.engines(src, core)[:8]), {})
+            calls.append(("g", [gs + str(u)], [h + str(u)], SEND + (OPEN if t + u == 0 else 0.0), FAR, 0, issue))
 
         def land(u):
-            mm(pf[u], 0, "bw", cols(h[u], u), h[u], H[u], False, True)
-            mm(pe[u], 0, "idn", cols(h[u], u), h[u], H[u], False, True)
+            pm(pf, "bn", h, u, False, False)
+            cm(pf, "idn", "c8", u, False, False)
+            pm(pf, "bw", h, u, False, True)
 
-        def low(u):
-            mm(pe[u], 0, "idb", cols(gs[u], u), gs[u], H[u], True, False)
-            mm(pe[u], 0, "idn", part("rl", u), "rl%d" % u, H[u], False, True)
-
-        def rest():
-            fetch(len(FETCH))
-            fetched[0] = 0
-
-        tp = [["tp%d0" % u, "tp%d1" % u] for u in range(2)]
         parts = {
-            "j": judge, "w": mark, "G": guards, "N": names, "P": lambda u: masks("pk", u), "L": lambda u: masks(pe[u], u),
-            "u": und, "kh": kh, "lh": lh, "s": alive, "si": implied, "so": old, "gs": send, "R": ready, "land": land, "low": low,
-            "a": lambda u: counted(part("pv", u), "a", u), "b": lambda u: counted(part("b", u), "b", u),
-            "d": lambda u: act(part("dead", u), ["dead%d" % u, "cnt%d" % u], part("b", u), ["b%d" % u], F.Relu, scale=-1.0 / 16, bias=257.0,
-                               accum_out=T.cnt[:, u:u + 1]),
-            "sk": lambda u: diagonal("pk", "sk", u), "sl": lambda u: diagonal(pe[u], "sl", u), "sq": lambda u: diagonal(pf[u], "sq", u),
-            "ks": lambda u: copy(listed("ks", u), "ks%d" % u, picked("sk", u), ["sk%d" % u]),
-            "ls": lambda u: ts(listed("ls", u), "ls%d" % u, picked("sl", u), ["sl%d" % u], -1.0, None, A.add),
-            "md": lambda u: ts(part("md", u), "md%d" % u, T.rel0[:, 0:W].indirect(listed("ls", u)), ["rel0", "ls%d" % u], -1023.5, 1.0 / 2048,
-                               A.add, A.mult),
-            "t": lambda u: tt(part("t1", u), "t1%d" % u, part("md", u), cols(pa[u], u), ["md%d" % u, pa[u]], A.subtract),
-            "o": lambda u: tt(part("t2", u), "t2%d" % u, part("mo", u), cols(pa[u], u, M), ["mo%d_%d" % (u, k) for k in range(16)] + [pa[u]],
-                              A.subtract),
-            "m": lambda u: tt(own(u), pns[u], part("t1", u), cols(pa[u], u, 2 * M), ["t1%d" % u, pa[u]], A.max),
-            "n": lambda u: tt(own(u), pns[u], part("t2", u), own(u), ["t2%d" % u, pns[u]], A.max),
-            "k": lambda u: ts(part("k16", u), "k16%d" % u, own(u), [pns[u]], ROUND, -ROUND, A.add, A.add),
-            "l": lambda u: tt(part("l16", u), "l16%d" % u, own(u), part("k16", u), [pns[u], "k16%d" % u], A.subtract),
-            "turn": lambda u: turn("tp", "pv", pns + ["pad"], 256, u),
-            "kt": lambda u: ts(part("kt", u), "kt%d" % u, turned("tp", u), tp[u], ROUND, -ROUND, A.add, A.add),
-            "lt": lambda u: tt(part("lt", u), "lt%d" % u, turned("tp", u), part("kt", u), tp[u] + ["kt%d" % u], A.subtract),
-            "lu": lambda u: ts(part("lu", u), "lu%d" % u, part("lt", u), ["lt%d" % u], 2048.0, 1023.5, A.mult, A.add),
-            "ku": lambda u: copy(part("ku", u), "ku%d" % u, part("kt", u), ["kt%d" % u]),
-            "hp": lambda u: (act(cols(pf[u], u), pf[u], cols(gs[u], u), [gs[u]], bias=-UP) if last else
-                             act(part("hp", u), "hp%d" % u, cols(h[u], u), [h[u]], bias=up - 0.5)),
-            "rl": lambda u: act(part("rl", u), "rl%d" % u, cols(pe[u], u), [pe[u]], F.Relu, bias=-2.0),
-            "gj": lambda u: limits(cols(pe[u], u), pe[u], up, u),
-            "gr": lambda u: act(part("gr", u), "gr%d" % u, cols(pe[u], u), [pe[u]], bias=up),
-            "h": lambda u: ts(part("gm", u), "gm%d" % u, cols(h[u], u), [h[u]], 2.0 - UP, None, A.add), "y": limits_out,
-            "og": lambda u: (ts(part("og", u), "og%d" % u, own(u), [pns[u]], ROUND, -ROUND, A.add, A.add),
-                             load("s", "d_og", part("yg", u), part("og", u), ["og%d" % u], ["yg%d" % u])),
-            "ot": lambda u: tt(part("lt", u), "lt%d" % u, own(u), part("og", u), [pns[u], "og%d" % u], A.subtract),
-            "on": lambda u: (ts(part("on", u), "on%d" % u, part("lt", u), ["lt%d" % u], 2048.0, 1023.5, A.mult, A.add),
-                             load("s", "d_on", part("yn", u), part("on", u), ["on%d" % u], ["yn%d" % u])),
+            "kv": clip, "D": decided, "E": fetched, "c": old, "gs": send, "R": ready, "land": land, "turn": turn, "ti": listing,
+            "j": judge, "w": mark, "f": fetch,
+            "S": lambda u: mm(pa[u], 0, cst[u], cols("one", u), ["one"] + [cst[u] + str(p) for p in (0, 32, 64, 96)], H[u], True, False),
+            "G": lambda u: pm(pe, "idf", "v", u, True, False), "U": lambda u: pm(pe, "tr", "und", u, False, True),
+            "M": lambda u: cm(pq, "idb", "mk", u, True, False), "P": lambda u: pm(pq, "bdf", "kv", u, False, True),
+            "T": lambda u: cm(pe, "idb", "two", u, True, False), "H": lambda u: pm(pe, "idb", h, u, False, True),
+            "gk": lambda u: limits("gr", "gr%d" % u, OWN[u], u, 1),
+            "b": lambda u: ts(part("b", u), "b%d" % u, cols(pa[u], u), [pa[u], "thr"], 3.75, T.thr[:], A.add, A.max),
+            "a": lambda u: ts(cols(pa[u], u, M), "a%d" % u, cols(pa[u], u), [pa[u], "thr"], T.thr[:], None, A.max),
+            "u": lambda u: tt(part("und", u), "und%d" % u, cols(pa[u], u, M), part("b", u), [pa[u], "a%d" % u, "b%d" % u], A.is_lt),
+            "r": lambda u: tt(part("r2", u), "r2%d" % u, part("md", u), cols(pq[u], u), ["md%d" % u, pq[u]], A.max),
+            "n": lambda u: tt(part("vi", u) if last else own(u), vs[u], part("r2", u), cols(pa[u], u), ["r2%d" % u, pa[u]], A.max),
+            "d": lambda u: act(part("dead", u), ["dead%d" % u, "cnt%d" % u], part("b", u), ["b%d" % u, "tb"], F.Sigmoid, scale=-32.0,
+                               bias=T.tb[:], accum_out=T.cnt[:, u:u + 1]),
+            "sk": lambda u: diagonal(pq[u], "sk", u), "sq": lambda u: diagonal(pf[u], "sq", u),
+            "ks": lambda u: ts(listed("ks", u), "ks%d" % u, picked("sk", u), ["sk%d" % u], 1.0 / 2048, 16 - 2048 - HALF, A.mult, A.add),
+            "si": lambda u: tt(listed("si", u), "si%d" % u, picked("sk", u), entries("ti", u, 0, 1), ["sk%d" % u, "ti%d" % u], A.max),
+            "sa": lambda u: ts(listed("sa", u), keys("sa", u), listed("si", u), keys("si", u), 2047, None, A.bitwise_and),
+            "ls": lambda u: copy(listed("ls", u), keys("ls", u), listed("sa", u), keys("sa", u)),
+            "md": lambda u: tt(part("md", u), keys("md", u), T.rel0[:, 0:W].indirect(listed("ls", u)), part("dead", u),
+                               ["rel0"] + keys("ls", u) + keys("dead", u), A.mult, GATHER),
+            "ku": lambda u: ts(part("ku", u), keys("ku", u), part("ti", u), keys("ti", u), 1.0 / 2048, -HALF, A.mult, A.add),
+            "la": lambda u: ts(part("la", u), keys("la", u), part("ti", u), keys("ti", u), 2047, None, A.bitwise_and),
+            "lu": lambda u: copy(part("lu", u), keys("lu", u), part("la", u), keys("la", u)),
+            "hp": lambda u: act(part("hp", u), keys("hp", u), part(h, u), keys(h, u), bias=-0.5),
+            "gr": lambda u: tt(part("gr", u), "gr%d" % u, part(gs, u), cols(pe[u], u), [gs + str(u), pe[u]], A.min),
+            "gj": lambda u: limits("gr", "gr%d" % u, OWN[u], u),
+            "cu": lambda u: ts(listed("cu", u), keys("cu", u), picked("sq", u), keys("sq", u), -8.0 * O[u], None, A.add),
+            "bl": lambda u: tt(part("bl", u), keys("bl", u), xp(u).indirect(listed("cu", u)), part("hp", u),
+                               keys("x", u) + keys("cu", u) + keys("hp", u), A.add, GATHER),
+            "put": lambda u: tt(xp(u).indirect(listed("cu", u)), keys("x", u), part("bl", u), part("half", u),
+                                keys("bl", u) + keys("cu", u) + ["half"], A.mult, SCATTER),
+            "g": lambda u: act(cols(pf[u], u), pf[u], part(gs, u), [gs + str(u)], bias=-UP),
+            "h": lambda u: ts(part("gm", u), keys("gm", u), part(h, u), keys(h, u), 2.0 - UP, None, A.add), "y": limits_out,
+            "k": lambda u: ts(part("ti", u), keys("ti", u), part("vi", u), keys("v", u), 11, None, A.arith_shift_right),
+            "l": lambda u: ts(part("la", u), keys("la", u), part("vi", u), keys("v", u), 2047, None, A.bitwise_and),
+            "og": lambda u: (copy(part("og", u), keys("og", u), part("ti", u), keys("ti", u)),
+                             load("s", "d_og", part("yg", u), part("og", u), keys("og", u), keys("yg", u), 512 * H[u])),
+            "on": lambda u: (copy(part("on", u), keys("on", u), part("la", u), keys("la", u)),
+                             load("s", "d_on", part("yn", u), part("on", u), keys("on", u), keys("yn", u), 512 * H[u])),
         }
-        whole = {
-            "E": lambda: fetch(firsts - fetched[0]), "F": rest, "f": lambda: fetch(1), "C": deaths,
-            "r": lambda: tt(T.f8[:], "f8", T.sq[:, 15::16], T[bm][:], ["sq0", "sq1", bm], A.subtract),
-            "z": lambda: tt(T.z[:], "z", T.sq[:, 15::16], T.f8[:], ["sq0", "sq1", "f8"], A.subtract),
-            "cu": lambda: ts(T.cu[:], "cu", T.z[:], ["z"], 1032.0 - 64 * (UP - up), None, A.add),
-            "bl": lambda: tt(T.bl[:], "bl", xw.indirect(T.cu[:]), T.hp[:], ["x", "cu", "hp0", "hp1"], A.add),
-            "put": lambda: tt(xw.indirect(T.cu[:]), "x", T.bl[:], T.half[:], ["bl", "cu", "half"], A.mult),
-            "pi": lambda: copy(T.pi[:], "pi", T.pk[:, 0:1], ["pk"]),
-            "pj": lambda: ts(T.pj[:], "pj", T.pi[:], ["pi"], 1, None, A.bitwise_and),
-            "thr": lambda: ts(T.thr[:], "thr", T.pj[:], ["pj"], 32.0, 192 + 4100.5, A.mult, A.add),
-        }
-        order = ORDER.split()
-        if last:
-            order = [s for n, s in enumerate(order) if s not in END.split() and (s not in whole or n <= order.index("F"))] + END.split()
-        for s in order:
-            if s in whole:
-                if not (last and s not in "EFf"):
-                    whole[s]()
-            elif s in LATE:
-                if t > 0:
-                    parts[s[:-1]](int(s[-1]))
-            elif not (last and s[:-1] in NEXT):
-                parts[s[:-1]](int(s[-1]))
-            if t == 0:
-                first(s)
+
+        return parts
+
+    rounds = [steps(t) for t in range(RO)]
+    tags = {}
+    for n in range(ahead, len(calls)):
+        s = "." + calls[n][2][0]
+        tags[(0, s + "x" if (0, s) in tags else s)] = [n]
+    for t in range(RO):
+        for s in ((START + " " + ROUND0 if t == 0 else LATE + " " + ROUND) + " " + (END if t == RO - 1 else BLEND)).split():
+            r, s = t + {"<": -1, ">": 1}.get(s[0], 0), s.lstrip("<>")
+            more = {"J": [c + s[1:] + str(j) for j in range(len(JUDGE[int(s[1:] == "1")])) for c in "jw"],
+                    "F": ["f%d" % j for j in range(len(FETCH)) if str(FETCH[j][0]) == s[1:]]}
+            for s in more.get(s[0], [s]):
+                n = len(calls)
+                if s in constants:
+                    constants[s]()
+                elif s[0] in "jw":
+                    rounds[r][s[0]](int(s[1]))
+                else:
+                    rounds[r][s[:-1]](int(s[-1]))
+                for i in range(n, len(calls)):
+                    if i > n and (calls[i][0] == "s" or calls[i][0] == calls[i - 1][0] == "t"):
+                        tags[(r, s)].append(i)
+                    else:
+                        s += "'" * (i > n)
+                        tags[(r, s)] = [i]
+    if not PLAN and ORDER:
+        PLAN.extend(range(ahead))
+        for t in range(RO):
+            for s in (FIRST if t == 0 else LAST if t == RO - 1 else ORDER).split():
+                PLAN.extend(tags[(t + {"<": -1, ">": 1}.get(s[0], 0), s.lstrip("<>"))])
+    if not PLAN:
+        PLAN.extend(arrange([c[:6] for c in calls], ahead))
+    for n in PLAN:
+        calls[n][6]()
     g.wait_ge(T.sem.sent, 2 * sum(len(topo.engines(core, T.cores[(rank + 1 + t % 7) % 8])[:8]) for t in range(RO)))
     for q in ("v", "a", "t", "g"):
         if known["g"].get("c" + q, 0) < count[q]:
             g.wait_ge(T.sem["c" + q], count[q])
     for s in ("d_up", "d_on", "d_og", "d_ol"):
-        g.wait_ge(T.sem[s], dcount[s])
+        if known["g"].get(s, 0) < dcount.get(s, 0):
+            g.wait_ge(T.sem[s], dcount[s])

@@ -6,14 +6,19 @@ WX = 1792
 W = 2048
 RO = 4
 NC = (8, 6)
-JUDGE = [[4, 8, 12, 16], [5, 10, 13, 16]]
-VL = (16, 13)
+JUDGE = [[7, 12, 16], [8, 12, 14, 16]]
+VL = (12, 8)
 FETCH = [(0, 0, 5), (0, 5, 10), (0, 10, 16), (1, 0, 6), (1, 6, 11), (1, 11, 16)]
 OWN = (2, 2)
+SL = (3, 4)
+KD = (0, 0)
+HYP = 0
+MP = (1, 1)
+CB = "pq1"
 KV = "vv"
-START = "pads rs ka lima zz cst kb limb nbk tr idf mk na nb va vb bdf xg gr2 ids cc bw mq c8"
+START = "pads half ka lima zz cst kb limb nbk tr idf idg big mk th na nb va vb bdf xg gr2 ids cc bw c8"
 LATE = ""
-ROUND = "F0 F1 S0 S1 G0 G1 M0 M1 J0 J1 b0 a0 u0 d0 U0 kv0 P0 sk0 ks0 gs0 b1 a1 u1 d1 U1 kv1 P1 sk1 ks1 gs1 si0 sa0 ls0 md0 D0 E0 r0 c0 n0 si1 sa1 ls1 md1 D1 E1 r1 c1 n1"
+ROUND = "F0 F1 G0 G1 M0 M1 J0 J1 b0 a0 u0 d0 U0 kv0 P0 sk0 ks0 gs0 b1 a1 u1 d1 U1 kv1 P1 sk1 ks1 gs1 si0 sa0 ls0 md0 c0 E0 e0 V0 D0 n0 si1 sa1 ls1 md1 c1 E1 e1 V1 D1 n1"
 BLEND = "turn0 ti0 ku0 la0 lu0 turn1 ti1 ku1 la1 lu1 R0 land0 sq0 cu0 hp0 bl0 put0 T0 H0 gr0 gj0 gk0 R1 land1 sq1 cu1 hp1 bl1 put1 T1 H1 gr1 gj1 gk1 C tb thr"
 ROUND0 = ROUND
 FILL = "v"
@@ -23,6 +28,11 @@ END = "g0 h0 y0 g1 h1 y1 k0 l0 og0 on0 k1 l1 og1 on1"
 FIRST = ".ip cst' zz'' cst .ones pads'' .c1 pads' .c2 .c5 .c6 .ff .g16 pads''' .c3 cst'''' .rc .f cst'' .c4 pads zz .fk1 .par0 .par1 .a2 mk'' .fk0 .t16 .idb .bd cst'''''' cst'''''''' .a11 ids .a10 .bdx cc'''' lima''' lima' limb''' limb'' lima'' limb'''' lima cc''' gr2 rs limb ka' .a31 kb .a30 cst''''' ka .sel0 kb' zz' .sel1 ka'' nbk mk' mk xg j00 j02 na j01 j03 na' kb'' tr xg' mq tr' bdf limb' w00 idf w02 w01 w03 M1 na'' cst''' cc' nb' S0 w00' w01' w02' w03' j10 va cst''''''' j11 vb b0 a0 S1 j12 u0 j13 cc'' nb zz''' w13 f0 w10 f2 w11 w12 f1 d0 w10' M0 G0 G1 U0 w11' w12' w13' kv0 nb'' .pada cc c8 .wd a1 b1 na''' P0 sk0 nb''' u1 .wc si0 ks0 ids' ids'' .padb f3 f5 f4 d1 U1 sa0 gs0 kv1 ls0 mq' D0 c0 P1 T0 E0 gs0' md0 sk1 c8' c8'' bw' ks1 si1 r0 gs1 n0 bw sa1 turn0' ls1 gs1' bw'' turn0 md1 ti0 la0 R0 R1 D1 c1 E1 r1 ku0 lu0 n1 H0 land0 land1 T1 H1 gr0 sq0 turn1 sq1 turn1' cu0 cu1 gr1 ti1 hp1 hp0 gj0 gj0' bl1 bl0 la1 put1 put0 >S1 >M1 C >S0 gk0 >f2 >G1"
 ORDER = "<ku1 <lu1 j00 R1 j01 <tb <gj1' <gj1 f1 f0 w00 w01 j02 j03 <thr w02 w03 <gk1 <gk1' j10 w10 w00' M0 w01' w02' w03' G0 R0 w10' j11 w11 w11' j12 a0 b0 j13 u0 w13 w12 w12' U0 w13' kv0 P0 b1 a1 u1 sk0 U1 c0 si0 ks0 kv1 sa0 gs0 ls0 gs0' P1 f3 f4 d0 f5 D0 E0 d1 sk1 md0 ks1 r0 gs1 si1 n0 gs1' sa1 turn0 turn0' ls1 ti0 md1 T0 c1 D1 E1 >S0 H0 T1 land0 la0 r1 ku0 lu0 n1 gr0 sq0 turn1 turn1' cu0 land1 H1 sq1 gr1 ti1 cu1 hp0 hp1 gj0 gj0' bl0 la1 bl1 put0 put1 >M1 >S1 gk0 C >f2 >G1"
 LAST = "<ku1 <lu1 j01 <gj1' <tb <thr <gj1 f1 f0 w01 j00 w00 G0 <gk1' <gk1 j02 j03 j10 w02 w03 w00' w01' M0 w02' w03' w10 w10' j11 j12 w11 a0 b0 w11' j13 u0 w12 U0 w12' w13 w13' d0 f3 f5 f4 kv0 P0 a1 b1 sk0 u1 U1 D0 E0 si0 ks0 sa0 kv1 P1 c0 ls0 gs0 gs0' md0 sk1 ks1 r0 si1 gs1 gs1' g0 d1 c1 D1 E1 sa1 n0 ls1 l0 md1 k0 on0 r1 h0 og0 n1 y0 k1 l1 g1 y0' og1 h1 on1 y1 y1'"
+ORDERS = [
+    ".ff .ones zz th' .ip pads' half pads .bd .a11 .a10 .c5 .c4 pads''' pads'' .idb cst .rc1 .rc0 .g16 cst' .bdx .fk1 .fk0 .par0 zz'' ids .par1 xg .a30 .a31 big kb ka' lima''' lima lima'' A0 .sel0 A1 lima'''' ka kb' limb' limb'' lima' cst''' .sel1 zz''' ka'' zz' limb''' limb cst'''' kb'' cst'' x0 j00 nbk na' B0 na j01 nb' gr2 x1 B1 w00 idg idf m0 na'' xg' j02 w01 w00' j10 m0' f0 w01' j11 m1 w02 j12 j13 w10 va tr mk w02' w11 b0 vb w10' a0 tr' bdf f2 f1 w12 m1' cst''''' nb u0 mk' w11' G0 w13 nb'' vb' w12' U0 mk'''' .c6 w13' th kv0 f3 f5 G1 M0 na''' mk'' a1 P0 b1 .padb ids'' .pada M1 c0 u1 sk0 ids' mk''' U1 nb''' c1 .wc ks0 >M0 kv1 si0 gs0 .wd c8 P1 f4 d0 sa0 .padc E0 bw' d1 sk1 gs0' cc'' e0 ls0 bw cc' c8'' V0 ks1 md0 D0 R0 gs1 R1 n0 si1 cc c8' T0 turn0 turn0' gs1' T1 sa1 bw'' E1 ti0 ls1 e1 V1 la0 D1 md1 lu0 n1 ku0 land0 hp0 >f0 turn1' H0 land1 sq0 H1 C gr0 sq1 cu0 turn1 hp1 gr1 gj0 gj0' cu1 bl0 >A0 ti1 >f1 bl1 >G0 gk0 put0 >A1 put1 >G1 la1 ku1 gj1' gj1 gk0'",
+    "x0 j00 <gk1 x1 j01 B0 B1 <lu1 j10 <thr <tb w00 w00' j02 M1 m0 w01 j12 m1 w10 w02 m0' j11 w01' f2 j13 w02' w11 w10' m1' b0 w12 a0 w11' w13 u0 w12' w13' f3 f5 R1 U0 c0 a1 b1 R0 kv0 u1 f4 P0 U1 c1 d0 sk0 T0 kv1 d1 si0 >M0 ks0 P1 sa0 E0 gs0 sk1 e0 ls0 V0 gs0' ks1 md0 D0 T1 si1 gs1 n0 gs1' sa1 E1 e1 turn0 turn0' V1 ls1 D1 ti0 md1 hp0 H0 land0 la0 n1 gr0 lu0 land1 sq0 gj0 hp1 gj0' H1 C turn1' ku0 cu0 turn1 sq1 gr1 gk0 bl0 cu1 >A0 ti1 >A1 >f1 bl1 gk0' put0 >G0 put1 >G1 la1 ku1 gj1' gj1 >f0",
+    "j01 x0 <gk1 x1 j00 B0 w01 B1 w00 j10 j02 m0 w00' <thr j11 w02 f2 m0' w01' j12 w11 j13 w02' w10 R0 m1 a0 b0 w10' w13 <tb u0 m1' d0 <lu1 w12 M1 U0 w11' kv0 w12' w13' P0 f3 f5 a1 b1 c0 sk0 E0 u1 f4 e0 si0 ks0 U1 V0 sa0 gs0 D0 d1 T0 kv1 c1 ls0 gs0' P1 md0 R1 T1 >M0 sk1 n0 ks1 C si1 turn0 gs1 sa1 turn0' gs1' ls1 land0 hp0 ti0 tb md1 thr H0 E1 la0 e1 sq0 V1 gr0 lu0 D1 >M1 cu0 ku0 >A0 gj0 gj0' bl0 >f0 n1 land1 gk0 put0 H1 >G0 sq1 turn1 hp1 gr1 cu1 turn1' >f2 gk0' bl1 >A1 ti1 >G1 put1 la1 ku1 gj1' gj1",
+    "j00 x0 <gk1 B0 j01 x1 w00 j10 j02 w00' m0 w01 B1 m0' j11 w02 w10 j12 <lu1 j13 w01' m1 w02' w12 w11 f1 w10' m1' a0 b0 w13 w11' u0 w12' w13' U0 c0 f5 f3 a1 b1 kv0 u1 P0 f4 U1 c1 sk0 d0 kv1 d1 si0 ks0 P1 sa0 E0 gs0 sk1 e0 ls0 V0 gs0' g0 ks1 md0 D0 gs1 si1 n0 gs1' g1 sa1 l0 E1 e1 ls1 k0 V1 on0 D1 md1 og0 h0 n1 y0 k1 l1 y0' h1 og1 on1 y1 y1'"]
 FIXED = {"v": 0.02, "a": 0.04, "t": 0.015, "g": 0.17}
 LEAST = {"v": 48, "a": 0, "t": 0, "g": 0}
 CYCLE = {"v": 0.00092, "a": 0.00092, "t": 0.00047, "g": 0.00092}
@@ -36,10 +46,11 @@ SPAN = 6.0
 SEED = 1
 HALF = 1023.5 / 2048
 BIG = 2.0 ** 22
+HUGE = 1.5 * 2.0 ** 48
 EIGHT = 1.5 * 2.0 ** 26
 KILO = 1.5 * 2.0 ** 33
 UP = 144.0
-M = 160
+M = 128
 TOP = 4096.0
 
 SB = "sbuf"
@@ -49,25 +60,26 @@ SCRATCH = {
     "grd0": (SB, [128, 256], I32), "nam0": (SB, [128, 256], I32), "grd0t": (SB, [128, 512], I32), "nam0t": (SB, [128, 512], I32), "rel0": (SB, [128, W], I32),
     "u": (SB, [128, 16 * I], BF), "w": (SB, [128, 16 * I], BF), "wv": (SB, [128, 16 * I], F16), "nb": (SB, [128, 16 * I], F32),
     "ku": (SB, [128, I], U16), "lu": (SB, [128, I], U16), "tp": (SB, [128, 512], F32),
-    "v": (SB, [128, 256], F32), "ti": (SB, [128, I], I32), "la": (SB, [128, I], I32), "vi": (SB, [128, I], I32),
+    "v": (SB, [128, 272], F32), "ti": (SB, [128, I], I32), "la": (SB, [128, I], I32), "vi": (SB, [128, I], I32),
     "gj": (SB, [128, 1536], F32), "gr": (SB, [128, I], BF), "gm": (SB, [128, I], BF), "hp": (SB, [128, I], F32),
     "b": (SB, [128, I], BF), "und": (SB, [128, I], BF), "dead": (SB, [128, I], BF),
     "kv": (SB, [128, I], F32), "r2": (SB, [128, I], F32), "sk": (SB, [128, I], F32), "sq": (SB, [128, I], F32),
     "ks": (SB, [128, 14], U16), "ls": (SB, [128, 14], U16), "cu": (SB, [128, 14], U16), "sel": (SB, [128, 14], U16),
-    "si": (SB, [128, 14], I32), "sa": (SB, [128, 14], I32), "bl": (SB, [128, I], BF), "half": (SB, [128, I], BF),
+    "si": (SB, [128, 14], I32), "sa": (SB, [128, 14], I32), "bl": (SB, [128, I], BF), "half": (SB, [128, M], BF),
     "md": (SB, [128, I], F32), "mo": (SB, [128, I], F32), "cnt": (SB, [128, 2], F32), "tb": (SB, [128, 1], F32), "thr": (SB, [128, 1], F32), "kc": (SB, [128, 2], BF),
     "ip": (SB, [128, 1], I32), "c1": (SB, [128, 1], I32), "c2": (SB, [128, 1], I32), "c3": (SB, [128, 1], I32), "c4": (SB, [128, 1], I32),
     "c5": (SB, [128, 1], I32), "c6": (SB, [128, 1], I32), "par": (SB, [128, 2], F32),
-    "g16": (SB, [128, 1], F32), "wc": (SB, [128, 1], F32), "wd": (SB, [128, 1], F32), "wn": (SB, [128, 1], F32), "rc": (SB, [128, 1], F32),
+    "g16": (SB, [128, 1], F32), "wc": (SB, [128, 1], F32), "wd": (SB, [128, 1], F32), "wn": (SB, [128, 1], F32), "rc": (SB, [128, 2], F32),
     "ff": (SB, [128, 14], F32), "f": (SB, [128, 14], F32), "fk": (SB, [128, 14], I32), "a1": (SB, [128, 14], F32), "a2": (SB, [128, 14], F32),
     "a3": (SB, [128, 14], F32),
-    "t16": (SB, [128, I], BF), "t8": (SB, [128, I], BF), "mk": (SB, [128, I], BF), "mq": (SB, [128, I], BF), "rs": (SB, [128, I], BF),
+    "ek": (SB, [128, M], BF), "t8": (SB, [128, I], BF), "mk": (SB, [128, M], BF), "mq": (SB, [128, I], BF), "rs": (SB, [128, M], BF),
     "cc": (SB, [128, M], BF), "two": (SB, [128, M], BF), "c8": (SB, [128, M], BF),
     "one": (SB, [128, M], BF), "ones": (SB, [128, 128], BF), "onp": (SB, [128, 128], F32), "onn": (SB, [128, 128], F32), "idb": (SB, [128, 128], BF),
     "idn": (SB, [128, 128], BF), "idf": (SB, [128, 128], F32), "idg": (SB, [128, 128], F32), "bdf": (SB, [128, 128], F32),
-    "idp": (SB, [128, 128], BF), "idm": (SB, [128, 128], BF), "id4": (SB, [128, 128], BF), "bd": (SB, [128, 128], BF),
+    "idh": (SB, [128, 128], BF), "idk": (SB, [128, 128], BF), "big": (SB, [128, 512], BF), "idm": (SB, [128, 128], BF), "id4": (SB, [128, 128], BF), "bd": (SB, [128, 128], BF),
     "nbk": (SB, [128, 128], BF), "low": (SB, [128, 128], BF), "tr": (SB, [128, 128], BF), "trn": (SB, [128, 128], BF),
-    "bw": (SB, [128, 128], BF), "bn": (SB, [128, 128], BF), "cst0": (SB, [128, 128], BF), "cst1": (SB, [128, 128], BF),
+    "bw": (SB, [128, 128], BF), "bn": (SB, [128, 128], BF),
+    "so0": (SB, [128, 1], F32), "so1": (SB, [128, 1], F32), "st0": (SB, [128, 1], F32), "st1": (SB, [128, 1], F32), "sb0": (SB, [128, 1], F32), "sb1": (SB, [128, 1], F32),
     "zz": (SB, [128, 144], BF), "zv": (SB, [128, 144], BF),
     "on": (SB, [128, I], F32), "og": (SB, [128, I], F32), "ol": (SB, [128, I], BF),
 }
@@ -150,6 +162,7 @@ def arrange(calls, ahead):
 
 
 PLAN = []
+SEEN = {}
 
 
 def rank_program(g, core, T, topo):
@@ -205,7 +218,7 @@ def rank_program(g, core, T, topo):
             snap = dict(known[q])
             snap["c" + q] = count[q]
             note((q, "c" + q, count[q], snap), reads + list(also), writes)
-        calls.append((q, reads, writes, FIXED[q] + max(LEAST[q], cycles) * CYCLE[q], 0.0, 0, issue))
+        calls.append((q, reads, writes, FIXED[q] + max(LEAST[q], cycles) * CYCLE[q], 0.0, 0, issue, list(also), None))
 
     def load(q, sem, out, in_, reads, writes, size, whole=(), **kw):
         def issue():
@@ -218,7 +231,7 @@ def rank_program(g, core, T, topo):
             if whole and dcount[sem] % (16 * len(whole)) == 0:
                 for k in whole:
                     wrote[k] = wrote[writes[0]]
-        calls.append((q, reads, writes, ISSUE[q], LAND, size, issue))
+        calls.append((q, reads, writes, ISSUE[q], LAND, size, issue, [], sem if whole else None))
 
     def copy(out, okey, in_, ikeys, per=1.0):
         op("v", ikeys, okey, lambda e: e.tensor_copy(out, in_), per * out.shape[1])
@@ -252,15 +265,16 @@ def rank_program(g, core, T, topo):
         else:
             ts(T[name][:], name, T[src][:], keys_, by, None, A.mult, per=0.5)
 
-    def select(name, src, pattern, cmp, fill_, base, mult):
-        op("g", [src], name, lambda e: e.affine_select(T[name][:], T[src][:], pattern, cmp, fill_, base, mult), 2 * T[name].shape[1])
+    def select(name, src, pattern, cmp, fill_, base, mult, rows=128):
+        n = T[name].shape[1]
+        op("g", [src], name, lambda e: e.affine_select(T[name][0:rows, :], T[src][0:rows, 0:n], pattern, cmp, fill_, base, mult), 2 * n)
 
     def iota(name, pattern, mult, base=0, okeys=None):
         op("g", [], okeys or name, lambda e: e.iota(T[name][:], pattern, base, mult, allow_small_or_imprecise_dtypes=True), 2 * T[name].shape[1])
 
     H = [16 * n for n in NC] + [I]
     O = [0, H[0], 0]
-    wide = [max(b - a for a, b in zip([0] + JUDGE[u], JUDGE[u])) for u in range(2)]
+    wide = [max(b - a for a, b in zip([SL[u]] + JUDGE[u], JUDGE[u])) for u in range(2)]
     xw = T.x[:, 16:16 + WX]
     vs, xs, pa, pe, pf, pq = ["v0", "v1"], ["x0", "x1"], ["pa0", "pa1"], ["pe0", "pe1"], ["pf0", "pf1"], ["pq0", "pq1"]
 
@@ -277,7 +291,7 @@ def rank_program(g, core, T, topo):
         return T.x[:, 16 + 8 * O[u]:16 + 8 * (O[u] + H[u])]
 
     def own(u):
-        return part("v", u, 16)
+        return part("v", u, 16 + 16 * u)
 
     def lanes(name, u, a, b):
         return T[name][:, 16 * O[u] + H[u] * a:16 * O[u] + H[u] * b]
@@ -299,13 +313,21 @@ def rank_program(g, core, T, topo):
 
     def turn(u):
         a, n = (2 * H[0] + 32) * u, H[u]
-        op("v", [vs[u], "pada", "padb"], "tp%d0" % u, lambda q: q.transpose(T.tp[:, a:a + n], own(u)), n)
-        op("v", [vs[u], "pada", "padb"], "tp%d1" % u, lambda q: q.transpose(T.tp[:, a + n:a + 2 * n + 32], T.v[:, O[u]:O[u] + n + 32]), n + 32,
-           [vs[1 - u]])
+        op("v", [vs[u]], "tp%d0" % u, lambda q: q.transpose(T.tp[:, a:a + n], own(u)), n)
+        op("v", [vs[u], "pada", "padb", "padc"], "tp%d1" % u,
+           lambda q: q.transpose(T.tp[:, a + n:a + 2 * n + 32], T.v[:, O[u] + 16 * u:O[u] + 16 * u + n + 32]), n + 32)
 
     def listing(u):
         a = (2 * H[0] + 32) * u
         copy(part("ti", u), "ti%d" % u, T.tp[:, a:a + 2 * H[u] + 32].indirect(listed("sel", u)), ["tp%d0" % u, "tp%d1" % u, "sel%d" % u], GATHER)
+
+    def guards(u):
+        a = (2 * H[0] + 32) * u
+        if KD[u]:
+            ts(part("ku", u), "ku%d" % u, T.tp[:, a:a + 2 * H[u] + 32].indirect(listed("sel", u)), ["tp%d0" % u, "tp%d1" % u, "sel%d" % u],
+               1.0 / 2048, -HALF, A.mult, A.add)
+        else:
+            ts(part("ku", u), keys("ku", u), part("ti", u), keys("ti", u), 1.0 / 2048, -HALF, A.mult, A.add)
 
     def diagonal(bank, out, u):
         op("v", [bank, "rs"], out + str(u), lambda e: e.tensor_tensor_scan(part(out, u), cols("rs", u), cols(bank, u), 0.0, A.mult, A.max), H[u])
@@ -336,27 +358,25 @@ def rank_program(g, core, T, topo):
         else:
             act(part("kv", u), "kv%d" % u, cols(pe[u], u), [pe[u]], F.Relu, bias=-BIG)
 
-    def decided(u):
-        pm(pq, "id4", "und", u, True, False)
-        pm(pq, "id4", "dead", u, False, False)
-
     def fetched(u):
-        mm(pq[u], 0, "idf", part("mo", u), ["mo%d_%d" % (u, k) for k in range(16)], H[u], False, True)
+        mm(pa[u], 0, "idf", part("mo", u), ["mo%d_%d" % (u, k) for k in range(16)], H[u], False, False)
 
-    def old(u):
-        cm(pa, "idb", "cc", u, True, False)
-        pm(pa, "idp", "und", u, False, False)
-        pm(pa, "idf", "v", u, False, True)
+    def wiped(u):
+        pm(pa, "idh", "und", u, False, False)
+        pm(pa, "idk", "und", u, False, False)
+
+    def classes(u):
+        ts(part("b", u), "b%d" % u, cols(pa[u], u), [pa[u], "thr", "sb" + cst[u]], T["sb" + cst[u]][:], T.thr[:], A.add, A.max)
 
     def deaths():
         for n, (lkey, rhs, key) in enumerate((("onp", T.cnt[:, 0:1], "cnt0"), ("onp", T.cnt[:, 1:2], "cnt1"), ("idb", T.kc[:, 0:1], "kc0"),
                                               ("idb", T.kc[:, 1:2], "kc1"), ("idn", T.kc[:, 1:2], "kc1"),
                                               ("onn", T.cnt[:, 0:1], "cnt0"), ("onn", T.cnt[:, 1:2], "cnt1"))):
-            mm(pe[0], 2 * M, lkey, rhs, [key], 1, n == 0, n == 6)
+            mm(CB, 2 * M, lkey, rhs, [key], 1, n == 0, n == 6)
 
     def ready(u):
         cm(pf, "idb", "c8", u, True, False)
-        mm(pf[u], 0, "idb", part("mq", u), ["mq"], H[u], False, False)
+        mm(pf[u], 0, "ek", T.mq[0:16, O[u]:O[u] + H[u]], ["mq"], H[u], False, False, lhs=T.ek[0:16, :])
 
     def limits_out(u):
         tt(part("ol", u), "ol%d" % u, part("gm", u), cols(pf[u], u), ["gm%d" % u, pf[u]], A.min)
@@ -369,36 +389,27 @@ def rank_program(g, core, T, topo):
         load(*inputs[s])
     ahead = len(calls)
 
-    iota("ip", [[0, 1]], 1)
-    iota("ff", [[16, 14]], 1)
+    iota("ip", [[0, 1]], 17)
+    iota("ff", [[32, 14]], 0)
     memset(T.ones[:], "ones", 1.0)
-    iota("t16", [[0, I // 16], [1, 16]], 0)
     select("bd", "ones", [[-16, 8], [0, 16]], A.is_ge, 0.0, 0, 1)
     select("bd", "bd", [[16, 8], [0, 16]], A.is_ge, 0.0, 15, -1)
     select("idb", "ones", [[-1, 128]], A.is_equal, 0.0, 0, 1)
-    memset(T.v[:, 0:16], "pada", 0.0)
-    ts(T.c1[:], "c1", T.ip[:], ["ip"], 112, None, A.bitwise_and)
-    ts(T.c2[:], "c2", T.ip[:], ["ip"], 4, None, A.arith_shift_right)
+    for n, a in enumerate((0, 16 + H[0], 32 + I)):
+        memset(T.v[:, a:a + 16], "pad" + "abc"[n], 0.0)
     ts(T.c5[:], "c5", T.ip[:], ["ip"], 15, None, A.bitwise_and)
-    copy(T.g16[:], "g16", T.c1[:], ["c1"])
-    tt(T.c3[:], "c3", T.c2[:], T.ip[:], ["c2", "ip"], A.add)
+    ts(T.c4[:], "c4", T.ip[:], ["ip"], 4, 1, A.arith_shift_right, A.bitwise_and)
     ts(T.c6[:], "c6", T.ip[:], ["ip"], 3, None, A.bitwise_and)
-    ts(T.f[:], "f", T.ff[:], ["ff", "g16"], T.g16[:], None, A.subtract)
-    ts(T.c4[:], "c4", T.c3[:], ["c3"], 1, None, A.bitwise_and)
-    memset(T.v[:, 16 + I:256], "padb", 0.0)
+    ts(T.g16[:], "g16", T.c5[:], ["c5"], 16.0, None, A.mult)
     for u in range(2):
-        ts(listed("fk", u), "fk%d" % u, T.f[:, 0:NC[u]], ["f"], 1.0 / NC[u], (1.0 / NC[u] - 1) / 2, A.mult, A.add)
-        ts(T.par[:, u:u + 1], "par%d" % u, T.c4[:], ["c4"], H[u] + 16.0, None, A.mult)
-    ts(T.a2[:], "a2", T.f[:], ["f"], 16.0, None, A.mult)
-    for u in range(2):
-        ts(listed("a1", u), "a1%d" % u, listed("fk", u), ["fk%d" % u, "par%d" % u], 1.0 - H[u], T.par[:, u:u + 1], A.mult, A.add)
-    copy(T.rc[:], "rc", T.c5[:], ["c5"])
-    for u in range(2):
-        tt(listed("a3", u), "a3%d" % u, listed("a1", u), T.a2[:, 0:NC[u]], ["a1%d" % u, "a2"], A.add)
+        ts(T.rc[:, u:u + 1], "rc%d" % u, T.c5[:], ["c5"], 2.0, 1.0 - NC[u], A.mult, A.add)
+        ts(listed("fk", u), "fk%d" % u, T.ff[:, 0:NC[u]], ["ff", "rc%d" % u], T.rc[:, u:u + 1], 0.5 / NC[u], A.add, A.mult)
+        ts(T.par[:, u:u + 1], "par%d" % u, T.c4[:], ["c4", "g16"], H[u] + 16.0, T.g16[:], A.mult, A.add)
+        ts(listed("a1", u), "a1%d" % u, T.ff[:, 0:NC[u]], ["ff"], 8.0 / (H[u] - 1), None, A.mult)
+        tt(listed("a3", u), "a3%d" % u, listed("a1", u), listed("fk", u), ["a1%d" % u, "fk%d" % u], A.subtract)
+        ts(listed("sel", u), "sel%d" % u, listed("a3", u), ["a3%d" % u, "par%d" % u], H[u] - 1.0, T.par[:, u:u + 1], A.mult, A.add)
     ts(T.wc[:], "wc", T.c6[:], ["c6"], 2.0, 1.0, A.mult, A.add)
     ts(T.wd[:], "wd", T.c5[:], ["c5"], 0.5, 3.0 / 128, A.is_lt, A.mult)
-    for u in range(2):
-        copy(listed("sel", u), "sel%d" % u, listed("a3", u), ["a3%d" % u])
 
     def sums():
         for name, by in (("zz", -17.0), ("zv", -4.0))[:1 + (min(VL) < 16)]:
@@ -406,16 +417,19 @@ def rank_program(g, core, T, topo):
             ts(T[name][:, 15:143:16], name, T.bd[:, 0:128:16], ["bd"], by, None, A.mult)
 
     def offsets():
-        fill("one", 1.0)
         for u in range(1 + (VL[0] != VL[1])):
-            name = "cst%d" % u
-            fill(name, 0.0)
-            for p, val in ((0, TOP), (32, 4.5)):
-                ts(T[name][p:p + 1, :], name + str(p), T[name][p:p + 1, :], [name], val, None, A.add, per=0.5)
-            for p, val in ((64, 32768.0), (96, -16.0))[:2 * (VL[u] < 16)]:
-                ts(T[name][p:p + 1, :], name + str(p), T.t16[p:p + 1, 0:128], ["t16", name], VL[u] - 0.5, val, A.is_ge, A.mult, 0.5)
+            ts(T["so%d" % u][:], "so%d" % u, T.c5[:], ["c5"], VL[u] - 0.5, 64 * 511.75, A.is_ge, A.mult)
+            for name, by in (("st%d" % u, 4.5), ("sb%d" % u, 8.25)):
+                ts(T[name][:], name, T["so%d" % u][:], ["so%d" % u], TOP + by, None, A.add)
 
-    cst = ["cst0", "cst1" if VL[0] != VL[1] else "cst0"]
+    def masks():
+        select("ek", "ones", [[0, 8], [-1, 16]], A.is_equal, 0.0, 0, 1, 16)
+        select("mk", "big", [[0, 8], [-1, 16]], A.not_equal, 0.0, 0, 1, 16)
+        iota("t8", [[8, I]], 0)
+        select("mq", "t8", [[0, I // 16], [-1, 16]], A.is_equal, -8 * BIG, 0, 1, 16)
+        select("rs", "ones", [[0, 8], [1, 16]], A.is_gt, 0.0, 0, 0)
+
+    cst = ["0", "1" if VL[0] != VL[1] else "0"]
 
     def plain(name, src, u):
         a, n = (2 * H[0] + 32) * u, H[u]
@@ -434,19 +448,18 @@ def rank_program(g, core, T, topo):
 
     constants = {
         "zz": sums, "cst": offsets, "xg": raised,
-        "rs": lambda: act(T.rs[:], "rs", T.t16[:], ["t16"], F.Sigmoid, more=1600, scale=256.0, bias=-128.0),
+        "half": lambda: act(T.half[:], "half", T.ones[:], ["ones"], F.Sigmoid, scale=0.0), "mk": masks,
         "idf": lambda: times("idf", "idb", 1.0), "idg": lambda: times("idg", "idb", -1.0), "bdf": lambda: times("bdf", "bd", 1.0),
         "nbk": lambda: times("nbk", "bd", -2 * BIG), "trn": lambda: times("trn", "tr", -1.0),
         "tr": lambda: (select("low", "nbk", [[1, 128]], A.is_gt, 0.0, 0, -1), select("tr", "low", [[-1, 128]], A.not_equal, 2 * BIG, 0, 1)),
-        "mk": lambda: (ts(T.mk[:], "mk", T.t16[:], ["t16", "rc"], T.rc[:], -8 * BIG, A.not_equal, A.mult), memset(T.tb[:], "tb", 32 * (TOP - 88)),
-                       memset(T.thr[:], "thr", TOP - 96)),
-        "ids": lambda: [times(name, "idb", by) for name, by in (("id4", -2 * BIG), ("idp", BIG), ("idn", -1.0))],
-        "cc": lambda: (fill("cc", -BIG), fill("two", 2.0), fill("half", 0.5), times("onp", "ones", 512.0), times("onn", "ones", -512.0)),
+        "th": lambda: (memset(T.tb[:], "tb", 32 * (TOP - 88)), memset(T.thr[:], "thr", TOP - 96)),
+        "ids": lambda: [times(name, "idb", by) for name, by in (("idn", -1.0), ("idh", HUGE), ("idk", -HUGE))],
+        "big": lambda: fill("big", -8 * BIG),
+        "cc": lambda: (fill("two", 2.0), times("onp", "ones", 512.0), times("onn", "ones", -512.0)),
         "bw": lambda: (tt(T.wn[:], "wn", T.wd[:], T.wc[:], ["wd", "wc"], A.subtract), times("bw", "bd", "wc"), times("bn", "bd", "wn")),
-        "mq": lambda: (iota("t8", [[8, I]], 0), tt(T.mq[:], "mq", T.mk[:], T.t8[:], ["mk", "t8"], A.add, 2.0)),
         "c8": lambda: (fill("c8", EIGHT), memset(T.kc[:, 0:1], "kc0", -256.0), memset(T.kc[:, 1:2], "kc1", KILO)),
-        "va": lambda: ts(T.md[:], keys("md", 2), part("grd0", 2, 16), ["grd0"], 2048.0, None, A.mult),
-        "vb": lambda: tt(own(2), vs, T.md[:], part("nam0", 2, 16), ["md0", "nam0"], A.add, 2.0),
+        "va": lambda: ts(cols(pq[0], 2), pq[0], part("grd0", 2, 16), ["grd0"], 2048.0, None, A.mult),
+        "vb": lambda: [tt(own(u), vs[u], part(pq[0], u), part("nam0", u, 16), [pq[0], "nam0"], A.add) for u in range(2)],
         "pads": lambda: [memset(T[name][:, a:a + 16], name + key, 0) for name in ("grd0", "nam0") for a, key in ((0, "a"), (16 + I, "b"))],
         "ka": lambda: plain("ku", "grd0", 0), "kb": lambda: plain("ku", "grd0", 1),
         "na": lambda: (plain("lu", "nam0", 0), copy(entries("ti", 0, 0, 1), "ti0", entries("lu", 0, 0, 1), ["lu0"])),
@@ -456,20 +469,20 @@ def rank_program(g, core, T, topo):
         "xz": lambda: memset(T.x[:, 0:16], "xz", UP),
         "xa": lambda: act(xp(0), xs[0], T.x0[:, 0:8 * H[0]], ["xc"], bias=UP),
         "xb": lambda: act(xp(1), xs[1], T.x0[:, 8 * H[0]:WX], ["xc"], bias=UP),
-        "C": deaths, "tb": lambda: act(T.tb[:], "tb", T[pe[0]][:, 2 * M:2 * M + 1], [pe[0]], bias=32 * (TOP - 88)),
-        "thr": lambda: act(T.thr[:], "thr", T[pe[0]][:, 2 * M:2 * M + 1], [pe[0]], scale=1.0 / 32, bias=TOP - 96),
+        "C": deaths, "tb": lambda: act(T.tb[:], "tb", T[CB][:, 2 * M:2 * M + 1], [CB], bias=32 * (TOP - 88)),
+        "thr": lambda: act(T.thr[:], "thr", T[CB][:, 2 * M:2 * M + 1], [CB], scale=1.0 / 32, bias=TOP - 96),
     }
 
     def steps(t):
         last = t == RO - 1
         xj, xk = (T.x0[:], ["xc"]) if t == 0 else (xw, xs)
         h, gs = "h%d" % t, "gs%d" % t
-        done = {"j0": 0, "j1": 0, "w0": 0, "w1": 0}
+        done = {"j0": 0, "j1": 0, "w0": 0, "w1": 0, "k0": 0, "k1": 0}
 
         def piece(s, u):
             j = done[s + str(u)]
             done[s + str(u)] = j + 1
-            return ([0] + JUDGE[u])[j], JUDGE[u][j], "%d%d" % (u, j)
+            return ([SL[u]] + JUDGE[u])[j], JUDGE[u][j], "%d%d" % (u, j)
 
         def judge(u):
             a, b, key = piece("j", u)
@@ -480,12 +493,34 @@ def rank_program(g, core, T, topo):
             a, b, key = piece("w", u)
             if a < VL[u]:
                 w, z = "w", "zz"
-                act(lanes(w, u, a, b), "w" + key, lanes("u", u, a, b), ["u" + key, "rs"], F.Sigmoid, scale=8.0, bias=-8.0 * 512 - math.log(16.0))
+                act(lanes(w, u, a, b), "w" + key, lanes("u", u, a, b), ["u" + key, "half"], F.Sigmoid, scale=8.0, bias=-8.0 * 512 - math.log(16.0))
             else:
                 w, z = "wv", "zv"
                 ts(lanes(w, u, a, b), "w" + key, lanes("u", u, a, b), ["u" + key], 511.75, 516.0, A.max, A.min, 0.5)
+            rows(w, z, u, a, b, key)
+
+        def rows(w, z, u, a, b, key):
             for k in range(a, b):
-                mm(pa[u], 0, z, lanes(w, u, k, k + 1), ["w" + key], H[u], False, k == 15, lhs=T[z][:, 15 - k:143 - k])
+                done["k%d" % u] += 1
+                mm(pa[u], 0, z, lanes(w, u, k, k + 1), ["w" + key], H[u], done["k%d" % u] == 1, done["k%d" % u] == 16, lhs=T[z][:, 15 - k:143 - k])
+
+        def less(u):
+            g_, key = ("lim0", "lim0") if t == 0 else ("gr", "gr%d" % u)
+            for k in range(SL[u]):
+                mm(pf[u], H[u] * k, "idn", part(g_, u), [key], H[u], k == 0, False)
+
+        def take(u):
+            act(lanes("u", u, 0, SL[u]), "us%d" % u, xj.indirect(entries("ku", u, 0, SL[u])), xk + ["ku%d" % u], bias=-2.0)
+
+        def cells(u):
+            n = SL[u] * H[u]
+            mm(pf[u], 0, "idb", lanes("u", u, 0, SL[u]), ["us%d" % u], n, False, False)
+            mm(pf[u], 0, "idn", T.big[:, 0:n], ["big"], n, False, False)
+            mm(pf[u], 0, "idb", T.big[:, 0:n], ["big"], n, False, True)
+
+        def marks(u):
+            act(lanes("w", u, 0, SL[u]), "ws%d" % u, T[pf[u]][:, 0:SL[u] * H[u]], [pf[u], "half"], F.Sigmoid, scale=8.0, bias=-math.log(16.0))
+            rows("w", "zz", u, 0, SL[u], "s%d" % u)
 
         def send(u):
             tt(part(gs, u), gs + str(u), T.x[:, 0:16 + WX].indirect(listed("ks", u)), part("gr", u), xs + ["xz", "ks%d" % u, "gr%d" % u], A.max, GATHER)
@@ -498,7 +533,7 @@ def rank_program(g, core, T, topo):
                 waits("g", [gs + str(u)], [])
                 g.remote_dma(part(h, u), part(gs, u), T.sem["arr%d%d" % (t, u)], T.sem.sent, pid, rid, sum(1 << e for e in eng))
                 wrote[h + str(u)] = ("remote", "arr%d%d" % (t, u), len(topo.engines(src, core)[:8]), {})
-            calls.append(("g", [gs + str(u)], [h + str(u)], SEND + (OPEN if t + u == 0 else 0.0), FAR, 0, issue))
+            calls.append(("g", [gs + str(u)], [h + str(u)], SEND + (OPEN if t + u == 0 else 0.0), FAR, 0, issue, [], None))
 
         def land(u):
             pm(pf, "bn", h, u, False, False)
@@ -506,28 +541,27 @@ def rank_program(g, core, T, topo):
             pm(pf, "bw", h, u, False, True)
 
         parts = {
-            "kv": clip, "D": decided, "E": fetched, "c": old, "gs": send, "R": ready, "land": land, "turn": turn, "ti": listing,
+            "kv": clip, "E": fetched, "b": classes, "A": less, "x": take, "B": cells, "m": marks, "gs": send,
+            "c": lambda u: pm(pa, "idg", "v", u, True, False), "D": lambda u: pm(pa, "idk", "dead", u, False, True), "R": ready, "land": land, "turn": turn, "ti": listing,
             "j": judge, "w": mark, "f": fetch,
-            "S": lambda u: mm(pa[u], 0, cst[u], cols("one", u), ["one"] + [cst[u] + str(p) for p in (0, 32, 64, 96)], H[u], True, False),
             "G": lambda u: pm(pe, "idf", "v", u, True, False), "U": lambda u: pm(pe, "tr", "und", u, False, True),
-            "M": lambda u: cm(pq, "idb", "mk", u, True, False), "P": lambda u: pm(pq, "bdf", "kv", u, False, True),
+            "M": lambda u: mm(pq[u], 0, "ek", T.mk[0:16, 0:H[u]], ["mk"], H[u], True, False, lhs=T.ek[0:16, :]), "P": lambda u: pm(pq, "bdf", "kv", u, False, True),
             "T": lambda u: cm(pe, "idb", "two", u, True, False), "H": lambda u: pm(pe, "idb", h, u, False, True),
             "gk": lambda u: limits("gr", "gr%d" % u, OWN[u], u, 1),
-            "b": lambda u: ts(part("b", u), "b%d" % u, cols(pa[u], u), [pa[u], "thr"], 3.75, T.thr[:], A.add, A.max),
-            "a": lambda u: ts(cols(pa[u], u, M), "a%d" % u, cols(pa[u], u), [pa[u], "thr"], T.thr[:], None, A.max),
+            "a": lambda u: ts(cols(pa[u], u, M), "a%d" % u, cols(pa[u], u), [pa[u], "thr", "st" + cst[u]], T["st" + cst[u]][:], T.thr[:], A.add, A.max),
+            "e": wiped, "V": lambda u: pm(pa, "idf", "v", u, False, False),
             "u": lambda u: tt(part("und", u), "und%d" % u, cols(pa[u], u, M), part("b", u), [pa[u], "a%d" % u, "b%d" % u], A.is_lt),
-            "r": lambda u: tt(part("r2", u), "r2%d" % u, part("md", u), cols(pq[u], u), ["md%d" % u, pq[u]], A.max),
-            "n": lambda u: tt(part("vi", u) if last else own(u), vs[u], part("r2", u), cols(pa[u], u), ["r2%d" % u, pa[u]], A.max),
+            "n": lambda u: tt(part("vi", u) if last else own(u), vs[u], part("md", u), cols(pa[u], u), ["md%d" % u, pa[u]], A.max),
             "d": lambda u: act(part("dead", u), ["dead%d" % u, "cnt%d" % u], part("b", u), ["b%d" % u, "tb"], F.Sigmoid, scale=-32.0,
                                bias=T.tb[:], accum_out=T.cnt[:, u:u + 1]),
             "sk": lambda u: diagonal(pq[u], "sk", u), "sq": lambda u: diagonal(pf[u], "sq", u),
             "ks": lambda u: ts(listed("ks", u), "ks%d" % u, picked("sk", u), ["sk%d" % u], 1.0 / 2048, 16 - 2048 - HALF, A.mult, A.add),
             "si": lambda u: tt(listed("si", u), "si%d" % u, picked("sk", u), entries("ti", u, 0, 1), ["sk%d" % u, "ti%d" % u], A.max),
             "sa": lambda u: ts(listed("sa", u), keys("sa", u), listed("si", u), keys("si", u), 2047, None, A.bitwise_and),
-            "ls": lambda u: copy(listed("ls", u), keys("ls", u), listed("sa", u), keys("sa", u)),
+            "ls": lambda u: copy(listed("ls", u), keys("ls", u), listed("sa", u), keys("sk" if HYP else "sa", u)),
             "md": lambda u: tt(part("md", u), keys("md", u), T.rel0[:, 0:W].indirect(listed("ls", u)), part("dead", u),
                                ["rel0"] + keys("ls", u) + keys("dead", u), A.mult, GATHER),
-            "ku": lambda u: ts(part("ku", u), keys("ku", u), part("ti", u), keys("ti", u), 1.0 / 2048, -HALF, A.mult, A.add),
+            "ku": guards,
             "la": lambda u: ts(part("la", u), keys("la", u), part("ti", u), keys("ti", u), 2047, None, A.bitwise_and),
             "lu": lambda u: copy(part("lu", u), keys("lu", u), part("la", u), keys("la", u)),
             "hp": lambda u: act(part("hp", u), keys("hp", u), part(h, u), keys(h, u), bias=-0.5),
@@ -536,7 +570,7 @@ def rank_program(g, core, T, topo):
             "cu": lambda u: ts(listed("cu", u), keys("cu", u), picked("sq", u), keys("sq", u), -8.0 * O[u], None, A.add),
             "bl": lambda u: tt(part("bl", u), keys("bl", u), xp(u).indirect(listed("cu", u)), part("hp", u),
                                keys("x", u) + keys("cu", u) + keys("hp", u), A.add, GATHER),
-            "put": lambda u: tt(xp(u).indirect(listed("cu", u)), keys("x", u), part("bl", u), part("half", u),
+            "put": lambda u: tt(xp(u).indirect(listed("cu", u)), keys("x", u), part("bl", u), cols("half", u),
                                 keys("bl", u) + keys("cu", u) + ["half"], A.mult, SCATTER),
             "g": lambda u: act(cols(pf[u], u), pf[u], part(gs, u), [gs + str(u)], bias=-UP),
             "h": lambda u: ts(part("gm", u), keys("gm", u), part(h, u), keys(h, u), 2.0 - UP, None, A.add), "y": limits_out,
@@ -558,7 +592,9 @@ def rank_program(g, core, T, topo):
     for t in range(RO):
         for s in ((START + " " + ROUND0 if t == 0 else LATE + " " + ROUND) + " " + (END if t == RO - 1 else BLEND)).split():
             r, s = t + {"<": -1, ">": 1}.get(s[0], 0), s.lstrip("<>")
-            more = {"J": [c + s[1:] + str(j) for j in range(len(JUDGE[int(s[1:] == "1")])) for c in "jw"],
+            u = int(s[1:] == "1")
+            both = [c + s[1:] + str(j) for j in range(len(JUDGE[u])) for c in "jw"]
+            more = {"J": both[:2 * MP[u]] + [c + s[1:] for c in "AxBm"[:4 * (SL[u] > 0)]] + both[2 * MP[u]:],
                     "F": ["f%d" % j for j in range(len(FETCH)) if str(FETCH[j][0]) == s[1:]]}
             for s in more.get(s[0], [s]):
                 n = len(calls)
@@ -574,10 +610,13 @@ def rank_program(g, core, T, topo):
                     else:
                         s += "'" * (i > n)
                         tags[(r, s)] = [i]
-    if not PLAN and ORDER:
+    SEEN.update(calls=calls, tags=tags, ahead=ahead)
+    if PLAN[:1] == [None]:
+        PLAN[:] = range(len(calls))
+    if not PLAN:
         PLAN.extend(range(ahead))
         for t in range(RO):
-            for s in (FIRST if t == 0 else LAST if t == RO - 1 else ORDER).split():
+            for s in ORDERS[t if len(ORDERS) == RO else min(t, 1) + (t == RO - 1)].split():
                 PLAN.extend(tags[(t + {"<": -1, ">": 1}.get(s[0], 0), s.lstrip("<>"))])
     if not PLAN:
         PLAN.extend(arrange([c[:6] for c in calls], ahead))

@@ -6,161 +6,71 @@ WX = 1792
 W = 2048
 RO = 4
 NC = (8, 6)
-JUDGE = [[7, 12, 16], [8, 12, 14, 16]]
+SL = (4, 4)
+SX = (2, 4)
+JUDGE = [[8, 12, 16], [8, 12, 14, 16]]
 VL = (12, 8)
-FETCH = [(0, 0, 5), (0, 5, 10), (0, 10, 16), (1, 0, 6), (1, 6, 11), (1, 11, 16)]
-OWN = (2, 2)
-SL = (3, 4)
-KD = (0, 0)
-HYP = 0
 MP = (1, 1)
-CB = "pq1"
-KV = "vv"
-START = "pads half ka lima zz cst kb limb nbk tr idf idg big mk th na nb va vb bdf xg gr2 ids cc bw c8"
-LATE = ""
-ROUND = "F0 F1 G0 G1 M0 M1 J0 J1 b0 a0 u0 d0 U0 kv0 P0 sk0 ks0 gs0 b1 a1 u1 d1 U1 kv1 P1 sk1 ks1 gs1 si0 sa0 ls0 md0 c0 E0 e0 V0 D0 n0 si1 sa1 ls1 md1 c1 E1 e1 V1 D1 n1"
-BLEND = "turn0 ti0 ku0 la0 lu0 turn1 ti1 ku1 la1 lu1 R0 land0 sq0 cu0 hp0 bl0 put0 T0 H0 gr0 gj0 gk0 R1 land1 sq1 cu1 hp1 bl1 put1 T1 H1 gr1 gj1 gk1 C tb thr"
-ROUND0 = ROUND
-FILL = "v"
-FILLX = "g"
-LOADS = "glxnr"
+FETCH = [(0, 0, 5), (0, 5, 10), (0, 10, 16), (1, 0, 7), (1, 7, 12), (1, 12, 14), (1, 14, 16)]
+FV = ((6,), (), (), (6,))
+OWN = (1, 1)
+OWN0 = (4, 1)
+KD = (0, 1)
+NI = (1, 1)
+TB = 1
+GFILL = "csa tb two pad0a pad0b pad1a pad1b idh idk xz zv gnb idn idp"
+CE = "gaaa"
+LOADS = "glx"
+AFTER = ["grd0"]
+START = "nam pads half ka lima zz onp cst kb limb nbk tr idf idg idq big mk th na nb va vb xg rel ids cc bw c8"
+ROUND = ("F0 F1 S0 S1 G0 G1 M0 M1 J0 J1 b0 u0 dv0 U0 kv0 kw0 P0 sk0 ks0 gs0 b1 u1 dv1 U1 kv1 kw1 P1 sk1 ks1 gs1 "
+         "N0 Q0 sw0 ls0 md0 c0 E0 e0 V0 D0 n0 N1 Q1 sw1 ls1 md1 co1 Do1 Eo1 ro1 no1")
+BLEND = ("nf0 turn0 ku0 la0 lu0 nf1 turn1 ku1 la1 lu1 R0 land0 sq0 cu0 hp0 bl0 put0 T0 H0 gr0 gj0 gk0 "
+         "R1 land1 sq1 cu1 hp1 bl1 put1 T1 H1 gr1 gj1 gk1 dc0 dc1 C tb")
 END = "g0 h0 y0 g1 h1 y1 k0 l0 og0 on0 k1 l1 og1 on1"
-FIRST = ".ip cst' zz'' cst .ones pads'' .c1 pads' .c2 .c5 .c6 .ff .g16 pads''' .c3 cst'''' .rc .f cst'' .c4 pads zz .fk1 .par0 .par1 .a2 mk'' .fk0 .t16 .idb .bd cst'''''' cst'''''''' .a11 ids .a10 .bdx cc'''' lima''' lima' limb''' limb'' lima'' limb'''' lima cc''' gr2 rs limb ka' .a31 kb .a30 cst''''' ka .sel0 kb' zz' .sel1 ka'' nbk mk' mk xg j00 j02 na j01 j03 na' kb'' tr xg' mq tr' bdf limb' w00 idf w02 w01 w03 M1 na'' cst''' cc' nb' S0 w00' w01' w02' w03' j10 va cst''''''' j11 vb b0 a0 S1 j12 u0 j13 cc'' nb zz''' w13 f0 w10 f2 w11 w12 f1 d0 w10' M0 G0 G1 U0 w11' w12' w13' kv0 nb'' .pada cc c8 .wd a1 b1 na''' P0 sk0 nb''' u1 .wc si0 ks0 ids' ids'' .padb f3 f5 f4 d1 U1 sa0 gs0 kv1 ls0 mq' D0 c0 P1 T0 E0 gs0' md0 sk1 c8' c8'' bw' ks1 si1 r0 gs1 n0 bw sa1 turn0' ls1 gs1' bw'' turn0 md1 ti0 la0 R0 R1 D1 c1 E1 r1 ku0 lu0 n1 H0 land0 land1 T1 H1 gr0 sq0 turn1 sq1 turn1' cu0 cu1 gr1 ti1 hp1 hp0 gj0 gj0' bl1 bl0 la1 put1 put0 >S1 >M1 C >S0 gk0 >f2 >G1"
-ORDER = "<ku1 <lu1 j00 R1 j01 <tb <gj1' <gj1 f1 f0 w00 w01 j02 j03 <thr w02 w03 <gk1 <gk1' j10 w10 w00' M0 w01' w02' w03' G0 R0 w10' j11 w11 w11' j12 a0 b0 j13 u0 w13 w12 w12' U0 w13' kv0 P0 b1 a1 u1 sk0 U1 c0 si0 ks0 kv1 sa0 gs0 ls0 gs0' P1 f3 f4 d0 f5 D0 E0 d1 sk1 md0 ks1 r0 gs1 si1 n0 gs1' sa1 turn0 turn0' ls1 ti0 md1 T0 c1 D1 E1 >S0 H0 T1 land0 la0 r1 ku0 lu0 n1 gr0 sq0 turn1 turn1' cu0 land1 H1 sq1 gr1 ti1 cu1 hp0 hp1 gj0 gj0' bl0 la1 bl1 put0 put1 >M1 >S1 gk0 C >f2 >G1"
-LAST = "<ku1 <lu1 j01 <gj1' <tb <thr <gj1 f1 f0 w01 j00 w00 G0 <gk1' <gk1 j02 j03 j10 w02 w03 w00' w01' M0 w02' w03' w10 w10' j11 j12 w11 a0 b0 w11' j13 u0 w12 U0 w12' w13 w13' d0 f3 f5 f4 kv0 P0 a1 b1 sk0 u1 U1 D0 E0 si0 ks0 sa0 kv1 P1 c0 ls0 gs0 gs0' md0 sk1 ks1 r0 si1 gs1 gs1' g0 d1 c1 D1 E1 sa1 n0 ls1 l0 md1 k0 on0 r1 h0 og0 n1 y0 k1 l1 g1 y0' og1 h1 on1 y1 y1'"
 ORDERS = [
-    ".ff .ones zz th' .ip pads' half pads .bd .a11 .a10 .c5 .c4 pads''' pads'' .idb cst .rc1 .rc0 .g16 cst' .bdx .fk1 .fk0 .par0 zz'' ids .par1 xg .a30 .a31 big kb ka' lima''' lima lima'' A0 .sel0 A1 lima'''' ka kb' limb' limb'' lima' cst''' .sel1 zz''' ka'' zz' limb''' limb cst'''' kb'' cst'' x0 j00 nbk na' B0 na j01 nb' gr2 x1 B1 w00 idg idf m0 na'' xg' j02 w01 w00' j10 m0' f0 w01' j11 m1 w02 j12 j13 w10 va tr mk w02' w11 b0 vb w10' a0 tr' bdf f2 f1 w12 m1' cst''''' nb u0 mk' w11' G0 w13 nb'' vb' w12' U0 mk'''' .c6 w13' th kv0 f3 f5 G1 M0 na''' mk'' a1 P0 b1 .padb ids'' .pada M1 c0 u1 sk0 ids' mk''' U1 nb''' c1 .wc ks0 >M0 kv1 si0 gs0 .wd c8 P1 f4 d0 sa0 .padc E0 bw' d1 sk1 gs0' cc'' e0 ls0 bw cc' c8'' V0 ks1 md0 D0 R0 gs1 R1 n0 si1 cc c8' T0 turn0 turn0' gs1' T1 sa1 bw'' E1 ti0 ls1 e1 V1 la0 D1 md1 lu0 n1 ku0 land0 hp0 >f0 turn1' H0 land1 sq0 H1 C gr0 sq1 cu0 turn1 hp1 gr1 gj0 gj0' cu1 bl0 >A0 ti1 >f1 bl1 >G0 gk0 put0 >A1 put1 >G1 la1 ku1 gj1' gj1 gk0'",
-    "x0 j00 <gk1 x1 j01 B0 B1 <lu1 j10 <thr <tb w00 w00' j02 M1 m0 w01 j12 m1 w10 w02 m0' j11 w01' f2 j13 w02' w11 w10' m1' b0 w12 a0 w11' w13 u0 w12' w13' f3 f5 R1 U0 c0 a1 b1 R0 kv0 u1 f4 P0 U1 c1 d0 sk0 T0 kv1 d1 si0 >M0 ks0 P1 sa0 E0 gs0 sk1 e0 ls0 V0 gs0' ks1 md0 D0 T1 si1 gs1 n0 gs1' sa1 E1 e1 turn0 turn0' V1 ls1 D1 ti0 md1 hp0 H0 land0 la0 n1 gr0 lu0 land1 sq0 gj0 hp1 gj0' H1 C turn1' ku0 cu0 turn1 sq1 gr1 gk0 bl0 cu1 >A0 ti1 >A1 >f1 bl1 gk0' put0 >G0 put1 >G1 la1 ku1 gj1' gj1 >f0",
-    "j01 x0 <gk1 x1 j00 B0 w01 B1 w00 j10 j02 m0 w00' <thr j11 w02 f2 m0' w01' j12 w11 j13 w02' w10 R0 m1 a0 b0 w10' w13 <tb u0 m1' d0 <lu1 w12 M1 U0 w11' kv0 w12' w13' P0 f3 f5 a1 b1 c0 sk0 E0 u1 f4 e0 si0 ks0 U1 V0 sa0 gs0 D0 d1 T0 kv1 c1 ls0 gs0' P1 md0 R1 T1 >M0 sk1 n0 ks1 C si1 turn0 gs1 sa1 turn0' gs1' ls1 land0 hp0 ti0 tb md1 thr H0 E1 la0 e1 sq0 V1 gr0 lu0 D1 >M1 cu0 ku0 >A0 gj0 gj0' bl0 >f0 n1 land1 gk0 put0 H1 >G0 sq1 turn1 hp1 gr1 cu1 turn1' >f2 gk0' bl1 >A1 ti1 >G1 put1 la1 ku1 gj1' gj1",
-    "j00 x0 <gk1 B0 j01 x1 w00 j10 j02 w00' m0 w01 B1 m0' j11 w02 w10 j12 <lu1 j13 w01' m1 w02' w12 w11 f1 w10' m1' a0 b0 w13 w11' u0 w12' w13' U0 c0 f5 f3 a1 b1 kv0 u1 P0 f4 U1 c1 sk0 d0 kv1 d1 si0 ks0 P1 sa0 E0 gs0 sk1 e0 ls0 V0 gs0' g0 ks1 md0 D0 gs1 si1 n0 gs1' g1 sa1 l0 E1 e1 ls1 k0 V1 on0 D1 md1 og0 h0 n1 y0 k1 l1 y0' h1 og1 on1 y1 y1'"]
-FIXED = {"v": 0.02, "a": 0.04, "t": 0.015, "g": 0.17}
-LEAST = {"v": 48, "a": 0, "t": 0, "g": 0}
-CYCLE = {"v": 0.00092, "a": 0.00092, "t": 0.00047, "g": 0.00092}
-ISSUE = {"s": 0.05, "a": 0.05, "g": 2.0}
-WAKE = 0.21
-FAR = 1.5
-GATHER, SCATTER, LAND, RATE, SEND, OPEN = 1.3, 2.6, 1.1, 420e3, 0.2, 1.0
-PASSES = 150
-SHAKE = 0.6
-SPAN = 6.0
-SEED = 1
+    ".ip .ones nam .ff half cst zz big .c5 .c4 c8 .a11 .a10 .bd .rc1 .rc0 cst' cst''' .g16 .fk0 .fk1 cc' pads .par0 .a30 ka .par1 .a31 rel .sel0 ka' lima lima'' lima' lima''' .idb .bdx .pad0b ids xg pads' th S1 kb cst'' .sel1 ka'' va zz' nbk limb onp idq idg x0 j00 S0 A1 A0 limb' limb'' kb' X0 na na' B0 kb'' mk'''' mk tr zz'' w00 j01 Y0 x1 w00' m0 B1 j10 na'' j02 w01 m0' w10 m1 zz''' vb w01' f1 f2 tr' mk'' .pad0a mk''' ids''' mk' ids'' .pad1b idf ids' w02 w10' w02' G0 m1' j11 j12 w11 tr'' b0 j13 u0 w11' dv0 f0 U0 w12 w13 nb' nb vb' w12' N1 M1 w13' kv0 nb'' M0 .hk1 b1 .hk0 .c6 P0 sk0 G1 c0 u1 cc dv1 ks0 >M0 .wc kw0 U1 gs0 co1 N0 kv1 kw1 Q0 gs0' bw' f3 f4 f6 P1 Q1 T1 sk1 sw0 .wd ks1 E0 f5 ls0 sw1 gs1 dc1 xg' xg'' gr0 dc0 hp0 e0 md0 V0 bw ls1 c8' D0 gs1' n0 md1 bw'' T0 R1 Do1 R0 turn0' turn0 nf0 ro1 Eo1 la0 ku0 no1 lu0 nf1 H0 land0 gr0' C C' hp1 turn1' gr1 land1 sq0 H1 gj0 turn1 >S0 C'' sq1 cu0 gk0 gr1' cu1 bl0 bl1 gk0' put0 put1 >G1 >S1 >G0 >f0 >f1 gj1 ku1 la1",
+    "x0 <gk1 j00 X0 x1 <gk1' j01 j02 A1 A0 B0 w00 Y0 j10 B1 m0 w01 <tb w00' m0' w02 j12 j11 w02' w01' w10 m1 f2 w10' w12 j13 m1' w11 w12' b0 <lu1 w13 w11' u0 dv0 w13' U0 b1 kv0 M1 N1 N0 u1 dv1 kw0 c0 P0 U1 sk0 Q0 T0 kv1 ks0 sw0 P1 gs0 E0 sk1 e0 ls0 kw1 gs0' V0 ks1 f4 f3 f6 f5 Q1 md0 D0 gs1 sw1 n0 gs1' nf0 ls1 >M0 co1 T1 turn0' turn0 md1 la0 R1 Do1 >S0 R0 ro1 ku0 land0 dc0 dc1 C' hp0 C hp1 H0 lu0 Eo1 sq0 gr0 >S1 no1 land1 gj0 nf1 cu0 H1 C'' >G0 turn1 >f0 >f1 sq1 gk0 bl0 cu1 turn1' gr1 bl1 gk0' put0 put1 >A1 >A0 >G1 ku1 la1 tb gj1",
+    "j00 x0 <gk1 X0 B0 <gk1' x1 Y0 w00 j02 j01 B1 m0 w00' w02 j10 w01 m1 j11 w10 m0' w02' w01' j12 m1' f2 w11 w11' w10' j13 b0 w12 w13 u0 w12' dv0 <lu1 w13' U0 f3 f6 f4 f5 b1 kv0 u1 dv1 kw0 N1 c0 N0 M1 P0 U1 T0 Q0 sk0 kv1 >M0 P1 ks0 sw0 gs0 E0 sk1 e0 ls0 kw1 V0 gs0' ks1 md0 Q1 D0 gs1 sw1 n0 gs1' nf0 ls1 turn0' turn0 co1 R0 T1 R1 Do1 >S0 md1 la0 ro1 ku0 H0 gr0 lu0 dc1 dc0 C' hp0 C hp1 gj0 land0 Eo1 >S1 sq0 no1 land1 nf1 cu0 H1 turn1' >f2 >f0 >G0 C'' gk0 sq1 bl0 cu1 turn1 gr1 bl1 gk0' put0 put1 ku1 la1 gj1",
+    "x0 j00 <gk1 A1 A0 G1 <tb X0 B0 x1 <gk1' Y0 w00 j02 j01 B1 m0 w00' w02 j10 w01 <lu1 j11 j12 m1 m0' w02' w10 w01' m1' w11 j13 f1 w10' w11' b0 w12 w13 u0 f3 w12' dv0 f4 f6 w13' U0 M1 N0 N1 c0 b1 kv0 u1 dv1 kw0 P0 U1 f5 sk0 Q0 co1 kv1 ks0 kw1 sw0 P1 gs0 Q1 E0 sk1 ls0 sw1 e0 gs0' ks1 V0 md0 gs1 D0 Do1 ls1 n0 gs1' g1 g0 md1 Eo1 l0 ro1 k0 on0 no1 og0 l1 k1 h0 on1 og1 h1 y0 y1 y0' y1'"]
+OLDER = [
+    ".ip .ones nam pads zz c8' cst c8 .c5 cc' .ff .c6 .c4 .rc0 .rc1 .g16 cst' th .bd .fk0 .a10 .par0 cst'' .par1 .a30 .pad0b .bdx cst''' .fk1 .a11 big rel .idb pads' .a31 ka .sel0 onp half S0 ka' nbk .wc zz' S1 kb ka'' ids lima''' limb lima' lima lima'' va .sel1 limb' idg idq mk'' j00 x0 A1 A0 mk .pad1b limb'' zz'' ids'' mk''' .pad0a X0 kb' B0 na' w00 kb'' Y0 na j01 x1 w00' m0 j10 B1 w01 na'' j02 m0' w10 w01' vb G0 zz''' w02 j11 f0 m1 f1 N0 w02' w10' tr mk'''' tr' j12 w11 b0 j13 w12 w11' m1' u0 tr'' d0 w13 w12' f2 nb vb' nb' U0 w13' .wd c0 kv0 b1 mk' M1 M0 nb'' P0 G1 .hk0 u1 d1 .hk1 f3 sk0 U1 bw kw0 ks0 cc idf ids''' xg co1 ids' bw' kv1 gs0 Q0 N1 f4 kw1 P1 T0 sw0 gs0' f6 Q1 f5 sk1 E0 ls0 sw1 ks1 e0 xg' md0 V0 ls1 gr0 gs1 D0 bw'' md1 gs1' n0 ro1 turn0 T1 R1 R0 turn0' nf0 Do1 >S1 la0 xg'' ku0 Eo1 hp0 C' C H0 lu0 land0 no1 gr1 gr0' land1 hp1 nf1 turn1 H1 sq0 gj0 turn1' sq1 gk0 C'' >S0 cu0 gr1' cu1 bl0 >A1 >A0 bl1 >f0 >f1 gj1 tb gk0' put0 >G0 >G1 put1 ku1 la1",
+    "x0 j00 <gk1 X0 B0 j01 j02 x1 <gk1' Y0 w00 B1 m0 j10 w00' w01 N0 m0' j12 w02 w12 j11 w10 w02' w01' m1 w10' f2 j13 w11 b0 <lu1 m1' w12' w11' w13 u0 d0 f6 f5 w13' U0 M1 b1 c0 M0 kv0 d1 u1 f3 kw0 P0 U1 Q0 N1 T0 sk0 kv1 ks0 sw0 P1 f4 E0 gs0 sk1 e0 ls0 V0 kw1 gs0' ks1 md0 D0 Q1 gs1 T1 co1 n0 sw1 gs1' nf0 R1 R0 Do1 turn0 ls1 turn0' >S0 md1 la0 hp0 H0 ro1 land0 lu0 Eo1 gr0 sq0 ku0 gj0 land1 no1 C hp1 C' H1 >S1 cu0 >A0 gk0 nf1 sq1 gr1 turn1 C'' cu1 bl0 gk0' turn1' >A1 >G0 >G1 bl1 >f1 >f0 put0 put1 tb gj1 gk1 gk1'",
+    "x0 <la1 <ku1 j00 X0 B0 x1 j02 j01 Y0 w00 B1 m0 w00' w01 N0 w02 w02' m0' m1 w01' j10 j11 j12 w10 j13 w11 f2 m1' w12 b0 w10' w12' w11' <lu1 w13 d0 u0 f6 f5 w13' U0 M1 c0 M0 b1 kv0 u1 d1 kw0 f3 P0 U1 sk0 Q0 N1 kv1 ks0 sw0 P1 gs0 E0 sk1 f4 e0 ls0 kw1 gs0' V0 ks1 md0 Q1 D0 gs1 T0 >M0 sw1 co1 Do1 n0 gs1' nf0 ls1 turn0' turn0 R0 T1 >S0 md1 R1 hp0 C' C la0 H0 land0 ro1 ku0 Eo1 gr0 lu0 >S1 sq0 gj0 no1 land1 hp1 nf1 H1 cu0 >f2 >f0 >G0 gk0 turn1' sq1 bl0 C'' cu1 gr1 turn1 gk0' >A0 bl1 put0 >A1 put1 ku1 la1 tb gj1",
+    "j00 x0 M1 G1 <gk1 X0 B0 j02 j01 x1 <gk1' Y0 w00 B1 m0 j10 w00' w01 w02 m0' N0 j11 w10 w02' m1 j12 w01' w11 w10' f1 j13 w11' m1' w12 b0 w13 <lu1 u0 w12' d0 w13' f4 f6 U0 b1 N1 c0 kv0 d1 u1 f3 kw0 P0 U1 Q0 sk0 co1 kv1 f5 kw1 ks0 sw0 P1 Q1 E0 gs0 sk1 e0 ls0 sw1 V0 gs0' ks1 md0 D0 Do1 gs1 ls1 n0 gs1' g1 g0 md1 k0 l0 ro1 og0 Eo1 on0 no1 h0 l1 y0 k1 y0' on1 h1 og1 y1 y1'"]
+OLD = [
+    ".ip .ones cst zz rel .ff half .c5 big .rc1 .rc0 .g16 .c4 .a11 .fk1 .fk0 .bd .idb .a10 .par0 .a31 .par1 pads .a30 .bdx zz'' ids .sel1 .hk0 .sel0 cst' onp ka kb ka' k8 lima' lima'' lima''' lima limb' ka'' nbk zz' zz''' va A0 j00 x0 limb tr idf limb'' G0 A1 S0 G1 kb' na' w00 B0 mk'' cst'' kb'' j01 na x1 j10 m0 w00' B1 na'' w01 j02 S1 m0' j13 w02 m1 w10 w01' j11 f1 f0 w02' w10' j12 b0 mk''' mk mk' tr' pads' th w11 m1' M1 w12 mk'''' xg ids''' idg ids'' w11' w13 tr'' u0 d0 .hk1 nb' vb' w12' f2 w13' U0 N0 nb vb b1 kv0 M0 ids' .padc cc nb'' P0 kw0 u1 c8 sk0 d1 c8' f3 Q0 U1 c0 co1 N1 ks0 .c6 kw1 gs0 kv1 sw0 .wd gs0' P1 Q1 >M0 f4 f6 .wc sk1 ls0 sw1 E0 ks1 md0 e0 f5 .pada gs1 V0 cc' gr0 bw c8'' bw' ls1 D0 gs1' .padb n0 onn idq md1 turn0 xg'' xg' R0 R1 turn0' ro1 ti0 bw'' la0 ku0 T1 T0 Do1 Eo1 hp0 hp1 H0 land0 no1 gr0' land1 lu0 sq0 gr1 gj0 turn1 >f0 >f1 sq1 cu0 turn1' gk0 cu1 bl0 >S1 H1 >S0 gr1' bl1 >G0 gk0' put0 put1 ku1 ti1 >A0 C >A1 >G1 gj1",
+    "x0 j01 <gk1 B0 x1 j00 <gk1' w01 j02 w00 B1 m0 w00' m0' j10 w02 j11 j12 <la1 j13 <lu1 w11 <tb w10 m1 w01' f2 w02' w10' b0 m1' w12 w13 w11' d0 u0 f6 w12' f5 w13' U0 b1 kv0 N0 c0 u1 d1 kw0 P0 U1 sk0 M1 N1 Q0 kv1 f4 f3 ks0 sw0 P1 E0 gs0 sk1 e0 ls0 kw1 V0 gs0' ks1 md0 D0 Q1 gs1 n0 sw1 gs1' turn0 T1 R0 co1 R1 T0 Do1 >M0 >S0 ls1 turn0' md1 ti0 ro1 land0 hp0 la0 ku0 H0 >S1 sq0 gr0 cu0 lu0 land1 gj0 hp1 bl0 Eo1 H1 sq1 >A0 gk0 no1 gr1 cu1 put0 gk0' bl1 turn1 turn1' C >G0 put1 ku1 >G1 >f0 gj1 >f1",
+    "x0 j00 <tb w00 A1 B0 <gk1 x1 <gk1' w00' m0 B1 j01 w01 j10 j02 j12 w02 <ti1 m0' j11 <la1 w01' w10 m1 w02' j13 f2 w11 w10' <lu1 b0 w12 w13 m1' w11' d0 u0 f6 w12' f5 w13' U0 N0 M1 c0 b1 kv0 d1 u1 kw0 f3 P0 N1 U1 Q0 sk0 co1 kv1 f4 ks0 sw0 >M0 P1 E0 gs0 e0 sk1 ls0 kw1 gs0' ks1 md0 V0 D0 Q1 R0 gs1 n0 sw1 gs1' turn0' ls1 >S0 T1 T0 Do1 turn0 md1 ti0 ro1 R1 land0 hp0 la0 H0 sq0 Eo1 gr0 lu0 land1 hp1 cu0 ku0 gj0 no1 sq1 >S1 H1 >G0 bl0 gk0 turn1 cu1 turn1' gr1 bl1 >f2 >f0 gk0' put0 put1 >A0 ku1 ti1 gj1 C >G1 >A1",
+    "j00 x0 <gk1 j02 <la1 j01 x1 w00 <tb <gk1' B0 B1 m0 w00' w01 m0' M1 N0 j10 w10 w01' m1 f1 j11 w02 w02' j13 j12 w11 w10' b0 m1' <lu1 w11' w12 w13 d0 u0 f4 w12' f6 w13' U0 c0 b1 kv0 u1 d1 kw0 f3 P0 U1 N1 sk0 Q0 co1 kv1 kw1 ks0 sw0 P1 f5 Q1 E0 gs0 sk1 e0 ls0 V0 sw1 gs0' ks1 md0 g0 D0 Do1 gs1 ls1 n0 gs1' md1 k0 l0 ro1 og0 on0 Eo1 h0 no1 y0 l1 k1 g1 y0' on1 h1 og1 y1 y1'"]
 HALF = 1023.5 / 2048
-BIG = 2.0 ** 22
+FLAG = 2.0 ** 15
+LOW = -2.0 ** 25
 HUGE = 1.5 * 2.0 ** 48
 EIGHT = 1.5 * 2.0 ** 26
-KILO = 1.5 * 2.0 ** 33
+TWO = 1.5 * 2.0 ** 24
 UP = 144.0
 M = 128
 TOP = 4096.0
 
-SB = "sbuf"
 BF, F32, F16, I32, U16 = "bfloat16", "float32", "float16", "int32", "uint16"
-SCRATCH = {
-    "x": (SB, [128, 16 + WX], BF), "x0": (SB, [128, WX], BF), "lim0": (SB, [128, I], BF),
-    "grd0": (SB, [128, 256], I32), "nam0": (SB, [128, 256], I32), "grd0t": (SB, [128, 512], I32), "nam0t": (SB, [128, 512], I32), "rel0": (SB, [128, W], I32),
-    "u": (SB, [128, 16 * I], BF), "w": (SB, [128, 16 * I], BF), "wv": (SB, [128, 16 * I], F16), "nb": (SB, [128, 16 * I], F32),
-    "ku": (SB, [128, I], U16), "lu": (SB, [128, I], U16), "tp": (SB, [128, 512], F32),
-    "v": (SB, [128, 272], F32), "ti": (SB, [128, I], I32), "la": (SB, [128, I], I32), "vi": (SB, [128, I], I32),
-    "gj": (SB, [128, 1536], F32), "gr": (SB, [128, I], BF), "gm": (SB, [128, I], BF), "hp": (SB, [128, I], F32),
-    "b": (SB, [128, I], BF), "und": (SB, [128, I], BF), "dead": (SB, [128, I], BF),
-    "kv": (SB, [128, I], F32), "r2": (SB, [128, I], F32), "sk": (SB, [128, I], F32), "sq": (SB, [128, I], F32),
-    "ks": (SB, [128, 14], U16), "ls": (SB, [128, 14], U16), "cu": (SB, [128, 14], U16), "sel": (SB, [128, 14], U16),
-    "si": (SB, [128, 14], I32), "sa": (SB, [128, 14], I32), "bl": (SB, [128, I], BF), "half": (SB, [128, M], BF),
-    "md": (SB, [128, I], F32), "mo": (SB, [128, I], F32), "cnt": (SB, [128, 2], F32), "tb": (SB, [128, 1], F32), "thr": (SB, [128, 1], F32), "kc": (SB, [128, 2], BF),
-    "ip": (SB, [128, 1], I32), "c1": (SB, [128, 1], I32), "c2": (SB, [128, 1], I32), "c3": (SB, [128, 1], I32), "c4": (SB, [128, 1], I32),
-    "c5": (SB, [128, 1], I32), "c6": (SB, [128, 1], I32), "par": (SB, [128, 2], F32),
-    "g16": (SB, [128, 1], F32), "wc": (SB, [128, 1], F32), "wd": (SB, [128, 1], F32), "wn": (SB, [128, 1], F32), "rc": (SB, [128, 2], F32),
-    "ff": (SB, [128, 14], F32), "f": (SB, [128, 14], F32), "fk": (SB, [128, 14], I32), "a1": (SB, [128, 14], F32), "a2": (SB, [128, 14], F32),
-    "a3": (SB, [128, 14], F32),
-    "ek": (SB, [128, M], BF), "t8": (SB, [128, I], BF), "mk": (SB, [128, M], BF), "mq": (SB, [128, I], BF), "rs": (SB, [128, M], BF),
-    "cc": (SB, [128, M], BF), "two": (SB, [128, M], BF), "c8": (SB, [128, M], BF),
-    "one": (SB, [128, M], BF), "ones": (SB, [128, 128], BF), "onp": (SB, [128, 128], F32), "onn": (SB, [128, 128], F32), "idb": (SB, [128, 128], BF),
-    "idn": (SB, [128, 128], BF), "idf": (SB, [128, 128], F32), "idg": (SB, [128, 128], F32), "bdf": (SB, [128, 128], F32),
-    "idh": (SB, [128, 128], BF), "idk": (SB, [128, 128], BF), "big": (SB, [128, 512], BF), "idm": (SB, [128, 128], BF), "id4": (SB, [128, 128], BF), "bd": (SB, [128, 128], BF),
-    "nbk": (SB, [128, 128], BF), "low": (SB, [128, 128], BF), "tr": (SB, [128, 128], BF), "trn": (SB, [128, 128], BF),
-    "bw": (SB, [128, 128], BF), "bn": (SB, [128, 128], BF),
-    "so0": (SB, [128, 1], F32), "so1": (SB, [128, 1], F32), "st0": (SB, [128, 1], F32), "st1": (SB, [128, 1], F32), "sb0": (SB, [128, 1], F32), "sb1": (SB, [128, 1], F32),
-    "zz": (SB, [128, 144], BF), "zv": (SB, [128, 144], BF),
-    "on": (SB, [128, I], F32), "og": (SB, [128, I], F32), "ol": (SB, [128, I], BF),
-}
-for _t in range(RO):
-    SCRATCH["gs%d" % _t] = (SB, [128, I], BF)
-    SCRATCH["h%d" % _t] = (SB, [128, I], BF)
+SCRATCH = {}
+for _d, _n, _names in (
+        (BF, 16 + WX, "x x0"), (I32, W, "rel0"), (I32, 32 + 2 * I, "gn"), (I32, 512, "grd0t nam0t"),
+        (BF, 16 * I, "u w"), (F16, 16 * I, "wv"), (F32, 16 * I, "nb"), (F32, 512, "tp"), (F32, 272, "v"), (F32, 1536, "gj"),
+        (BF, I, "lim0 gr gm b und dead kw bl ol t8 mq gs0 gs1 gs2 gs3 h0 h1 h2 h3"), (F16, I, "kv k8"), (U16, I, "ku lu"), (I32, I, "ti la"), (I32, 272, "vi"), (I32, 512, "tq"),
+        (F32, I, "hp sk sw sq md r2 mo on og"), (U16, 14, "ks ls cu sel"), (F32, 14, "ff a1 a3"), (I32, 14, "fk"),
+        (F32, 2, "cnt par rc hk"), (BF, 1, "kc"), (BF, 4, "cb"), (BF, M, "lane"), (F16, M, "csa cs0 cs1"), (I32, 1, "ip c4 c5 c6"), (F32, 1, "tb g16 wc wd wn"),
+        (BF, M, "half ek mk rs two c8 ones idb idn idh idk idp bd nbk low tr trn bw bn"), (F16, M, "ch"),
+        (F32, M, "onp idf idg idq"), (BF, 144, "zz zv"), (BF, 512, "big"), (BF, 226, "up")):
+    for _b in _names.split():
+        SCRATCH[_b] = ("sbuf", [128, _n], _d)
 PSUM = ("pa0", "pa1", "pe0", "pe1", "pf0", "pf1", "pq0", "pq1")
 for _b in PSUM:
     SCRATCH[_b] = ("psum", [128, 512], F32)
 
-SEMAPHORES = ["cv", "ca", "ct", "cg", "sent", "d_x", "d_lim", "d_grd", "d_nam", "d_rel", "d_up", "d_on", "d_og", "d_ol", "d_m0", "d_m1"]
+SEMAPHORES = ["cv", "ca", "ct", "cg", "sent", "d_x", "d_lim", "d_grd", "d_nam", "d_rel", "d_up", "d_fill", "d_on", "d_og", "d_ol", "d_m0", "d_m1"]
 SEMAPHORES += ["arr%d%d" % (_t, _u) for _t in range(RO) for _u in range(2)]
-
-
-def arrange(calls, ahead):
-    n = len(calls)
-    before, after, wrote, seen = [{} for _ in calls], [{} for _ in calls], {}, {}
-    for i, (q, reads, writes, busy, late, size) in enumerate(calls):
-        for j in [wrote[k] for k in reads + writes if k in wrote] + [j for k in writes for j in seen.get(k, [])]:
-            before[i][j] = after[j][i] = 0.0 if q == calls[j][0] == "t" else WAKE
-        for k in reads:
-            seen.setdefault(k, []).append(i)
-        for k in writes:
-            wrote[k], seen[k] = i, []
-    banks = [sorted(set(k for k in c[1] + c[2] if k in PSUM)) for c in calls]
-
-    def room(taken, at, length, gap, q):
-        for a, b, o in taken:
-            if a - gap >= at + length:
-                break
-            if o != q and at < b + gap:
-                at = b + gap
-        return at
-
-    def lay(rank, back):
-        need, give = (after, before) if back else (before, after)
-        taken, start, end = {}, [0.0] * n, [0.0] * n
-        left = [len(b) for b in need]
-        ready = [i for i in range(n) if not left[i]]
-        while ready:
-            i = min(ready, key=lambda j: rank[j])
-            ready.remove(i)
-            q, busy, late, size = calls[i][0], calls[i][3], calls[i][4], calls[i][5]
-            at, was = max([0.0] + [end[j] + w for j, w in need[i].items()]) + (late + size / RATE if back else 0.0), -1.0
-            while at != was:
-                was = at
-                at = room(taken.get(q, []), at, busy, 0.0, None)
-                for k in banks[i]:
-                    at = room(taken.get(k, []), at, busy, WAKE, q)
-            start[i], end[i] = at, at + busy
-            if not back:
-                end[i] += late
-            if size and not back:
-                end[i] = room(taken.get("dma", []), end[i], size / RATE, 0.0, None) + size / RATE
-                taken["dma"] = sorted(taken.get("dma", []) + [(end[i] - size / RATE, end[i], q)])
-            for k in [q] + banks[i]:
-                taken[k] = sorted(taken.get(k, []) + [(at, at + busy, q)])
-            for j in give[i]:
-                left[j] -= 1
-                if not left[j]:
-                    ready.append(j)
-        return start, end
-
-    def better(rank):
-        start, end = lay(rank, False)
-        plain = max(end), start
-        start, end = lay([-e for e in end], True)
-        start, end = lay([i - 1e9 if i < ahead else -end[i] for i in range(n)], False)
-        return min(plain, (max(end), start))
-
-    best, seed = better(list(range(n))), SEED
-    for k in range(PASSES):
-        rank = []
-        for i in range(n):
-            seed = (seed * 1103515245 + 12345) % 2 ** 31
-            near = abs(best[1][i] - best[0] * (k * 0.618 % 1)) < SPAN
-            rank.append(i - 1e9 if i < ahead else best[1][i] + near * SHAKE * seed / 2 ** 31)
-        best = min(best, better(rank))
-    return sorted(range(n), key=lambda i: (best[1][i], i))
-
-
 PLAN = []
 SEEN = {}
 
@@ -207,20 +117,20 @@ def rank_program(g, core, T, topo):
 
     calls = []
 
-    def op(q, reads, writes, fn, cycles, also=()):
+    def op(q, reads, writes, fn):
         writes = writes if isinstance(writes, list) else [writes]
 
         def issue():
-            waits(q, reads + list(also), writes)
+            waits(q, reads, writes)
             ins = fn(queue[q])
             count[q] += 1
             ins.then_inc(T.sem["c" + q], 1)
             snap = dict(known[q])
             snap["c" + q] = count[q]
-            note((q, "c" + q, count[q], snap), reads + list(also), writes)
-        calls.append((q, reads, writes, FIXED[q] + max(LEAST[q], cycles) * CYCLE[q], 0.0, 0, issue, list(also), None))
+            note((q, "c" + q, count[q], snap), reads, writes)
+        calls.append((q, reads, writes, issue, [], None))
 
-    def load(q, sem, out, in_, reads, writes, size, whole=(), **kw):
+    def load(q, sem, out, in_, reads, writes, whole=(), **kw):
         def issue():
             waits(q, reads, writes)
             queue[q].dma_start(out, in_, **kw).then_inc(T.sem[sem], 16)
@@ -231,46 +141,47 @@ def rank_program(g, core, T, topo):
             if whole and dcount[sem] % (16 * len(whole)) == 0:
                 for k in whole:
                     wrote[k] = wrote[writes[0]]
-        calls.append((q, reads, writes, ISSUE[q], LAND, size, issue, [], sem if whole else None))
+        calls.append((q, reads, writes, issue, [], sem if whole else None))
 
-    def copy(out, okey, in_, ikeys, per=1.0):
-        op("v", ikeys, okey, lambda e: e.tensor_copy(out, in_), per * out.shape[1])
+    def copy(out, okey, in_, ikeys):
+        op("v", ikeys, okey, lambda e: e.tensor_copy(out, in_))
 
-    def ts(out, okey, in_, ikeys, s1, s2, op0, op1=None, per=1.0):
+    def ts(out, okey, in_, ikeys, s1, s2, op0, op1=None):
         if op1 is None:
-            op("v", ikeys, okey, lambda e: e.tensor_scalar(out, in_, s1, None, op0), per * out.shape[1])
+            op("v", ikeys, okey, lambda e: e.tensor_scalar(out, in_, s1, None, op0))
         else:
-            op("v", ikeys, okey, lambda e: e.tensor_scalar(out, in_, s1, s2, op0, op1), per * out.shape[1])
+            op("v", ikeys, okey, lambda e: e.tensor_scalar(out, in_, s1, s2, op0, op1))
 
-    def tt(out, okey, a, b, ikeys, o, per=1.0):
-        op("v", ikeys, okey, lambda e: e.tensor_tensor(out, a, b, o), per * b.shape[1])
+    def tt(out, okey, a, b, ikeys, o):
+        op("v", ikeys, okey, lambda e: e.tensor_tensor(out, a, b, o))
 
-    def act(out, okey, in_, ikeys, f=F.Copy, per=1.0, more=0, **kw):
-        op("a", ikeys, okey, lambda e: e.activation(out, in_, f, **kw), per * out.shape[1] + more)
+    def act(out, okey, in_, ikeys, f=F.Copy, **kw):
+        op("a", ikeys, okey, lambda e: e.activation(out, in_, f, **kw))
 
-    def mm(bank, a, lkey, rhs, rkeys, n, start, stop, lhs=None):
-        op("t", [lkey] + rkeys, bank, lambda e: e.matmul(T[bank][:, a:a + n], T[lkey][:] if lhs is None else lhs, rhs, start, stop),
-           max(64, n) * (4 if SCRATCH[lkey][2] == F32 else 1))
+    def mm(bank, a, lkey, rhs, rkeys, start, stop, lhs=None):
+        op("t", [lkey] + rkeys, bank, lambda e: e.matmul(T[bank][:, a:a + rhs.shape[1]], T[lkey][:] if lhs is None else lhs, rhs, start, stop))
 
     def memset(ap, key, val):
-        op("v", [], key, lambda e: e.memset(ap, val), ap.shape[1])
+        if (key[0] if isinstance(key, list) else key) in GFILL.split():
+            op("g", [], key, lambda e: e.iota(ap, [[0, ap.shape[1]]], int(val), 0, allow_small_or_imprecise_dtypes=True))
+        else:
+            op("v", [], key, lambda e: e.memset(ap, val))
 
     def fill(name, val):
-        op("v", [], name, lambda e: e.memset(T[name][:], val), T[name].shape[1] / 2)
+        memset(T[name][:], name, val)
 
     def times(name, src, by):
+        if name in GFILL.split():
+            return select(name, src, [[-1, 128]], A.not_equal, by, 0, 1)
         keys_, by = ([src, by], T[by][:]) if isinstance(by, str) else ([src], by)
-        if FILL == "a" or SCRATCH[name][2] == F32:
-            act(T[name][:], name, T[src][:], keys_, scale=by)
-        else:
-            ts(T[name][:], name, T[src][:], keys_, by, None, A.mult, per=0.5)
+        ts(T[name][:], name, T[src][:], keys_, by, None, A.mult)
 
     def select(name, src, pattern, cmp, fill_, base, mult, rows=128):
         n = T[name].shape[1]
-        op("g", [src], name, lambda e: e.affine_select(T[name][0:rows, :], T[src][0:rows, 0:n], pattern, cmp, fill_, base, mult), 2 * n)
+        op("g", [src], name, lambda e: e.affine_select(T[name][0:rows, :], T[src][0:rows, 0:n], pattern, cmp, fill_, base, mult))
 
     def iota(name, pattern, mult, base=0, okeys=None):
-        op("g", [], okeys or name, lambda e: e.iota(T[name][:], pattern, base, mult, allow_small_or_imprecise_dtypes=True), 2 * T[name].shape[1])
+        op("g", [], okeys or name, lambda e: e.iota(T[name][:], pattern, base, mult, allow_small_or_imprecise_dtypes=True))
 
     H = [16 * n for n in NC] + [I]
     O = [0, H[0], 0]
@@ -305,98 +216,98 @@ def rank_program(g, core, T, topo):
     def listed(name, u):
         return T[name][:, O[u] // 16:(O[u] + H[u]) // 16]
 
+    def turned(name, u):
+        a = (2 * H[0] + 32) * u
+        return T[name][:, a:a + 2 * H[u] + 32].indirect(listed("sel", u))
+
     def pm(bank, lkey, name, u, start, stop):
-        mm(bank[u], 0, lkey, own(u) if name == "v" else part(name, u), [name + str(u)], H[u], start, stop)
+        mm(bank[u], 0, lkey, own(u) if name == "v" else part(name, u), [name + str(u)], start, stop)
 
     def cm(bank, lkey, name, u, start, stop):
-        mm(bank[u], 0, lkey, cols(name, u), [name], H[u], start, stop)
+        mm(bank[u], 0, lkey, cols(name, u), [name], start, stop)
 
-    def turn(u):
-        a, n = (2 * H[0] + 32) * u, H[u]
-        op("v", [vs[u]], "tp%d0" % u, lambda q: q.transpose(T.tp[:, a:a + n], own(u)), n)
-        op("v", [vs[u], "pada", "padb", "padc"], "tp%d1" % u,
-           lambda q: q.transpose(T.tp[:, a + n:a + 2 * n + 32], T.v[:, O[u] + 16 * u:O[u] + 16 * u + n + 32]), n + 32)
+    def masked(bank, name, a, u, start):
+        mm(bank[u], 0, "ek", T[name][0:16, a:a + H[u]], [name], start, False, lhs=T.ek[0:16, :])
 
-    def listing(u):
-        a = (2 * H[0] + 32) * u
-        copy(part("ti", u), "ti%d" % u, T.tp[:, a:a + 2 * H[u] + 32].indirect(listed("sel", u)), ["tp%d0" % u, "tp%d1" % u, "sel%d" % u], GATHER)
+    def first(name, u):
+        return part("gn", u, 16 + I * (name == "nam0"))
+
+    def turn(u, out, src, o, key, pads, okey=None):
+        a, n, okey = (2 * H[0] + 32) * u, H[u], okey or out
+        op("v", [key], okey + "%d0" % u, lambda q: q.transpose(T[out][:, a:a + n], T[src][:, o + 16:o + 16 + n]))
+        op("v", [key] + list(pads), okey + "%d1" % u, lambda q: q.transpose(T[out][:, a + n:a + 2 * n + 32], T[src][:, o:o + n + 32]))
 
     def guards(u):
-        a = (2 * H[0] + 32) * u
-        if KD[u]:
-            ts(part("ku", u), "ku%d" % u, T.tp[:, a:a + 2 * H[u] + 32].indirect(listed("sel", u)), ["tp%d0" % u, "tp%d1" % u, "sel%d" % u],
-               1.0 / 2048, -HALF, A.mult, A.add)
+        if KD[u] or NI[u]:
+            ts(part("ku", u), "ku%d" % u, turned("tq" if NI[u] else "tp", u), ["tp%d0" % u, "tp%d1" % u, "sel%d" % u], 1.0 / 2048, -HALF, A.mult, A.add)
         else:
-            ts(part("ku", u), keys("ku", u), part("ti", u), keys("ti", u), 1.0 / 2048, -HALF, A.mult, A.add)
+            ts(part("ku", u), "ku%d" % u, part("ti", u), ["ti%d" % u], 1.0 / 2048, -HALF, A.mult, A.add)
 
     def diagonal(bank, out, u):
-        op("v", [bank, "rs"], out + str(u), lambda e: e.tensor_tensor_scan(part(out, u), cols("rs", u), cols(bank, u), 0.0, A.mult, A.max), H[u])
+        op("v", [bank, "rs"], out + str(u), lambda e: e.tensor_tensor_scan(part(out, u), cols("rs", u), cols(bank, u), 0.0, A.mult, A.max))
 
-    def fetch(j):
+    def fetch(j, t):
         u, a, b = FETCH[j]
-        act(lanes("nb", u, a, b), "nb%d" % j, T.rel0[:, 0:W].indirect(entries("lu", u, a, b)), ["rel0", "lu%d" % u], per=GATHER)
+        (copy if j in FV[t] else act)(lanes("nb", u, a, b), "nb%d" % j, T.rel0[:, 0:W].indirect(entries("lu", u, a, b)), ["rel0", "lu%d" % u])
         for k in range(a, b):
             c = 16 * O[u] + H[u] * k
-            load("s", "d_m%d" % u, T.mo[k::16, O[u]:O[u] + H[u]], T.nb[k::16, c:c + H[u]], ["nb%d" % j], ["mo%d_%d" % (u, k)], 32 * H[u],
+            load("s", "d_m%d" % u, T.mo[k::16, O[u]:O[u] + H[u]], T.nb[k::16, c:c + H[u]], ["nb%d" % j], ["mo%d_%d" % (u, k)],
                  ["mo%d_%d" % (u, c) for c in range(16)])
 
     def double(u, n, m):
         a, ks = 768 * u, ["gj%d%d" % (u, c) for c in range(wide[u])]
         op("g", ks[:m], ks[n:n + m], lambda e: e.affine_select(T.gj[:, a + H[u] * n:a + H[u] * (n + m)], T.gj[:, a:a + H[u] * m],
-                                                               [[0, H[u] * m]], A.is_ge, 0.0, 0, 0), 2 * H[u] * m)
+                                                               [[0, H[u] * m]], A.is_ge, 0.0, 0, 0))
 
-    def limits(name, key, n, u, late=0):
-        for c in range(0 if late else n):
+    def copies(name, key, n, u):
+        for c in range(n):
             act(cols("gj", u, 768 * u + H[u] * c), "gj%d%d" % (u, c), part(name, u), [key], bias=-510.0)
-        while late and n < wide[u]:
+
+    def doubled(n, u):
+        while n < wide[u]:
             double(u, n, min(n, wide[u] - n))
             n += min(n, wide[u] - n)
 
-    def clip(u):
-        if KV[u] == "v":
-            ts(part("kv", u), "kv%d" % u, cols(pe[u], u), [pe[u]], -BIG, 0.0, A.add, A.max)
-        else:
-            act(part("kv", u), "kv%d" % u, cols(pe[u], u), [pe[u]], F.Relu, bias=-BIG)
-
-    def fetched(u):
-        mm(pa[u], 0, "idf", part("mo", u), ["mo%d_%d" % (u, k) for k in range(16)], H[u], False, False)
-
-    def wiped(u):
-        pm(pa, "idh", "und", u, False, False)
-        pm(pa, "idk", "und", u, False, False)
-
-    def classes(u):
-        ts(part("b", u), "b%d" % u, cols(pa[u], u), [pa[u], "thr", "sb" + cst[u]], T["sb" + cst[u]][:], T.thr[:], A.add, A.max)
+    def eights(u, t):
+        if t == 0 and " k8 " in START:
+            mm(pe[u], 0, "idb", part("k8", u), ["k8"], True, False)
+            return cm(pe, "idb", "c8", u, False, False)
+        cm(pe, "idb", "ch", u, True, False)
+        pm(pe, "idq", "v", u, False, False)
+        cm(pe, "idb", "c8", u, False, False)
 
     def deaths():
-        for n, (lkey, rhs, key) in enumerate((("onp", T.cnt[:, 0:1], "cnt0"), ("onp", T.cnt[:, 1:2], "cnt1"), ("idb", T.kc[:, 0:1], "kc0"),
-                                              ("idb", T.kc[:, 1:2], "kc1"), ("idn", T.kc[:, 1:2], "kc1"),
-                                              ("onn", T.cnt[:, 0:1], "cnt0"), ("onn", T.cnt[:, 1:2], "cnt1"))):
-            mm(CB, 2 * M, lkey, rhs, [key], 1, n == 0, n == 6)
-
-    def ready(u):
-        cm(pf, "idb", "c8", u, True, False)
-        mm(pf[u], 0, "ek", T.mq[0:16, O[u]:O[u] + H[u]], ["mq"], H[u], False, False, lhs=T.ek[0:16, :])
+        act(T.cb[:, 0:2], "cbp", T.cnt[:], keys("cnt", 2))
+        act(T.cb[:, 2:4], "cbn", T.cnt[:], keys("cnt", 2), scale=-1.0)
+        for n, (lkey, rhs, key) in enumerate((("ones", T.cb[:, 0:1], "cbp"), ("ones", T.cb[:, 1:2], "cbp"), ("idn", T.half[:, 0:1], "half"),
+                                              ("idb", T.kc[:], "kc"), ("idn", T.kc[:], "kc"),
+                                              ("ones", T.cb[:, 2:3], "cbn"), ("ones", T.cb[:, 3:4], "cbn"))):
+            mm(pq[1], 2 * M, lkey, rhs, [key], n == 0, n == 6)
 
     def limits_out(u):
         tt(part("ol", u), "ol%d" % u, part("gm", u), cols(pf[u], u), ["gm%d" % u, pf[u]], A.min)
-        load("a", "d_ol", part("yl", u), part("ol", u), ["ol%d" % u], ["yl%d" % u], 256 * H[u])
+        load("a", "d_ol", part("yl", u), part("ol", u), ["ol%d" % u], ["yl%d" % u])
 
-    inputs = {"g": ("s", "d_grd", part("grd0", 2, 16), T.grd[:], [], ["grd0"], 512 * I), "n": ("s", "d_nam", part("nam0", 2, 16), T.nam[:], [], ["nam0"], 512 * I),
-              "l": ("a", "d_lim", T.lim0[:], T.lim[:], [], ["lim0"], 256 * I), "x": ("s", "d_x", T.x0[:], T.xc[:], [], ["xc"], 256 * WX),
-              "r": ("s", "d_rel", T.rel0[:], T.rel[:], [], ["rel0"], 512 * W)}
+    def numbers_out(name, src, out, u):
+        copy(part(name, u), name + str(u), part(src, u), [src + str(u)])
+        load("s", "d_" + name, part(out, u), part(name, u), [name + str(u)], [out + str(u)])
+
+    inputs = {"g": ("s", "d_grd", first("grd0", 2), T.grd[:], [], ["grd0"]), "n": ("s", "d_nam", first("nam0", 2), T.nam[:], [], ["nam0"]),
+              "l": ("a", "d_lim", T.lim0[:], T.lim[:], [], ["lim0"]), "x": ("s", "d_x", T.x0[:, 16:16 + WX], T.xc[:], [], ["xc"]),
+              "r": ("s", "d_rel", T.rel0[:], T.rel[:], AFTER, ["rel0"])}
     for s in LOADS:
         load(*inputs[s])
     ahead = len(calls)
 
     iota("ip", [[0, 1]], 17)
     iota("ff", [[32, 14]], 0)
-    memset(T.ones[:], "ones", 1.0)
+    fill("ones", 1.0)
     select("bd", "ones", [[-16, 8], [0, 16]], A.is_ge, 0.0, 0, 1)
     select("bd", "bd", [[16, 8], [0, 16]], A.is_ge, 0.0, 15, -1)
     select("idb", "ones", [[-1, 128]], A.is_equal, 0.0, 0, 1)
-    for n, a in enumerate((0, 16 + H[0], 32 + I)):
-        memset(T.v[:, a:a + 16], "pad" + "abc"[n], 0.0)
+    for key, a in (("pad0a", 0), ("pad0b", 16 + H[0]), ("pad1a", 16 + H[0]), ("pad1b", 32 + I)):
+        if key != "pad1a" or NI[0] != NI[1]:
+            memset(T["vi" if NI[int(key[3])] else "v"][:, a:a + 16], [key] + ["pad1a"] * (key == "pad0b" and NI[0] == NI[1]), 0)
     ts(T.c5[:], "c5", T.ip[:], ["ip"], 15, None, A.bitwise_and)
     ts(T.c4[:], "c4", T.ip[:], ["ip"], 4, 1, A.arith_shift_right, A.bitwise_and)
     ts(T.c6[:], "c6", T.ip[:], ["ip"], 3, None, A.bitwise_and)
@@ -408,74 +319,81 @@ def rank_program(g, core, T, topo):
         ts(listed("a1", u), "a1%d" % u, T.ff[:, 0:NC[u]], ["ff"], 8.0 / (H[u] - 1), None, A.mult)
         tt(listed("a3", u), "a3%d" % u, listed("a1", u), listed("fk", u), ["a1%d" % u, "fk%d" % u], A.subtract)
         ts(listed("sel", u), "sel%d" % u, listed("a3", u), ["a3%d" % u, "par%d" % u], H[u] - 1.0, T.par[:, u:u + 1], A.mult, A.add)
+        ts(T.hk[:, u:u + 1], "hk%d" % u, T.c5[:], ["c5"], 8.0 * H[u], None, A.mult)
     ts(T.wc[:], "wc", T.c6[:], ["c6"], 2.0, 1.0, A.mult, A.add)
     ts(T.wd[:], "wd", T.c5[:], ["c5"], 0.5, 3.0 / 128, A.is_lt, A.mult)
 
     def sums():
-        for name, by in (("zz", -17.0), ("zv", -4.0))[:1 + (min(VL) < 16)]:
+        for name, by in (("zz", -17.0), ("zv", -4.0)):
             fill(name, 0.0)
             ts(T[name][:, 15:143:16], name, T.bd[:, 0:128:16], ["bd"], by, None, A.mult)
 
     def offsets():
-        for u in range(1 + (VL[0] != VL[1])):
-            ts(T["so%d" % u][:], "so%d" % u, T.c5[:], ["c5"], VL[u] - 0.5, 64 * 511.75, A.is_ge, A.mult)
-            for name, by in (("st%d" % u, 4.5), ("sb%d" % u, 8.25)):
-                ts(T[name][:], name, T["so%d" % u][:], ["so%d" % u], TOP + by, None, A.add)
+        iota("lane", [[0, 8], [1, 16]], 0)
+        ts(T.csa[0:1, :], "csa", T.ones[0:1, :], ["ones"], TOP + 4, None, A.mult)
+        for u in range(2):
+            ts(T["cs%d" % u][0:1, :], "cs%d" % u, T.lane[0:1, :], ["lane"], VL[u] - 0.5, 64 * 511.75, A.is_ge, A.mult)
 
     def masks():
         select("ek", "ones", [[0, 8], [-1, 16]], A.is_equal, 0.0, 0, 1, 16)
         select("mk", "big", [[0, 8], [-1, 16]], A.not_equal, 0.0, 0, 1, 16)
         iota("t8", [[8, I]], 0)
-        select("mq", "t8", [[0, I // 16], [-1, 16]], A.is_equal, -8 * BIG, 0, 1, 16)
+        select("mq", "t8", [[0, I // 16], [-1, 16]], A.is_equal, LOW, 0, 1, 16)
         select("rs", "ones", [[0, 8], [1, 16]], A.is_gt, 0.0, 0, 0)
 
-    cst = ["0", "1" if VL[0] != VL[1] else "0"]
-
     def plain(name, src, u):
-        a, n = (2 * H[0] + 32) * u, H[u]
-        op("v", [src, src + "a", src + "b"], name + "t0%d" % u, lambda q: q.transpose(T[src + "t"][:, a:a + n], part(src, u, 16)), n)
-        op("v", [src, src + "a", src + "b"], name + "t1%d" % u,
-           lambda q: q.transpose(T[src + "t"][:, a + n:a + 2 * n + 32], T[src][:, O[u]:O[u] + n + 32]), n + 32)
-        copy(part(name, u), name + str(u), T[src + "t"][:, a:a + 2 * n + 32].indirect(listed("sel", u)),
-             [name + "t0%d" % u, name + "t1%d" % u, "sel%d" % u], GATHER)
+        turn(u, src + "t", "gn", I * (src == "nam0") + O[u], src, [{"grd0": ["gna", "nam0"], "nam0": ["grd0", "gnb"]}[src][u]])
+        copy(part(name, u), name + str(u), turned(src + "t", u), [src + "t%d0" % u, src + "t%d1" % u, "sel%d" % u])
 
     def raised():
-        if FILLX == "g":
-            iota("x", [[0, 16 + WX]], 0, int(UP), xs + ["xz"])
+        memset(T.x0[:, 0:16], "xz", 0.0)
+        for u in range(2):
+            a, b = (16 + 8 * O[u]) * u, 16 + 8 * (O[u] + H[u])
+            act(T.x[:, a:b], xs[u], T.x0[:, a:b], ["xc", "xz"], bias=UP)
+
+    def unit(name, by, e):
+        if e == "g":
+            select(name, "idf", [[-1, 128]], A.not_equal, by, 0, 1)
         else:
-            op("v", [], xs + ["xz"], lambda e: e.memset(T.x[:], UP), (16 + WX) / 2)
-        load("g", "d_up", xw, T.xc[:], [], xs, 512 * WX, accum_op=A.add)
+            act(T[name][:], name, T.idb[:], ["idb"], scale=by)
+
+    def level(name, val, e):
+        if e == "g":
+            iota(name, [[0, 128]], 0, val)
+        else:
+            act(T[name][:], name, T.ones[:], ["ones"], scale=float(val))
 
     constants = {
-        "zz": sums, "cst": offsets, "xg": raised,
-        "half": lambda: act(T.half[:], "half", T.ones[:], ["ones"], F.Sigmoid, scale=0.0), "mk": masks,
-        "idf": lambda: times("idf", "idb", 1.0), "idg": lambda: times("idg", "idb", -1.0), "bdf": lambda: times("bdf", "bd", 1.0),
-        "nbk": lambda: times("nbk", "bd", -2 * BIG), "trn": lambda: times("trn", "tr", -1.0),
-        "tr": lambda: (select("low", "nbk", [[1, 128]], A.is_gt, 0.0, 0, -1), select("tr", "low", [[-1, 128]], A.not_equal, 2 * BIG, 0, 1)),
-        "th": lambda: (memset(T.tb[:], "tb", 32 * (TOP - 88)), memset(T.thr[:], "thr", TOP - 96)),
-        "ids": lambda: [times(name, "idb", by) for name, by in (("idn", -1.0), ("idh", HUGE), ("idk", -HUGE))],
-        "big": lambda: fill("big", -8 * BIG),
-        "cc": lambda: (fill("two", 2.0), times("onp", "ones", 512.0), times("onn", "ones", -512.0)),
+        "zz": sums, "cst": offsets, "xg": raised, "mk": masks,
+        "half": lambda: act(T.half[:], "half", T.ones[:], ["ones"], F.Sigmoid, scale=0.0),
+        "idf": lambda: select("idf", "onp", [[-1, 128]], A.is_equal, 0.0, 0, 1) if CE[0] == "g" else unit("idf", 1.0, "a"),
+        "idg": lambda: unit("idg", -1.0, CE[1]), "idq": lambda: unit("idq", 1.0 / 256, CE[2]),
+        "onp": lambda: level("onp", 1, CE[3]), "rel": lambda: load(*inputs["r"]), "nam": lambda: load(*inputs["n"]),
+        "nbk": lambda: times("nbk", "bd", -2 * FLAG),
+        "tr": lambda: (select("low", "nbk", [[1, 128]], A.is_gt, 0.0, 0, -1), select("tr", "low", [[-1, 128]], A.not_equal, 2 * FLAG, 0, 1),
+                       times("trn", "tr", -1.0)),
+        "th": lambda: memset(T.tb[:], "tb", TB * (TOP - 88)),
+        "ids": lambda: [times(name, "idb", by) for name, by in (("idn", -1.0), ("idh", HUGE), ("idk", -HUGE), ("idp", -LOW))
+                        if name in ("idn", "idk") or (name == "idh" and " e" in ROUND) or (name == "idp" and " co" in ROUND)],
+        "big": lambda: fill("big", LOW),
+        "cc": lambda: (fill("two", 2.0), times("ch", "ones", -8 * HALF)),
         "bw": lambda: (tt(T.wn[:], "wn", T.wd[:], T.wc[:], ["wd", "wc"], A.subtract), times("bw", "bd", "wc"), times("bn", "bd", "wn")),
-        "c8": lambda: (fill("c8", EIGHT), memset(T.kc[:, 0:1], "kc0", -256.0), memset(T.kc[:, 1:2], "kc1", KILO)),
-        "va": lambda: ts(cols(pq[0], 2), pq[0], part("grd0", 2, 16), ["grd0"], 2048.0, None, A.mult),
-        "vb": lambda: [tt(own(u), vs[u], part(pq[0], u), part("nam0", u, 16), [pq[0], "nam0"], A.add) for u in range(2)],
-        "pads": lambda: [memset(T[name][:, a:a + 16], name + key, 0) for name in ("grd0", "nam0") for a, key in ((0, "a"), (16 + I, "b"))],
+        "c8": lambda: (fill("c8", EIGHT), fill("kc", TWO)),
+        "k8": lambda: ts(T.k8[:], "k8", first("grd0", 2), ["grd0"], 8.0, None, A.mult),
+        "va": lambda: ts(cols(pq[0], 2), pq[0], first("grd0", 2), ["grd0"], 2048.0, None, A.mult),
+        "vb": lambda: [tt(own(u), vs[u], part(pq[0], u), first("nam0", u), [pq[0], "nam0"], A.add) for u in range(2)],
+        "pads": lambda: [memset(T.gn[:, a:a + 16], key, 0) for a, key in ((0, "gna"), (16 + 2 * I, "gnb"))],
         "ka": lambda: plain("ku", "grd0", 0), "kb": lambda: plain("ku", "grd0", 1),
-        "na": lambda: (plain("lu", "nam0", 0), copy(entries("ti", 0, 0, 1), "ti0", entries("lu", 0, 0, 1), ["lu0"])),
-        "nb": lambda: (plain("lu", "nam0", 1), copy(entries("ti", 1, 0, 1), "ti1", entries("lu", 1, 0, 1), ["lu1"])),
-        "lima": lambda: limits("lim0", "lim0", wide[0], 0), "limb": lambda: limits("lim0", "lim0", wide[1], 1),
-        "gr2": lambda: act(T.gr[:], keys("gr", 2), T.lim0[:], ["lim0"], bias=UP),
-        "xz": lambda: memset(T.x[:, 0:16], "xz", UP),
-        "xa": lambda: act(xp(0), xs[0], T.x0[:, 0:8 * H[0]], ["xc"], bias=UP),
-        "xb": lambda: act(xp(1), xs[1], T.x0[:, 8 * H[0]:WX], ["xc"], bias=UP),
-        "C": deaths, "tb": lambda: act(T.tb[:], "tb", T[CB][:, 2 * M:2 * M + 1], [CB], bias=32 * (TOP - 88)),
-        "thr": lambda: act(T.thr[:], "thr", T[CB][:, 2 * M:2 * M + 1], [CB], scale=1.0 / 32, bias=TOP - 96),
+        "na": lambda: plain("lu", "nam0", 0), "nb": lambda: plain("lu", "nam0", 1),
+        "lima": lambda: (copies("lim0", "lim0", OWN0[0], 0), doubled(OWN0[0], 0)),
+        "limb": lambda: (copies("lim0", "lim0", OWN0[1], 1), doubled(OWN0[1], 1)),
+        "C": deaths, "tb": lambda: act(T.tb[:], "tb", T[pq[1]][:, 2 * M:2 * M + 1], [pq[1]], scale=16.0 * TB, bias=TB * (TOP - 88)),
     }
 
     def steps(t):
         last = t == RO - 1
-        xj, xk = (T.x0[:], ["xc"]) if t == 0 else (xw, xs)
+        x, xk, gr, gk = (T.x0, ["xc"], "lim0", ["lim0", "lim0"]) if t == 0 else (T.x, xs, "gr", keys("gr", 2))
+        xj = x[:, 16:16 + WX]
         h, gs = "h%d" % t, "gs%d" % t
         done = {"j0": 0, "j1": 0, "w0": 0, "w1": 0, "k0": 0, "k1": 0}
 
@@ -487,7 +405,7 @@ def rank_program(g, core, T, topo):
         def judge(u):
             a, b, key = piece("j", u)
             tt(lanes("u", u, a, b), "u" + key, xj.indirect(entries("ku", u, a, b)), T.gj[:, 768 * u:768 * u + H[u] * (b - a)],
-               xk + ["ku%d" % u] + ["gj%d%d" % (u, c) for c in range(b - a)], A.subtract, GATHER)
+               xk + ["ku%d" % u] + ["gj%d%d" % (u, c) for c in range(b - a)], A.subtract)
 
         def mark(u):
             a, b, key = piece("w", u)
@@ -496,34 +414,35 @@ def rank_program(g, core, T, topo):
                 act(lanes(w, u, a, b), "w" + key, lanes("u", u, a, b), ["u" + key, "half"], F.Sigmoid, scale=8.0, bias=-8.0 * 512 - math.log(16.0))
             else:
                 w, z = "wv", "zv"
-                ts(lanes(w, u, a, b), "w" + key, lanes("u", u, a, b), ["u" + key], 511.75, 516.0, A.max, A.min, 0.5)
+                ts(lanes(w, u, a, b), "w" + key, lanes("u", u, a, b), ["u" + key], 511.75, 516.0, A.max, A.min)
             rows(w, z, u, a, b, key)
 
         def rows(w, z, u, a, b, key):
-            for k in range(a, b):
+            def add(e, k):
                 done["k%d" % u] += 1
-                mm(pa[u], 0, z, lanes(w, u, k, k + 1), ["w" + key], H[u], done["k%d" % u] == 1, done["k%d" % u] == 16, lhs=T[z][:, 15 - k:143 - k])
+                return e.matmul(cols(pa[u], u), T[z][:, 15 - k:143 - k], lanes(w, u, k, k + 1), False, done["k%d" % u] == 16)
+            for k in range(a, b):
+                op("t", [z, "w" + key], pa[u], lambda e, k=k: add(e, k))
 
         def less(u):
-            g_, key = ("lim0", "lim0") if t == 0 else ("gr", "gr%d" % u)
             for k in range(SL[u]):
-                mm(pf[u], H[u] * k, "idn", part(g_, u), [key], H[u], k == 0, False)
+                mm(pf[u], H[u] * k, "idn", part(gr, u), [gk[u]], k == 0, False)
 
-        def take(u):
-            act(lanes("u", u, 0, SL[u]), "us%d" % u, xj.indirect(entries("ku", u, 0, SL[u])), xk + ["ku%d" % u], bias=-2.0)
+        def take(u, a, b):
+            act(lanes("u", u, a, b), "us%d%d" % (u, a), xj.indirect(entries("ku", u, a, b)), xk + ["ku%d" % u], bias=-2.0)
 
-        def cells(u):
-            n = SL[u] * H[u]
-            mm(pf[u], 0, "idb", lanes("u", u, 0, SL[u]), ["us%d" % u], n, False, False)
-            mm(pf[u], 0, "idn", T.big[:, 0:n], ["big"], n, False, False)
-            mm(pf[u], 0, "idb", T.big[:, 0:n], ["big"], n, False, True)
+        def cells(u, a, b):
+            n = (b - a) * H[u]
+            mm(pf[u], a * H[u], "idb", lanes("u", u, a, b), ["us%d%d" % (u, a)], False, False)
+            mm(pf[u], a * H[u], "idn", T.big[:, 0:n], ["big"], False, False)
+            mm(pf[u], a * H[u], "idb", T.big[:, 0:n], ["big"], False, b == SL[u])
 
         def marks(u):
             act(lanes("w", u, 0, SL[u]), "ws%d" % u, T[pf[u]][:, 0:SL[u] * H[u]], [pf[u], "half"], F.Sigmoid, scale=8.0, bias=-math.log(16.0))
             rows("w", "zz", u, 0, SL[u], "s%d" % u)
 
         def send(u):
-            tt(part(gs, u), gs + str(u), T.x[:, 0:16 + WX].indirect(listed("ks", u)), part("gr", u), xs + ["xz", "ks%d" % u, "gr%d" % u], A.max, GATHER)
+            tt(part(gs, u), gs + str(u), x[:].indirect(listed("ks", u)), part(gr, u), xk + ["xz", "ks%d" % u, gk[u]], A.max)
             dst = T.cores[(rank + 1 + t % 7) % 8]
             src = T.cores[(rank - 1 - t % 7) % 8]
             eng = topo.engines(core, dst)[:8]
@@ -533,56 +452,90 @@ def rank_program(g, core, T, topo):
                 waits("g", [gs + str(u)], [])
                 g.remote_dma(part(h, u), part(gs, u), T.sem["arr%d%d" % (t, u)], T.sem.sent, pid, rid, sum(1 << e for e in eng))
                 wrote[h + str(u)] = ("remote", "arr%d%d" % (t, u), len(topo.engines(src, core)[:8]), {})
-            calls.append(("g", [gs + str(u)], [h + str(u)], SEND + (OPEN if t + u == 0 else 0.0), FAR, 0, issue, [], None))
+            calls.append(("g", [gs + str(u)], [h + str(u)], issue, [], None))
 
         def land(u):
             pm(pf, "bn", h, u, False, False)
+            if t == 0:
+                cm(pf, "idb", "c8", u, False, False)
             cm(pf, "idn", "c8", u, False, False)
             pm(pf, "bw", h, u, False, True)
 
-        parts = {
-            "kv": clip, "E": fetched, "b": classes, "A": less, "x": take, "B": cells, "m": marks, "gs": send,
-            "c": lambda u: pm(pa, "idg", "v", u, True, False), "D": lambda u: pm(pa, "idk", "dead", u, False, True), "R": ready, "land": land, "turn": turn, "ti": listing,
-            "j": judge, "w": mark, "f": fetch,
-            "G": lambda u: pm(pe, "idf", "v", u, True, False), "U": lambda u: pm(pe, "tr", "und", u, False, True),
-            "M": lambda u: mm(pq[u], 0, "ek", T.mk[0:16, 0:H[u]], ["mk"], H[u], True, False, lhs=T.ek[0:16, :]), "P": lambda u: pm(pq, "bdf", "kv", u, False, True),
-            "T": lambda u: cm(pe, "idb", "two", u, True, False), "H": lambda u: pm(pe, "idb", h, u, False, True),
-            "gk": lambda u: limits("gr", "gr%d" % u, OWN[u], u, 1),
-            "a": lambda u: ts(cols(pa[u], u, M), "a%d" % u, cols(pa[u], u), [pa[u], "thr", "st" + cst[u]], T["st" + cst[u]][:], T.thr[:], A.add, A.max),
-            "e": wiped, "V": lambda u: pm(pa, "idf", "v", u, False, False),
-            "u": lambda u: tt(part("und", u), "und%d" % u, cols(pa[u], u, M), part("b", u), [pa[u], "a%d" % u, "b%d" % u], A.is_lt),
-            "n": lambda u: tt(part("vi", u) if last else own(u), vs[u], part("md", u), cols(pa[u], u), ["md%d" % u, pa[u]], A.max),
+        def ready(u):
+            masked(pf, "mq", O[u], u, True)
+            for name in ("two", "half", "half", "half") if t == 0 else ("c8",):
+                cm(pf, "idb", name, u, False, False)
+
+        def above(u):
+            for n, (lkey, name) in enumerate((("idb", "two"), ("bw", "two"), ("bd", "half"), ("bd", "half"))[:4 if t == 0 else 1]):
+                cm(pe, lkey, name, u, n == 0, False)
+
+        def lower(u):
+            if t == 0:
+                act(*one("gm", u), part(gs, u), [gs + str(u)], bias=UP)
+            name = "gm" if t == 0 else gs
+            tt(*one("gr", u), part(name, u), cols(pe[u], u), [name + str(u), pe[u]], A.min)
+
+        def new(u):
+            return (part("vi", u, 16 + 16 * u), "vi%d" % u) if last or NI[u] else (own(u), vs[u])
+
+        def one(name, u):
+            return part(name, u), name + str(u)
+
+        return {
+            "j": judge, "w": mark, "f": lambda j: fetch(j, t), "A": less, "m": marks, "gs": send, "land": land,
+            "turn": lambda u: turn(u, "tq" if NI[u] else "tp", "vi" if NI[u] else "v", O[u] + 16 * u, "vi%d" % u if NI[u] else vs[u],
+                                   ["pad%d%s" % (u, c) for c in "ab"], "tp"), "ku": guards,
+            "nf": lambda u: tt(own(u), vs[u], part(("md", "r2")[u], u), cols((pa, pq)[u][u], u), [("md", "r2")[u] + str(u), (pa, pq)[u][u]], A.max),
+            "G": lambda u: eights(u, t),
+            "x": lambda u: take(u, 0, SX[u]), "B": lambda u: cells(u, 0, SX[u]),
+            "X": lambda u: take(u, SX[u], SL[u]), "Y": lambda u: cells(u, SX[u], SL[u]),
+            "S": lambda u: [mm(pa[u], 0, a, T[b][0:1, 0:H[u]], [b], a == "csa", False, lhs=T[a][0:1, :])
+                            for a, b in (("csa", "ones"), ("ones", "half"), ("cs%d" % u, "ones"))],
+            "b": lambda u: ts(*one("b", u), cols(pa[u], u), [pa[u]], 3.75, None, A.add),
+            "u": lambda u: tt(*one("und", u), cols(pa[u], u), part("b", u), [pa[u], "b%d" % u], A.is_lt),
             "d": lambda u: act(part("dead", u), ["dead%d" % u, "cnt%d" % u], part("b", u), ["b%d" % u, "tb"], F.Sigmoid, scale=-32.0,
                                bias=T.tb[:], accum_out=T.cnt[:, u:u + 1]),
-            "sk": lambda u: diagonal(pq[u], "sk", u), "sq": lambda u: diagonal(pf[u], "sq", u),
-            "ks": lambda u: ts(listed("ks", u), "ks%d" % u, picked("sk", u), ["sk%d" % u], 1.0 / 2048, 16 - 2048 - HALF, A.mult, A.add),
-            "si": lambda u: tt(listed("si", u), "si%d" % u, picked("sk", u), entries("ti", u, 0, 1), ["sk%d" % u, "ti%d" % u], A.max),
-            "sa": lambda u: ts(listed("sa", u), keys("sa", u), listed("si", u), keys("si", u), 2047, None, A.bitwise_and),
-            "ls": lambda u: copy(listed("ls", u), keys("ls", u), listed("sa", u), keys("sk" if HYP else "sa", u)),
-            "md": lambda u: tt(part("md", u), keys("md", u), T.rel0[:, 0:W].indirect(listed("ls", u)), part("dead", u),
-                               ["rel0"] + keys("ls", u) + keys("dead", u), A.mult, GATHER),
-            "ku": guards,
-            "la": lambda u: ts(part("la", u), keys("la", u), part("ti", u), keys("ti", u), 2047, None, A.bitwise_and),
-            "lu": lambda u: copy(part("lu", u), keys("lu", u), part("la", u), keys("la", u)),
-            "hp": lambda u: act(part("hp", u), keys("hp", u), part(h, u), keys(h, u), bias=-0.5),
-            "gr": lambda u: tt(part("gr", u), "gr%d" % u, part(gs, u), cols(pe[u], u), [gs + str(u), pe[u]], A.min),
-            "gj": lambda u: limits("gr", "gr%d" % u, OWN[u], u),
-            "cu": lambda u: ts(listed("cu", u), keys("cu", u), picked("sq", u), keys("sq", u), -8.0 * O[u], None, A.add),
-            "bl": lambda u: tt(part("bl", u), keys("bl", u), xp(u).indirect(listed("cu", u)), part("hp", u),
-                               keys("x", u) + keys("cu", u) + keys("hp", u), A.add, GATHER),
-            "put": lambda u: tt(xp(u).indirect(listed("cu", u)), keys("x", u), part("bl", u), cols("half", u),
-                                keys("bl", u) + keys("cu", u) + ["half"], A.mult, SCATTER),
+            "dv": lambda u: ts(*one("dead", u), part("b", u), ["b%d" % u, "tb"], T.tb[:], None, A.is_lt),
+            "dc": lambda u: act(part("kw", u), ["kw%d" % u, "cnt%d" % u], part("dead", u), ["dead%d" % u], accum_out=T.cnt[:, u:u + 1]),
+            "U": lambda u: (pm(pe, "tr", "und", u, False, False), pm(pe, "trn", "dead", u, False, True)),
+            "kv": lambda u: ts(*one("kv", u), cols(pe[u], u), [pe[u]], 128 - 2 * FLAG - EIGHT, 0.0, A.add, A.max),
+            "kw": lambda u: ts(*one("kw", u), cols(pe[u], u), [pe[u], "hk%d" % u], FLAG + EIGHT, T.hk[:, u:u + 1], A.is_ge, A.mult),
+            "M": lambda u: masked(pq, "mk", 0, u, True), "P": lambda u: pm(pq, "bd", "kv", u, False, True),
+            "N": lambda u: masked(pf, "mq", O[u], u, True), "Q": lambda u: pm(pf, "bd", "kw", u, False, True),
+            "sk": lambda u: diagonal(pq[u], "sk", u), "sw": lambda u: diagonal(pf[u], "sw", u), "sq": lambda u: diagonal(pf[u], "sq", u),
+            "ks": lambda u: ts(listed("ks", u), "ks%d" % u, picked("sk", u), ["sk%d" % u], 1.0 / 8, None, A.mult),
+            "ls": lambda u: ts(listed("ls", u), "ls%d" % u, picked("sw", u), ["sw%d" % u], 1.0 / 8, -1.0 * O[u], A.mult, A.add),
+            "md": lambda u: tt(*one("md", u), lanes("nb", u, 0, 16).indirect(listed("ls", u)), part("dead", u),
+                               ["nb%d" % j for j in range(len(FETCH)) if FETCH[j][0] == u] + ["ls%d" % u, "dead%d" % u], A.mult),
+            "c": lambda u: pm(pa, "idg", "v", u, True, False),
+            "E": lambda u: mm(pa[u], 0, "idf", part("mo", u), ["mo%d_%d" % (u, k) for k in range(16)], False, False),
+            "e": lambda u: (pm(pa, "idh", "und", u, False, False), pm(pa, "idk", "und", u, False, False)),
+            "V": lambda u: pm(pa, "idf", "v", u, False, False), "D": lambda u: pm(pa, "idk", "dead", u, False, True),
+            "n": lambda u: tt(*new(u), part("md", u), cols(pa[u], u), ["md%d" % u, pa[u]], A.max),
+            "Do": lambda u: pm(pq, "idk", "und", u, True, False),
+            "Eo": lambda u: mm(pq[u], 0, "idf", part("mo", u), ["mo%d_%d" % (u, k) for k in range(16)], False, True),
+            "co": lambda u: (cm(pa, "idb", "big", u, True, False), pm(pa, "idp", "und", u, False, False), pm(pa, "idk", "dead", u, False, False),
+                             pm(pa, "idf", "v", u, False, True)),
+            "ro": lambda u: tt(*one("r2", u), part("md", u), cols(pa[u], u), ["md%d" % u, pa[u]], A.max),
+            "no": lambda u: tt(*new(u), part("r2", u), cols(pq[u], u), ["r2%d" % u, pq[u]], A.max),
+            "ti": lambda u: copy(*one("ti", u), turned("tp", u), ["tp%d0" % u, "tp%d1" % u, "sel%d" % u]),
+            "la": lambda u: (ts(*one("la", u), turned("tq", u), ["tp%d0" % u, "tp%d1" % u, "sel%d" % u], 2047, None, A.bitwise_and) if NI[u] else
+                             ts(*one("la", u), part("ti", u), ["ti%d" % u], 2047, None, A.bitwise_and)),
+            "lu": lambda u: copy(*one("lu", u), part("la", u), ["la%d" % u]),
+            "R": ready, "T": above, "gr": lower,
+            "cu": lambda u: ts(listed("cu", u), "cu%d" % u, picked("sq", u), ["sq%d" % u], -8.0 * O[u], None, A.add),
+            "hp": lambda u: act(*one("hp", u), part(h, u), [h + str(u)], bias=UP * (t == 0) - 0.5),
+            "bl": lambda u: tt(*one("bl", u), xp(u).indirect(listed("cu", u)), part("hp", u), [xs[u], "cu%d" % u, "hp%d" % u], A.add),
+            "put": lambda u: tt(xp(u).indirect(listed("cu", u)), xs[u], part("bl", u), cols("half", u), ["bl%d" % u, "cu%d" % u, "half"], A.mult),
+            "H": lambda u: pm(pe, "idb", h, u, False, True),
+            "gj": lambda u: copies("gr", "gr%d" % u, OWN[u], u), "gk": lambda u: doubled(OWN[u], u),
             "g": lambda u: act(cols(pf[u], u), pf[u], part(gs, u), [gs + str(u)], bias=-UP),
-            "h": lambda u: ts(part("gm", u), keys("gm", u), part(h, u), keys(h, u), 2.0 - UP, None, A.add), "y": limits_out,
-            "k": lambda u: ts(part("ti", u), keys("ti", u), part("vi", u), keys("v", u), 11, None, A.arith_shift_right),
-            "l": lambda u: ts(part("la", u), keys("la", u), part("vi", u), keys("v", u), 2047, None, A.bitwise_and),
-            "og": lambda u: (copy(part("og", u), keys("og", u), part("ti", u), keys("ti", u)),
-                             load("s", "d_og", part("yg", u), part("og", u), keys("og", u), keys("yg", u), 512 * H[u])),
-            "on": lambda u: (copy(part("on", u), keys("on", u), part("la", u), keys("la", u)),
-                             load("s", "d_on", part("yn", u), part("on", u), keys("on", u), keys("yn", u), 512 * H[u])),
+            "h": lambda u: ts(*one("gm", u), part(h, u), [h + str(u)], 2.0 - UP, None, A.add), "y": limits_out,
+            "k": lambda u: ts(*one("ti", u), new(u)[0], ["vi%d" % u], 11, None, A.arith_shift_right),
+            "l": lambda u: ts(*one("la", u), new(u)[0], ["vi%d" % u], 2047, None, A.bitwise_and),
+            "og": lambda u: numbers_out("og", "ti", "yg", u), "on": lambda u: numbers_out("on", "la", "yn", u),
         }
-
-        return parts
 
     rounds = [steps(t) for t in range(RO)]
     tags = {}
@@ -590,42 +543,39 @@ def rank_program(g, core, T, topo):
         s = "." + calls[n][2][0]
         tags[(0, s + "x" if (0, s) in tags else s)] = [n]
     for t in range(RO):
-        for s in ((START + " " + ROUND0 if t == 0 else LATE + " " + ROUND) + " " + (END if t == RO - 1 else BLEND)).split():
-            r, s = t + {"<": -1, ">": 1}.get(s[0], 0), s.lstrip("<>")
+        for s in ((START + " ") * (t == 0) + ROUND + " " + (END if t == RO - 1 else BLEND)).split():
             u = int(s[1:] == "1")
             both = [c + s[1:] + str(j) for j in range(len(JUDGE[u])) for c in "jw"]
-            more = {"J": both[:2 * MP[u]] + [c + s[1:] for c in "AxBm"[:4 * (SL[u] > 0)]] + both[2 * MP[u]:],
+            more = {"J": both[:2 * MP[u]] + [c + s[1:] for c in "AxB" + "XY" * (SX[u] < SL[u]) + "m"] + both[2 * MP[u]:],
                     "F": ["f%d" % j for j in range(len(FETCH)) if str(FETCH[j][0]) == s[1:]]}
             for s in more.get(s[0], [s]):
                 n = len(calls)
                 if s in constants:
                     constants[s]()
                 elif s[0] in "jw":
-                    rounds[r][s[0]](int(s[1]))
+                    rounds[t][s[0]](int(s[1]))
                 else:
-                    rounds[r][s[:-1]](int(s[-1]))
+                    rounds[t][s[:-1]](int(s[-1]))
                 for i in range(n, len(calls)):
                     if i > n and (calls[i][0] == "s" or calls[i][0] == calls[i - 1][0] == "t"):
-                        tags[(r, s)].append(i)
+                        tags[(t, s)].append(i)
                     else:
                         s += "'" * (i > n)
-                        tags[(r, s)] = [i]
+                        tags[(t, s)] = [i]
     SEEN.update(calls=calls, tags=tags, ahead=ahead)
     if PLAN[:1] == [None]:
         PLAN[:] = range(len(calls))
     if not PLAN:
         PLAN.extend(range(ahead))
         for t in range(RO):
-            for s in ORDERS[t if len(ORDERS) == RO else min(t, 1) + (t == RO - 1)].split():
+            for s in ORDERS[t].split():
                 PLAN.extend(tags[(t + {"<": -1, ">": 1}.get(s[0], 0), s.lstrip("<>"))])
-    if not PLAN:
-        PLAN.extend(arrange([c[:6] for c in calls], ahead))
     for n in PLAN:
-        calls[n][6]()
+        calls[n][3]()
     g.wait_ge(T.sem.sent, 2 * sum(len(topo.engines(core, T.cores[(rank + 1 + t % 7) % 8])[:8]) for t in range(RO)))
     for q in ("v", "a", "t", "g"):
         if known["g"].get("c" + q, 0) < count[q]:
             g.wait_ge(T.sem["c" + q], count[q])
-    for s in ("d_up", "d_on", "d_og", "d_ol"):
+    for s in ("d_on", "d_og", "d_ol"):
         if known["g"].get(s, 0) < dcount.get(s, 0):
             g.wait_ge(T.sem[s], dcount[s])

import math
from concourse.mybir import dt, AluOpType, AxisListType, ActivationFunctionType

I = 224
WX = 1792
W = 2048
RO = 4
NC = (8, 6)
SL = (4, 4)
SX = (2, 4)
JUDGE = [[8, 12, 16], [8, 12, 14, 16]]
VL = (12, 8)
MP = (1, 1)
FETCH = [(0, 0, 5), (0, 5, 10), (0, 10, 16), (1, 0, 7), (1, 7, 12), (1, 12, 14), (1, 14, 16)]
FV = ((6,), (), (), (6,))
OWN = (1, 1)
OWN0 = (4, 1)
KD = (0, 1)
NI = (1, 1)
TB = 1
GFILL = "csa tb two pad0a pad0b pad1a pad1b idh idk xz zv gnb idn idp"
CE = "gaaa"
LOADS = "glx"
AFTER = ["grd0"]
START = "nam pads half ka lima zz onp cst kb limb nbk tr idf idg idq big mk th na nb va vb xg rel ids cc bw c8"
ROUND = ("F0 F1 S0 S1 G0 G1 M0 M1 J0 J1 b0 u0 dv0 U0 kv0 kw0 P0 sk0 ks0 gs0 b1 u1 dv1 U1 kv1 kw1 P1 sk1 ks1 gs1 "
         "N0 Q0 sw0 ls0 md0 c0 E0 e0 V0 D0 n0 N1 Q1 sw1 ls1 md1 co1 Do1 Eo1 ro1 no1")
BLEND = ("nf0 turn0 ku0 la0 lu0 nf1 turn1 ku1 la1 lu1 R0 land0 sq0 cu0 hp0 bl0 put0 T0 H0 gr0 gj0 gk0 "
         "R1 land1 sq1 cu1 hp1 bl1 put1 T1 H1 gr1 gj1 gk1 dc0 dc1 C tb")
END = "g0 h0 y0 g1 h1 y1 k0 l0 og0 on0 k1 l1 og1 on1"
ORDERS = [
    ".ip .ones nam .ff half cst zz big .c5 .c4 c8 .a11 .a10 .bd .rc1 .rc0 cst' cst''' .g16 .fk0 .fk1 cc' pads .par0 .a30 ka .par1 .a31 rel .sel0 ka' lima lima'' lima' lima''' .idb .bdx .pad0b ids xg pads' th S1 kb cst'' .sel1 ka'' va zz' nbk limb onp idq idg x0 j00 S0 A1 A0 limb' limb'' kb' X0 na na' B0 kb'' mk'''' mk tr zz'' w00 j01 Y0 x1 w00' m0 B1 j10 na'' j02 w01 m0' w10 m1 zz''' vb w01' f1 f2 tr' mk'' .pad0a mk''' ids''' mk' ids'' .pad1b idf ids' w02 w10' w02' G0 m1' j11 j12 w11 tr'' b0 j13 u0 w11' dv0 f0 U0 w12 w13 nb' nb vb' w12' N1 M1 w13' kv0 nb'' M0 .hk1 b1 .hk0 .c6 P0 sk0 G1 c0 u1 cc dv1 ks0 >M0 .wc kw0 U1 gs0 co1 N0 kv1 kw1 Q0 gs0' bw' f3 f4 f6 P1 Q1 T1 sk1 sw0 .wd ks1 E0 f5 ls0 sw1 gs1 dc1 xg' xg'' gr0 dc0 hp0 e0 md0 V0 bw ls1 c8' D0 gs1' n0 md1 bw'' T0 R1 Do1 R0 turn0' turn0 nf0 ro1 Eo1 la0 ku0 no1 lu0 nf1 H0 land0 gr0' C C' hp1 turn1' gr1 land1 sq0 H1 gj0 turn1 >S0 C'' sq1 cu0 gk0 gr1' cu1 bl0 bl1 gk0' put0 put1 >G1 >S1 >G0 >f0 >f1 gj1 ku1 la1",
    "x0 <gk1 j00 X0 x1 <gk1' j01 j02 A1 A0 B0 w00 Y0 j10 B1 m0 w01 <tb w00' m0' w02 j12 j11 w02' w01' w10 m1 f2 w10' w12 j13 m1' w11 w12' b0 <lu1 w13 w11' u0 dv0 w13' U0 b1 kv0 M1 N1 N0 u1 dv1 kw0 c0 P0 U1 sk0 Q0 T0 kv1 ks0 sw0 P1 gs0 E0 sk1 e0 ls0 kw1 gs0' V0 ks1 f4 f3 f6 f5 Q1 md0 D0 gs1 sw1 n0 gs1' nf0 ls1 >M0 co1 T1 turn0' turn0 md1 la0 R1 Do1 >S0 R0 ro1 ku0 land0 dc0 dc1 C' hp0 C hp1 H0 lu0 Eo1 sq0 gr0 >S1 no1 land1 gj0 nf1 cu0 H1 C'' >G0 turn1 >f0 >f1 sq1 gk0 bl0 cu1 turn1' gr1 bl1 gk0' put0 put1 >A1 >A0 >G1 ku1 la1 tb gj1",
    "j00 x0 <gk1 X0 B0 <gk1' x1 Y0 w00 j02 j01 B1 m0 w00' w02 j10 w01 m1 j11 w10 m0' w02' w01' j12 m1' f2 w11 w11' w10' j13 b0 w12 w13 u0 w12' dv0 <lu1 w13' U0 f3 f6 f4 f5 b1 kv0 u1 dv1 kw0 N1 c0 N0 M1 P0 U1 T0 Q0 sk0 kv1 >M0 P1 ks0 sw0 gs0 E0 sk1 e0 ls0 kw1 V0 gs0' ks1 md0 Q1 D0 gs1 sw1 n0 gs1' nf0 ls1 turn0' turn0 co1 R0 T1 R1 Do1 >S0 md1 la0 ro1 ku0 H0 gr0 lu0 dc1 dc0 C' hp0 C hp1 gj0 land0 Eo1 >S1 sq0 no1 land1 nf1 cu0 H1 turn1' >f2 >f0 >G0 C'' gk0 sq1 bl0 cu1 turn1 gr1 bl1 gk0' put0 put1 ku1 la1 gj1",
    "x0 j00 <gk1 A1 A0 G1 <tb X0 B0 x1 <gk1' Y0 w00 j02 j01 B1 m0 w00' w02 j10 w01 <lu1 j11 j12 m1 m0' w02' w10 w01' m1' w11 j13 f1 w10' w11' b0 w12 w13 u0 f3 w12' dv0 f4 f6 w13' U0 M1 N0 N1 c0 b1 kv0 u1 dv1 kw0 P0 U1 f5 sk0 Q0 co1 kv1 ks0 kw1 sw0 P1 gs0 Q1 E0 sk1 ls0 sw1 e0 gs0' ks1 V0 md0 gs1 D0 Do1 ls1 n0 gs1' g1 g0 md1 Eo1 l0 ro1 k0 on0 no1 og0 l1 k1 h0 on1 og1 h1 y0 y1 y0' y1'"]
OLDER = [
    ".ip .ones nam pads zz c8' cst c8 .c5 cc' .ff .c6 .c4 .rc0 .rc1 .g16 cst' th .bd .fk0 .a10 .par0 cst'' .par1 .a30 .pad0b .bdx cst''' .fk1 .a11 big rel .idb pads' .a31 ka .sel0 onp half S0 ka' nbk .wc zz' S1 kb ka'' ids lima''' limb lima' lima lima'' va .sel1 limb' idg idq mk'' j00 x0 A1 A0 mk .pad1b limb'' zz'' ids'' mk''' .pad0a X0 kb' B0 na' w00 kb'' Y0 na j01 x1 w00' m0 j10 B1 w01 na'' j02 m0' w10 w01' vb G0 zz''' w02 j11 f0 m1 f1 N0 w02' w10' tr mk'''' tr' j12 w11 b0 j13 w12 w11' m1' u0 tr'' d0 w13 w12' f2 nb vb' nb' U0 w13' .wd c0 kv0 b1 mk' M1 M0 nb'' P0 G1 .hk0 u1 d1 .hk1 f3 sk0 U1 bw kw0 ks0 cc idf ids''' xg co1 ids' bw' kv1 gs0 Q0 N1 f4 kw1 P1 T0 sw0 gs0' f6 Q1 f5 sk1 E0 ls0 sw1 ks1 e0 xg' md0 V0 ls1 gr0 gs1 D0 bw'' md1 gs1' n0 ro1 turn0 T1 R1 R0 turn0' nf0 Do1 >S1 la0 xg'' ku0 Eo1 hp0 C' C H0 lu0 land0 no1 gr1 gr0' land1 hp1 nf1 turn1 H1 sq0 gj0 turn1' sq1 gk0 C'' >S0 cu0 gr1' cu1 bl0 >A1 >A0 bl1 >f0 >f1 gj1 tb gk0' put0 >G0 >G1 put1 ku1 la1",
    "x0 j00 <gk1 X0 B0 j01 j02 x1 <gk1' Y0 w00 B1 m0 j10 w00' w01 N0 m0' j12 w02 w12 j11 w10 w02' w01' m1 w10' f2 j13 w11 b0 <lu1 m1' w12' w11' w13 u0 d0 f6 f5 w13' U0 M1 b1 c0 M0 kv0 d1 u1 f3 kw0 P0 U1 Q0 N1 T0 sk0 kv1 ks0 sw0 P1 f4 E0 gs0 sk1 e0 ls0 V0 kw1 gs0' ks1 md0 D0 Q1 gs1 T1 co1 n0 sw1 gs1' nf0 R1 R0 Do1 turn0 ls1 turn0' >S0 md1 la0 hp0 H0 ro1 land0 lu0 Eo1 gr0 sq0 ku0 gj0 land1 no1 C hp1 C' H1 >S1 cu0 >A0 gk0 nf1 sq1 gr1 turn1 C'' cu1 bl0 gk0' turn1' >A1 >G0 >G1 bl1 >f1 >f0 put0 put1 tb gj1 gk1 gk1'",
    "x0 <la1 <ku1 j00 X0 B0 x1 j02 j01 Y0 w00 B1 m0 w00' w01 N0 w02 w02' m0' m1 w01' j10 j11 j12 w10 j13 w11 f2 m1' w12 b0 w10' w12' w11' <lu1 w13 d0 u0 f6 f5 w13' U0 M1 c0 M0 b1 kv0 u1 d1 kw0 f3 P0 U1 sk0 Q0 N1 kv1 ks0 sw0 P1 gs0 E0 sk1 f4 e0 ls0 kw1 gs0' V0 ks1 md0 Q1 D0 gs1 T0 >M0 sw1 co1 Do1 n0 gs1' nf0 ls1 turn0' turn0 R0 T1 >S0 md1 R1 hp0 C' C la0 H0 land0 ro1 ku0 Eo1 gr0 lu0 >S1 sq0 gj0 no1 land1 hp1 nf1 H1 cu0 >f2 >f0 >G0 gk0 turn1' sq1 bl0 C'' cu1 gr1 turn1 gk0' >A0 bl1 put0 >A1 put1 ku1 la1 tb gj1",
    "j00 x0 M1 G1 <gk1 X0 B0 j02 j01 x1 <gk1' Y0 w00 B1 m0 j10 w00' w01 w02 m0' N0 j11 w10 w02' m1 j12 w01' w11 w10' f1 j13 w11' m1' w12 b0 w13 <lu1 u0 w12' d0 w13' f4 f6 U0 b1 N1 c0 kv0 d1 u1 f3 kw0 P0 U1 Q0 sk0 co1 kv1 f5 kw1 ks0 sw0 P1 Q1 E0 gs0 sk1 e0 ls0 sw1 V0 gs0' ks1 md0 D0 Do1 gs1 ls1 n0 gs1' g1 g0 md1 k0 l0 ro1 og0 Eo1 on0 no1 h0 l1 y0 k1 y0' on1 h1 og1 y1 y1'"]
OLD = [
    ".ip .ones cst zz rel .ff half .c5 big .rc1 .rc0 .g16 .c4 .a11 .fk1 .fk0 .bd .idb .a10 .par0 .a31 .par1 pads .a30 .bdx zz'' ids .sel1 .hk0 .sel0 cst' onp ka kb ka' k8 lima' lima'' lima''' lima limb' ka'' nbk zz' zz''' va A0 j00 x0 limb tr idf limb'' G0 A1 S0 G1 kb' na' w00 B0 mk'' cst'' kb'' j01 na x1 j10 m0 w00' B1 na'' w01 j02 S1 m0' j13 w02 m1 w10 w01' j11 f1 f0 w02' w10' j12 b0 mk''' mk mk' tr' pads' th w11 m1' M1 w12 mk'''' xg ids''' idg ids'' w11' w13 tr'' u0 d0 .hk1 nb' vb' w12' f2 w13' U0 N0 nb vb b1 kv0 M0 ids' .padc cc nb'' P0 kw0 u1 c8 sk0 d1 c8' f3 Q0 U1 c0 co1 N1 ks0 .c6 kw1 gs0 kv1 sw0 .wd gs0' P1 Q1 >M0 f4 f6 .wc sk1 ls0 sw1 E0 ks1 md0 e0 f5 .pada gs1 V0 cc' gr0 bw c8'' bw' ls1 D0 gs1' .padb n0 onn idq md1 turn0 xg'' xg' R0 R1 turn0' ro1 ti0 bw'' la0 ku0 T1 T0 Do1 Eo1 hp0 hp1 H0 land0 no1 gr0' land1 lu0 sq0 gr1 gj0 turn1 >f0 >f1 sq1 cu0 turn1' gk0 cu1 bl0 >S1 H1 >S0 gr1' bl1 >G0 gk0' put0 put1 ku1 ti1 >A0 C >A1 >G1 gj1",
    "x0 j01 <gk1 B0 x1 j00 <gk1' w01 j02 w00 B1 m0 w00' m0' j10 w02 j11 j12 <la1 j13 <lu1 w11 <tb w10 m1 w01' f2 w02' w10' b0 m1' w12 w13 w11' d0 u0 f6 w12' f5 w13' U0 b1 kv0 N0 c0 u1 d1 kw0 P0 U1 sk0 M1 N1 Q0 kv1 f4 f3 ks0 sw0 P1 E0 gs0 sk1 e0 ls0 kw1 V0 gs0' ks1 md0 D0 Q1 gs1 n0 sw1 gs1' turn0 T1 R0 co1 R1 T0 Do1 >M0 >S0 ls1 turn0' md1 ti0 ro1 land0 hp0 la0 ku0 H0 >S1 sq0 gr0 cu0 lu0 land1 gj0 hp1 bl0 Eo1 H1 sq1 >A0 gk0 no1 gr1 cu1 put0 gk0' bl1 turn1 turn1' C >G0 put1 ku1 >G1 >f0 gj1 >f1",
    "x0 j00 <tb w00 A1 B0 <gk1 x1 <gk1' w00' m0 B1 j01 w01 j10 j02 j12 w02 <ti1 m0' j11 <la1 w01' w10 m1 w02' j13 f2 w11 w10' <lu1 b0 w12 w13 m1' w11' d0 u0 f6 w12' f5 w13' U0 N0 M1 c0 b1 kv0 d1 u1 kw0 f3 P0 N1 U1 Q0 sk0 co1 kv1 f4 ks0 sw0 >M0 P1 E0 gs0 e0 sk1 ls0 kw1 gs0' ks1 md0 V0 D0 Q1 R0 gs1 n0 sw1 gs1' turn0' ls1 >S0 T1 T0 Do1 turn0 md1 ti0 ro1 R1 land0 hp0 la0 H0 sq0 Eo1 gr0 lu0 land1 hp1 cu0 ku0 gj0 no1 sq1 >S1 H1 >G0 bl0 gk0 turn1 cu1 turn1' gr1 bl1 >f2 >f0 gk0' put0 put1 >A0 ku1 ti1 gj1 C >G1 >A1",
    "j00 x0 <gk1 j02 <la1 j01 x1 w00 <tb <gk1' B0 B1 m0 w00' w01 m0' M1 N0 j10 w10 w01' m1 f1 j11 w02 w02' j13 j12 w11 w10' b0 m1' <lu1 w11' w12 w13 d0 u0 f4 w12' f6 w13' U0 c0 b1 kv0 u1 d1 kw0 f3 P0 U1 N1 sk0 Q0 co1 kv1 kw1 ks0 sw0 P1 f5 Q1 E0 gs0 sk1 e0 ls0 V0 sw1 gs0' ks1 md0 g0 D0 Do1 gs1 ls1 n0 gs1' md1 k0 l0 ro1 og0 on0 Eo1 h0 no1 y0 l1 k1 g1 y0' on1 h1 og1 y1 y1'"]
HALF = 1023.5 / 2048
FLAG = 2.0 ** 15
LOW = -2.0 ** 25
HUGE = 1.5 * 2.0 ** 48
EIGHT = 1.5 * 2.0 ** 26
TWO = 1.5 * 2.0 ** 24
UP = 144.0
M = 128
TOP = 4096.0

BF, F32, F16, I32, U16 = "bfloat16", "float32", "float16", "int32", "uint16"
SCRATCH = {}
for _d, _n, _names in (
        (BF, 16 + WX, "x x0"), (I32, W, "rel0"), (I32, 32 + 2 * I, "gn"), (I32, 512, "grd0t nam0t"),
        (BF, 16 * I, "u w"), (F16, 16 * I, "wv"), (F32, 16 * I, "nb"), (F32, 512, "tp"), (F32, 272, "v"), (F32, 1536, "gj"),
        (BF, I, "lim0 gr gm b und dead kw bl ol t8 mq gs0 gs1 gs2 gs3 h0 h1 h2 h3"), (F16, I, "kv k8"), (U16, I, "ku lu"), (I32, I, "ti la"), (I32, 272, "vi"), (I32, 512, "tq"),
        (F32, I, "hp sk sw sq md r2 mo on og"), (U16, 14, "ks ls cu sel"), (F32, 14, "ff a1 a3"), (I32, 14, "fk"),
        (F32, 2, "cnt par rc hk"), (BF, 1, "kc"), (BF, 4, "cb"), (BF, M, "lane"), (F16, M, "csa cs0 cs1"), (I32, 1, "ip c4 c5 c6"), (F32, 1, "tb g16 wc wd wn"),
        (BF, M, "half ek mk rs two c8 ones idb idn idh idk idp bd nbk low tr trn bw bn"), (F16, M, "ch"),
        (F32, M, "onp idf idg idq"), (BF, 144, "zz zv"), (BF, 512, "big"), (BF, 226, "up")):
    for _b in _names.split():
        SCRATCH[_b] = ("sbuf", [128, _n], _d)
PSUM = ("pa0", "pa1", "pe0", "pe1", "pf0", "pf1", "pq0", "pq1")
for _b in PSUM:
    SCRATCH[_b] = ("psum", [128, 512], F32)

SEMAPHORES = ["cv", "ca", "ct", "cg", "sent", "d_x", "d_lim", "d_grd", "d_nam", "d_rel", "d_up", "d_fill", "d_on", "d_og", "d_ol", "d_m0", "d_m1"]
SEMAPHORES += ["arr%d%d" % (_t, _u) for _t in range(RO) for _u in range(2)]
PLAN = []
SEEN = {}


def rank_program(g, core, T, topo):
    rank = T.rank_of(core)
    if rank is None:
        return
    A, F = AluOpType, ActivationFunctionType
    queue = {"v": g.vector, "a": g.scalar, "t": g.tensor, "g": g, "s": g.sync}
    count = {q: 0 for q in queue}
    known = {q: {} for q in queue}
    wrote, seen = {}, {}
    dcount = {}

    def need(q, rec):
        sem, val, snap = rec[1], rec[2], rec[3]
        if known[q].get(sem, 0) < val:
            queue[q].wait_ge(T.sem[sem], val)
            known[q][sem] = val
            for s in snap:
                known[q][s] = max(known[q].get(s, 0), snap[s])

    def waits(q, reads, writes):
        recs = []
        for k in reads:
            if k in wrote:
                recs.append(wrote[k])
            if k in PSUM:
                recs += [r for r in seen.get(k, {}).values() if r[0] != q]
        for k in writes:
            if k in wrote and (wrote[k][0] != q or q != "t"):
                recs.append(wrote[k])
            recs += [r for r in seen.get(k, {}).values() if r[0] != q or q != "t"]
        for r in sorted(recs, key=lambda r: -r[2]):
            need(q, r)

    def note(rec, reads, writes):
        for k in reads:
            seen.setdefault(k, {})[rec[0]] = rec
        for k in writes:
            wrote[k] = rec
            seen[k] = {}

    calls = []

    def op(q, reads, writes, fn):
        writes = writes if isinstance(writes, list) else [writes]

        def issue():
            waits(q, reads, writes)
            ins = fn(queue[q])
            count[q] += 1
            ins.then_inc(T.sem["c" + q], 1)
            snap = dict(known[q])
            snap["c" + q] = count[q]
            note((q, "c" + q, count[q], snap), reads, writes)
        calls.append((q, reads, writes, issue, [], None))

    def load(q, sem, out, in_, reads, writes, whole=(), **kw):
        def issue():
            waits(q, reads, writes)
            queue[q].dma_start(out, in_, **kw).then_inc(T.sem[sem], 16)
            dcount[sem] = dcount.get(sem, 0) + 16
            snap = dict(known[q])
            snap[sem] = dcount[sem]
            note(("dma" + sem, sem, dcount[sem], snap), reads, writes)
            if whole and dcount[sem] % (16 * len(whole)) == 0:
                for k in whole:
                    wrote[k] = wrote[writes[0]]
        calls.append((q, reads, writes, issue, [], sem if whole else None))

    def copy(out, okey, in_, ikeys):
        op("v", ikeys, okey, lambda e: e.tensor_copy(out, in_))

    def ts(out, okey, in_, ikeys, s1, s2, op0, op1=None):
        if op1 is None:
            op("v", ikeys, okey, lambda e: e.tensor_scalar(out, in_, s1, None, op0))
        else:
            op("v", ikeys, okey, lambda e: e.tensor_scalar(out, in_, s1, s2, op0, op1))

    def tt(out, okey, a, b, ikeys, o):
        op("v", ikeys, okey, lambda e: e.tensor_tensor(out, a, b, o))

    def act(out, okey, in_, ikeys, f=F.Copy, **kw):
        op("a", ikeys, okey, lambda e: e.activation(out, in_, f, **kw))

    def mm(bank, a, lkey, rhs, rkeys, start, stop, lhs=None):
        op("t", [lkey] + rkeys, bank, lambda e: e.matmul(T[bank][:, a:a + rhs.shape[1]], T[lkey][:] if lhs is None else lhs, rhs, start, stop))

    def memset(ap, key, val):
        if (key[0] if isinstance(key, list) else key) in GFILL.split():
            op("g", [], key, lambda e: e.iota(ap, [[0, ap.shape[1]]], int(val), 0, allow_small_or_imprecise_dtypes=True))
        else:
            op("v", [], key, lambda e: e.memset(ap, val))

    def fill(name, val):
        memset(T[name][:], name, val)

    def times(name, src, by):
        if name in GFILL.split():
            return select(name, src, [[-1, 128]], A.not_equal, by, 0, 1)
        keys_, by = ([src, by], T[by][:]) if isinstance(by, str) else ([src], by)
        ts(T[name][:], name, T[src][:], keys_, by, None, A.mult)

    def select(name, src, pattern, cmp, fill_, base, mult, rows=128):
        n = T[name].shape[1]
        op("g", [src], name, lambda e: e.affine_select(T[name][0:rows, :], T[src][0:rows, 0:n], pattern, cmp, fill_, base, mult))

    def iota(name, pattern, mult, base=0, okeys=None):
        op("g", [], okeys or name, lambda e: e.iota(T[name][:], pattern, base, mult, allow_small_or_imprecise_dtypes=True))

    H = [16 * n for n in NC] + [I]
    O = [0, H[0], 0]
    wide = [max(b - a for a, b in zip([SL[u]] + JUDGE[u], JUDGE[u])) for u in range(2)]
    xw = T.x[:, 16:16 + WX]
    vs, xs, pa, pe, pf, pq = ["v0", "v1"], ["x0", "x1"], ["pa0", "pa1"], ["pe0", "pe1"], ["pf0", "pf1"], ["pq0", "pq1"]

    def keys(name, u):
        return [name + "0", name + "1"] if u == 2 else [name + str(u)]

    def part(name, u, at=0):
        return T[name][:, at + O[u]:at + O[u] + H[u]]

    def cols(name, u, at=0):
        return T[name][:, at:at + H[u]]

    def xp(u):
        return T.x[:, 16 + 8 * O[u]:16 + 8 * (O[u] + H[u])]

    def own(u):
        return part("v", u, 16 + 16 * u)

    def lanes(name, u, a, b):
        return T[name][:, 16 * O[u] + H[u] * a:16 * O[u] + H[u] * b]

    def entries(name, u, a, b):
        return T[name][:, O[u] + NC[u] * a:O[u] + NC[u] * b]

    def picked(name, u):
        return T[name][:, O[u] + 15:O[u] + H[u]:16]

    def listed(name, u):
        return T[name][:, O[u] // 16:(O[u] + H[u]) // 16]

    def turned(name, u):
        a = (2 * H[0] + 32) * u
        return T[name][:, a:a + 2 * H[u] + 32].indirect(listed("sel", u))

    def pm(bank, lkey, name, u, start, stop):
        mm(bank[u], 0, lkey, own(u) if name == "v" else part(name, u), [name + str(u)], start, stop)

    def cm(bank, lkey, name, u, start, stop):
        mm(bank[u], 0, lkey, cols(name, u), [name], start, stop)

    def masked(bank, name, a, u, start):
        mm(bank[u], 0, "ek", T[name][0:16, a:a + H[u]], [name], start, False, lhs=T.ek[0:16, :])

    def first(name, u):
        return part("gn", u, 16 + I * (name == "nam0"))

    def turn(u, out, src, o, key, pads, okey=None):
        a, n, okey = (2 * H[0] + 32) * u, H[u], okey or out
        op("v", [key], okey + "%d0" % u, lambda q: q.transpose(T[out][:, a:a + n], T[src][:, o + 16:o + 16 + n]))
        op("v", [key] + list(pads), okey + "%d1" % u, lambda q: q.transpose(T[out][:, a + n:a + 2 * n + 32], T[src][:, o:o + n + 32]))

    def guards(u):
        if KD[u] or NI[u]:
            ts(part("ku", u), "ku%d" % u, turned("tq" if NI[u] else "tp", u), ["tp%d0" % u, "tp%d1" % u, "sel%d" % u], 1.0 / 2048, -HALF, A.mult, A.add)
        else:
            ts(part("ku", u), "ku%d" % u, part("ti", u), ["ti%d" % u], 1.0 / 2048, -HALF, A.mult, A.add)

    def diagonal(bank, out, u):
        op("v", [bank, "rs"], out + str(u), lambda e: e.tensor_tensor_scan(part(out, u), cols("rs", u), cols(bank, u), 0.0, A.mult, A.max))

    def fetch(j, t):
        u, a, b = FETCH[j]
        (copy if j in FV[t] else act)(lanes("nb", u, a, b), "nb%d" % j, T.rel0[:, 0:W].indirect(entries("lu", u, a, b)), ["rel0", "lu%d" % u])
        for k in range(a, b):
            c = 16 * O[u] + H[u] * k
            load("s", "d_m%d" % u, T.mo[k::16, O[u]:O[u] + H[u]], T.nb[k::16, c:c + H[u]], ["nb%d" % j], ["mo%d_%d" % (u, k)],
                 ["mo%d_%d" % (u, c) for c in range(16)])

    def double(u, n, m):
        a, ks = 768 * u, ["gj%d%d" % (u, c) for c in range(wide[u])]
        op("g", ks[:m], ks[n:n + m], lambda e: e.affine_select(T.gj[:, a + H[u] * n:a + H[u] * (n + m)], T.gj[:, a:a + H[u] * m],
                                                               [[0, H[u] * m]], A.is_ge, 0.0, 0, 0))

    def copies(name, key, n, u):
        for c in range(n):
            act(cols("gj", u, 768 * u + H[u] * c), "gj%d%d" % (u, c), part(name, u), [key], bias=-510.0)

    def doubled(n, u):
        while n < wide[u]:
            double(u, n, min(n, wide[u] - n))
            n += min(n, wide[u] - n)

    def eights(u, t):
        if t == 0 and " k8 " in START:
            mm(pe[u], 0, "idb", part("k8", u), ["k8"], True, False)
            return cm(pe, "idb", "c8", u, False, False)
        cm(pe, "idb", "ch", u, True, False)
        pm(pe, "idq", "v", u, False, False)
        cm(pe, "idb", "c8", u, False, False)

    def deaths():
        act(T.cb[:, 0:2], "cbp", T.cnt[:], keys("cnt", 2))
        act(T.cb[:, 2:4], "cbn", T.cnt[:], keys("cnt", 2), scale=-1.0)
        for n, (lkey, rhs, key) in enumerate((("ones", T.cb[:, 0:1], "cbp"), ("ones", T.cb[:, 1:2], "cbp"), ("idn", T.half[:, 0:1], "half"),
                                              ("idb", T.kc[:], "kc"), ("idn", T.kc[:], "kc"),
                                              ("ones", T.cb[:, 2:3], "cbn"), ("ones", T.cb[:, 3:4], "cbn"))):
            mm(pq[1], 2 * M, lkey, rhs, [key], n == 0, n == 6)

    def limits_out(u):
        tt(part("ol", u), "ol%d" % u, part("gm", u), cols(pf[u], u), ["gm%d" % u, pf[u]], A.min)
        load("a", "d_ol", part("yl", u), part("ol", u), ["ol%d" % u], ["yl%d" % u])

    def numbers_out(name, src, out, u):
        copy(part(name, u), name + str(u), part(src, u), [src + str(u)])
        load("s", "d_" + name, part(out, u), part(name, u), [name + str(u)], [out + str(u)])

    inputs = {"g": ("s", "d_grd", first("grd0", 2), T.grd[:], [], ["grd0"]), "n": ("s", "d_nam", first("nam0", 2), T.nam[:], [], ["nam0"]),
              "l": ("a", "d_lim", T.lim0[:], T.lim[:], [], ["lim0"]), "x": ("s", "d_x", T.x0[:, 16:16 + WX], T.xc[:], [], ["xc"]),
              "r": ("s", "d_rel", T.rel0[:], T.rel[:], AFTER, ["rel0"])}
    for s in LOADS:
        load(*inputs[s])
    ahead = len(calls)

    iota("ip", [[0, 1]], 17)
    iota("ff", [[32, 14]], 0)
    fill("ones", 1.0)
    select("bd", "ones", [[-16, 8], [0, 16]], A.is_ge, 0.0, 0, 1)
    select("bd", "bd", [[16, 8], [0, 16]], A.is_ge, 0.0, 15, -1)
    select("idb", "ones", [[-1, 128]], A.is_equal, 0.0, 0, 1)
    for key, a in (("pad0a", 0), ("pad0b", 16 + H[0]), ("pad1a", 16 + H[0]), ("pad1b", 32 + I)):
        if key != "pad1a" or NI[0] != NI[1]:
            memset(T["vi" if NI[int(key[3])] else "v"][:, a:a + 16], [key] + ["pad1a"] * (key == "pad0b" and NI[0] == NI[1]), 0)
    ts(T.c5[:], "c5", T.ip[:], ["ip"], 15, None, A.bitwise_and)
    ts(T.c4[:], "c4", T.ip[:], ["ip"], 4, 1, A.arith_shift_right, A.bitwise_and)
    ts(T.c6[:], "c6", T.ip[:], ["ip"], 3, None, A.bitwise_and)
    ts(T.g16[:], "g16", T.c5[:], ["c5"], 16.0, None, A.mult)
    for u in range(2):
        ts(T.rc[:, u:u + 1], "rc%d" % u, T.c5[:], ["c5"], 2.0, 1.0 - NC[u], A.mult, A.add)
        ts(listed("fk", u), "fk%d" % u, T.ff[:, 0:NC[u]], ["ff", "rc%d" % u], T.rc[:, u:u + 1], 0.5 / NC[u], A.add, A.mult)
        ts(T.par[:, u:u + 1], "par%d" % u, T.c4[:], ["c4", "g16"], H[u] + 16.0, T.g16[:], A.mult, A.add)
        ts(listed("a1", u), "a1%d" % u, T.ff[:, 0:NC[u]], ["ff"], 8.0 / (H[u] - 1), None, A.mult)
        tt(listed("a3", u), "a3%d" % u, listed("a1", u), listed("fk", u), ["a1%d" % u, "fk%d" % u], A.subtract)
        ts(listed("sel", u), "sel%d" % u, listed("a3", u), ["a3%d" % u, "par%d" % u], H[u] - 1.0, T.par[:, u:u + 1], A.mult, A.add)
        ts(T.hk[:, u:u + 1], "hk%d" % u, T.c5[:], ["c5"], 8.0 * H[u], None, A.mult)
    ts(T.wc[:], "wc", T.c6[:], ["c6"], 2.0, 1.0, A.mult, A.add)
    ts(T.wd[:], "wd", T.c5[:], ["c5"], 0.5, 3.0 / 128, A.is_lt, A.mult)

    def sums():
        for name, by in (("zz", -17.0), ("zv", -4.0)):
            fill(name, 0.0)
            ts(T[name][:, 15:143:16], name, T.bd[:, 0:128:16], ["bd"], by, None, A.mult)

    def offsets():
        iota("lane", [[0, 8], [1, 16]], 0)
        ts(T.csa[0:1, :], "csa", T.ones[0:1, :], ["ones"], TOP + 4, None, A.mult)
        for u in range(2):
            ts(T["cs%d" % u][0:1, :], "cs%d" % u, T.lane[0:1, :], ["lane"], VL[u] - 0.5, 64 * 511.75, A.is_ge, A.mult)

    def masks():
        select("ek", "ones", [[0, 8], [-1, 16]], A.is_equal, 0.0, 0, 1, 16)
        select("mk", "big", [[0, 8], [-1, 16]], A.not_equal, 0.0, 0, 1, 16)
        iota("t8", [[8, I]], 0)
        select("mq", "t8", [[0, I // 16], [-1, 16]], A.is_equal, LOW, 0, 1, 16)
        select("rs", "ones", [[0, 8], [1, 16]], A.is_gt, 0.0, 0, 0)

    def plain(name, src, u):
        turn(u, src + "t", "gn", I * (src == "nam0") + O[u], src, [{"grd0": ["gna", "nam0"], "nam0": ["grd0", "gnb"]}[src][u]])
        copy(part(name, u), name + str(u), turned(src + "t", u), [src + "t%d0" % u, src + "t%d1" % u, "sel%d" % u])

    def raised():
        memset(T.x0[:, 0:16], "xz", 0.0)
        for u in range(2):
            a, b = (16 + 8 * O[u]) * u, 16 + 8 * (O[u] + H[u])
            act(T.x[:, a:b], xs[u], T.x0[:, a:b], ["xc", "xz"], bias=UP)

    def unit(name, by, e):
        if e == "g":
            select(name, "idf", [[-1, 128]], A.not_equal, by, 0, 1)
        else:
            act(T[name][:], name, T.idb[:], ["idb"], scale=by)

    def level(name, val, e):
        if e == "g":
            iota(name, [[0, 128]], 0, val)
        else:
            act(T[name][:], name, T.ones[:], ["ones"], scale=float(val))

    constants = {
        "zz": sums, "cst": offsets, "xg": raised, "mk": masks,
        "half": lambda: act(T.half[:], "half", T.ones[:], ["ones"], F.Sigmoid, scale=0.0),
        "idf": lambda: select("idf", "onp", [[-1, 128]], A.is_equal, 0.0, 0, 1) if CE[0] == "g" else unit("idf", 1.0, "a"),
        "idg": lambda: unit("idg", -1.0, CE[1]), "idq": lambda: unit("idq", 1.0 / 256, CE[2]),
        "onp": lambda: level("onp", 1, CE[3]), "rel": lambda: load(*inputs["r"]), "nam": lambda: load(*inputs["n"]),
        "nbk": lambda: times("nbk", "bd", -2 * FLAG),
        "tr": lambda: (select("low", "nbk", [[1, 128]], A.is_gt, 0.0, 0, -1), select("tr", "low", [[-1, 128]], A.not_equal, 2 * FLAG, 0, 1),
                       times("trn", "tr", -1.0)),
        "th": lambda: memset(T.tb[:], "tb", TB * (TOP - 88)),
        "ids": lambda: [times(name, "idb", by) for name, by in (("idn", -1.0), ("idh", HUGE), ("idk", -HUGE), ("idp", -LOW))
                        if name in ("idn", "idk") or (name == "idh" and " e" in ROUND) or (name == "idp" and " co" in ROUND)],
        "big": lambda: fill("big", LOW),
        "cc": lambda: (fill("two", 2.0), times("ch", "ones", -8 * HALF)),
        "bw": lambda: (tt(T.wn[:], "wn", T.wd[:], T.wc[:], ["wd", "wc"], A.subtract), times("bw", "bd", "wc"), times("bn", "bd", "wn")),
        "c8": lambda: (fill("c8", EIGHT), fill("kc", TWO)),
        "k8": lambda: ts(T.k8[:], "k8", first("grd0", 2), ["grd0"], 8.0, None, A.mult),
        "va": lambda: ts(cols(pq[0], 2), pq[0], first("grd0", 2), ["grd0"], 2048.0, None, A.mult),
        "vb": lambda: [tt(own(u), vs[u], part(pq[0], u), first("nam0", u), [pq[0], "nam0"], A.add) for u in range(2)],
        "pads": lambda: [memset(T.gn[:, a:a + 16], key, 0) for a, key in ((0, "gna"), (16 + 2 * I, "gnb"))],
        "ka": lambda: plain("ku", "grd0", 0), "kb": lambda: plain("ku", "grd0", 1),
        "na": lambda: plain("lu", "nam0", 0), "nb": lambda: plain("lu", "nam0", 1),
        "lima": lambda: (copies("lim0", "lim0", OWN0[0], 0), doubled(OWN0[0], 0)),
        "limb": lambda: (copies("lim0", "lim0", OWN0[1], 1), doubled(OWN0[1], 1)),
        "C": deaths, "tb": lambda: act(T.tb[:], "tb", T[pq[1]][:, 2 * M:2 * M + 1], [pq[1]], scale=16.0 * TB, bias=TB * (TOP - 88)),
    }

    def steps(t):
        last = t == RO - 1
        x, xk, gr, gk = (T.x0, ["xc"], "lim0", ["lim0", "lim0"]) if t == 0 else (T.x, xs, "gr", keys("gr", 2))
        xj = x[:, 16:16 + WX]
        h, gs = "h%d" % t, "gs%d" % t
        done = {"j0": 0, "j1": 0, "w0": 0, "w1": 0, "k0": 0, "k1": 0}

        def piece(s, u):
            j = done[s + str(u)]
            done[s + str(u)] = j + 1
            return ([SL[u]] + JUDGE[u])[j], JUDGE[u][j], "%d%d" % (u, j)

        def judge(u):
            a, b, key = piece("j", u)
            tt(lanes("u", u, a, b), "u" + key, xj.indirect(entries("ku", u, a, b)), T.gj[:, 768 * u:768 * u + H[u] * (b - a)],
               xk + ["ku%d" % u] + ["gj%d%d" % (u, c) for c in range(b - a)], A.subtract)

        def mark(u):
            a, b, key = piece("w", u)
            if a < VL[u]:
                w, z = "w", "zz"
                act(lanes(w, u, a, b), "w" + key, lanes("u", u, a, b), ["u" + key, "half"], F.Sigmoid, scale=8.0, bias=-8.0 * 512 - math.log(16.0))
            else:
                w, z = "wv", "zv"
                ts(lanes(w, u, a, b), "w" + key, lanes("u", u, a, b), ["u" + key], 511.75, 516.0, A.max, A.min)
            rows(w, z, u, a, b, key)

        def rows(w, z, u, a, b, key):
            def add(e, k):
                done["k%d" % u] += 1
                return e.matmul(cols(pa[u], u), T[z][:, 15 - k:143 - k], lanes(w, u, k, k + 1), False, done["k%d" % u] == 16)
            for k in range(a, b):
                op("t", [z, "w" + key], pa[u], lambda e, k=k: add(e, k))

        def less(u):
            for k in range(SL[u]):
                mm(pf[u], H[u] * k, "idn", part(gr, u), [gk[u]], k == 0, False)

        def take(u, a, b):
            act(lanes("u", u, a, b), "us%d%d" % (u, a), xj.indirect(entries("ku", u, a, b)), xk + ["ku%d" % u], bias=-2.0)

        def cells(u, a, b):
            n = (b - a) * H[u]
            mm(pf[u], a * H[u], "idb", lanes("u", u, a, b), ["us%d%d" % (u, a)], False, False)
            mm(pf[u], a * H[u], "idn", T.big[:, 0:n], ["big"], False, False)
            mm(pf[u], a * H[u], "idb", T.big[:, 0:n], ["big"], False, b == SL[u])

        def marks(u):
            act(lanes("w", u, 0, SL[u]), "ws%d" % u, T[pf[u]][:, 0:SL[u] * H[u]], [pf[u], "half"], F.Sigmoid, scale=8.0, bias=-math.log(16.0))
            rows("w", "zz", u, 0, SL[u], "s%d" % u)

        def send(u):
            tt(part(gs, u), gs + str(u), x[:].indirect(listed("ks", u)), part(gr, u), xk + ["xz", "ks%d" % u, gk[u]], A.max)
            dst = T.cores[(rank + 1 + t % 7) % 8]
            src = T.cores[(rank - 1 - t % 7) % 8]
            eng = topo.engines(core, dst)[:8]
            rid, pid = topo.addr(dst, core)

            def issue():
                waits("g", [gs + str(u)], [])
                g.remote_dma(part(h, u), part(gs, u), T.sem["arr%d%d" % (t, u)], T.sem.sent, pid, rid, sum(1 << e for e in eng))
                wrote[h + str(u)] = ("remote", "arr%d%d" % (t, u), len(topo.engines(src, core)[:8]), {})
            calls.append(("g", [gs + str(u)], [h + str(u)], issue, [], None))

        def land(u):
            pm(pf, "bn", h, u, False, False)
            if t == 0:
                cm(pf, "idb", "c8", u, False, False)
            cm(pf, "idn", "c8", u, False, False)
            pm(pf, "bw", h, u, False, True)

        def ready(u):
            masked(pf, "mq", O[u], u, True)
            for name in ("two", "half", "half", "half") if t == 0 else ("c8",):
                cm(pf, "idb", name, u, False, False)

        def above(u):
            for n, (lkey, name) in enumerate((("idb", "two"), ("bw", "two"), ("bd", "half"), ("bd", "half"))[:4 if t == 0 else 1]):
                cm(pe, lkey, name, u, n == 0, False)

        def lower(u):
            if t == 0:
                act(*one("gm", u), part(gs, u), [gs + str(u)], bias=UP)
            name = "gm" if t == 0 else gs
            tt(*one("gr", u), part(name, u), cols(pe[u], u), [name + str(u), pe[u]], A.min)

        def new(u):
            return (part("vi", u, 16 + 16 * u), "vi%d" % u) if last or NI[u] else (own(u), vs[u])

        def one(name, u):
            return part(name, u), name + str(u)

        return {
            "j": judge, "w": mark, "f": lambda j: fetch(j, t), "A": less, "m": marks, "gs": send, "land": land,
            "turn": lambda u: turn(u, "tq" if NI[u] else "tp", "vi" if NI[u] else "v", O[u] + 16 * u, "vi%d" % u if NI[u] else vs[u],
                                   ["pad%d%s" % (u, c) for c in "ab"], "tp"), "ku": guards,
            "nf": lambda u: tt(own(u), vs[u], part(("md", "r2")[u], u), cols((pa, pq)[u][u], u), [("md", "r2")[u] + str(u), (pa, pq)[u][u]], A.max),
            "G": lambda u: eights(u, t),
            "x": lambda u: take(u, 0, SX[u]), "B": lambda u: cells(u, 0, SX[u]),
            "X": lambda u: take(u, SX[u], SL[u]), "Y": lambda u: cells(u, SX[u], SL[u]),
            "S": lambda u: [mm(pa[u], 0, a, T[b][0:1, 0:H[u]], [b], a == "csa", False, lhs=T[a][0:1, :])
                            for a, b in (("csa", "ones"), ("ones", "half"), ("cs%d" % u, "ones"))],
            "b": lambda u: ts(*one("b", u), cols(pa[u], u), [pa[u]], 3.75, None, A.add),
            "u": lambda u: tt(*one("und", u), cols(pa[u], u), part("b", u), [pa[u], "b%d" % u], A.is_lt),
            "d": lambda u: act(part("dead", u), ["dead%d" % u, "cnt%d" % u], part("b", u), ["b%d" % u, "tb"], F.Sigmoid, scale=-32.0,
                               bias=T.tb[:], accum_out=T.cnt[:, u:u + 1]),
            "dv": lambda u: ts(*one("dead", u), part("b", u), ["b%d" % u, "tb"], T.tb[:], None, A.is_lt),
            "dc": lambda u: act(part("kw", u), ["kw%d" % u, "cnt%d" % u], part("dead", u), ["dead%d" % u], accum_out=T.cnt[:, u:u + 1]),
            "U": lambda u: (pm(pe, "tr", "und", u, False, False), pm(pe, "trn", "dead", u, False, True)),
            "kv": lambda u: ts(*one("kv", u), cols(pe[u], u), [pe[u]], 128 - 2 * FLAG - EIGHT, 0.0, A.add, A.max),
            "kw": lambda u: ts(*one("kw", u), cols(pe[u], u), [pe[u], "hk%d" % u], FLAG + EIGHT, T.hk[:, u:u + 1], A.is_ge, A.mult),
            "M": lambda u: masked(pq, "mk", 0, u, True), "P": lambda u: pm(pq, "bd", "kv", u, False, True),
            "N": lambda u: masked(pf, "mq", O[u], u, True), "Q": lambda u: pm(pf, "bd", "kw", u, False, True),
            "sk": lambda u: diagonal(pq[u], "sk", u), "sw": lambda u: diagonal(pf[u], "sw", u), "sq": lambda u: diagonal(pf[u], "sq", u),
            "ks": lambda u: ts(listed("ks", u), "ks%d" % u, picked("sk", u), ["sk%d" % u], 1.0 / 8, None, A.mult),
            "ls": lambda u: ts(listed("ls", u), "ls%d" % u, picked("sw", u), ["sw%d" % u], 1.0 / 8, -1.0 * O[u], A.mult, A.add),
            "md": lambda u: tt(*one("md", u), lanes("nb", u, 0, 16).indirect(listed("ls", u)), part("dead", u),
                               ["nb%d" % j for j in range(len(FETCH)) if FETCH[j][0] == u] + ["ls%d" % u, "dead%d" % u], A.mult),
            "c": lambda u: pm(pa, "idg", "v", u, True, False),
            "E": lambda u: mm(pa[u], 0, "idf", part("mo", u), ["mo%d_%d" % (u, k) for k in range(16)], False, False),
            "e": lambda u: (pm(pa, "idh", "und", u, False, False), pm(pa, "idk", "und", u, False, False)),
            "V": lambda u: pm(pa, "idf", "v", u, False, False), "D": lambda u: pm(pa, "idk", "dead", u, False, True),
            "n": lambda u: tt(*new(u), part("md", u), cols(pa[u], u), ["md%d" % u, pa[u]], A.max),
            "Do": lambda u: pm(pq, "idk", "und", u, True, False),
            "Eo": lambda u: mm(pq[u], 0, "idf", part("mo", u), ["mo%d_%d" % (u, k) for k in range(16)], False, True),
            "co": lambda u: (cm(pa, "idb", "big", u, True, False), pm(pa, "idp", "und", u, False, False), pm(pa, "idk", "dead", u, False, False),
                             pm(pa, "idf", "v", u, False, True)),
            "ro": lambda u: tt(*one("r2", u), part("md", u), cols(pa[u], u), ["md%d" % u, pa[u]], A.max),
            "no": lambda u: tt(*new(u), part("r2", u), cols(pq[u], u), ["r2%d" % u, pq[u]], A.max),
            "ti": lambda u: copy(*one("ti", u), turned("tp", u), ["tp%d0" % u, "tp%d1" % u, "sel%d" % u]),
            "la": lambda u: (ts(*one("la", u), turned("tq", u), ["tp%d0" % u, "tp%d1" % u, "sel%d" % u], 2047, None, A.bitwise_and) if NI[u] else
                             ts(*one("la", u), part("ti", u), ["ti%d" % u], 2047, None, A.bitwise_and)),
            "lu": lambda u: copy(*one("lu", u), part("la", u), ["la%d" % u]),
            "R": ready, "T": above, "gr": lower,
            "cu": lambda u: ts(listed("cu", u), "cu%d" % u, picked("sq", u), ["sq%d" % u], -8.0 * O[u], None, A.add),
            "hp": lambda u: act(*one("hp", u), part(h, u), [h + str(u)], bias=UP * (t == 0) - 0.5),
            "bl": lambda u: tt(*one("bl", u), xp(u).indirect(listed("cu", u)), part("hp", u), [xs[u], "cu%d" % u, "hp%d" % u], A.add),
            "put": lambda u: tt(xp(u).indirect(listed("cu", u)), xs[u], part("bl", u), cols("half", u), ["bl%d" % u, "cu%d" % u, "half"], A.mult),
            "H": lambda u: pm(pe, "idb", h, u, False, True),
            "gj": lambda u: copies("gr", "gr%d" % u, OWN[u], u), "gk": lambda u: doubled(OWN[u], u),
            "g": lambda u: act(cols(pf[u], u), pf[u], part(gs, u), [gs + str(u)], bias=-UP),
            "h": lambda u: ts(*one("gm", u), part(h, u), [h + str(u)], 2.0 - UP, None, A.add), "y": limits_out,
            "k": lambda u: ts(*one("ti", u), new(u)[0], ["vi%d" % u], 11, None, A.arith_shift_right),
            "l": lambda u: ts(*one("la", u), new(u)[0], ["vi%d" % u], 2047, None, A.bitwise_and),
            "og": lambda u: numbers_out("og", "ti", "yg", u), "on": lambda u: numbers_out("on", "la", "yn", u),
        }

    rounds = [steps(t) for t in range(RO)]
    tags = {}
    for n in range(ahead, len(calls)):
        s = "." + calls[n][2][0]
        tags[(0, s + "x" if (0, s) in tags else s)] = [n]
    for t in range(RO):
        for s in ((START + " ") * (t == 0) + ROUND + " " + (END if t == RO - 1 else BLEND)).split():
            u = int(s[1:] == "1")
            both = [c + s[1:] + str(j) for j in range(len(JUDGE[u])) for c in "jw"]
            more = {"J": both[:2 * MP[u]] + [c + s[1:] for c in "AxB" + "XY" * (SX[u] < SL[u]) + "m"] + both[2 * MP[u]:],
                    "F": ["f%d" % j for j in range(len(FETCH)) if str(FETCH[j][0]) == s[1:]]}
            for s in more.get(s[0], [s]):
                n = len(calls)
                if s in constants:
                    constants[s]()
                elif s[0] in "jw":
                    rounds[t][s[0]](int(s[1]))
                else:
                    rounds[t][s[:-1]](int(s[-1]))
                for i in range(n, len(calls)):
                    if i > n and (calls[i][0] == "s" or calls[i][0] == calls[i - 1][0] == "t"):
                        tags[(t, s)].append(i)
                    else:
                        s += "'" * (i > n)
                        tags[(t, s)] = [i]
    SEEN.update(calls=calls, tags=tags, ahead=ahead)
    if PLAN[:1] == [None]:
        PLAN[:] = range(len(calls))
    if not PLAN:
        PLAN.extend(range(ahead))
        for t in range(RO):
            for s in ORDERS[t].split():
                PLAN.extend(tags[(t + {"<": -1, ">": 1}.get(s[0], 0), s.lstrip("<>"))])
    for n in PLAN:
        calls[n][3]()
    g.wait_ge(T.sem.sent, 2 * sum(len(topo.engines(core, T.cores[(rank + 1 + t % 7) % 8])[:8]) for t in range(RO)))
    for q in ("v", "a", "t", "g"):
        if known["g"].get("c" + q, 0) < count[q]:
            g.wait_ge(T.sem["c" + q], count[q])
    for s in ("d_on", "d_og", "d_ol"):
        if known["g"].get(s, 0) < dcount.get(s, 0):
            g.wait_ge(T.sem[s], dcount[s])
